import numpy as np, ml_dtypes
CORES = [13,21,141,149]
N = 4
BF = ml_dtypes.bfloat16
P, CAP, J, W, D, RO = 512, 128, 8, 4096, 3, 8
WT = np.array([1, 3, 7, 13, 21, 35, 49, 67, 85, 107, 129, 155, 181, 211, 241, 253], np.int32)
KA = np.array([17, 101, 263, 389, 547, 701, 859, 1021], np.int32)
def mark(s):
    return np.add.reduce(s * WT[:, None], axis=-2) & 4095
def columns(u, e):
    return ((u * u >> 4)[..., None, :] + KA[:, None] * u[..., None, :] + 811 * e) & (W - 1)
def lanes(rng, v, k):
    return np.minimum((rng.random((N, 8, 16, k), dtype=np.float32) * (v + 1)[:, None, None]).astype(np.int32), v[:, None, None])
def toward(s, r):
    z = np.array(s); z[0] = (s[0] & (64 - N)) + ((s[0] + r - mark(s)) & (N - 1))
    return z
def pack(o, s, c):
    return {"opr": np.ascontiguousarray(o.reshape(N, 128, W)).astype(np.float32).astype(BF), "s0": np.ascontiguousarray(s.reshape(N, 128, P)).astype(np.float32).astype(BF),
            "f0": np.ascontiguousarray(c).astype(np.int32)}
def setup_inputs(rng):
    t = rng.permutation(8); v = np.full(8, 63); v[t[0]] = rng.choice(np.array([1, 3])); v[t[1]] = 15
    span = rng.choice(np.array([40, 100, 200, 400]), (8, 1)); span[t[0]] = 1
    c = (rng.random((N, 8, P)) * (span + 1)).astype(np.int64)
    c = np.where(rng.random((N, 8, P)) < rng.choice(np.array([0.0, 0.1, 0.3]), (N, 8, 1)), 1023, c)
    return pack(lanes(rng, v, W), lanes(rng, v, P), c)
def setup_inputs_spread(rng):
    o = np.minimum((np.exp2(6 * rng.random((N, 8, 1, W))) * rng.random((N, 8, 16, W))).astype(np.int64), 63)
    s = np.minimum((np.exp2(6 * rng.random((N, 8, 1, P))) * rng.random((N, 8, 16, P))).astype(np.int64), 63)
    c = np.minimum(np.exp2(10 * rng.random((N, 8, P))).astype(np.int64) - 1, 1022)
    return pack(o, s, np.where(rng.random((N, 8, P)) < 0.125, 1023, c))
def setup_inputs_ends(rng):
    o = 63 * rng.integers(0, 2, (N, 8, 16, W)); s = 63 * rng.integers(0, 2, (N, 8, 16, P))
    share = rng.permutation(np.array([1.0, 1.0, 1.0, 0.9, 0.7, 0.5, 0.3, 0.1]))
    c = np.where(rng.random((N, 8, P)) < share[:, None], 0, 1023)
    m = 63 * ((np.arange(65536)[:, None] >> np.arange(16)) & 1)
    u = np.arange(4096); free = np.zeros((4096, 16), np.int64)
    free[:, 15] = u // 253; free[:, 4] = (u % 253) // 21; free[:, 0] = (u % 253) % 21
    every = columns(mark(free.T), 0)
    for k, x in ((P - 3, int(np.max(every))), (P // 2, int(np.min(every)))):
        for b in (m, free):
            z = np.nonzero(np.any(columns(mark(b.T), 0) == x, axis=0))[0]
            if len(z):
                s[:, :, :, k] = b[rng.choice(z, (N, 8))]; c[:, :, k] = 0
                break
    s[..., [0, 1, P - 2, P - 1]] = 63; c[..., [0, P - 1]] = 0; c[..., [1, P - 2]] = 1023
    a = columns(mark(np.full((16, 1), 63)), 0)[:, 0]
    o[..., a[0]] = 0; o[..., a[J - 1]] = 63
    return pack(o, s, c)
def setup_inputs_corners(rng):
    t = rng.permutation(8); v = np.full(8, 63); v[t[6]] = 1; v[t[7]] = 7
    o = lanes(rng, v, W); s = lanes(rng, v, P); c = np.full((N, 8, P), 1023); n = CAP // J; big = int(rng.integers(0, N))
    o[:, t[7]] = 0; c[:, t[0]] = 0; c[N - 1, t[2], P - 1] = 0
    c[:, t[6]] = rng.integers(1012, 1024, (N, P)); c[:, t[7]] = rng.integers(0, 101, (N, P))
    a = columns(mark(np.full((16, 1), 63)), 0)[:, 0]
    for q in range(N):
        for k in (3, 4, 5):
            g = int(t[k]); x = rng.integers(0, 16, 16); x[0] = 0
            x[0] = (q + 1 - int(mark(x[:, None])[0])) & (N - 1)
            o[q, g][:, a] = (63 - x)[:, None]; b = 300 - (int(np.add.reduce(x)) >> 2)
            if k == 5: c[q, g] = np.where(rng.random(P) < 0.5, rng.integers(400, 700, P), 1023)
            w = n + k - 3 if k < 5 else n + 1 if q == big else int(rng.integers(0, n + 1))
            p = np.append(P - 1, rng.permutation(P - 1))[:w]
            s[q, g][:, p] = 63; c[q, g, p] = b
            if k == 4: c[q, g, p[-1]] = b + 1
    return pack(o, s, c)
def setup_inputs_edges(rng):
    t = [int(k) for k in rng.permutation(8)]; v = np.full(8, 63); v[t[7]] = 15
    n = CAP // J; r = int(rng.integers(0, N)); big = int(rng.integers(0, N)); top = int(rng.integers(520, 1001))
    o = lanes(rng, v, W); s = lanes(rng, v, P)
    c = (rng.random((N, 8, P)) * rng.choice(np.array([41, 101, 201]), (8, 1))).astype(np.int64)
    c = np.where(rng.random((N, 8, P)) < 0.1, 1023, c)
    o[:, t[:3]] = 0; c[:, t[0]] = rng.integers(1, 201, (N, P)); c[:, t[1:5]] = 1023
    for q in range(N):
        for k in range(3):
            w = n if k == 1 else n + (k == 0) if q == big else int(rng.integers(0, n + 1))
            p = np.append(P - 1, rng.permutation(P - 1))[:w]
            z = toward(s[q, t[k]][:, p], r)
            if k == 0: z = 0 * z
            s[q, t[k]][:, p] = z; h = np.add.reduce(z, axis=0) >> 2
            if k == 0: c[q, t[k], p] = 0
            elif k == 1: c[q, t[k], p] = top + np.arange(q * n, q * n + n) * 8 // (N * n) - 2 * h
            else: c[q, t[k], p] = 1022 - 2 * h
    for k in (3, 4):
        x = t[k]; z = rng.integers(1, 8, 16); z[0] += (2 - int(mark(z[:, None])[0])) & 3
        h = int(np.add.reduce(z)) >> 2; o[:, x] = rng.integers(56, 64, (N, 16, W))
        for e in range(D): o[:, x, :, int(columns(mark(z[:, None]), e)[0, 0])] = 0
        q = rng.permutation(N); a = int(q[0]); p = np.append(P - 1, rng.permutation(P - 1))[:CAP + 1]
        if k == 3: b = int(q[1]); low = 1022 - 3 * h; more = 1
        else: b = a; low = int(rng.integers(850, 911)); more = h
        s[a, x][:, p[1:]] = z[:, None]; c[a, x, p[1:]] = low + more
        s[b, x, :, P - 1] = z; c[b, x, P - 1] = low
    return pack(o, s, c)
def setup_inputs_ties(rng):
    v = rng.permutation(np.array([1, 1, 3, 3, 7, 15, 31, 63])); o = lanes(rng, v, W); s = lanes(rng, v, P)
    c = rng.choice(np.array([0, 5, 9]), (1, 8, 1)) + rng.integers(0, 2, (N, 8, P)) * rng.choice(np.array([0, 1, 3]), (1, 8, 1))
    s[:, 1::2, :, P // 2:] = s[:, 1::2, :, :P // 2]
    c = np.where(rng.random((N, 8, P)) < 0.05, 1023, c)
    x = int(np.nonzero(v == 1)[0][0]); y = int(np.nonzero(v == 3)[0][0])
    o[:, x] = 0; c[:, x] = 1023
    s[:, x] = rng.integers(0, 64, (N, 16, P)); s[:, x, 0] = np.maximum(s[:, x, 0], 4)
    for q in range(N):
        p = np.append(P - 1, rng.permutation(P - 1))[:CAP // J]
        a = np.add.reduce(s[q, x][:, p], axis=0) >> 2
        c[q, x, p] = 1022 - a - rng.integers(0, a)
    z = rng.integers(1, 8, 16); z[0] += (2 - int(mark(z[:, None])[0])) & 3
    a = int(np.add.reduce(z)) >> 2; b = int(rng.integers(850, 931))
    o[:, y] = rng.integers(56, 64, (N, 16, W)); c[:, y] = 1023
    for e in range(D): o[:, y, :, int(columns(mark(z[:, None]), e)[0, 0])] = 0
    q = rng.permutation(N); p = rng.permutation(P)[:CAP]
    s[int(q[0]), y][:, p] = z[:, None]; c[int(q[0]), y, p] = b + a
    s[int(q[1]), y, :, P - 1] = z; c[int(q[1]), y, P - 1] = b
    return pack(o, s, c)
def check_inputs(d):
    bad = []
    for k, lo, hi in (("opr", 0, 63), ("s0", 0, 63), ("f0", 0, 1023)):
        x = np.asarray(d[k]).astype(np.float64)
        if not (np.min(x) >= lo and np.max(x) <= hi): bad.append("range of " + k)
        elif np.any(x != np.floor(x)): bad.append("whole numbers of " + k)
    return bad
def reference(opr, s0, f0):
    o = opr.astype(np.float32).astype(np.int32).reshape(N, 8, 16, W); gi = np.arange(8)
    S = np.zeros((N, 8, D + 1, 16, P), np.int32); F = np.full((N, 8, D + 1, P), 1023, np.int32)
    S[:, :, 0] = s0.astype(np.float32).astype(np.int32).reshape(N, 8, 16, P); F[:, :, 0] = f0
    lo = np.zeros((8, D), np.int32); hi = np.zeros((8, D), np.int32); U = np.full(8, 1023, np.int32); lev = np.zeros(8, np.int32)
    for rnd in range(RO):
        s = S[:, gi, lev]; f = F[:, gi, lev]; low = lo[gi, lev][:, None]
        h = columns(mark(s), lev[:, None, None]).reshape(N, 8, 1, J * P)
        c = np.abs(np.tile(s, (1, 1, 1, J)) - np.take_along_axis(o, h.astype(np.int64), axis=3))
        fc = np.tile(f, (1, 1, J)) + (np.add.reduce(c, axis=2) >> 2); own = mark(c) & (N - 1)
        B = np.full(8, 1023, np.int32)
        for a in range(N):
            x = np.partition(np.where((fc >= low) & (own == a), fc, 4000), CAP, axis=2)[:, :, CAP]
            B = np.minimum(B, np.min(x, axis=0))
        keep = (fc >= low) & (fc < B[:, None])
        m = np.min(np.where(keep, fc, 4000), axis=(0, 2))
        ns = np.zeros((N, 8, 16, P), np.int32); nf = np.full((N, 8, P), 1023, np.int32)
        for a in range(N):
            k = keep & (own == a); place = np.add.accumulate(k, axis=2, dtype=np.int64) - 1
            qi, ji, ci = np.nonzero(k); t = qi * CAP + place[qi, ji, ci]
            ns[a, ji, :, t] = c[qi, ji, :, ci]; nf[a, ji, t] = fc[qi, ji, ci]
        S[:, gi, lev + 1] = ns; F[:, gi, lev + 1] = nf; hi[gi, lev] = B
        U = np.where(lev == D - 1, np.minimum(U, m), U)
        for g in range(8):
            e = int(lev[g])
            if e == D - 1 or m[g] >= U[g]:
                lo[g, e] = max(int(B[g]), int(lo[g, e]) + 1)
                if lo[g, e] >= U[g] and e > 0:
                    lo[g, e] = 0; e -= 1; lo[g, e] = max(int(hi[g, e]), int(lo[g, e]) + 1)
            else:
                e += 1; lo[g, e] = 0
            lev[g] = e
    yl = np.ascontiguousarray(S[:, :, 1:].transpose(0, 1, 3, 2, 4)).reshape(N, 128, D * P)
    yt = np.concatenate([lo, hi, lev[:, None], U[:, None]], axis=1)
    return {"yl": yl.astype(np.float32).astype(BF), "yf": np.ascontiguousarray(F[:, :, 1:]).reshape(N, 8, D * P).astype(np.float32), "yt": np.stack([yt] * N).astype(np.float32)}

@@ -1,0 +1,675 @@
+from concourse.bass import DstId, RemoteDMATransfer
+from concourse.mybir import AluOpType as O, AxisListType, ActivationFunctionType as F
+
+NR = 8
+SL = 576
+EMPTY = 9
+WT = [1, 3, 7, 13, 21, 35, 49, 67, 85, 107, 129, 155, 181, 211, 241, 253]
+KA = [17, 101, 263, 389, 547, 701, 859, 1021]
+MAGIC = float(3 << 22)
+
+_f, _b, _h, _i, _u = "float32", "bfloat16", "float16", "int32", "uint16"
+PSUM = ("PU", "PX", "PN", "PC0", "PC1", "PEA", "PEB", "PL")
+SCRATCH = {}
+for _n, _w, _d in (
+        ("A", 10 * SL, _b), ("OPW", 4096, _b), ("SND", NR * SL, _b), ("MB", NR * 16, _f), ("S", 512, _b), ("FS", 128, _b), ("D", 4096, _b),
+        ("GA", 1024, _b), ("CH", 4112, _b), ("OFA", 40, _u), ("OFO", 256, _u), ("OFB", 32, _u), ("OFW", 32, _u), ("OFV", 16, _u),
+        ("OFC", 32, _u), ("OFN", 32, _u), ("UI", 32, _i), ("UU", 32, _i), ("UF", 32, _f), ("USQ", 32, _i), ("BB", 32, _i),
+        ("TJ", 256, _f), ("VJ", 256, _i), ("VK", 256, _i), ("XI", 256, _i), ("Y", 256, _i), ("OW", 256, _i), ("OW3", 256, _f), ("OW4", 256, _f),
+        ("Z", 256, _f), ("YW", 272, _f), ("X", 768, _f), ("XH", 1024, _h), ("DA", 512, _b), ("DV", 512, _b), ("KP", 1024, _b), ("R", 1024, _b),
+        ("W", 1088, _b), ("IA", 1536, _b), ("IB", 512, _b), ("OH", 1536, _b), ("CG", 1536, _h), ("EBW", 128, _b), ("AB", 96, _b), ("CB", 32, _b),
+        ("EM", 96, _f), ("EA", 12, _f), ("T8", 64, _f), ("P8", 64, _f), ("TT", 4, _f), ("TLO", 4, _f), ("THI", 4, _f), ("CN", 4, _f), ("QN", 4, _f),
+        ("SV", 64, _f), ("SW", 64, _f), ("MD", 16, _f),
+        ("ONE", 256, _b), ("ZERO", 256, _b), ("BLK", 128, _b), ("BLKF", 128, _f), ("NBF", 128, _f), ("NB", 128, _b), ("CQ", 2, _b), ("CA", 2, _b),
+        ("NUT", 128, _b), ("ID", 128, _b), ("IDN", 128, _b), ("IDF", 128, _b), ("ID16", 128, _b), ("S1", 144, _b), ("SD", 144, _b), ("SE", 144, _b),
+        ("S32", 144, _h), ("WM", 144, _b), ("XB", 144, _h), ("K", 512, _b), ("K1", 512, _b), ("CL", 40, _f), ("O32", 32, _b), ("O272", 32, _b),
+        ("DM", 64, _f), ("LM", 16, _f), ("WR", 16, _f), ("W2", 16, _f), ("LC", 16, _f), ("LI", 8, _i), ("BO", 4, _f), ("E8C", 4, _f),
+        ("G8", 8, _h), ("G8F", 8, _f),
+        ("S3", 3072, _b), ("FF", 384, _b), ("F3", 96, _f), ("KP3", 96, _b), ("R3", 96, _b), ("RM", 96, _b), ("W3", 96, _b),
+        ("OF3", 96, _u), ("OG3", 120, _u), ("OP3", 96, _u), ("B8C", 96, _b), ("B256", 96, _b), ("DM3", 96, _f), ("YL", 1536, _b), ("YT", 8, _f)):
+    SCRATCH[_n] = ("sbuf", [128, _w], _d)
+for _n, _w, _d in (("B8", 144, _h), ("F8I", 512, _i), ("F8", 512, _h), ("YF", 1536, _f), ("YT8", 8, _f)):
+    SCRATCH[_n] = ("sbuf", [8, _w], _d)
+for _n in PSUM:
+    SCRATCH[_n] = ("psum", [128, 512], _f)
+SEMAPHORES = (["sV", "sS", "sT", "sG", "ls"] + ["%s%d" % (s, r) for s in "ab" for r in range(NR)]
+              + ["l%d" % k for k in range(9)] + ["o%d" % k for k in range(5)])
+
+
+def ways(core, T, topo):
+    hop, used = {}, []
+    for d in T.cores:
+        if d == core:
+            continue
+        if topo.may_write(core, d):
+            hop[d] = d
+        else:
+            c = [x for x in topo.cores_of(core) if x != core and x not in used and topo.die(x) == topo.die(core) and topo.may_write(x, d)]
+            hop[d] = c[0]
+            used.append(c[0])
+    return hop
+
+
+def bits(es):
+    m = 0
+    for e in es:
+        m |= 1 << e
+    return m
+
+
+def hop_engines(core, hop, topo, s):
+    far = [d for d in hop if hop[d] != d]
+    res = {d: topo.engines(core, d) for d in hop if hop[d] == d}
+    used = [] if s == "a" else [e for d in res for e in res[d]]
+    for k, d in enumerate(far):
+        rest = [e for e in topo.engines(core, hop[d]) if e not in used]
+        n = len(rest) // len(far)
+        res[d] = rest[k * n:(k + 1) * n]
+    return res
+
+
+def relay(g, core, T, topo):
+    local = 0
+    for q, rk in enumerate(T.cores):
+        hop = ways(rk, T, topo)
+        for d in hop:
+            if hop[d] != core or d == core:
+                continue
+            rid, pid = topo.addr(d, core)
+            m = topo.mask(core, d)
+            for r in range(NR):
+                for s, buf, x, w in (("b", T.MB, r * 16 + q * 4, 2), ("a", T.A, (r + 1) * SL + q * 144, 144)):
+                    sem = T.sem["%s%d" % (s, r)]
+                    g.wait_ge(sem, len(hop_engines(rk, hop, topo, s)[d]))
+                    g.remote_dma(buf[:, x:x + w], buf[:, x:x + w], sem, T.sem.ls, pid, rid, m)
+                    local += len(topo.engines(core, d))
+    if local:
+        g.wait_ge(T.sem.ls, local)
+
+
+def rank_program(g, core, T, topo):
+    me = T.rank_of(core)
+    if me is None:
+        relay(g, core, T, topo)
+        return
+    hop = ways(core, T, topo)
+    queue = {"V": g.vector, "S": g.scalar, "T": g.tensor, "G": g, "Y": g.sync}
+    count = {"V": 0, "S": 0, "T": 0, "G": 0, "ls": 0}
+    known = {q: {} for q in queue}
+    logs = {}
+
+    def V(name, a=None, b=None, s=1, P=128):
+        t = T[name]
+        if a is None:
+            a, b = 0, t.shape[-1]
+        ap = t[0:P, a:b:s] if s != 1 else t[0:P, a:b]
+        return {"ap": ap, "r": [(name, 0, 512) if name in PSUM else (name, a, b)]}
+
+    def IND(w, o):
+        return {"ap": w["ap"].indirect(o["ap"]), "r": w["r"] + o["r"]}
+
+    def begin(e, outs, ins):
+        recs = {}
+        for views, wr in ((ins, False), (outs, True)):
+            for v in views:
+                for n, a, b in v["r"]:
+                    for (x, y, w, e2, sem, val, clk) in logs.get(n, []):
+                        if x < b and a < y and (wr or w):
+                            if sem not in recs or recs[sem][1] < val:
+                                recs[sem] = (sem, val, clk)
+        k = known[e]
+        for sem, val, clk in sorted(recs.values(), key=lambda z: -len(z[2])):
+            if k.get(sem, 0) < val:
+                queue[e].wait_ge(T.sem[sem], val)
+                k[sem] = val
+                for x in clk:
+                    if k.get(x, 0) < clk[x]:
+                        k[x] = clk[x]
+
+    def done(e, clk, sem, val, outs, ins):
+        clk = dict(clk)
+        clk[sem] = val
+        for views, wr in ((ins, False), (outs, True)):
+            for v in views:
+                for n, a, b in v["r"]:
+                    old = logs.get(n, [])
+                    if wr:
+                        old = [z for z in old if not (a <= z[0] and z[1] <= b)]
+                    else:
+                        old = [z for z in old if z[2] or z[3] != e or not (a <= z[0] and z[1] <= b)]
+                    logs[n] = old + [(a, b, wr, e, sem, val, clk)]
+
+    def op(e, outs, ins, call):
+        begin(e, outs, ins)
+        count[e] += 1
+        call(queue[e]).then_inc(T.sem["s" + e], 1)
+        done(e, known[e], "s" + e, count[e], outs, ins)
+
+    def dma(e, out, in_, sem):
+        begin(e, [out], [in_])
+        queue[e].dma_start(out["ap"], in_["ap"]).then_inc(T.sem[sem], 16)
+        done("dma" + sem, {}, sem, 16, [out], [in_])
+
+    def EXT(ap):
+        return {"ap": ap, "r": []}
+
+    def val(s):
+        return s["ap"] if isinstance(s, dict) else s
+
+    def vs(*a):
+        return [x for x in a if isinstance(x, dict)]
+
+    def ts(out, a, s1, op0, s2=None, op1=None):
+        if op1 is None:
+            op("V", [out], vs(a, s1), lambda q: q.tensor_scalar(out["ap"], a["ap"], val(s1), None, op0))
+        else:
+            op("V", [out], vs(a, s1, s2), lambda q: q.tensor_scalar(out["ap"], a["ap"], val(s1), val(s2), op0, op1))
+
+    def tt(out, a, b, o):
+        op("V", [out], [a, b], lambda q: q.tensor_tensor(out["ap"], a["ap"], b["ap"], o))
+
+    def cp(out, a):
+        op("V", [out], [a], lambda q: q.tensor_copy(out["ap"], a["ap"]))
+
+    def red(out, a, o):
+        op("V", [out], [a], lambda q: q.tensor_reduce(out["ap"], a["ap"], AxisListType.X, o))
+
+    def fill(out, c):
+        op("V", [out], [], lambda q: q.memset(out["ap"], c))
+
+    def scan(out, a, z, op0, op1):
+        op("V", [out], [a, z], lambda q: q.tensor_tensor_scan(out["ap"], a["ap"], z["ap"], 0.0, op0, op1))
+
+    def act(out, a, f, bias=None, scale=None, acc=None):
+        kw = {}
+        if bias is not None:
+            kw["bias"] = val(bias)
+        if scale is not None:
+            kw["scale"] = scale
+        if acc is not None:
+            kw["accum_out"] = acc["ap"]
+        op("S", vs(out, acc), vs(a, bias), lambda q: q.activation(out["ap"], a["ap"], f, **kw))
+
+    def mm(out, pairs, start=True, stop=True):
+        n = len(pairs)
+
+        def call(q):
+            x = None
+            for k, (l, r) in enumerate(pairs):
+                x = q.matmul(out["ap"], l["ap"], r["ap"], start and k == 0, stop and k == n - 1)
+            return x
+        op("T", [out], [v for p in pairs for v in p], call)
+
+    def mm2(out, early, late):
+        mm(out, early, True, False)
+        mm(out, late, False, True)
+
+    def iota(out, pattern, base, cm):
+        op("G", [out], [], lambda q: q.iota(out["ap"], pattern, base, cm, allow_small_or_imprecise_dtypes=True))
+
+    def sel(out, a, pattern, cmp_, base, cm):
+        op("G", [out], [a], lambda q: q.affine_select(out["ap"], a["ap"], pattern, cmp_, 0.0, base, cm))
+
+    def wrap(base, buf, i, w=512, x=0):
+        return (V(base, 15 - i, 143 - i), V(buf, x + i, x + w, 16))
+
+    def wraps(base, buf, w=512, x=0):
+        return [wrap(base, buf, i, w, x) for i in range(16)]
+
+    def send(r, s, src, dst, w, width):
+        begin("G", [], [V(src, w[d], w[d] + width) for d in hop])
+        eng = hop_engines(core, hop, topo, s)
+        far, near = [d for d in hop if hop[d] != d], [d for d in hop if hop[d] == d]
+        for ds in ([far, near] if s == "a" else [far + near]):
+            tr = []
+            for d in ds:
+                rid, pid = topo.addr(hop[d], core)
+                tr.append(RemoteDMATransfer(dst_ids=[DstId(rid=rid, pnc=pid)], dma_engine_mask=bits(eng[d]), remote_sem=T.sem["%s%d" % (s, r)],
+                                            src=T[src][:, w[d]:w[d] + width], dst=T[dst[0]][:, dst[1]:dst[1] + width]))
+                count["ls"] += len(eng[d])
+            g.remote_dma_fused(tr, local_sem=T.sem.ls)
+
+    def arrive(r, s, name, x, stride, width):
+        n = 0
+        for c in T.cores:
+            if c != core:
+                h = ways(c, T, topo)
+                n += len(hop_engines(c, h, topo, s)[core]) if h[core] == core else len(topo.engines(h[core], core))
+        sem = "%s%d" % (s, r)
+        for q in range(4):
+            if q != me:
+                logs[name] = logs.get(name, []) + [(x + q * stride, x + q * stride + width, True, "net", sem, n, {sem: n})]
+
+    dma("Y", V("F8I", P=8), EXT(T.f0[:, :]), "l0")
+    for q in range(4):
+        dma("Y" if q % 2 else "S", V("A", q * 144, q * 144 + 128), EXT(T.s0[:, q * 128:q * 128 + 128]), "l%d" % (1 + q))
+    for q in range(4):
+        dma("S" if q % 2 else "Y", V("OPW", q * 1024, q * 1024 + 1024), EXT(T.opr[:, q * 1024:q * 1024 + 1024]), "l%d" % (5 + q))
+
+    fill(V("ONE"), 1.0)
+    iota(V("LI", 0, 1), [[1, 1]], 0, 1)
+    iota(V("LM"), [[1, 16]], 0, 0)
+    iota(V("CL", 0, 32), [[144, 4], [16, 8]], 0, 0)
+    iota(V("CL", 32, 40), [[8, 2], [0, 2], [288, 2]], 128, 0)
+    sel(V("S1"), V("ONE", 0, 144), [[0, 9], [1, 16]], O.is_equal, -15, 0)
+    sel(V("S1"), V("S1"), [[-16, 9], [0, 16]], O.is_ge, 0, 1)
+    sel(V("S1"), V("S1"), [[16, 9], [0, 16]], O.is_ge, 15, -1)
+    sel(V("B8", P=8), V("ONE", 0, 144, P=8), [[0, 9], [1, 16]], O.is_equal, -15, 0)
+    sel(V("B8", P=8), V("B8", P=8), [[1, 9], [0, 16]], O.is_equal, 0, -1)
+    sel(V("ID"), V("ONE", 0, 128), [[-1, 128]], O.is_equal, 0, 1)
+    sel(V("BLK"), V("ONE", 0, 128), [[-16, 8], [0, 16]], O.is_ge, 0, 1)
+    sel(V("BLK"), V("BLK"), [[16, 8], [0, 16]], O.is_ge, 15, -1)
+    sel(V("NUT"), V("BLK"), [[-1, 128]], O.is_gt, 0, 1)
+    iota(V("DM"), [[0, 4], [1, 16]], 0, 0)
+    iota(V("K"), [[0, 4], [1, 128]], 0, 0)
+    iota(V("O32"), [[32, 4], [0, 8]], 0, 0)
+    iota(V("O272"), [[272, 4], [0, 8]], 0, 0)
+    iota(V("K1"), [[0, 4], [1, 128]], 1, 0)
+    iota(V("B8C"), [[8, 12], [0, 8]], 0, 0)
+    iota(V("B256"), [[256, 12], [0, 8]], 128, 0)
+    iota(V("DM3"), [[0, 12], [1, 8]], 0, 0)
+    sel(V("G8"), V("ONE", 0, 8), [[-16, 8]], O.is_ge, 0, 1)
+    sel(V("G8"), V("G8"), [[16, 8]], O.is_ge, 15, -1)
+    for i in range(16):
+        fill(V("WR", i, i + 1), float(WT[i]))
+    for o in range(3):
+        fill(V("E8C", o, o + 1), 811.0 * o)
+    ts(V("LI", 1, 2), V("LI", 0, 1), 15, O.bitwise_and)
+    lane = V("LC", 0, 1)
+    cp(lane, V("LI", 1, 2))
+    ts(V("LI", 2, 3), V("LI", 1, 2), 7, O.bitwise_and)
+    ts(V("LI", 3, 4), V("LI", 1, 2), 3, O.arith_shift_right)
+    ts(V("LM"), V("LM"), lane, O.is_equal)
+    ts(V("LC", 3, 4), V("LI", 3, 4), 144.0, O.mult)
+    tt(V("W2"), V("WR"), V("LM"), O.mult)
+    tt(V("LC", 4, 5), V("LC", 3, 4), V("LI", 2, 3), O.add)
+    red(V("LC", 1, 2), V("W2"), O.add)
+    ts(V("CL", 0, 32), V("CL", 0, 32), lane, O.add)
+    ts(V("CL", 32, 40), V("CL", 32, 40), V("LC", 4, 5), O.add)
+    cp(V("LI", 4, 5), V("LC", 1, 2))
+    ts(V("LI", 5, 6), V("LI", 4, 5), 3, O.bitwise_and)
+    ts(V("LC", 2, 3), V("LI", 5, 6), -1.0, O.mult, 1026.0, O.add)
+    ts(V("WM"), V("S1"), V("LC", 1, 2), O.mult)
+    ts(V("F8", P=8), V("F8I", P=8), -1023.0, O.add)
+    ts(V("B8", P=8), V("B8", P=8), 1.0 / 32, O.mult)
+
+    def consts1():
+        ts(V("XB"), V("S1"), V("LC", 2, 3), O.mult)
+        ts(V("IDF"), V("ID"), 131072.0, O.mult)
+        ts(V("IDN"), V("ID"), -1.0, O.mult)
+        for o in range(4):
+            fill(V("BO", o, o + 1), -8192.0 * o)
+        fill(V("CH", 4096, 4112), 0.0)
+
+    def consts2():
+        cp(V("BLKF"), V("BLK"))
+        ts(V("NBF"), V("BLK"), -4096.0, O.mult)
+        ts(V("NB"), V("BLK"), -4096.0, O.mult)
+        fill(V("CQ", 0, 1), 524288.0)
+        fill(V("CQ", 1, 2), 2048.0)
+        ts(V("LC", 8, 9), lane, 0.0, O.is_equal, -15728640.0, O.mult)
+        ts(V("LC", 9, 10), lane, 1.0, O.is_equal, 4096.0, O.mult)
+        for o in range(2):
+            tt(V("CA", o, o + 1), V("LC", 8, 9), V("LC", 9, 10), O.add)
+        ts(V("NUT"), V("NUT"), -1.0, O.mult)
+        ts(V("ID16"), V("ID"), 16.0, O.mult)
+        ts(V("SD"), V("S1"), lane, O.mult)
+        ts(V("S32"), V("S1"), 1.0 / 32, O.mult)
+        ts(V("DM"), V("DM"), lane, O.is_equal)
+        fill(V("ZERO"), 0.0)
+        fill(V("YW", 256, 272), 0.0)
+        fill(V("W"), 0.0)
+        fill(V("EBW"), 1000.0)
+
+    def consts3():
+        fill(V("A", EMPTY * SL, EMPTY * SL + SL), 0.0)
+        ts(V("LC", 6, 7), lane, -128.0, O.add)
+        ts(V("RM"), V("DM3"), 0.0, O.is_gt)
+        ts(V("DM3"), V("DM3"), lane, O.is_equal)
+        ts(V("LC", 5, 6), lane, 6.5, O.is_gt, 1000.0, O.mult)
+        ts(V("SE"), V("S1"), V("LC", 6, 7), O.mult)
+        ts(V("G8F"), V("G8"), 1.0 / 16, O.mult)
+        ts(V("G8"), V("G8"), 32.0, O.mult)
+        fill(V("S3"), 0.0)
+
+    def C(k):
+        return V("SV", k, k + 1)
+
+    def w_(k, n=1):
+        return V("SW", k, k + n)
+
+    LO, HI, PT, U, EE, EL, ER = V("SV", 0, 3), V("SV", 4, 7), V("SV", 8, 11), C(12), V("SV", 17, 20), V("SV", 18, 21), V("SV", 16, 19)
+    LOE, BASE, E8, CC, LIM, LMN, THR = C(24), C(25), C(26), C(27), C(28), C(29), C(30)
+    fill(V("SV"), 0.0)
+    fill(U, 1023.0)
+    fill(C(3), 100000.0)
+    fill(C(17), 1.0)
+    fill(V("SV", 9, 12), float(EMPTY * SL))
+
+    def split(blocks):
+        for o, (buf, x) in blocks:
+            ts(V(buf, x, x + 8), V("PN", o * 8, o * 8 + 8), MAGIC, O.add, MAGIC, O.subtract)
+        for o, (buf, x) in blocks:
+            tt(V(buf, x + 8, x + 16), V("PN", o * 8, o * 8 + 8), V(buf, x, x + 8), O.subtract)
+
+    mm(V("PN", 0, 32), [(V("B8", 15 - i, 143 - i, P=8), V("F8", i, 512, 16, P=8)) for i in range(16)])
+    split([(q, ("A", q * 144 + 128)) for q in range(4)])
+
+    def parents(r):
+        if r:
+            level_a(r - 1)
+        tt(w_(0, 3), PT, EE, O.mult)
+        red(BASE, w_(0, 3), O.add)
+        ts(V("OFA"), V("CL"), BASE, O.add)
+        tt(w_(3, 3), V("E8C", 0, 3), EE, O.mult)
+        tt(w_(23, 3), V("SV", 3, 6), EE, O.mult)
+        red(E8, w_(3, 3), O.add)
+        red(THR, w_(23, 3), O.add)
+        if r:
+            level_b()
+        tt(w_(6, 3), LO, EE, O.mult)
+        ts(THR, THR, -1023.0, O.add, 1.0 / 32, O.mult)
+        red(LOE, w_(6, 3), O.add)
+        fill(V("TT"), 511.5)
+        ts(CC, LOE, -4096.0, O.mult, 444.0 + 4096.0 * 1023, O.add)
+        ts(LIM, LOE, -1.0, O.mult, 1022.5, O.add)
+        ts(LMN, LOE, -1023.0, O.add)
+        lay = V("A", 0, (r + 1) * SL)
+        cp(V("S", 0, 256), IND(lay, V("OFA", 0, 16)))
+        act(V("S", 256, 512), IND(lay, V("OFA", 16, 32)), F.Copy)
+        act(V("FS"), IND(lay, V("OFA", 32, 40)), F.Copy)
+        mm(V("PU", 0, 32), wraps("WM", "S"))
+        tt(V("T8"), V("FS", 0, 64), V("FS", 64, 128), O.add)
+        ts(V("P8"), V("T8"), THR, O.is_ge, 32.0, O.mult)
+        tt(V("FS", 0, 64), V("FS", 0, 64), V("P8"), O.add)
+        if not r:
+            consts1()
+        for k in range(2):
+            mm(V("PC%d" % k, 0, 512), [(V("IDN"), V("S"))], True, False)
+
+    def pre(r):
+        tt(w_(22, 3), V("SV", 9, 12), EE, O.mult)
+        ts(w_(19, 3), EE, float((r + 1) * SL), O.mult)
+        ts(w_(13, 3), EE, -1.0, O.mult, 1.0, O.add)
+        ts(w_(36), LOE, 1.0, O.add)
+        ts(w_(38), C(17), -1.0, O.mult, 1.0, O.add)
+        ts(w_(40, 3), LO, 1.0, O.add)
+        tt(w_(19, 3), w_(19, 3), w_(22, 3), O.subtract)
+        tt(HI, HI, w_(13, 3), O.mult)
+        tt(V("SV", 9, 12), V("SV", 9, 12), w_(19, 3), O.add)
+
+    def level_a(r):
+        B, m, rt, lp, bk, up, st = [w_(k) for k in (10, 11, 27, 28, 29, 30, 39)]
+        red(w_(12), V("MB", r * 16 + 1, r * 16 + 16, 4), O.min)
+        red(B, V("MB", r * 16, r * 16 + 16, 4), O.min)
+        ts(V("MD"), V("LM"), w_(12), O.mult)
+        mm(V("PN", 0, 16), [(V("BLKF"), V("MD"))])
+        ts(w_(13, 3), EE, B, O.mult)
+        tt(lp, w_(36), B, O.max)
+        tt(HI, HI, w_(13, 3), O.add)
+        red(m, V("PN", 0, 16), O.min)
+        tt(w_(26), m, B, O.is_lt)
+        tt(w_(35), m, B, O.is_ge)
+        tt(w_(31), w_(26), C(19), O.mult)
+        tt(w_(35), w_(35), C(19), O.max)
+        ts(w_(32), w_(31), -4000.0, O.mult, 4000.0, O.add)
+        tt(w_(33), w_(32), m, O.max)
+        tt(U, U, w_(33), O.min)
+        tt(w_(34), m, U, O.is_ge)
+        tt(w_(37), lp, U, O.is_ge)
+        tt(rt, w_(34), w_(35), O.max)
+        tt(w_(37), w_(37), w_(38), O.mult)
+        ts(up, rt, -1.0, O.mult, 1.0, O.add)
+        tt(bk, w_(37), rt, O.mult)
+        ts(w_(46, 3), ER, up, O.mult)
+        tt(st, rt, bk, O.subtract)
+        ts(w_(49, 3), EL, bk, O.mult)
+        ts(w_(43, 3), EE, bk, O.mult)
+        ts(w_(52, 3), EE, st, O.mult)
+        ts(w_(55, 3), EE, st, O.mult, lp, O.mult)
+        tt(w_(16, 3), w_(46, 3), w_(49, 3), O.add)
+        tt(EE, w_(16, 3), w_(52, 3), O.add)
+
+    def level_b():
+        tt(w_(40, 3), w_(40, 3), HI, O.max)
+        tt(w_(43, 3), w_(43, 3), EE, O.add)
+        ts(w_(43, 3), w_(43, 3), -1.0, O.mult, 1.0, O.add)
+        tt(w_(40, 3), w_(40, 3), w_(49, 3), O.mult)
+        tt(LO, LO, w_(43, 3), O.mult)
+        tt(w_(40, 3), w_(40, 3), w_(55, 3), O.add)
+        tt(LO, LO, w_(40, 3), O.add)
+
+    def rnd(r):
+        parents(r)
+        cp(V("UI"), V("PU", 0, 32))
+        ts(V("UU"), V("UI"), 4095, O.bitwise_and)
+        tt(V("USQ"), V("UU"), V("UU"), O.mult)
+        cp(V("UF"), V("UU"))
+        ts(V("BB"), V("USQ"), 4, O.arith_shift_right)
+        for j in range(2):
+            ts(V("TJ", j * 32, j * 32 + 32), V("UU"), float(KA[j]), O.mult, E8, O.add)
+        for j in range(2, 8):
+            act(V("TJ", j * 32, j * 32 + 32), V("UF"), F.Identity, bias=E8, scale=float(KA[j]))
+
+        def numbers(j0, j1):
+            for j in range(j0, j1):
+                tt(V("VJ", j * 32, j * 32 + 32), V("TJ", j * 32, j * 32 + 32), V("BB"), O.add)
+            a, b = j0 * 32, j1 * 32
+            ts(V("VK", a, b), V("VJ", a, b), 4095, O.bitwise_and)
+            cp(V("OFO", a, b), V("VK", a, b))
+
+        def gather(k):
+            x, y = k * 512, k * 512 + 512
+            tt(V("D", x, y), IND(V("OPW"), V("OFO", k * 32, k * 32 + 32)), V("S"), O.subtract)
+
+        def other(k):
+            z = k // 2 * 512
+            act(V("GA", z, z + 512), IND(V("OPW"), V("OFO", k * 32, k * 32 + 32)), F.Copy)
+            mm(V("PC%d" % (k // 2), 0, 512), [(V("ID"), V("GA", z, z + 512))], False, True)
+
+        def size(k):
+            x, y = k * 512, k * 512 + 512
+            act(V("CH", x, y), V("PC%d" % (k // 2), 0, 512) if k in (1, 3) else V("D", x, y), F.Abs)
+
+        def sums(k):
+            mm2(V("PX" if k < 2 else "PEA", k * 64, k * 64 + 64), [(V("IDF"), V("FS", 0, 64)), (V("IDF"), V("FS", 64, 128))],
+                wraps("XB", "CH", 1024, k * 1024))
+
+        numbers(0, 2)
+        other(1)
+        gather(0)
+        size(0)
+        size(1)
+        sums(0)
+        numbers(2, 8)
+        other(3)
+        for k in (2, 4, 5, 6, 7):
+            gather(k)
+        size(2)
+        size(3)
+        sums(1)
+        for k in (4, 5, 6, 7):
+            size(k)
+            if k % 2:
+                sums(k // 2)
+        if not r:
+            consts2()
+        for p, a, b in (("PX", 0, 128), ("PEA", 128, 256)):
+            ts(V("XI", a, b), V(p, a, b), CC, O.add)
+            ts(V("OW", a, b), V("XI", a, b), 3, O.bitwise_and)
+            ts(V("Y", a, b), V("XI", a, b), 12, O.arith_shift_right, 4095, O.bitwise_and)
+            ts(V("OW4", a, b), V("OW", a, b), 8192.0, O.mult)
+            tt(V("Z", a, b), V("Y", a, b), V("OW4", a, b), O.add)
+            for o in (0, 1, 2):
+                act(V("X", o * 256 + a, o * 256 + b), V("Z", a, b), F.Abs, bias=V("BO", o, o + 1))
+            ts(V("OW3", a, b), V("OW", a, b), 3.0, O.not_equal, 8192.0, O.mult)
+            tt(V("XH", 768 + a, 768 + b), V("OW3", a, b), V("Y", a, b), O.add)
+            if not a:
+                cp(V("XH", 512, 640), V("X", 512, 640))
+        cp(V("XH", 640, 768), V("X", 640, 768))
+        for k in range(2):
+            mm(V("PC%d" % k, 64, 66), [(V("ID"), V("CQ"))])
+        s = 512
+        while s:
+            mm(V("PN", 0, 2), [(V("BLK"), V("CA"))], True, False)
+            for o in (0, 1):
+                act(V("DA", o * 256, o * 256 + 256), V("X", o * 256, o * 256 + 256), F.Sign, bias=V("TT", o, o + 1), scale=-1.0, acc=V("CN", o, o + 1))
+            for o in (3, 2):
+                z = o * 256 - 512
+                ts(V("DV", z, z + 256), V("XH", z + 512, z + 768), V("TT", o, o + 1), O.is_lt)
+                mm(V("PC%d" % (o - 2), 0, 64), [(V("NB"), V("DV", z + 64 * x, z + 64 * x + 64)) for x in range(4)])
+            mm(V("PN", 0, 2), [(V("NBF"), V("CN", 0, 2))], False, True)
+            if s > 1:
+                ts(V("TLO"), V("TT"), -s / 2.0, O.add)
+                ts(V("THI"), V("TT"), s / 2.0, O.add)
+            else:
+                ts(V("TLO"), V("TT"), -1.0, O.add, LIM, O.min)
+                ts(V("THI"), V("TT"), LIM, O.min)
+            if s in (256, 128):
+                o = s // 128 - 1
+                cp(V("XH", o * 256, o * 256 + 256), V("X", o * 256, o * 256 + 256))
+            for o in (3, 2):
+                red(V("QN", o, o + 1), V("PC%d" % (o - 2), 0, 66), O.add)
+            for o in (3, 2, 0, 1):
+                ts(V("TT", o, o + 1), V("PN", o, o + 1) if o < 2 else V("QN", o, o + 1), V("TLO", o, o + 1), O.max, V("THI", o, o + 1), O.min)
+            s //= 2
+        for p in ((2, 3), (0, 1)):
+            for o in p:
+                ts(V("KP", o * 256, o * 256 + 256), V("XH", o * 256, o * 256 + 256), V("TT", o, o + 1), O.is_lt)
+            for o in p:
+                scan(V("R", o * 256, o * 256 + 256), V("KP", o * 256, o * 256 + 256), V("ZERO"), O.add, O.add)
+
+        def places(o):
+            mm(V("PC%d" % (o // 2), o % 2 * 256, o % 2 * 256 + 256), [(V("BLK"), V("R", o * 256, o * 256 + 256)), (V("NUT"), V("KP", o * 256, o * 256 + 256))])
+
+        def heads(o):
+            tt(V("W", o * 272, o * 272 + 256), V("PC%d" % (o // 2), o % 2 * 256, o % 2 * 256 + 256), V("KP", o * 256, o * 256 + 256), O.mult)
+
+        places(2)
+        mm(V("PEA", 0, 64), [(V("BLK"), V("R", 15, 1024, 16))])
+        mm(V("PEB", 0, 64), [wrap("S1", "R", b, 1024) for b in range(16)])
+        tt(V("EM", 0, 64), V("PEA", 0, 64), V("DM"), O.mult)
+        for o in range(4):
+            red(V("EA", o, o + 1), V("EM", o * 16, o * 16 + 16), O.add)
+        for o in range(4):
+            ts(V("IA", o * 128, o * 128 + 128), V("K", 0, 128), V("EA", o, o + 1), O.is_ge)
+        mm2(V("PL", 0, 32), [(V("ID"), V("O32"))], wraps("S1", "IA"))
+        for o in range(4):
+            act(V("EBW", o * 32, o * 32 + 16), V("PEB", o * 16, o * 16 + 16), F.Copy)
+        mb = r * 16 + me * 4
+        red(w_(61), V("TT"), O.min)
+        red(w_(60), V("Y"), O.min)
+        ts(V("MB", mb, mb + 1), w_(61), LOE, O.add, 0.5, O.add)
+        ts(V("MB", mb + 1, mb + 2), w_(60), LOE, O.add, 1023.0, O.min)
+        send(r, "b", "MB", ("MB", mb), {d: mb for d in hop}, 2)
+        arrive(r, "b", "MB", r * 16, 4, 2)
+        ts(V("YW", 0, 256), V("Y"), LMN, O.add)
+        cp(V("OFB"), V("PL", 0, 32))
+        tt(V("AB", 0, 32), V("PL", 0, 32), V("O32"), O.subtract)
+        places(3)
+        tt(V("IB"), IND(V("EBW"), V("OFB")), V("K"), O.is_le)
+        mm2(V("PL", 0, 32), [(V("ID"), V("O272")), (V("ID16"), V("AB", 0, 32))], wraps("S1", "IB"))
+        places(0)
+        places(1)
+        heads(2)
+        heads(3)
+        ts(V("OFV"), V("PL", 16, 32), -544.0, O.add)
+        cp(V("OFW", 0, 16), V("PL", 0, 16))
+        tt(V("CB"), V("PL", 0, 32), V("O272"), O.subtract)
+        cp(V("OFC"), V("CB"))
+        tt(V("OH", 256, 512), IND(V("W", 544, 1088), V("OFV")), V("K1", 0, 256), O.is_equal)
+        heads(0)
+        heads(1)
+        tt(V("OH", 0, 256), IND(V("W", 0, 544), V("OFW", 0, 16)), V("K1", 0, 256), O.is_equal)
+        mm2(V("PU", 0, 32), [(V("ID16"), V("CB"))], wraps("SD", "OH"))
+        tt(V("CG", 0, 512), IND(V("YW"), V("OFC")), V("OH", 0, 512), O.mult)
+        mm(V("PN", 0, 32), wraps("S32", "CG"))
+        cp(V("OFN"), V("PU", 0, 32))
+        order = [T.cores.index(d) for d in hop] + [me]
+        blk = {o: ("SND", r * SL + o * 144) for o in order}
+        blk[me] = ("A", (r + 1) * SL + me * 144)
+        for k, o in enumerate(order):
+            out, v = V(blk[o][0], blk[o][1], blk[o][1] + 128), IND(V("CH"), V("OFN", o * 8, o * 8 + 8))
+            if k == 1:
+                cp(out, v)
+            else:
+                act(out, v, F.Copy)
+        pre(r)
+        split([(o, (blk[o][0], blk[o][1] + 128)) for o in order[:3]])
+        send(r, "a", "SND", ("A", (r + 1) * SL + me * 144), {d: blk[T.cores.index(d)][1] for d in hop}, 144)
+        split([(me, (blk[me][0], blk[me][1] + 128))])
+        arrive(r, "a", "A", (r + 1) * SL, 144, 144)
+        if not r:
+            consts3()
+
+    for r in range(NR):
+        rnd(r)
+    level_a(NR - 1)
+
+    for l in range(3):
+        ts(V("OG3", l * 40, l * 40 + 40), V("CL"), C(9 + l), O.add)
+    ts(w_(0, 3), HI, -1023.0, O.add, 1.0 / 32, O.mult)
+    for l in range(3):
+        cp(V("FF", l * 128, l * 128 + 128), IND(V("A"), V("OG3", l * 40 + 32, l * 40 + 40)))
+    for k in range(12):
+        l, q = k // 4, k % 4
+        act(V("S3", k * 256, k * 256 + 128), IND(V("A"), V("OG3", l * 40 + q * 8, l * 40 + q * 8 + 8)), F.Copy)
+    for l in range(3):
+        a, b = l * 32, l * 32 + 32
+        tt(V("F3", a, b), V("FF", l * 128, l * 128 + 32), V("FF", l * 128 + 64, l * 128 + 96), O.add)
+    for l in range(3):
+        a, b = l * 32, l * 32 + 32
+        ts(V("KP3", a, b), V("F3", a, b), w_(l), O.is_lt)
+    scan(V("R3"), V("RM"), V("KP3"), O.mult, O.add)
+    mm(V("PEA", 0, 96), [(V("BLK"), V("R3"))])
+    mm(V("PC0", 0, 96), [(V("BLK"), V("R3")), (V("NUT"), V("KP3"))])
+    tt(V("EM"), V("PEA", 0, 96), V("DM3"), O.mult)
+    for k in range(12):
+        red(V("EA", k, k + 1), V("EM", k * 8, k * 8 + 8), O.add)
+    ts(V("EA"), V("EA"), V("LC", 5, 6), O.add)
+    for k in range(12):
+        ts(V("IA", k * 128, k * 128 + 128), V("K", 0, 128), V("EA", k, k + 1), O.is_ge)
+    mm2(V("PL", 0, 96), [(V("ID"), V("B8C"))], wraps("S1", "IA", 1536))
+    tt(V("W3"), V("PC0", 0, 96), V("KP3"), O.mult)
+    level_b()
+    cp(V("YT", 0, 3), LO)
+    cp(V("YT", 3, 6), HI)
+    tt(w_(60), C(19), C(19), O.add)
+    tt(V("YT", 6, 7), w_(60), C(18), O.add)
+    cp(V("YT", 7, 8), U)
+    mm(V("PX", 0, 8, P=8), [(V("G8F"), V("YT"))])
+    cp(V("OF3"), V("PL", 0, 96))
+    tt(V("AB"), V("PL", 0, 96), V("B8C"), O.subtract)
+    for l in range(3):
+        a, b = l * 512, l * 512 + 512
+        tt(V("OH", a, b), IND(V("W3"), V("OF3", l * 32, l * 32 + 32)), V("K1"), O.is_equal)
+    mm2(V("PU", 0, 96), [(V("ID16"), V("AB")), (V("ID"), V("B256"))], wraps("SE", "OH", 1536))
+    cp(V("YT8", P=8), V("PX", 0, 8, P=8))
+    dma("Y", EXT(T.yt[:, :]), V("YT8", P=8), "o0")
+
+    def costs(l):
+        a, b = l * 512, l * 512 + 512
+        tt(V("CG", a, b), IND(V("F3"), V("OF3", l * 32, l * 32 + 32)), V("OH", a, b), O.mult)
+        p = ("PC0", "PC1", "PEB")[l]
+        mm(V(p, 0, 512, P=8), [(V("G8"), V("CG", a, b))])
+
+    costs(0)
+    cp(V("OP3"), V("PU", 0, 96))
+    for l in range(3):
+        a, b = l * 512, l * 512 + 512
+        act(V("YL", a, b), IND(V("S3"), V("OP3", l * 32, l * 32 + 32)), F.Copy)
+        dma("Y", EXT(T.yl[:, a:b]), V("YL", a, b), "o%d" % (1 + l))
+    costs(1)
+    costs(2)
+    for l in range(3):
+        a, b = l * 512, l * 512 + 512
+        ts(V("YF", a, b, P=8), V(("PC0", "PC1", "PEB")[l], 0, 512, P=8), 1023.0, O.add)
+    dma("S", EXT(T.yf[:, :]), V("YF", P=8), "o4")
+    for k in range(4):
+        g.sync.wait_ge(T.sem["o%d" % k], 16)
+    for k in range(9):
+        g.sync.wait_ge(T.sem["l%d" % k], 16)
+    g.scalar.wait_ge(T.sem.o4, 16)
+    for e in ("V", "S", "T", "G"):
+        g.wait_ge(T.sem["s" + e], count[e])
+    g.wait_ge(T.sem.ls, count["ls"])

@@ -2,38 +2,42 @@ from concourse.bass import DstId, RemoteDMATransfer
 from concourse.mybir import AluOpType as O, AxisListType, ActivationFunctionType as F
 
 NR = 8
-SL = 576
+SL = 512
 EMPTY = 9
 WT = [1, 3, 7, 13, 21, 35, 49, 67, 85, 107, 129, 155, 181, 211, 241, 253]
 KA = [17, 101, 263, 389, 547, 701, 859, 1021]
 MAGIC = float(3 << 22)
+OFFS = 6144.0
+STEPS = [256, 64, 16, 4, 1]
 
 _f, _b, _h, _i, _u = "float32", "bfloat16", "float16", "int32", "uint16"
-PSUM = ("PU", "PX", "PN", "PC0", "PC1", "PEA", "PEB", "PL")
+PSUM = ["P%d" % k for k in range(8)]
 SCRATCH = {}
 for _n, _w, _d in (
-        ("A", 10 * SL, _b), ("OPW", 4096, _b), ("SND", NR * SL, _b), ("MB", NR * 16, _f), ("S", 512, _b), ("FS", 128, _b), ("D", 4096, _b),
-        ("GA", 1024, _b), ("CH", 4112, _b), ("OFA", 40, _u), ("OFO", 256, _u), ("OFB", 32, _u), ("OFW", 32, _u), ("OFV", 16, _u),
-        ("OFC", 32, _u), ("OFN", 32, _u), ("UI", 32, _i), ("UU", 32, _i), ("UF", 32, _f), ("USQ", 32, _i), ("BB", 32, _i),
-        ("TJ", 256, _f), ("VJ", 256, _i), ("VK", 256, _i), ("XI", 256, _i), ("Y", 256, _i), ("OW", 256, _i), ("OW3", 256, _f), ("OW4", 256, _f),
-        ("Z", 256, _f), ("YW", 272, _f), ("X", 768, _f), ("XH", 1024, _h), ("DA", 512, _b), ("DV", 512, _b), ("KP", 1024, _b), ("R", 1024, _b),
-        ("W", 1088, _b), ("IA", 1536, _b), ("IB", 512, _b), ("OH", 1536, _b), ("CG", 1536, _h), ("EBW", 128, _b), ("AB", 96, _b), ("CB", 32, _b),
-        ("EM", 96, _f), ("EA", 12, _f), ("T8", 64, _f), ("P8", 64, _f), ("TT", 4, _f), ("TLO", 4, _f), ("THI", 4, _f), ("CN", 4, _f), ("QN", 4, _f),
-        ("SV", 64, _f), ("SW", 64, _f), ("MD", 16, _f),
-        ("ONE", 256, _b), ("ZERO", 256, _b), ("BLK", 128, _b), ("BLKF", 128, _f), ("NBF", 128, _f), ("NB", 128, _b), ("CQ", 2, _b), ("CA", 2, _b),
-        ("NUT", 128, _b), ("ID", 128, _b), ("IDN", 128, _b), ("IDF", 128, _b), ("ID16", 128, _b), ("S1", 144, _b), ("SD", 144, _b), ("SE", 144, _b),
-        ("S32", 144, _h), ("WM", 144, _b), ("XB", 144, _h), ("K", 512, _b), ("K1", 512, _b), ("CL", 40, _f), ("O32", 32, _b), ("O272", 32, _b),
-        ("DM", 64, _f), ("LM", 16, _f), ("WR", 16, _f), ("W2", 16, _f), ("LC", 16, _f), ("LI", 8, _i), ("BO", 4, _f), ("E8C", 4, _f),
-        ("G8", 8, _h), ("G8F", 8, _f),
-        ("S3", 3072, _b), ("FF", 384, _b), ("F3", 96, _f), ("KP3", 96, _b), ("R3", 96, _b), ("RM", 96, _b), ("W3", 96, _b),
-        ("OF3", 96, _u), ("OG3", 120, _u), ("OP3", 96, _u), ("B8C", 96, _b), ("B256", 96, _b), ("DM3", 96, _f), ("YL", 1536, _b), ("YT", 8, _f)):
+        ("A", 10 * SL, _b), ("AC", 320, _f), ("OPW", 4096, _b), ("SND", NR * SL, _b), ("SNC", NR * 32, _f), ("MB", NR * 16, _f),
+        ("S", 512, _b), ("FSA", 64, _f), ("FSP", 64, _f), ("FS", 64, _h), ("D", 4096, _b), ("GA", 1024, _b), ("CH", 4112, _b),
+        ("OFA", 32, _u), ("OFF", 4, _u), ("OFO", 256, _u), ("OFB", 32, _u), ("OFW", 32, _u), ("OFN", 32, _u), ("OFQ", 2, _u),
+        ("MR", 32, _f), ("MZ", 32, _f), ("SQ", 32, _f), ("TJ", 256, _f), ("VJ", 256, _i), ("VK", 256, _i),
+        ("YH", 256, _h), ("QQ", 256, _f), ("DD", 256, _b), ("PEN", 768, _b), ("XH", 512, _h), ("YW", 544, _f),
+        ("DV", 1536, _h), ("RS", 1536, _h), ("DA", 1536, _b), ("CN", 8, _f), ("CAND", 64, _f), ("TT", 32, _f),
+        ("KP", 1024, _b), ("R", 1024, _b), ("V1", 768, _b), ("EBW", 1088, _b), ("W", 1088, _b), ("IB", 512, _b), ("OH", 1536, _b), ("CG", 1536, _h),
+        ("TB", 64, _f), ("SV", 32, _f), ("MD", 16, _h),
+        ("ONE", 256, _b), ("ZH", 256, _h), ("BLK", 128, _b), ("NBH", 128, _h), ("NBF", 128, _f), ("NBD", 128, _b), ("NUT", 128, _b),
+        ("ID", 128, _b), ("IDN", 128, _b), ("ID16", 128, _b), ("ID2K", 128, _b), ("IDP", 128, _b), ("IDM", 128, _b), ("IDF", 128, _f),
+        ("S1", 144, _b), ("S16", 144, _b), ("SD", 144, _b), ("SN", 144, _b), ("WM", 144, _b), ("XB", 144, _h),
+        ("K", 256, _b), ("K1", 256, _b), ("K13", 512, _b), ("KD", 256, _b), ("DT", 256, _b), ("CL", 32, _f), ("CLF", 4, _f),
+        ("CM", 32, _b), ("CZ", 64, _h), ("M2", 64, _b), ("CA", 4, _b), ("CO", 16, _b), ("CE", 16, _h), ("CT", 80, _f), ("CK", 16, _f), ("C8", 2, _f),
+        ("LM", 16, _f), ("RW", 80, _f), ("RX", 80, _f), ("LC", 24, _f), ("LI", 8, _i), ("G8", 8, _h), ("G8F", 8, _f),
+        ("DB", 24, _f), ("FIN", 16, _f), ("F3", 96, _f), ("KP3", 96, _b), ("R3", 96, _b), ("RM", 96, _b), ("W3", 96, _b), ("V3", 96, _f),
+        ("KD3", 768, _b), ("DT3", 768, _b), ("C3", 96, _b), ("OF3", 96, _u), ("OG3", 8, _u), ("OP3", 96, _u), ("YL", 1536, _b)):
     SCRATCH[_n] = ("sbuf", [128, _w], _d)
 for _n, _w, _d in (("B8", 144, _h), ("F8I", 512, _i), ("F8", 512, _h), ("YF", 1536, _f), ("YT8", 8, _f)):
     SCRATCH[_n] = ("sbuf", [8, _w], _d)
 for _n in PSUM:
     SCRATCH[_n] = ("psum", [128, 512], _f)
-SEMAPHORES = (["sV", "sS", "sT", "sG", "ls"] + ["%s%d" % (s, r) for s in "ab" for r in range(NR)]
-              + ["l%d" % k for k in range(9)] + ["o%d" % k for k in range(5)])
+SEMAPHORES = (["sV", "sS", "sT", "sG", "ls"] + ["%s%d" % (s, r) for s in "abc" for r in range(NR)]
+              + ["l%d" % k for k in range(7)] + ["o%d" % k for k in range(5)])
+MSG = {"b": ("MB", 16, 4, 0), "a": ("A", SL, 128, 1), "c": ("AC", 32, 8, 1)}
 
 
 def ways(core, T, topo):
@@ -78,10 +82,12 @@ def relay(g, core, T, topo):
             rid, pid = topo.addr(d, core)
             m = topo.mask(core, d)
             for r in range(NR):
-                for s, buf, x, w in (("b", T.MB, r * 16 + q * 4, 2), ("a", T.A, (r + 1) * SL + q * 144, 144)):
+                for s in "bac":
+                    buf, wr, w, r0 = MSG[s]
+                    x = (r + r0) * wr + q * w
                     sem = T.sem["%s%d" % (s, r)]
                     g.wait_ge(sem, len(hop_engines(rk, hop, topo, s)[d]))
-                    g.remote_dma(buf[:, x:x + w], buf[:, x:x + w], sem, T.sem.ls, pid, rid, m)
+                    g.remote_dma(T[buf][:, x:x + w], T[buf][:, x:x + w], sem, T.sem.ls, pid, rid, m)
                     local += len(topo.engines(core, d))
     if local:
         g.wait_ge(T.sem.ls, local)
@@ -93,6 +99,8 @@ def rank_program(g, core, T, topo):
         relay(g, core, T, topo)
         return
     hop = ways(core, T, topo)
+    far = [T.cores.index(d) for d in hop if hop[d] != d]
+    own = sorted([(2, 0), (1, 3)], key=lambda p: -len([o for o in p if o in far]))
     queue = {"V": g.vector, "S": g.scalar, "T": g.tensor, "G": g, "Y": g.sync}
     count = {"V": 0, "S": 0, "T": 0, "G": 0, "ls": 0}
     known = {q: {} for q in queue}
@@ -114,7 +122,7 @@ def rank_program(g, core, T, topo):
             for v in views:
                 for n, a, b in v["r"]:
                     for (x, y, w, e2, sem, val, clk) in logs.get(n, []):
-                        if x < b and a < y and (wr or w):
+                        if x < b and a < y and (wr or w or (n in PSUM and e2 != e)):
                             if sem not in recs or recs[sem][1] < val:
                                 recs[sem] = (sem, val, clk)
         k = known[e]
@@ -177,8 +185,8 @@ def rank_program(g, core, T, topo):
     def fill(out, c):
         op("V", [out], [], lambda q: q.memset(out["ap"], c))
 
-    def scan(out, a, z, op0, op1):
-        op("V", [out], [a, z], lambda q: q.tensor_tensor_scan(out["ap"], a["ap"], z["ap"], 0.0, op0, op1))
+    def scan(out, a, z, first, op0, op1):
+        op("V", [out], vs(a, z, first), lambda q: q.tensor_tensor_scan(out["ap"], a["ap"], z["ap"], val(first), op0, op1))
 
     def act(out, a, f, bias=None, scale=None, acc=None):
         kw = {}
@@ -190,46 +198,44 @@ def rank_program(g, core, T, topo):
             kw["accum_out"] = acc["ap"]
         op("S", vs(out, acc), vs(a, bias), lambda q: q.activation(out["ap"], a["ap"], f, **kw))
 
-    def mm(out, pairs, start=True, stop=True):
-        n = len(pairs)
+    def mms(triples, start=True, stop=True):
+        n = len(triples)
 
         def call(q):
             x = None
-            for k, (l, r) in enumerate(pairs):
-                x = q.matmul(out["ap"], l["ap"], r["ap"], start and k == 0, stop and k == n - 1)
+            for k, (o, l, r) in enumerate(triples):
+                x = q.matmul(o["ap"], l["ap"], r["ap"], start and k == 0, stop and k == n - 1)
             return x
-        op("T", [out], [v for p in pairs for v in p], call)
+        op("T", [triples[0][0]], [v for p in triples for v in p[1:]], call)
 
-    def mm2(out, early, late):
-        mm(out, early, True, False)
-        mm(out, late, False, True)
+    def mm(out, pairs, start=True, stop=True):
+        mms([(out, l, r) for l, r in pairs], start, stop)
 
-    def iota(out, pattern, base, cm):
+    def iota(out, pattern, base, cm=0):
         op("G", [out], [], lambda q: q.iota(out["ap"], pattern, base, cm, allow_small_or_imprecise_dtypes=True))
 
     def sel(out, a, pattern, cmp_, base, cm):
         op("G", [out], [a], lambda q: q.affine_select(out["ap"], a["ap"], pattern, cmp_, 0.0, base, cm))
 
-    def wrap(base, buf, i, w=512, x=0):
-        return (V(base, 15 - i, 143 - i), V(buf, x + i, x + w, 16))
+    def wraps(base, buf, x, w):
+        return [(V(base, 15 - i, 143 - i), V(buf, x + i, x + w, 16)) for i in range(16)]
 
-    def wraps(base, buf, w=512, x=0):
-        return [wrap(base, buf, i, w, x) for i in range(16)]
-
-    def send(r, s, src, dst, w, width):
-        begin("G", [], [V(src, w[d], w[d] + width) for d in hop])
+    def send(r, s, src, owners):
+        buf, wr, w, r0 = MSG[s]
+        x = (r + r0) * wr + me * w
+        begin("G", [], [V(src(o)[0], src(o)[1], src(o)[1] + w) for o in owners])
         eng = hop_engines(core, hop, topo, s)
-        far, near = [d for d in hop if hop[d] != d], [d for d in hop if hop[d] == d]
-        for ds in ([far, near] if s == "a" else [far + near]):
-            tr = []
-            for d in ds:
-                rid, pid = topo.addr(hop[d], core)
-                tr.append(RemoteDMATransfer(dst_ids=[DstId(rid=rid, pnc=pid)], dma_engine_mask=bits(eng[d]), remote_sem=T.sem["%s%d" % (s, r)],
-                                            src=T[src][:, w[d]:w[d] + width], dst=T[dst[0]][:, dst[1]:dst[1] + width]))
-                count["ls"] += len(eng[d])
-            g.remote_dma_fused(tr, local_sem=T.sem.ls)
+        tr = []
+        for o in owners:
+            d = T.cores[o]
+            rid, pid = topo.addr(hop[d], core)
+            tr.append(RemoteDMATransfer(dst_ids=[DstId(rid=rid, pnc=pid)], dma_engine_mask=bits(eng[d]), remote_sem=T.sem["%s%d" % (s, r)],
+                                        src=T[src(o)[0]][:, src(o)[1]:src(o)[1] + w], dst=T[buf][:, x:x + w]))
+            count["ls"] += len(eng[d])
+        g.remote_dma_fused(tr, local_sem=T.sem.ls)
 
-    def arrive(r, s, name, x, stride, width):
+    def arrive(r, s):
+        buf, wr, w, r0 = MSG[s]
         n = 0
         for c in T.cores:
             if c != core:
@@ -238,252 +244,282 @@ def rank_program(g, core, T, topo):
         sem = "%s%d" % (s, r)
         for q in range(4):
             if q != me:
-                logs[name] = logs.get(name, []) + [(x + q * stride, x + q * stride + width, True, "net", sem, n, {sem: n})]
+                x = (r + r0) * wr + q * w
+                logs[buf] = logs.get(buf, []) + [(x, x + w, True, "net", sem, n, {sem: n})]
 
-    dma("Y", V("F8I", P=8), EXT(T.f0[:, :]), "l0")
-    for q in range(4):
-        dma("Y" if q % 2 else "S", V("A", q * 144, q * 144 + 128), EXT(T.s0[:, q * 128:q * 128 + 128]), "l%d" % (1 + q))
-    for q in range(4):
-        dma("S" if q % 2 else "Y", V("OPW", q * 1024, q * 1024 + 1024), EXT(T.opr[:, q * 1024:q * 1024 + 1024]), "l%d" % (5 + q))
+    others = [o for o in range(4) if o != me]
 
+    dma("Y", V("A", 0, SL), EXT(T.s0[:, :]), "l1")
+    dma("S", V("F8I", P=8), EXT(T.f0[:, :]), "l0")
+    for q in range(4):
+        dma("S" if q % 2 else "Y", V("OPW", q * 1024, q * 1024 + 1024), EXT(T.opr[:, q * 1024:q * 1024 + 1024]), "l%d" % (2 + q))
+
+    def L(k):
+        return V("LC", k, k + 1)
+
+    lane, L0, DA_, DB_, FB, WL, INI, T0 = L(0), L(1), L(2), L(3), L(4), L(5), L(8), L(9)
     fill(V("ONE"), 1.0)
     iota(V("LI", 0, 1), [[1, 1]], 0, 1)
-    iota(V("LM"), [[1, 16]], 0, 0)
-    iota(V("CL", 0, 32), [[144, 4], [16, 8]], 0, 0)
-    iota(V("CL", 32, 40), [[8, 2], [0, 2], [288, 2]], 128, 0)
+    iota(V("LM"), [[1, 16]], 0)
     sel(V("S1"), V("ONE", 0, 144), [[0, 9], [1, 16]], O.is_equal, -15, 0)
     sel(V("S1"), V("S1"), [[-16, 9], [0, 16]], O.is_ge, 0, 1)
     sel(V("S1"), V("S1"), [[16, 9], [0, 16]], O.is_ge, 15, -1)
-    sel(V("B8", P=8), V("ONE", 0, 144, P=8), [[0, 9], [1, 16]], O.is_equal, -15, 0)
-    sel(V("B8", P=8), V("B8", P=8), [[1, 9], [0, 16]], O.is_equal, 0, -1)
-    sel(V("ID"), V("ONE", 0, 128), [[-1, 128]], O.is_equal, 0, 1)
     sel(V("BLK"), V("ONE", 0, 128), [[-16, 8], [0, 16]], O.is_ge, 0, 1)
     sel(V("BLK"), V("BLK"), [[16, 8], [0, 16]], O.is_ge, 15, -1)
+    sel(V("ID"), V("ONE", 0, 128), [[-1, 128]], O.is_equal, 0, 1)
+    sel(V("B8", P=8), V("ONE", 0, 144, P=8), [[0, 9], [1, 16]], O.is_equal, -15, 0)
+    sel(V("B8", P=8), V("B8", P=8), [[1, 9], [0, 16]], O.is_equal, 0, -1)
+    iota(V("CLF"), [[0, 2], [256, 2]], 0)
+    iota(V("KD"), [[16, 8], [0, 32]], 0)
     sel(V("NUT"), V("BLK"), [[-1, 128]], O.is_gt, 0, 1)
-    iota(V("DM"), [[0, 4], [1, 16]], 0, 0)
-    iota(V("K"), [[0, 4], [1, 128]], 0, 0)
-    iota(V("O32"), [[32, 4], [0, 8]], 0, 0)
-    iota(V("O272"), [[272, 4], [0, 8]], 0, 0)
-    iota(V("K1"), [[0, 4], [1, 128]], 1, 0)
-    iota(V("B8C"), [[8, 12], [0, 8]], 0, 0)
-    iota(V("B256"), [[256, 12], [0, 8]], 128, 0)
-    iota(V("DM3"), [[0, 12], [1, 8]], 0, 0)
+    iota(V("DT"), [[0, 8], [272, 2], [16, 16]], 16)
+    iota(V("K"), [[16, 8], [0, 2], [1, 16]], 0)
+    iota(V("K1"), [[16, 8], [0, 2], [1, 16]], 129)
+    iota(V("CO"), [[0, 8], [-4352, 2]], 0)
+    iota(V("CL"), [[16, 32]], 0)
+    for k in range(4):
+        iota(V("RW", 16 * k, 16 * k + 16), [[1, 16]], (1, 0, -1, 8)[k])
+    for k, row in enumerate(({0: 15, 2: 0, 6: 3, 10: 7, 13: 11, 14: 18, 15: 15}, {0: 16},
+                             {0: 17, 1: 15, 3: 6, 7: 10, 11: 13, 14: 19, 15: 15}, {0: 3, 1: 4, 2: 5, 8: 19, 9: 20, 10: 21, 15: 8})):
+        for i in row:
+            iota(V("RW", 16 * k + i, 16 * k + i + 1), [[1, 1]], row[i])
+    iota(V("K13"), [[0, 4], [1, 128]], 129)
+    iota(V("KD3"), [[16, 8], [0, 96]], 0)
+    iota(V("DT3"), [[0, 8], [1, 96]], 1)
+    iota(V("RM"), [[0, 12], [1, 8]], 0)
     sel(V("G8"), V("ONE", 0, 8), [[-16, 8]], O.is_ge, 0, 1)
     sel(V("G8"), V("G8"), [[16, 8]], O.is_ge, 15, -1)
+
     for i in range(16):
-        fill(V("WR", i, i + 1), float(WT[i]))
-    for o in range(3):
-        fill(V("E8C", o, o + 1), 811.0 * o)
+        fill(V("RW", 64 + i, 65 + i), float(WT[i]))
     ts(V("LI", 1, 2), V("LI", 0, 1), 15, O.bitwise_and)
-    lane = V("LC", 0, 1)
     cp(lane, V("LI", 1, 2))
-    ts(V("LI", 2, 3), V("LI", 1, 2), 7, O.bitwise_and)
-    ts(V("LI", 3, 4), V("LI", 1, 2), 3, O.arith_shift_right)
     ts(V("LM"), V("LM"), lane, O.is_equal)
-    ts(V("LC", 3, 4), V("LI", 3, 4), 144.0, O.mult)
-    tt(V("W2"), V("WR"), V("LM"), O.mult)
-    tt(V("LC", 4, 5), V("LC", 3, 4), V("LI", 2, 3), O.add)
-    red(V("LC", 1, 2), V("W2"), O.add)
-    ts(V("CL", 0, 32), V("CL", 0, 32), lane, O.add)
-    ts(V("CL", 32, 40), V("CL", 32, 40), V("LC", 4, 5), O.add)
-    cp(V("LI", 4, 5), V("LC", 1, 2))
-    ts(V("LI", 5, 6), V("LI", 4, 5), 3, O.bitwise_and)
-    ts(V("LC", 2, 3), V("LI", 5, 6), -1.0, O.mult, 1026.0, O.add)
-    ts(V("WM"), V("S1"), V("LC", 1, 2), O.mult)
-    ts(V("F8", P=8), V("F8I", P=8), -1023.0, O.add)
-    ts(V("B8", P=8), V("B8", P=8), 1.0 / 32, O.mult)
+    tt(V("RX", 64, 80), V("RW", 64, 80), V("LM"), O.mult)
+    ts(L(10), lane, 0.0, O.is_equal)
+    ts(L(11), lane, 1.0, O.is_equal)
+    red(WL, V("RX", 64, 80), O.add)
+
+    def two(out, a, b, k):
+        ts(L(k), L(11), b, O.mult)
+        ts(L(k + 1), L(10), a, O.mult, L(k), O.add)
+        ts(out, V("ONE", 0, out["ap"].shape[-1]), L(k + 1), O.mult)
+
+    ts(V("WM"), V("S1"), WL, O.mult, 0.25, O.mult)
+    two(V("CM"), -512.0, 0.125, 12)
+    ts(L(14), L(11), -1.5 / 4096, O.mult)
+    ts(L(18), lane, 2.0, O.is_equal, -1.0, O.mult)
+    ts(L(15), L(10), -1600.0 / 4096, O.mult, L(14), O.add)
+    ts(V("M2"), V("ONE", 0, 64), L(18), O.mult)
+    for j in range(8):
+        fill(V("CK", j, j + 1), 2048.0 - KA[j] / 2.0 - 0.25)
+
+    def C(k, n=1):
+        return V("SV", k, k + n)
+
+    U, U0, U2, LO1, LIM, LMN, THR, MN = [C(k) for k in range(8)]
+    CJ = V("CK", 8, 16)
+    fill(V("TB"), 0.0)
+    fill(U, 1023.0)
+    fill(V("TB", 3, 4), 100000.0)
+    fill(V("TB", 8, 11), float(EMPTY * SL))
+    fill(V("TB", 11, 12), 1.0)
 
     def consts1():
-        ts(V("XB"), V("S1"), V("LC", 2, 3), O.mult)
-        ts(V("IDF"), V("ID"), 131072.0, O.mult)
+        cp(V("LI", 4, 5), WL)
+        ts(V("F8", P=8), V("F8I", P=8), -1023.0, O.add)
+        ts(V("LI", 5, 6), V("LI", 4, 5), 3, O.bitwise_and)
         ts(V("IDN"), V("ID"), -1.0, O.mult)
-        for o in range(4):
-            fill(V("BO", o, o + 1), -8192.0 * o)
+        ts(L(6), V("LI", 5, 6), -1.0, O.mult, 1026.0, O.add)
+        ts(L(7), lane, 16.0, O.mult)
+        mm(V("P5", 0, 32), [(V("B8", 15 - i, 143 - i, P=8), V("F8", i, 512, 16, P=8)) for i in range(16)])
+        ts(V("XB"), V("S1"), L(6), O.mult, 1.0 / 4096, O.mult)
+        ts(V("CLF"), V("CLF"), L(7), O.add)
+        act(V("AC", 0, 32), V("P5", 0, 32), F.Copy)
         fill(V("CH", 4096, 4112), 0.0)
 
     def consts2():
-        cp(V("BLKF"), V("BLK"))
-        ts(V("NBF"), V("BLK"), -4096.0, O.mult)
-        ts(V("NB"), V("BLK"), -4096.0, O.mult)
-        fill(V("CQ", 0, 1), 524288.0)
-        fill(V("CQ", 1, 2), 2048.0)
-        ts(V("LC", 8, 9), lane, 0.0, O.is_equal, -15728640.0, O.mult)
-        ts(V("LC", 9, 10), lane, 1.0, O.is_equal, 4096.0, O.mult)
-        for o in range(2):
-            tt(V("CA", o, o + 1), V("LC", 8, 9), V("LC", 9, 10), O.add)
-        ts(V("NUT"), V("NUT"), -1.0, O.mult)
+        ts(V("IDP"), V("ID"), 16777216.0, O.mult)
+        ts(V("IDM"), V("ID"), -16777216.0, O.mult)
+        ts(V("NBH"), V("BLK"), -32768.0, O.mult)
+        ts(V("NBF"), V("BLK"), -16384.0, O.mult)
+        ts(V("NBD"), V("BLK"), -2048.0, O.mult)
+        ts(V("ID2K"), V("ID"), 2048.0, O.mult)
+        two(V("CA"), -16384.0 * 3840, 16384.0, 16)
+        ts(INI, L(10), -128.5, O.mult)
+        fill(T0, 2.0 * STEPS[0] - 0.5 - OFFS)
+        fill(V("ZH"), 0.0)
+        for k, (a, b) in enumerate(((0, 2), (2, 4), (4, 6), (6, 7), (7, 8), (8, 9))):
+            fill(V("RX", a, b), (0.0, -1.0, -2.0, 1.0, 1.0, -1.0)[k])
+        for i, s in enumerate(STEPS):
+            ts(V("CT", 16 * i, 16 * i + 7), V("RX", 0, 7), float(s), O.mult, float(s // 2), O.add)
+            ts(V("CT", 16 * i + 7, 16 * i + 9), V("RX", 7, 9), float(s), O.mult)
+        ts(V("KD"), V("KD"), lane, O.add, 0.5, O.add)
+        fill(V("DT", 15, 256, 32), 272.0)
+        fill(V("KD", 15, 256, 16), 200.0)
+        fill(V("DT", 31, 256, 32), 0.0)
+        ts(V("ID16"), V("ID"), 128.0, O.mult)
+        tt(V("NUT"), V("ID16"), V("NUT"), O.subtract)
         ts(V("ID16"), V("ID"), 16.0, O.mult)
+        ts(V("S16"), V("S1"), 16.0, O.mult)
         ts(V("SD"), V("S1"), lane, O.mult)
-        ts(V("S32"), V("S1"), 1.0 / 32, O.mult)
-        ts(V("DM"), V("DM"), lane, O.is_equal)
-        fill(V("ZERO"), 0.0)
-        fill(V("YW", 256, 272), 0.0)
+        ts(V("CE"), V("ONE", 0, 16), L(10), O.mult, 1023.0, O.mult)
         fill(V("W"), 0.0)
-        fill(V("EBW"), 1000.0)
+        fill(V("EBW"), 0.0)
+        fill(V("YW", 256, 272), 0.0)
+        fill(V("YW", 528, 544), 0.0)
+        fill(V("MB", me * 4 + 3, NR * 16, 16), 5000.0)
 
     def consts3():
+        for k in range(4):
+            tt(V("RX", 16 * k, 16 * k + 16), V("RW", 16 * k, 16 * k + 16), V("LM"), O.mult)
+        for k in range(4):
+            red(L(1 + k), V("RX", 16 * k, 16 * k + 16), O.add)
+        ts(V("CL"), V("CL"), lane, O.add)
+        fill(V("C8", 0, 1), 811.0)
+        fill(V("C8", 1, 2), -811.0)
+        tt(DB_, DB_, DA_, O.subtract)
+        tt(DA_, DA_, L0, O.subtract)
+
+    def consts4():
         fill(V("A", EMPTY * SL, EMPTY * SL + SL), 0.0)
-        ts(V("LC", 6, 7), lane, -128.0, O.add)
-        ts(V("RM"), V("DM3"), 0.0, O.is_gt)
-        ts(V("DM3"), V("DM3"), lane, O.is_equal)
-        ts(V("LC", 5, 6), lane, 6.5, O.is_gt, 1000.0, O.mult)
-        ts(V("SE"), V("S1"), V("LC", 6, 7), O.mult)
+        fill(V("AC", EMPTY * 32, EMPTY * 32 + 32), 0.0)
+        ts(V("RM"), V("RM"), 0.0, O.is_gt)
+        ts(V("KD3"), V("KD3"), lane, O.add, 0.5, O.add)
+        ts(V("SN"), V("S1"), -8192.0, O.mult)
         ts(V("G8F"), V("G8"), 1.0 / 16, O.mult)
-        ts(V("G8"), V("G8"), 32.0, O.mult)
-        fill(V("S3"), 0.0)
+        ts(V("IDF"), V("ID"), 16.0, O.mult)
+        fill(V("DT3", 95, 768, 96), 0.0)
+        fill(V("KD3", 7, 768, 8), 200.0)
+        fill(V("C3"), 8192.0)
+        fill(V("DB"), 0.0)
 
-    def C(k):
-        return V("SV", k, k + 1)
+    def Q(r, k, n=1):
+        return V("TB", r % 2 * 32 + k, r % 2 * 32 + k + n)
 
-    def w_(k, n=1):
-        return V("SW", k, k + n)
+    def derived(r):
+        ts(CJ, V("CK", 0, 8), Q(r, 14), O.add)
+        ts(LMN, Q(r, 0), -1023.0, O.add)
+        ts(THR, Q(r, 3), -1023.0, O.add)
+        ts(V("CZ"), V("M2"), LMN, O.mult, L(15), O.add)
+        ts(LIM, Q(r, 0), -1.0, O.mult, 1022.5 - OFFS, O.add)
 
-    LO, HI, PT, U, EE, EL, ER = V("SV", 0, 3), V("SV", 4, 7), V("SV", 8, 11), C(12), V("SV", 17, 20), V("SV", 18, 21), V("SV", 16, 19)
-    LOE, BASE, E8, CC, LIM, LMN, THR = C(24), C(25), C(26), C(27), C(28), C(29), C(30)
-    fill(V("SV"), 0.0)
-    fill(U, 1023.0)
-    fill(C(3), 100000.0)
-    fill(C(17), 1.0)
-    fill(V("SV", 9, 12), float(EMPTY * SL))
+    def pre(r):
+        ts(LO1, Q(r, 0), 1.0, O.add)
+        ts(U0, Q(r, 11), 5000.0, O.mult, U, O.add)
+        ts(U2, Q(r, 12), -5000.0, O.mult, U, O.add)
+        ts(Q(r, 17), Q(r, 2), 1.0, O.add, Q(r, 3), O.max)
+        ts(Q(r, 18, 2), V("C8"), Q(r, 14), O.add)
+        fill(Q(r, 8), float((r + 1) * SL))
 
-    def split(blocks):
-        for o, (buf, x) in blocks:
-            ts(V(buf, x, x + 8), V("PN", o * 8, o * 8 + 8), MAGIC, O.add, MAGIC, O.subtract)
-        for o, (buf, x) in blocks:
-            tt(V(buf, x + 8, x + 16), V("PN", o * 8, o * 8 + 8), V(buf, x, x + 8), O.subtract)
-
-    mm(V("PN", 0, 32), [(V("B8", 15 - i, 143 - i, P=8), V("F8", i, 512, 16, P=8)) for i in range(16)])
-    split([(q, ("A", q * 144 + 128)) for q in range(4)])
+    def level(r):
+        B, m = Q(r, 4), MN
+        gone, over, last, rt, back, w = [C(k) for k in range(8, 14)]
+        red(B, V("MB", r * 16, r * 16 + 16, 2), O.min)
+        red(m, V("MB", r * 16 + 1, r * 16 + 16, 2), O.min)
+        ts(over, B, LO1, O.max, U0, O.is_ge)
+        ts(gone, m, B, O.is_ge, 4000.0, O.mult)
+        ts(last, m, B, O.is_lt, Q(r, 12), O.mult)
+        tt(Q(r, 16), B, LO1, O.max)
+        ts(rt, gone, m, O.max, U2, O.is_ge)
+        ts(back, over, last, O.max, DB_, O.mult)
+        ts(C(14), last, -5000.0, O.mult, m, O.add)
+        ts(w, back, DA_, O.add, rt, O.mult)
+        ts(U, C(14), 5000.0, O.add, U, O.min)
+        ts(V("OFQ", 0, 1), w, L0, O.add)
+        cp(Q(r + 1, 0, 16), IND(Q(r, 0, 24), V("OFQ", 0, 1)))
 
     def parents(r):
         if r:
-            level_a(r - 1)
-        tt(w_(0, 3), PT, EE, O.mult)
-        red(BASE, w_(0, 3), O.add)
-        ts(V("OFA"), V("CL"), BASE, O.add)
-        tt(w_(3, 3), V("E8C", 0, 3), EE, O.mult)
-        tt(w_(23, 3), V("SV", 3, 6), EE, O.mult)
-        red(E8, w_(3, 3), O.add)
-        red(THR, w_(23, 3), O.add)
+            ts(V("OFA"), V("CL"), Q(r, 7), O.add)
+        ts(V("OFF"), V("CLF"), Q(r, 7), O.add, 1.0 / 16, O.mult) if r else None
+        derived(r)
+        mm(V("P4", 0, 32), [(V("BLK"), V("CM"))], True, False)
         if r:
-            level_b()
-        tt(w_(6, 3), LO, EE, O.mult)
-        ts(THR, THR, -1023.0, O.add, 1.0 / 32, O.mult)
-        red(LOE, w_(6, 3), O.add)
-        fill(V("TT"), 511.5)
-        ts(CC, LOE, -4096.0, O.mult, 444.0 + 4096.0 * 1023, O.add)
-        ts(LIM, LOE, -1.0, O.mult, 1022.5, O.add)
-        ts(LMN, LOE, -1023.0, O.add)
-        lay = V("A", 0, (r + 1) * SL)
-        cp(V("S", 0, 256), IND(lay, V("OFA", 0, 16)))
-        act(V("S", 256, 512), IND(lay, V("OFA", 16, 32)), F.Copy)
-        act(V("FS"), IND(lay, V("OFA", 32, 40)), F.Copy)
-        mm(V("PU", 0, 32), wraps("WM", "S"))
-        tt(V("T8"), V("FS", 0, 64), V("FS", 64, 128), O.add)
-        ts(V("P8"), V("T8"), THR, O.is_ge, 32.0, O.mult)
-        tt(V("FS", 0, 64), V("FS", 0, 64), V("P8"), O.add)
+            lay = V("A", 0, (r + 1) * SL)
+            cp(V("S", 0, 256), IND(lay, V("OFA", 0, 16)))
+            act(V("S", 256, 512), IND(lay, V("OFA", 16, 32)), F.Copy)
+        mm(V("P4", 0, 32), wraps("WM", "S" if r else "A", 0, 512), False, True)
+
+    def children(r):
+        par = V("S" if r else "A", 0, 512)
         if not r:
             consts1()
+            ts(V("OFF"), V("CLF"), 1.0 / 16, O.mult)
         for k in range(2):
-            mm(V("PC%d" % k, 0, 512), [(V("IDN"), V("S"))], True, False)
-
-    def pre(r):
-        tt(w_(22, 3), V("SV", 9, 12), EE, O.mult)
-        ts(w_(19, 3), EE, float((r + 1) * SL), O.mult)
-        ts(w_(13, 3), EE, -1.0, O.mult, 1.0, O.add)
-        ts(w_(36), LOE, 1.0, O.add)
-        ts(w_(38), C(17), -1.0, O.mult, 1.0, O.add)
-        ts(w_(40, 3), LO, 1.0, O.add)
-        tt(w_(19, 3), w_(19, 3), w_(22, 3), O.subtract)
-        tt(HI, HI, w_(13, 3), O.mult)
-        tt(V("SV", 9, 12), V("SV", 9, 12), w_(19, 3), O.add)
-
-    def level_a(r):
-        B, m, rt, lp, bk, up, st = [w_(k) for k in (10, 11, 27, 28, 29, 30, 39)]
-        red(w_(12), V("MB", r * 16 + 1, r * 16 + 16, 4), O.min)
-        red(B, V("MB", r * 16, r * 16 + 16, 4), O.min)
-        ts(V("MD"), V("LM"), w_(12), O.mult)
-        mm(V("PN", 0, 16), [(V("BLKF"), V("MD"))])
-        ts(w_(13, 3), EE, B, O.mult)
-        tt(lp, w_(36), B, O.max)
-        tt(HI, HI, w_(13, 3), O.add)
-        red(m, V("PN", 0, 16), O.min)
-        tt(w_(26), m, B, O.is_lt)
-        tt(w_(35), m, B, O.is_ge)
-        tt(w_(31), w_(26), C(19), O.mult)
-        tt(w_(35), w_(35), C(19), O.max)
-        ts(w_(32), w_(31), -4000.0, O.mult, 4000.0, O.add)
-        tt(w_(33), w_(32), m, O.max)
-        tt(U, U, w_(33), O.min)
-        tt(w_(34), m, U, O.is_ge)
-        tt(w_(37), lp, U, O.is_ge)
-        tt(rt, w_(34), w_(35), O.max)
-        tt(w_(37), w_(37), w_(38), O.mult)
-        ts(up, rt, -1.0, O.mult, 1.0, O.add)
-        tt(bk, w_(37), rt, O.mult)
-        ts(w_(46, 3), ER, up, O.mult)
-        tt(st, rt, bk, O.subtract)
-        ts(w_(49, 3), EL, bk, O.mult)
-        ts(w_(43, 3), EE, bk, O.mult)
-        ts(w_(52, 3), EE, st, O.mult)
-        ts(w_(55, 3), EE, st, O.mult, lp, O.mult)
-        tt(w_(16, 3), w_(46, 3), w_(49, 3), O.add)
-        tt(EE, w_(16, 3), w_(52, 3), O.add)
-
-    def level_b():
-        tt(w_(40, 3), w_(40, 3), HI, O.max)
-        tt(w_(43, 3), w_(43, 3), EE, O.add)
-        ts(w_(43, 3), w_(43, 3), -1.0, O.mult, 1.0, O.add)
-        tt(w_(40, 3), w_(40, 3), w_(49, 3), O.mult)
-        tt(LO, LO, w_(43, 3), O.mult)
-        tt(w_(40, 3), w_(40, 3), w_(55, 3), O.add)
-        tt(LO, LO, w_(40, 3), O.add)
-
-    def rnd(r):
-        parents(r)
-        cp(V("UI"), V("PU", 0, 32))
-        ts(V("UU"), V("UI"), 4095, O.bitwise_and)
-        tt(V("USQ"), V("UU"), V("UU"), O.mult)
-        cp(V("UF"), V("UU"))
-        ts(V("BB"), V("USQ"), 4, O.arith_shift_right)
+            mm(V("P%d" % k), [(V("IDN"), par)], True, False)
+        ts(V("MR"), V("P4", 0, 32), MAGIC * 1024, O.add, MAGIC * 1024, O.subtract)
+        tt(V("MZ"), V("P4", 0, 32), V("MR"), O.subtract)
+        act(V("SQ"), V("MZ"), F.Square, bias=511.875)
         for j in range(2):
-            ts(V("TJ", j * 32, j * 32 + 32), V("UU"), float(KA[j]), O.mult, E8, O.add)
+            ts(V("TJ", j * 32, j * 32 + 32), V("MZ"), 4.0 * KA[j], O.mult, V("CK", 8 + j, 9 + j), O.add)
         for j in range(2, 8):
-            act(V("TJ", j * 32, j * 32 + 32), V("UF"), F.Identity, bias=E8, scale=float(KA[j]))
+            act(V("TJ", j * 32, j * 32 + 32), V("MZ"), F.Identity, bias=V("CK", 8 + j, 9 + j), scale=4.0 * KA[j])
 
         def numbers(j0, j1):
             for j in range(j0, j1):
-                tt(V("VJ", j * 32, j * 32 + 32), V("TJ", j * 32, j * 32 + 32), V("BB"), O.add)
+                tt(V("VJ", j * 32, j * 32 + 32), V("TJ", j * 32, j * 32 + 32), V("SQ"), O.add)
             a, b = j0 * 32, j1 * 32
             ts(V("VK", a, b), V("VJ", a, b), 4095, O.bitwise_and)
             cp(V("OFO", a, b), V("VK", a, b))
 
         def gather(k):
             x, y = k * 512, k * 512 + 512
-            tt(V("D", x, y), IND(V("OPW"), V("OFO", k * 32, k * 32 + 32)), V("S"), O.subtract)
+            tt(V("D", x, y), IND(V("OPW"), V("OFO", k * 32, k * 32 + 32)), par, O.subtract)
 
         def other(k):
             z = k // 2 * 512
             act(V("GA", z, z + 512), IND(V("OPW"), V("OFO", k * 32, k * 32 + 32)), F.Copy)
-            mm(V("PC%d" % (k // 2), 0, 512), [(V("ID"), V("GA", z, z + 512))], False, True)
+            mm(V("P%d" % (k // 2)), [(V("ID"), V("GA", z, z + 512))], False, True)
 
         def size(k):
             x, y = k * 512, k * 512 + 512
-            act(V("CH", x, y), V("PC%d" % (k // 2), 0, 512) if k in (1, 3) else V("D", x, y), F.Abs)
+            act(V("CH", x, y), V("P%d" % (k // 2)) if k in (1, 3) else V("D", x, y), F.Abs)
 
         def sums(k):
-            mm2(V("PX" if k < 2 else "PEA", k * 64, k * 64 + 64), [(V("IDF"), V("FS", 0, 64)), (V("IDF"), V("FS", 64, 128))],
-                wraps("XB", "CH", 1024, k * 1024))
+            z = V("P%d" % (2 + k // 2), k % 2 * 64, k % 2 * 64 + 64)
+            mm(z, [(V("ID"), V("FS")), (V("BLK"), V("CZ"))], True, False)
+            mm(z, wraps("XB", "CH", k * 1024, 1024), False, True)
+
+        def costs():
+            act(V("FSA"), IND(V("AC", 0, (r + 1) * 32), V("OFF")), F.Copy)
+            ts(V("FSP"), IND(V("AC", 0, (r + 1) * 32), V("OFF")), THR, O.is_lt, -4096.0, O.mult)
+
+        def costs2():
+            tt(V("FS"), V("FSA"), V("FSP"), O.max)
+
+        def keys(h):
+            a, b = h * 128, h * 128 + 128
+            z = V("P%d" % (2 + h), 0, 128)
+            ts(V("QQ", a, b), z, MAGIC / 1024, O.add, MAGIC / 1024, O.subtract)
+            ts(V("YH", a, b), z, MAGIC, O.add, MAGIC, O.subtract)
+            tt(V("DD", a, b), z, V("QQ", a, b), O.subtract)
+            ts(V("PEN", a, b), V("YH", a, b), 0.0, O.is_lt, 8192.0, O.mult)
+            base = [(V("ID"), V("YH", a, b)), (V("ID"), V("PEN", a, b))]
+            for c in range(2):
+                x = 256 + c * 256
+                ts(V("PEN", x + a, x + b), V("DD", a, b), (own[c][0] - 1.5) / 4096, O.not_equal, 8192.0, O.mult)
+            for c in range(2):
+                mm(V("P%d" % c, a, b), base + [(V("IDM" if own[c][1] else "IDP"), V("DD", a, b))])
+                mm(V("P%d" % (5 + c), a, b), base + [(V("ID"), V("PEN", 256 + c * 256 + a, 256 + c * 256 + b))])
+            mm(V("P4", a, b), base)
+
+        def halves(h, c):
+            cp(V("XH", c * 256 + h * 128, c * 256 + h * 128 + 128), V("P%d" % (5 + c), h * 128, h * 128 + 128))
 
         numbers(0, 2)
         other(1)
         gather(0)
         size(0)
         size(1)
-        sums(0)
         numbers(2, 8)
         other(3)
-        for k in (2, 4, 5, 6, 7):
+        gather(2)
+        costs()
+        gather(4)
+        costs2()
+        sums(0)
+        for k in (5, 6, 7):
             gather(k)
         size(2)
         size(3)
@@ -494,180 +530,259 @@ def rank_program(g, core, T, topo):
                 sums(k // 2)
         if not r:
             consts2()
-        for p, a, b in (("PX", 0, 128), ("PEA", 128, 256)):
-            ts(V("XI", a, b), V(p, a, b), CC, O.add)
-            ts(V("OW", a, b), V("XI", a, b), 3, O.bitwise_and)
-            ts(V("Y", a, b), V("XI", a, b), 12, O.arith_shift_right, 4095, O.bitwise_and)
-            ts(V("OW4", a, b), V("OW", a, b), 8192.0, O.mult)
-            tt(V("Z", a, b), V("Y", a, b), V("OW4", a, b), O.add)
-            for o in (0, 1, 2):
-                act(V("X", o * 256 + a, o * 256 + b), V("Z", a, b), F.Abs, bias=V("BO", o, o + 1))
-            ts(V("OW3", a, b), V("OW", a, b), 3.0, O.not_equal, 8192.0, O.mult)
-            tt(V("XH", 768 + a, 768 + b), V("OW3", a, b), V("Y", a, b), O.add)
-            if not a:
-                cp(V("XH", 512, 640), V("X", 512, 640))
-        cp(V("XH", 640, 768), V("X", 640, 768))
-        for k in range(2):
-            mm(V("PC%d" % k, 64, 66), [(V("ID"), V("CQ"))])
-        s = 512
-        while s:
-            mm(V("PN", 0, 2), [(V("BLK"), V("CA"))], True, False)
-            for o in (0, 1):
-                act(V("DA", o * 256, o * 256 + 256), V("X", o * 256, o * 256 + 256), F.Sign, bias=V("TT", o, o + 1), scale=-1.0, acc=V("CN", o, o + 1))
-            for o in (3, 2):
-                z = o * 256 - 512
-                ts(V("DV", z, z + 256), V("XH", z + 512, z + 768), V("TT", o, o + 1), O.is_lt)
-                mm(V("PC%d" % (o - 2), 0, 64), [(V("NB"), V("DV", z + 64 * x, z + 64 * x + 64)) for x in range(4)])
-            mm(V("PN", 0, 2), [(V("NBF"), V("CN", 0, 2))], False, True)
-            if s > 1:
-                ts(V("TLO"), V("TT"), -s / 2.0, O.add)
-                ts(V("THI"), V("TT"), s / 2.0, O.add)
+        keys(0)
+        for c in range(2):
+            cand(c, 0)
+        for c in range(2):
+            halves(0, c)
+        keys(1)
+        for c in range(2):
+            halves(1, c)
+
+    def TH(c, i):
+        return T0 if i == 0 else V("TT", c * 16 + i % 2 * 8 + 5, c * 16 + i % 2 * 8 + 6)
+
+    def cand(c, i):
+        x = c * 32 + i % 2 * 16
+        if i < 4:
+            ts(V("CAND", x, x + 9), V("CT", 16 * i, 16 * i + 9), TH(c, i), O.add)
+        else:
+            ts(V("CAND", x, x + 9), V("CT", 16 * i, 16 * i + 9), TH(c, i), O.add, LIM, O.min)
+
+    def signs(c, i):
+        x = c * 32 + i % 2 * 16
+        for k, bias in ((1, TH(c, i)), (0, V("CAND", x + 7, x + 8)), (2, V("CAND", x + 8, x + 9))):
+            y = c * 768 + k * 256
+            act(V("DA", y, y + 256), V("P%d" % c, 0, 256), F.Sign, bias=bias, scale=-1.0, acc=V("CN", c * 4 + k, c * 4 + k + 1))
+
+    def below(c, i):
+        for k in range(3):
+            y = c * 768 + k * 256
+            ts(V("DV", y, y + 256), V("XH", c * 256, c * 256 + 256), TH(c, i), O.subtract, OFFS + (1 - k) * STEPS[i], O.is_lt)
+
+    def tally(c, ks):
+        for k in ks:
+            y = c * 768 + k * 256
+            scan(V("RS", y, y + 256), V("DV", y, y + 256), V("ZH"), INI, O.add, O.add)
+
+    def totals(c):
+        p = "P%d" % (5 + c)
+        a, b, ca, cn, rs = V(p, 1, 6, 2), V(p, 0, 6, 2), V("CA", 0, 3), V("CN", c * 4, c * 4 + 3), V("RS", c * 768 + 255, c * 768 + 768, 256)
+
+        def call(q):
+            q.matmul(a["ap"], T.BLK[:, :], ca["ap"], True, False)
+            q.matmul(a["ap"], T.NBF[:, :], cn["ap"], False, True)
+            return q.matmul(b["ap"], T.NBH[:, :], rs["ap"], True, True)
+        op("T", [a], [V("BLK"), V("NBF"), V("NBH"), ca, cn, rs], call)
+
+    def decide(c, i):
+        x, y = c * 32 + i % 2 * 16, c * 16 + (i + 1) % 2 * 8
+        scan(V("TT", y, y + 6), V("P%d" % (5 + c), 0, 6), V("CAND", x, x + 6), V("CAND", x + 6, x + 7), O.min, O.max)
+
+    def search():
+        for c in range(2):
+            signs(c, 0)
+            mm(V("P%d" % (2 + c), 0, 256), [(V("ID2K"), V("KD"))], True, False)
+        below(0, 0)
+        tally(0, (0, 1, 2))
+        totals(0)
+        below(1, 0)
+        tally(1, (0,))
+        for n in range(9):
+            c, i = n % 2, n // 2
+            decide(c, i)
+            tally(1 - c, (1, 2))
+            totals(1 - c)
+            if i < 4:
+                cand(c, i + 1)
+                signs(c, i + 1)
+                below(c, i + 1)
+                tally(c, (0,))
+
+    def kept(c):
+        x = c * 512
+        ts(V("KP", x, x + 256), V("XH", c * 256, c * 256 + 256), TH(c, 5), O.subtract, OFFS, O.is_lt)
+        ts(V("KP", x + 256, x + 512), V("P%d" % c, 0, 256), TH(c, 5), O.is_lt)
+
+    def ranks(c):
+        x = c * 512
+        for o in range(2):
+            y = x + o * 256
+            scan(V("R", y, y + 256), V("KP", y, y + 256), V("ZH"), 0.0, O.add, O.add)
+        mms([(V("P%d" % (2 + c), k * 32, k * 32 + 32), V("NBD"), V("R", x + 15, x + 512, 16)) for k in range(8)], False, True)
+        mm(V("P%d" % (5 + c), 0, 32), wraps("S1", "R", x, 512))
+        for o in range(2):
+            y = c * 544 + o * 272
+            act(V("EBW", y, y + 256, 16), V("P%d" % (5 + c), o * 16, o * 16 + 16), F.Copy)
+
+    def places(c):
+        p = ("P7", "P4")[c]
+        for o in range(2):
+            y = c * 512 + o * 256
+            mm(V(p, o * 256, o * 256 + 256), [(V("BLK"), V("R", y, y + 256)), (V("NUT"), V("KP", y, y + 256))])
+        for o in range(2):
+            y = c * 544 + o * 272
+            act(V("W", y, y + 256), V(p, o * 256, o * 256 + 256), F.Copy)
+
+    def first(c):
+        scan(V("V1", c * 256, c * 256 + 256), V("P%d" % (2 + c), 0, 256), V("DT"), 0.0, O.max, O.min)
+
+    def first_list(c):
+        v1 = V("V1", c * 256 + 14, c * 256 + 256, 16)
+        cp(V("OFB", c * 16, c * 16 + 16), v1)
+        mm(V("P%d" % (2 + c), 0, 16), [(V("ID"), v1)], True, False)
+        mm(V("P%d" % c, 0, 16), [(V("ID16"), v1), (V("ID"), V("CO"))], True, False)
+
+    def second(c):
+        x = c * 256
+        tt(V("IB", x, x + 256), IND(V("EBW", c * 544, c * 544 + 544), V("OFB", c * 16, c * 16 + 16)), V("K"), O.is_le)
+        mm(V("P%d" % (2 + c), 0, 16), wraps("S1", "IB", x, 256), False, True)
+        mm(V("P%d" % c, 0, 16), wraps("S16", "IB", x, 256), False, False)
+
+    def second_list(c):
+        cp(V("OFW", c * 16, c * 16 + 16), V("P%d" % (2 + c), 0, 16))
+
+    def third(c):
+        x = c * 256
+        tt(V("OH", x, x + 256), IND(V("W", c * 544, c * 544 + 544), V("OFW", c * 16, c * 16 + 16)), V("K1"), O.is_equal)
+        mm(V("P%d" % c, 0, 16), wraps("SD", "OH", x, 256), False, True)
+
+    def where(r, buf, home, w):
+        return lambda o: (home, ((r + 1) * 4 + o) * w) if o == me else (buf, (r * 4 + o) * w)
+
+    def states(r, c):
+        at = where(r, "SND", "A", 128)
+        for o in (1, 0):
+            cp(V("OFN", c * 16 + o * 8, c * 16 + o * 8 + 8), V("P%d" % c, o, 16, 2))
+        for o in (1, 0):
+            buf, x = at(own[c][o])
+            v = IND(V("CH"), V("OFN", c * 16 + o * 8, c * 16 + o * 8 + 8))
+            if o:
+                act(V(buf, x, x + 128), v, F.Copy)
             else:
-                ts(V("TLO"), V("TT"), -1.0, O.add, LIM, O.min)
-                ts(V("THI"), V("TT"), LIM, O.min)
-            if s in (256, 128):
-                o = s // 128 - 1
-                cp(V("XH", o * 256, o * 256 + 256), V("X", o * 256, o * 256 + 256))
-            for o in (3, 2):
-                red(V("QN", o, o + 1), V("PC%d" % (o - 2), 0, 66), O.add)
-            for o in (3, 2, 0, 1):
-                ts(V("TT", o, o + 1), V("PN", o, o + 1) if o < 2 else V("QN", o, o + 1), V("TLO", o, o + 1), O.max, V("THI", o, o + 1), O.min)
-            s //= 2
-        for p in ((2, 3), (0, 1)):
-            for o in p:
-                ts(V("KP", o * 256, o * 256 + 256), V("XH", o * 256, o * 256 + 256), V("TT", o, o + 1), O.is_lt)
-            for o in p:
-                scan(V("R", o * 256, o * 256 + 256), V("KP", o * 256, o * 256 + 256), V("ZERO"), O.add, O.add)
+                cp(V(buf, x, x + 128), v)
+        send(r, "a", at, [o for o in own[c] if o != me])
 
-        def places(o):
-            mm(V("PC%d" % (o // 2), o % 2 * 256, o % 2 * 256 + 256), [(V("BLK"), V("R", o * 256, o * 256 + 256)), (V("NUT"), V("KP", o * 256, o * 256 + 256))])
+    def prices(r, c):
+        at = where(r, "SNC", "AC", 8)
+        x = c * 256
+        tt(V("CG", x, x + 256), IND(V("YW"), V("OFW", c * 16, c * 16 + 16)), V("OH", x, x + 256), O.mult)
+        mm(V("P%d" % (2 + c), 0, 16), wraps("S1", "CG", x, 256))
+        for o in range(2):
+            buf, y = at(own[c][o])
+            act(V(buf, y, y + 8), V("P%d" % (2 + c), o, 16, 2), F.Copy)
 
-        def heads(o):
-            tt(V("W", o * 272, o * 272 + 256), V("PC%d" % (o // 2), o % 2 * 256, o % 2 * 256 + 256), V("KP", o * 256, o * 256 + 256), O.mult)
-
-        places(2)
-        mm(V("PEA", 0, 64), [(V("BLK"), V("R", 15, 1024, 16))])
-        mm(V("PEB", 0, 64), [wrap("S1", "R", b, 1024) for b in range(16)])
-        tt(V("EM", 0, 64), V("PEA", 0, 64), V("DM"), O.mult)
-        for o in range(4):
-            red(V("EA", o, o + 1), V("EM", o * 16, o * 16 + 16), O.add)
-        for o in range(4):
-            ts(V("IA", o * 128, o * 128 + 128), V("K", 0, 128), V("EA", o, o + 1), O.is_ge)
-        mm2(V("PL", 0, 32), [(V("ID"), V("O32"))], wraps("S1", "IA"))
-        for o in range(4):
-            act(V("EBW", o * 32, o * 32 + 16), V("PEB", o * 16, o * 16 + 16), F.Copy)
+    def rnd(r):
+        parents(r)
+        children(r)
+        search()
         mb = r * 16 + me * 4
-        red(w_(61), V("TT"), O.min)
-        red(w_(60), V("Y"), O.min)
-        ts(V("MB", mb, mb + 1), w_(61), LOE, O.add, 0.5, O.add)
-        ts(V("MB", mb + 1, mb + 2), w_(60), LOE, O.add, 1023.0, O.min)
-        send(r, "b", "MB", ("MB", mb), {d: mb for d in hop}, 2)
-        arrive(r, "b", "MB", r * 16, 4, 2)
-        ts(V("YW", 0, 256), V("Y"), LMN, O.add)
-        cp(V("OFB"), V("PL", 0, 32))
-        tt(V("AB", 0, 32), V("PL", 0, 32), V("O32"), O.subtract)
-        places(3)
-        tt(V("IB"), IND(V("EBW"), V("OFB")), V("K"), O.is_le)
-        mm2(V("PL", 0, 32), [(V("ID"), V("O272")), (V("ID16"), V("AB", 0, 32))], wraps("S1", "IB"))
+        kept(0)
+        decide(1, 4)
+        for o in range(2):
+            act(V("YW", o * 272, o * 272 + 256), V("P4", 0, 256), F.Identity, bias=LMN)
+        ranks(0)
         places(0)
+        kept(1)
+        first(0)
+        ranks(1)
+        first_list(0)
+        red(C(16), V("YW", 0, 256), O.min)
+        second(0)
         places(1)
-        heads(2)
-        heads(3)
-        ts(V("OFV"), V("PL", 16, 32), -544.0, O.add)
-        cp(V("OFW", 0, 16), V("PL", 0, 16))
-        tt(V("CB"), V("PL", 0, 32), V("O272"), O.subtract)
-        cp(V("OFC"), V("CB"))
-        tt(V("OH", 256, 512), IND(V("W", 544, 1088), V("OFV")), V("K1", 0, 256), O.is_equal)
-        heads(0)
-        heads(1)
-        tt(V("OH", 0, 256), IND(V("W", 0, 544), V("OFW", 0, 16)), V("K1", 0, 256), O.is_equal)
-        mm2(V("PU", 0, 32), [(V("ID16"), V("CB"))], wraps("SD", "OH"))
-        tt(V("CG", 0, 512), IND(V("YW"), V("OFC")), V("OH", 0, 512), O.mult)
-        mm(V("PN", 0, 32), wraps("S32", "CG"))
-        cp(V("OFN"), V("PU", 0, 32))
-        order = [T.cores.index(d) for d in hop] + [me]
-        blk = {o: ("SND", r * SL + o * 144) for o in order}
-        blk[me] = ("A", (r + 1) * SL + me * 144)
-        for k, o in enumerate(order):
-            out, v = V(blk[o][0], blk[o][1], blk[o][1] + 128), IND(V("CH"), V("OFN", o * 8, o * 8 + 8))
-            if k == 1:
-                cp(out, v)
-            else:
-                act(out, v, F.Copy)
-        pre(r)
-        split([(o, (blk[o][0], blk[o][1] + 128)) for o in order[:3]])
-        send(r, "a", "SND", ("A", (r + 1) * SL + me * 144), {d: blk[T.cores.index(d)][1] for d in hop}, 144)
-        split([(me, (blk[me][0], blk[me][1] + 128))])
-        arrive(r, "a", "A", (r + 1) * SL, 144, 144)
+        ts(V("MD"), V("LM"), C(16), O.mult, 0.0, O.min)
+        mm(V("P6", 0, 16), [(V("BLK"), V("CE")), (V("BLK"), V("MD"))])
+        first(1)
+        second_list(0)
+        first_list(1)
+        third(0)
+        for c in range(2):
+            ts(V("MB", mb + 2 * c, mb + 2 * c + 1), TH(c, 5), Q(r, 0), O.add, OFFS + 0.5, O.add)
+        red(V("MB", mb + 1, mb + 2), V("P6", 0, 16), O.min)
+        send(r, "b", lambda o: ("MB", mb), others)
+        arrive(r, "b")
+        second(1)
+        states(r, 0)
+        second_list(1)
         if not r:
             consts3()
+        pre(r)
+        third(1)
+        prices(r, 0)
+        states(r, 1)
+        prices(r, 1)
+        send(r, "c", where(r, "SNC", "AC", 8), others)
+        arrive(r, "a")
+        arrive(r, "c")
+        if r == 1:
+            consts4()
+        level(r)
 
     for r in range(NR):
         rnd(r)
-    level_a(NR - 1)
 
+    for h in range(2):
+        mm(V("P%d" % (2 + h), 0, 384), [(V("ID2K"), V("KD3", h * 384, h * 384 + 384))], True, False)
+    ts(C(17), Q(NR, 12), 2.0, O.mult, Q(NR, 13), O.add)
+    for x, y, n in ((0, 0, 3), (3, 6, 4), (7, 14, 4)):
+        cp(V("DB", y, y + n), Q(NR, x, n))
+        act(V("DB", y + n, y + 2 * n), Q(NR, x, n), F.Copy)
+    ts(V("OFQ", 0, 1), FB, C(17), O.subtract)
+    cp(V("FIN"), IND(V("DB"), V("OFQ", 0, 1)))
     for l in range(3):
-        ts(V("OG3", l * 40, l * 40 + 40), V("CL"), C(9 + l), O.add)
-    ts(w_(0, 3), HI, -1023.0, O.add, 1.0 / 32, O.mult)
+        ts(V("OG3", l * 2, l * 2 + 2), V("CLF", 0, 2), V("FIN", 8 + l, 9 + l), O.add, 1.0 / 16, O.mult)
+    ts(C(18, 3), V("FIN", 3, 6), -1023.0, O.add)
     for l in range(3):
-        cp(V("FF", l * 128, l * 128 + 128), IND(V("A"), V("OG3", l * 40 + 32, l * 40 + 40)))
-    for k in range(12):
-        l, q = k // 4, k % 4
-        act(V("S3", k * 256, k * 256 + 128), IND(V("A"), V("OG3", l * 40 + q * 8, l * 40 + q * 8 + 8)), F.Copy)
-    for l in range(3):
-        a, b = l * 32, l * 32 + 32
-        tt(V("F3", a, b), V("FF", l * 128, l * 128 + 32), V("FF", l * 128 + 64, l * 128 + 96), O.add)
-    for l in range(3):
-        a, b = l * 32, l * 32 + 32
-        ts(V("KP3", a, b), V("F3", a, b), w_(l), O.is_lt)
-    scan(V("R3"), V("RM"), V("KP3"), O.mult, O.add)
-    mm(V("PEA", 0, 96), [(V("BLK"), V("R3"))])
-    mm(V("PC0", 0, 96), [(V("BLK"), V("R3")), (V("NUT"), V("KP3"))])
-    tt(V("EM"), V("PEA", 0, 96), V("DM3"), O.mult)
-    for k in range(12):
-        red(V("EA", k, k + 1), V("EM", k * 8, k * 8 + 8), O.add)
-    ts(V("EA"), V("EA"), V("LC", 5, 6), O.add)
-    for k in range(12):
-        ts(V("IA", k * 128, k * 128 + 128), V("K", 0, 128), V("EA", k, k + 1), O.is_ge)
-    mm2(V("PL", 0, 96), [(V("ID"), V("B8C"))], wraps("S1", "IA", 1536))
-    tt(V("W3"), V("PC0", 0, 96), V("KP3"), O.mult)
-    level_b()
-    cp(V("YT", 0, 3), LO)
-    cp(V("YT", 3, 6), HI)
-    tt(w_(60), C(19), C(19), O.add)
-    tt(V("YT", 6, 7), w_(60), C(18), O.add)
-    cp(V("YT", 7, 8), U)
-    mm(V("PX", 0, 8, P=8), [(V("G8F"), V("YT"))])
-    cp(V("OF3"), V("PL", 0, 96))
-    tt(V("AB"), V("PL", 0, 96), V("B8C"), O.subtract)
-    for l in range(3):
-        a, b = l * 512, l * 512 + 512
-        tt(V("OH", a, b), IND(V("W3"), V("OF3", l * 32, l * 32 + 32)), V("K1"), O.is_equal)
-    mm2(V("PU", 0, 96), [(V("ID16"), V("AB")), (V("ID"), V("B256"))], wraps("SE", "OH", 1536))
-    cp(V("YT8", P=8), V("PX", 0, 8, P=8))
+        ts(C(21 + l), V("FIN", 8 + l, 9 + l), -512.0 * l, O.add)
+    cp(V("FIN", 6, 7), C(17))
+    cp(V("FIN", 7, 8), U)
+    mm(V("P7", 0, 8, P=8), [(V("G8F"), V("FIN", 0, 8))])
+    act(V("YT8", P=8), V("P7", 0, 8, P=8), F.Copy)
     dma("Y", EXT(T.yt[:, :]), V("YT8", P=8), "o0")
+    for l in range(3):
+        a, b = l * 32, l * 32 + 32
+        ts(V("KP3", a, b), IND(V("AC"), V("OG3", l * 2, l * 2 + 2)), C(18 + l), O.is_lt)
+        act(V("F3", a, b), IND(V("AC"), V("OG3", l * 2, l * 2 + 2)), F.Copy)
+    scan(V("R3"), V("RM"), V("KP3"), 0.0, O.mult, O.add)
+    for h in range(2):
+        mms([(V("P%d" % (2 + h), k * 96, k * 96 + 96), V("NBD"), V("R3")) for k in range(4)], False, True)
+    mm(V("P4", 0, 96), [(V("BLK"), V("R3")), (V("NUT"), V("KP3"))])
+    act(V("W3"), V("P4", 0, 96), F.Copy)
+    for h in range(2):
+        scan(V("V1", h * 384, h * 384 + 384), V("P%d" % (2 + h), 0, 384), V("DT3", h * 384, h * 384 + 384), 0.0, O.max, O.min)
+    for k in range(8):
+        cp(V("OF3", k, 96, 8), V("V1", k * 96 + 6, k * 96 + 96, 8))
+    cp(V("V3"), V("OF3"))
+    for l in range(3):
+        a, b, p = l * 512, l * 512 + 512, V("P%d" % l, 0, 32)
+        tt(V("OH", a, b), IND(V("W3"), V("OF3", l * 32, l * 32 + 32)), V("K13"), O.is_equal)
+        mm(p, [(V("IDF"), V("V3", l * 32, l * 32 + 32)), (V("ID"), V("C3", 0, 32))], True, False)
+        mm(p, wraps("SD", "OH", a, 512) + wraps("SN", "OH", a, 512), False, True)
 
-    def costs(l):
+    def prices3(l):
         a, b = l * 512, l * 512 + 512
         tt(V("CG", a, b), IND(V("F3"), V("OF3", l * 32, l * 32 + 32)), V("OH", a, b), O.mult)
-        p = ("PC0", "PC1", "PEB")[l]
-        mm(V(p, 0, 512, P=8), [(V("G8"), V("CG", a, b))])
+        mm(V("P%d" % (4 + l), 0, 512, P=8), [(V("G8"), V("CG", a, b))])
 
-    costs(0)
-    cp(V("OP3"), V("PU", 0, 96))
-    for l in range(3):
+    def states3(l):
         a, b = l * 512, l * 512 + 512
-        act(V("YL", a, b), IND(V("S3"), V("OP3", l * 32, l * 32 + 32)), F.Copy)
+        ts(V("OP3", l * 32, l * 32 + 32), V("P%d" % l, 0, 32), C(21 + l), O.add, 10.0 * SL - 1, O.min)
+        act(V("YL", a, b), IND(V("A"), V("OP3", l * 32, l * 32 + 32)), F.Copy)
         dma("Y", EXT(T.yl[:, a:b]), V("YL", a, b), "o%d" % (1 + l))
-    costs(1)
-    costs(2)
+
+    states3(0)
+    prices3(0)
+    states3(1)
+    prices3(1)
+    states3(2)
+    prices3(2)
     for l in range(3):
         a, b = l * 512, l * 512 + 512
-        ts(V("YF", a, b, P=8), V(("PC0", "PC1", "PEB")[l], 0, 512, P=8), 1023.0, O.add)
+        ts(V("YF", a, b, P=8), V("P%d" % (4 + l), 0, 512, P=8), 1023.0, O.add)
     dma("S", EXT(T.yf[:, :]), V("YF", P=8), "o4")
     for k in range(4):
         g.sync.wait_ge(T.sem["o%d" % k], 16)
-    for k in range(9):
+    for k in range(6):
         g.sync.wait_ge(T.sem["l%d" % k], 16)
     g.scalar.wait_ge(T.sem.o4, 16)
     for e in ("V", "S", "T", "G"):

@@ -15,18 +15,18 @@ PSUM = ["P%d" % k for k in range(8)]
 SCRATCH = {}
 for _n, _w, _d in (
         ("A", 10 * SL, _b), ("AC", 320, _f), ("OPW", 4096, _b), ("SND", NR * SL, _b), ("SNC", NR * 32, _f), ("MB", NR * 16, _f),
-        ("S", 512, _b), ("FSA", 64, _f), ("FSP", 64, _f), ("FS", 64, _h), ("D", 4096, _b), ("GA", 1024, _b), ("CH", 4112, _b),
+        ("S", 512, _b), ("FSA", 64, _f), ("FSP", 64, _f), ("FS", 64, _h), ("D", 4096, _b), ("CH", 4112, _b),
         ("OFA", 32, _u), ("OFF", 4, _u), ("OFO", 256, _u), ("OFB", 32, _u), ("OFW", 32, _u), ("OFN", 32, _u), ("OFQ", 2, _u),
-        ("MR", 32, _f), ("MZ", 32, _f), ("SQ", 32, _f), ("TJ", 256, _f), ("VJ", 256, _i), ("VK", 256, _i),
+        ("MR", 32, _f), ("SQ", 32, _f), ("TJ", 256, _f), ("VJ", 256, _i), ("VK", 256, _i),
         ("YH", 256, _h), ("QQ", 256, _f), ("DD", 256, _b), ("PEN", 768, _b), ("XH", 512, _h), ("YW", 544, _f),
         ("DV", 1536, _h), ("RS", 1536, _h), ("DA", 1536, _b), ("CN", 8, _f), ("CAND", 64, _f), ("TT", 32, _f),
         ("KP", 1024, _b), ("R", 1024, _b), ("V1", 768, _b), ("EBW", 1088, _b), ("W", 1088, _b), ("IB", 512, _b), ("OH", 1536, _b), ("CG", 1536, _h),
-        ("TB", 64, _f), ("SV", 32, _f), ("MD", 16, _h),
-        ("ONE", 256, _b), ("ZH", 256, _h), ("BLK", 128, _b), ("NBH", 128, _h), ("NBF", 128, _f), ("NBD", 128, _b), ("NUT", 128, _b),
+        ("TB", 64, _f), ("CB", 32, _h), ("AM", NR * 32, _f), ("OLD", 32, _h), ("OFM", 2, _u), ("WMU", 144, _b), ("XBN", 144, _h), ("SV", 32, _f), ("MD", 16, _h),
+        ("ONE", 256, _b), ("ZH", 256, _h), ("BLK", 128, _b), ("NBH", 128, _b), ("NBF", 128, _f), ("NBD", 128, _b), ("NUT", 128, _b),
         ("ID", 128, _b), ("IDN", 128, _b), ("ID16", 128, _b), ("ID2K", 128, _b), ("IDP", 128, _b), ("IDM", 128, _b), ("IDF", 128, _f),
-        ("S1", 144, _b), ("S16", 144, _b), ("SD", 144, _b), ("SN", 144, _b), ("WM", 144, _b), ("XB", 144, _h),
+        ("S1", 144, _b), ("SD", 144, _b), ("SN", 144, _b), ("WM", 144, _b), ("XB", 144, _h),
         ("K", 256, _b), ("K1", 256, _b), ("K13", 512, _b), ("KD", 256, _b), ("DT", 256, _b), ("CL", 32, _f), ("CLF", 4, _f),
-        ("CM", 32, _b), ("CZ", 64, _h), ("M2", 64, _b), ("CA", 4, _b), ("CO", 16, _b), ("CE", 16, _h), ("CT", 80, _f), ("CK", 16, _f), ("C8", 2, _f),
+        ("CZ", 64, _h), ("M2", 64, _b), ("CA", 4, _b), ("CO", 16, _b), ("CT", 80, _f), ("C8", 2, _f),
         ("LM", 16, _f), ("RW", 80, _f), ("RX", 80, _f), ("LC", 24, _f), ("LI", 8, _i), ("G8", 8, _h), ("G8F", 8, _f),
         ("DB", 24, _f), ("FIN", 16, _f), ("F3", 96, _f), ("KP3", 96, _b), ("R3", 96, _b), ("RM", 96, _b), ("W3", 96, _b), ("V3", 96, _f),
         ("KD3", 768, _b), ("DT3", 768, _b), ("C3", 96, _b), ("OF3", 96, _u), ("OG3", 8, _u), ("OP3", 96, _u), ("YL", 1536, _b)):
@@ -111,18 +111,26 @@ def rank_program(g, core, T, topo):
         if a is None:
             a, b = 0, t.shape[-1]
         ap = t[0:P, a:b:s] if s != 1 else t[0:P, a:b]
-        return {"ap": ap, "r": [(name, 0, 512) if name in PSUM else (name, a, b)]}
+        return {"ap": ap, "r": [(name, a, b, s)]}
+
+    def meet(a, b, s, x, y, z):
+        return x < b and a < y and (s != z or (a - x) % s == 0)
+
+    def covers(a, b, s, x, y, z):
+        return a <= x and y <= b and (s == 1 or (s == z and (a - x) % s == 0))
 
     def IND(w, o):
         return {"ap": w["ap"].indirect(o["ap"]), "r": w["r"] + o["r"]}
 
-    def begin(e, outs, ins):
+    def begin(e, outs, ins, adds=False):
         recs = {}
         for views, wr in ((ins, False), (outs, True)):
             for v in views:
-                for n, a, b in v["r"]:
-                    for (x, y, w, e2, sem, val, clk) in logs.get(n, []):
-                        if x < b and a < y and (wr or w or (n in PSUM and e2 != e)):
+                for n, a, b, s in v["r"]:
+                    for (x, y, w, e2, sem, val, clk, z) in logs.get(n, []):
+                        if adds and wr and e2 == e and (x, y) == (a, b):
+                            continue
+                        if (meet(a, b, s, x, y, z) and (wr or w)) or (n in PSUM and e2 != e):
                             if sem not in recs or recs[sem][1] < val:
                                 recs[sem] = (sem, val, clk)
         k = known[e]
@@ -139,16 +147,12 @@ def rank_program(g, core, T, topo):
         clk[sem] = val
         for views, wr in ((ins, False), (outs, True)):
             for v in views:
-                for n, a, b in v["r"]:
-                    old = logs.get(n, [])
-                    if wr:
-                        old = [z for z in old if not (a <= z[0] and z[1] <= b)]
-                    else:
-                        old = [z for z in old if z[2] or z[3] != e or not (a <= z[0] and z[1] <= b)]
-                    logs[n] = old + [(a, b, wr, e, sem, val, clk)]
+                for n, a, b, s in v["r"]:
+                    old = [z for z in logs.get(n, []) if not (covers(a, b, s, z[0], z[1], z[7]) and (wr or (not z[2] and z[3] == e)))]
+                    logs[n] = old + [(a, b, wr, e, sem, val, clk, s)]
 
-    def op(e, outs, ins, call):
-        begin(e, outs, ins)
+    def op(e, outs, ins, call, adds=False):
+        begin(e, outs, ins, adds)
         count[e] += 1
         call(queue[e]).then_inc(T.sem["s" + e], 1)
         done(e, known[e], "s" + e, count[e], outs, ins)
@@ -193,10 +197,10 @@ def rank_program(g, core, T, topo):
         if bias is not None:
             kw["bias"] = val(bias)
         if scale is not None:
-            kw["scale"] = scale
+            kw["scale"] = val(scale)
         if acc is not None:
             kw["accum_out"] = acc["ap"]
-        op("S", vs(out, acc), vs(a, bias), lambda q: q.activation(out["ap"], a["ap"], f, **kw))
+        op("S", vs(out, acc), vs(a, bias, scale), lambda q: q.activation(out["ap"], a["ap"], f, **kw))
 
     def mms(triples, start=True, stop=True):
         n = len(triples)
@@ -206,7 +210,7 @@ def rank_program(g, core, T, topo):
             for k, (o, l, r) in enumerate(triples):
                 x = q.matmul(o["ap"], l["ap"], r["ap"], start and k == 0, stop and k == n - 1)
             return x
-        op("T", [triples[0][0]], [v for p in triples for v in p[1:]], call)
+        op("T", [p[0] for p in triples], [v for p in triples for v in p[1:]], call, not start)
 
     def mm(out, pairs, start=True, stop=True):
         mms([(out, l, r) for l, r in pairs], start, stop)
@@ -214,8 +218,8 @@ def rank_program(g, core, T, topo):
     def iota(out, pattern, base, cm=0):
         op("G", [out], [], lambda q: q.iota(out["ap"], pattern, base, cm, allow_small_or_imprecise_dtypes=True))
 
-    def sel(out, a, pattern, cmp_, base, cm):
-        op("G", [out], [a], lambda q: q.affine_select(out["ap"], a["ap"], pattern, cmp_, 0.0, base, cm))
+    def sel(out, a, pattern, cmp_, base, cm, other=0.0):
+        op("G", [out], [a], lambda q: q.affine_select(out["ap"], a["ap"], pattern, cmp_, other, base, cm))
 
     def wraps(base, buf, x, w):
         return [(V(base, 15 - i, 143 - i), V(buf, x + i, x + w, 16)) for i in range(16)]
@@ -245,7 +249,7 @@ def rank_program(g, core, T, topo):
         for q in range(4):
             if q != me:
                 x = (r + r0) * wr + q * w
-                logs[buf] = logs.get(buf, []) + [(x, x + w, True, "net", sem, n, {sem: n})]
+                logs[buf] = logs.get(buf, []) + [(x, x + w, True, "net", sem, n, {sem: n}, 1)]
 
     others = [o for o in range(4) if o != me]
 
@@ -261,18 +265,29 @@ def rank_program(g, core, T, topo):
     fill(V("ONE"), 1.0)
     iota(V("LI", 0, 1), [[1, 1]], 0, 1)
     iota(V("LM"), [[1, 16]], 0)
-    sel(V("S1"), V("ONE", 0, 144), [[0, 9], [1, 16]], O.is_equal, -15, 0)
-    sel(V("S1"), V("S1"), [[-16, 9], [0, 16]], O.is_ge, 0, 1)
-    sel(V("S1"), V("S1"), [[16, 9], [0, 16]], O.is_ge, 15, -1)
-    sel(V("BLK"), V("ONE", 0, 128), [[-16, 8], [0, 16]], O.is_ge, 0, 1)
-    sel(V("BLK"), V("BLK"), [[16, 8], [0, 16]], O.is_ge, 15, -1)
+    sel(V("S1"), V("ONE", 0, 144), [[1, 144]], O.is_equal, 1000, 0)
     sel(V("ID"), V("ONE", 0, 128), [[-1, 128]], O.is_equal, 0, 1)
-    sel(V("B8", P=8), V("ONE", 0, 144, P=8), [[0, 9], [1, 16]], O.is_equal, -15, 0)
-    sel(V("B8", P=8), V("B8", P=8), [[1, 9], [0, 16]], O.is_equal, 0, -1)
+    sel(V("RX", 0, 9), V("ONE", 0, 9), [[-16, 9]], O.is_ge, 0, 1)
+    sel(V("BLK"), V("ONE", 0, 128), [[-16, 8], [0, 16]], O.is_ge, 0, 1)
+    sel(V("S1", 15, 144, 16), V("RX", 0, 9), [[16, 9]], O.is_ge, 15, -1)
+    sel(V("B8", P=8), V("ONE", 0, 144, P=8), [[1, 144]], O.is_equal, -15, -16)
+    sel(V("BLK"), V("BLK"), [[16, 8], [0, 16]], O.is_ge, 15, -1)
     iota(V("CLF"), [[0, 2], [256, 2]], 0)
     iota(V("KD"), [[16, 8], [0, 32]], 0)
-    sel(V("NUT"), V("BLK"), [[-1, 128]], O.is_gt, 0, 1)
+    for i, s in enumerate(STEPS):
+        iota(V("CT", 16 * i, 16 * i + 6), [[-s, 3], [0, 2]], s // 2)
+        iota(V("CT", 16 * i + 6, 16 * i + 7), [[1, 1]], s + s // 2)
+        iota(V("CT", 16 * i + 7, 16 * i + 9), [[-2 * s, 2]], s)
     iota(V("DT"), [[0, 8], [272, 2], [16, 16]], 16)
+    act(V("IDN"), V("ID"), F.Copy, scale=-1.0)
+    act(V("NUT"), V("BLK"), F.Copy, scale=-1.0)
+    sel(V("NUT"), V("NUT"), [[-1, 128]], O.is_gt, 0, 1)
+    iota(V("DT", 15, 256, 32), [[0, 8]], 272)
+    sel(V("NUT"), V("NUT"), [[-1, 128]], O.not_equal, 0, 1, 128.0)
+    iota(V("DT", 31, 256, 32), [[0, 8]], 0)
+    for out, a, x in (("IDP", "ID", 16777216.0), ("IDM", "ID", -16777216.0), ("ID2K", "ID", 2048.0), ("IDF", "ID", 16.0), ("ID16", "ID", 16.0),
+                      ("NBH", "BLK", -32768.0), ("NBF", "BLK", -16384.0), ("NBD", "BLK", -2048.0)):
+        act(V(out), V(a), F.Copy, scale=x)
     iota(V("K"), [[16, 8], [0, 2], [1, 16]], 0)
     iota(V("K1"), [[16, 8], [0, 2], [1, 16]], 129)
     iota(V("CO"), [[0, 8], [-4352, 2]], 0)
@@ -283,42 +298,41 @@ def rank_program(g, core, T, topo):
                              {0: 17, 1: 15, 3: 6, 7: 10, 11: 13, 14: 19, 15: 15}, {0: 3, 1: 4, 2: 5, 8: 19, 9: 20, 10: 21, 15: 8})):
         for i in row:
             iota(V("RW", 16 * k + i, 16 * k + i + 1), [[1, 1]], row[i])
-    iota(V("K13"), [[0, 4], [1, 128]], 129)
-    iota(V("KD3"), [[16, 8], [0, 96]], 0)
-    iota(V("DT3"), [[0, 8], [1, 96]], 1)
-    iota(V("RM"), [[0, 12], [1, 8]], 0)
-    sel(V("G8"), V("ONE", 0, 8), [[-16, 8]], O.is_ge, 0, 1)
-    sel(V("G8"), V("G8"), [[16, 8]], O.is_ge, 15, -1)
 
     for i in range(16):
+        if i == 6:
+            ts(V("LI", 1, 2), V("LI", 0, 1), 15, O.bitwise_and)
+        if i == 11:
+            cp(lane, V("LI", 1, 2))
         fill(V("RW", 64 + i, 65 + i), float(WT[i]))
-    ts(V("LI", 1, 2), V("LI", 0, 1), 15, O.bitwise_and)
-    cp(lane, V("LI", 1, 2))
     ts(V("LM"), V("LM"), lane, O.is_equal)
-    tt(V("RX", 64, 80), V("RW", 64, 80), V("LM"), O.mult)
     ts(L(10), lane, 0.0, O.is_equal)
     ts(L(11), lane, 1.0, O.is_equal)
-    red(WL, V("RX", 64, 80), O.add)
-
-    def two(out, a, b, k):
-        ts(L(k), L(11), b, O.mult)
-        ts(L(k + 1), L(10), a, O.mult, L(k), O.add)
-        ts(out, V("ONE", 0, out["ap"].shape[-1]), L(k + 1), O.mult)
-
-    ts(V("WM"), V("S1"), WL, O.mult, 0.25, O.mult)
-    two(V("CM"), -512.0, 0.125, 12)
-    ts(L(14), L(11), -1.5 / 4096, O.mult)
     ts(L(18), lane, 2.0, O.is_equal, -1.0, O.mult)
-    ts(L(15), L(10), -1600.0 / 4096, O.mult, L(14), O.add)
+    ts(L(19), lane, 0.5, O.add)
+    ts(L(7), lane, 16.0, O.mult)
+    tt(V("RX", 64, 80), V("RW", 64, 80), V("LM"), O.mult)
+    ts(L(14), L(11), -1.5 / 4096, O.mult)
+    ts(L(16), L(11), 16384.0, O.mult)
+    ts(INI, L(10), -128.5, O.mult)
     ts(V("M2"), V("ONE", 0, 64), L(18), O.mult)
-    for j in range(8):
-        fill(V("CK", j, j + 1), 2048.0 - KA[j] / 2.0 - 0.25)
+    red(WL, V("RX", 64, 80), O.add)
+    ts(L(15), L(10), -1600.0 / 4096, O.mult, L(14), O.add)
+    ts(L(17), L(10), -16384.0 * 3840, O.mult, L(16), O.add)
+    fill(V("ZH"), 0.0)
+    fill(T0, 2.0 * STEPS[0] - 0.5 - OFFS)
+    ts(V("WM"), V("S1"), WL, O.mult)
+    cp(V("LI", 4, 5), WL)
+    act(V("CA"), V("ONE", 0, 4), F.Identity, scale=L(17))
+    act(V("SD"), V("S1"), F.Identity, scale=lane)
+    act(V("KD"), V("KD"), F.Identity, bias=L(19))
+    iota(V("KD", 15, 256, 16), [[0, 16]], 200)
 
     def C(k, n=1):
         return V("SV", k, k + n)
 
     U, U0, U2, LO1, LIM, LMN, THR, MN = [C(k) for k in range(8)]
-    CJ = V("CK", 8, 16)
+    CE8 = C(26)
     fill(V("TB"), 0.0)
     fill(U, 1023.0)
     fill(V("TB", 3, 4), 100000.0)
@@ -326,46 +340,18 @@ def rank_program(g, core, T, topo):
     fill(V("TB", 11, 12), 1.0)
 
     def consts1():
-        cp(V("LI", 4, 5), WL)
-        ts(V("F8", P=8), V("F8I", P=8), -1023.0, O.add)
         ts(V("LI", 5, 6), V("LI", 4, 5), 3, O.bitwise_and)
-        ts(V("IDN"), V("ID"), -1.0, O.mult)
+        ts(V("F8", P=8), V("F8I", P=8), -1023.0, O.add)
         ts(L(6), V("LI", 5, 6), -1.0, O.mult, 1026.0, O.add)
-        ts(L(7), lane, 16.0, O.mult)
+        fill(V("EBW"), 0.0)
         mm(V("P5", 0, 32), [(V("B8", 15 - i, 143 - i, P=8), V("F8", i, 512, 16, P=8)) for i in range(16)])
         ts(V("XB"), V("S1"), L(6), O.mult, 1.0 / 4096, O.mult)
         ts(V("CLF"), V("CLF"), L(7), O.add)
+        ts(V("XBN"), V("S1"), L(6), O.mult, -1.0 / 4096, O.mult)
         act(V("AC", 0, 32), V("P5", 0, 32), F.Copy)
         fill(V("CH", 4096, 4112), 0.0)
-
-    def consts2():
-        ts(V("IDP"), V("ID"), 16777216.0, O.mult)
-        ts(V("IDM"), V("ID"), -16777216.0, O.mult)
-        ts(V("NBH"), V("BLK"), -32768.0, O.mult)
-        ts(V("NBF"), V("BLK"), -16384.0, O.mult)
-        ts(V("NBD"), V("BLK"), -2048.0, O.mult)
-        ts(V("ID2K"), V("ID"), 2048.0, O.mult)
-        two(V("CA"), -16384.0 * 3840, 16384.0, 16)
-        ts(INI, L(10), -128.5, O.mult)
-        fill(T0, 2.0 * STEPS[0] - 0.5 - OFFS)
-        fill(V("ZH"), 0.0)
-        for k, (a, b) in enumerate(((0, 2), (2, 4), (4, 6), (6, 7), (7, 8), (8, 9))):
-            fill(V("RX", a, b), (0.0, -1.0, -2.0, 1.0, 1.0, -1.0)[k])
-        for i, s in enumerate(STEPS):
-            ts(V("CT", 16 * i, 16 * i + 7), V("RX", 0, 7), float(s), O.mult, float(s // 2), O.add)
-            ts(V("CT", 16 * i + 7, 16 * i + 9), V("RX", 7, 9), float(s), O.mult)
-        ts(V("KD"), V("KD"), lane, O.add, 0.5, O.add)
-        fill(V("DT", 15, 256, 32), 272.0)
-        fill(V("KD", 15, 256, 16), 200.0)
-        fill(V("DT", 31, 256, 32), 0.0)
-        ts(V("ID16"), V("ID"), 128.0, O.mult)
-        tt(V("NUT"), V("ID16"), V("NUT"), O.subtract)
-        ts(V("ID16"), V("ID"), 16.0, O.mult)
-        ts(V("S16"), V("S1"), 16.0, O.mult)
-        ts(V("SD"), V("S1"), lane, O.mult)
-        ts(V("CE"), V("ONE", 0, 16), L(10), O.mult, 1023.0, O.mult)
-        fill(V("W"), 0.0)
-        fill(V("EBW"), 0.0)
+        for c in range(4):
+            fill(V("W", c * 272 + 256, c * 272 + 272), 0.0)
         fill(V("YW", 256, 272), 0.0)
         fill(V("YW", 528, 544), 0.0)
         fill(V("MB", me * 4 + 3, NR * 16, 16), 5000.0)
@@ -381,6 +367,14 @@ def rank_program(g, core, T, topo):
         tt(DB_, DB_, DA_, O.subtract)
         tt(DA_, DA_, L0, O.subtract)
 
+    def counts4():
+        iota(V("K13"), [[0, 4], [1, 128]], 129)
+        iota(V("KD3"), [[16, 8], [0, 96]], 0)
+        iota(V("DT3"), [[0, 8], [1, 96]], 1)
+        iota(V("RM"), [[0, 12], [1, 8]], 0)
+        sel(V("G8"), V("ONE", 0, 8), [[-16, 8]], O.is_ge, 0, 1)
+        sel(V("G8"), V("G8"), [[16, 8]], O.is_ge, 15, -1)
+
     def consts4():
         fill(V("A", EMPTY * SL, EMPTY * SL + SL), 0.0)
         fill(V("AC", EMPTY * 32, EMPTY * 32 + 32), 0.0)
@@ -388,7 +382,6 @@ def rank_program(g, core, T, topo):
         ts(V("KD3"), V("KD3"), lane, O.add, 0.5, O.add)
         ts(V("SN"), V("S1"), -8192.0, O.mult)
         ts(V("G8F"), V("G8"), 1.0 / 16, O.mult)
-        ts(V("IDF"), V("ID"), 16.0, O.mult)
         fill(V("DT3", 95, 768, 96), 0.0)
         fill(V("KD3", 7, 768, 8), 200.0)
         fill(V("C3"), 8192.0)
@@ -398,7 +391,7 @@ def rank_program(g, core, T, topo):
         return V("TB", r % 2 * 32 + k, r % 2 * 32 + k + n)
 
     def derived(r):
-        ts(CJ, V("CK", 0, 8), Q(r, 14), O.add)
+        ts(CE8, Q(r, 14), 2047.75, O.add)
         ts(LMN, Q(r, 0), -1023.0, O.add)
         ts(THR, Q(r, 3), -1023.0, O.add)
         ts(V("CZ"), V("M2"), LMN, O.mult, L(15), O.add)
@@ -431,55 +424,78 @@ def rank_program(g, core, T, topo):
 
     def parents(r):
         if r:
+            ts(V("OFF"), V("CLF"), Q(r, 7), O.add, 1.0 / 16, O.mult)
             ts(V("OFA"), V("CL"), Q(r, 7), O.add)
-        ts(V("OFF"), V("CLF"), Q(r, 7), O.add, 1.0 / 16, O.mult) if r else None
+            ts(C(24), C(11), 4096.0, O.mult, -2048.0, O.add)
+            ts(C(25), C(11), -1.0, O.mult, 1.0, O.add)
+            ts(V("OFM"), V("OFF", 0, 2), r * 32 - 1.0, O.min)
+            ts(V("WMU"), V("WM"), C(25), O.mult)
         derived(r)
-        mm(V("P4", 0, 32), [(V("BLK"), V("CM"))], True, False)
+        if r:
+            ts(V("OLD"), IND(V("AM", 0, r * 32), V("OFM")), C(24), O.min)
+        else:
+            fill(V("OLD"), -2048.0)
+        mm(V("P4", 0, 32), [(V("ID"), V("OLD"))], True, False)
+        mm(V("P4", 0, 32), wraps("WMU" if r else "WM", "A", r * SL, 512), False, True)
         if r:
             lay = V("A", 0, (r + 1) * SL)
             cp(V("S", 0, 256), IND(lay, V("OFA", 0, 16)))
             act(V("S", 256, 512), IND(lay, V("OFA", 16, 32)), F.Copy)
-        mm(V("P4", 0, 32), wraps("WM", "S" if r else "A", 0, 512), False, True)
 
     def children(r):
         par = V("S" if r else "A", 0, 512)
         if not r:
             consts1()
             ts(V("OFF"), V("CLF"), 1.0 / 16, O.mult)
-        for k in range(2):
-            mm(V("P%d" % k), [(V("IDN"), par)], True, False)
-        ts(V("MR"), V("P4", 0, 32), MAGIC * 1024, O.add, MAGIC * 1024, O.subtract)
-        tt(V("MZ"), V("P4", 0, 32), V("MR"), O.subtract)
-        act(V("SQ"), V("MZ"), F.Square, bias=511.875)
-        for j in range(2):
-            ts(V("TJ", j * 32, j * 32 + 32), V("MZ"), 4.0 * KA[j], O.mult, V("CK", 8 + j, 9 + j), O.add)
-        for j in range(2, 8):
-            act(V("TJ", j * 32, j * 32 + 32), V("MZ"), F.Identity, bias=V("CK", 8 + j, 9 + j), scale=4.0 * KA[j])
+        apart = {1: "P0", 3: "P1", 5: "P7"}
+        for k in apart:
+            mm(V(apart[k]), [(V("IDN"), par)], True, False)
+        mz = V("AM", r * 32, r * 32 + 32)
+        ts(V("MR"), V("P4", 0, 32), MAGIC * 4096, O.add, MAGIC * 4096, O.subtract)
+        tt(mz, V("P4", 0, 32), V("MR"), O.subtract)
+        act(V("SQ"), mz, F.Square, bias=512.0, scale=0.25)
+        for j in range(4):
+            ts(V("TJ", j * 32, j * 32 + 32), mz, float(KA[j]), O.mult, CE8, O.add)
+        for j in range(4, 8):
+            act(V("TJ", j * 32, j * 32 + 32), mz, F.Identity, bias=CE8, scale=float(KA[j]))
 
-        def numbers(j0, j1):
+        def add(j0, j1):
             for j in range(j0, j1):
                 tt(V("VJ", j * 32, j * 32 + 32), V("TJ", j * 32, j * 32 + 32), V("SQ"), O.add)
-            a, b = j0 * 32, j1 * 32
-            ts(V("VK", a, b), V("VJ", a, b), 4095, O.bitwise_and)
-            cp(V("OFO", a, b), V("VK", a, b))
+
+        def rest(j0, j1):
+            ts(V("VK", j0 * 32, j1 * 32), V("VJ", j0 * 32, j1 * 32), 4095, O.bitwise_and)
+
+        def lists(j0, j1):
+            cp(V("OFO", j0 * 32, j1 * 32), V("VK", j0 * 32, j1 * 32))
 
         def gather(k):
             x, y = k * 512, k * 512 + 512
             tt(V("D", x, y), IND(V("OPW"), V("OFO", k * 32, k * 32 + 32)), par, O.subtract)
 
         def other(k):
-            z = k // 2 * 512
-            act(V("GA", z, z + 512), IND(V("OPW"), V("OFO", k * 32, k * 32 + 32)), F.Copy)
-            mm(V("P%d" % (k // 2)), [(V("ID"), V("GA", z, z + 512))], False, True)
+            x, y = k * 512, k * 512 + 512
+            act(V("D", x, y), IND(V("OPW"), V("OFO", k * 32, k * 32 + 32)), F.Copy)
+            mm(V(apart[k]), [(V("ID"), V("D", x, y))], False, True)
 
         def size(k):
             x, y = k * 512, k * 512 + 512
-            act(V("CH", x, y), V("P%d" % (k // 2)) if k in (1, 3) else V("D", x, y), F.Abs)
+            act(V("CH", x, y), V(apart[k]) if k in apart else V("D", x, y), F.Abs)
 
-        def sums(k):
+        def opens(k):
             z = V("P%d" % (2 + k // 2), k % 2 * 64, k % 2 * 64 + 64)
             mm(z, [(V("ID"), V("FS")), (V("BLK"), V("CZ"))], True, False)
-            mm(z, wraps("XB", "CH", k * 1024, 1024), False, True)
+            if k == 3:
+                mm(z, wraps("XBN", "D", k * 1024, 1024), False, False)
+
+        def sums(k):
+            if k < 3:
+                opens(k)
+            mm(V("P%d" % (2 + k // 2), k % 2 * 64, k % 2 * 64 + 64), wraps("XB", "CH", k * 1024, 1024), False, True)
+
+        def twice(k):
+            x, y = k * 512, k * 512 + 512
+            ts(V("CH", x, y), V("D", x, y), 0.0, O.max, 2.0, O.mult)
 
         def costs():
             act(V("FSA"), IND(V("AC", 0, (r + 1) * 32), V("OFF")), F.Copy)
@@ -495,49 +511,76 @@ def rank_program(g, core, T, topo):
             ts(V("YH", a, b), z, MAGIC, O.add, MAGIC, O.subtract)
             tt(V("DD", a, b), z, V("QQ", a, b), O.subtract)
             ts(V("PEN", a, b), V("YH", a, b), 0.0, O.is_lt, 8192.0, O.mult)
-            base = [(V("ID"), V("YH", a, b)), (V("ID"), V("PEN", a, b))]
+
+        def owners(h):
+            a, b = h * 128, h * 128 + 128
             for c in range(2):
                 x = 256 + c * 256
                 ts(V("PEN", x + a, x + b), V("DD", a, b), (own[c][0] - 1.5) / 4096, O.not_equal, 8192.0, O.mult)
-            for c in range(2):
-                mm(V("P%d" % c, a, b), base + [(V("IDM" if own[c][1] else "IDP"), V("DD", a, b))])
-                mm(V("P%d" % (5 + c), a, b), base + [(V("ID"), V("PEN", 256 + c * 256 + a, 256 + c * 256 + b))])
-            mm(V("P4", a, b), base)
+
+        def mix(h, p):
+            a, b = h * 128, h * 128 + 128
+            out, base = V("P%d" % p, a, b), [(V("ID"), V("YH", a, b)), (V("ID"), V("PEN", a, b))]
+            mm(out, base, True, p == 4)
+            if p < 2:
+                mm(out, [(V("IDM" if own[p][1] else "IDP"), V("DD", a, b))], False, True)
+            if p > 4:
+                mm(out, [(V("ID"), V("PEN", p * 256 - 1024 + a, p * 256 - 1024 + b))], False, True)
 
         def halves(h, c):
             cp(V("XH", c * 256 + h * 128, c * 256 + h * 128 + 128), V("P%d" % (5 + c), h * 128, h * 128 + 128))
 
-        numbers(0, 2)
+        add(0, 8)
+        rest(0, 4)
+        rest(4, 8)
+        lists(0, 4)
+        lists(4, 8)
         other(1)
         gather(0)
-        size(0)
-        size(1)
-        numbers(2, 8)
         other(3)
         gather(2)
         costs()
-        gather(4)
+        gather(6)
         costs2()
+        gather(7)
+        twice(6)
+        twice(7)
+        gather(4)
+        size(0)
+        size(1)
         sums(0)
-        for k in (5, 6, 7):
-            gather(k)
+        other(5)
+        opens(3)
         size(2)
         size(3)
         sums(1)
-        for k in (4, 5, 6, 7):
-            size(k)
-            if k % 2:
-                sums(k // 2)
-        if not r:
-            consts2()
-        keys(0)
+        sums(3)
+        size(5)
+        size(4)
         for c in range(2):
             cand(c, 0)
+        keys(0)
+        owners(0)
+        sums(2)
         for c in range(2):
-            halves(0, c)
+            mix(0, 5 + c)
+        mix(0, 4)
+        for c in range(2):
+            mix(0, c)
         keys(1)
-        for c in range(2):
-            halves(1, c)
+        halves(0, 0)
+        owners(1)
+        halves(0, 1)
+        for p in (4, 5, 0, 6, 1):
+            mix(1, p)
+        red(C(16), V("P4", 0, 256), O.min)
+        signs(0, 0)
+        signs(1, 0)
+        halves(1, 0)
+        ts(V("MD"), V("LM"), C(16), O.mult, 2047.0, O.min)
+        mm(V("P7", 0, 16), [(V("BLK"), V("MD"))])
+        below(0, 0)
+        halves(1, 1)
 
     def TH(c, i):
         return T0 if i == 0 else V("TT", c * 16 + i % 2 * 8 + 5, c * 16 + i % 2 * 8 + 6)
@@ -567,13 +610,8 @@ def rank_program(g, core, T, topo):
 
     def totals(c):
         p = "P%d" % (5 + c)
-        a, b, ca, cn, rs = V(p, 1, 6, 2), V(p, 0, 6, 2), V("CA", 0, 3), V("CN", c * 4, c * 4 + 3), V("RS", c * 768 + 255, c * 768 + 768, 256)
-
-        def call(q):
-            q.matmul(a["ap"], T.BLK[:, :], ca["ap"], True, False)
-            q.matmul(a["ap"], T.NBF[:, :], cn["ap"], False, True)
-            return q.matmul(b["ap"], T.NBH[:, :], rs["ap"], True, True)
-        op("T", [a], [V("BLK"), V("NBF"), V("NBH"), ca, cn, rs], call)
+        mm(V(p, 1, 6, 2), [(V("BLK"), V("CA", 0, 3)), (V("NBF"), V("CN", c * 4, c * 4 + 3))])
+        mm(V(p, 0, 6, 2), [(V("NBH"), V("RS", c * 768 + 255, c * 768 + 768, 256))])
 
     def decide(c, i):
         x, y = c * 32 + i % 2 * 16, c * 16 + (i + 1) % 2 * 8
@@ -581,9 +619,7 @@ def rank_program(g, core, T, topo):
 
     def search():
         for c in range(2):
-            signs(c, 0)
             mm(V("P%d" % (2 + c), 0, 256), [(V("ID2K"), V("KD"))], True, False)
-        below(0, 0)
         tally(0, (0, 1, 2))
         totals(0)
         below(1, 0)
@@ -593,6 +629,8 @@ def rank_program(g, core, T, topo):
             decide(c, i)
             tally(1 - c, (1, 2))
             totals(1 - c)
+            if n == 1:
+                red(C(27), V("P7", 0, 16), O.min)
             if i < 4:
                 cand(c, i + 1)
                 signs(c, i + 1)
@@ -610,6 +648,9 @@ def rank_program(g, core, T, topo):
             y = x + o * 256
             scan(V("R", y, y + 256), V("KP", y, y + 256), V("ZH"), 0.0, O.add, O.add)
         mms([(V("P%d" % (2 + c), k * 32, k * 32 + 32), V("NBD"), V("R", x + 15, x + 512, 16)) for k in range(8)], False, True)
+
+    def ends(c):
+        x = c * 512
         mm(V("P%d" % (5 + c), 0, 32), wraps("S1", "R", x, 512))
         for o in range(2):
             y = c * 544 + o * 272
@@ -631,16 +672,18 @@ def rank_program(g, core, T, topo):
         v1 = V("V1", c * 256 + 14, c * 256 + 256, 16)
         cp(V("OFB", c * 16, c * 16 + 16), v1)
         mm(V("P%d" % (2 + c), 0, 16), [(V("ID"), v1)], True, False)
-        mm(V("P%d" % c, 0, 16), [(V("ID16"), v1), (V("ID"), V("CO"))], True, False)
 
     def second(c):
         x = c * 256
         tt(V("IB", x, x + 256), IND(V("EBW", c * 544, c * 544 + 544), V("OFB", c * 16, c * 16 + 16)), V("K"), O.is_le)
         mm(V("P%d" % (2 + c), 0, 16), wraps("S1", "IB", x, 256), False, True)
-        mm(V("P%d" % c, 0, 16), wraps("S16", "IB", x, 256), False, False)
 
     def second_list(c):
         cp(V("OFW", c * 16, c * 16 + 16), V("P%d" % (2 + c), 0, 16))
+
+    def columns(c):
+        cp(V("CB", c * 16, c * 16 + 16), V("P%d" % (2 + c), 0, 16))
+        mm(V("P%d" % c, 0, 16), [(V("ID"), V("CO")), (V("ID16"), V("CB", c * 16, c * 16 + 16))], True, False)
 
     def third(c):
         x = c * 256
@@ -664,59 +707,74 @@ def rank_program(g, core, T, topo):
         send(r, "a", at, [o for o in own[c] if o != me])
 
     def prices(r, c):
-        at = where(r, "SNC", "AC", 8)
         x = c * 256
         tt(V("CG", x, x + 256), IND(V("YW"), V("OFW", c * 16, c * 16 + 16)), V("OH", x, x + 256), O.mult)
-        mm(V("P%d" % (2 + c), 0, 16), wraps("S1", "CG", x, 256))
+        mm(V("P%d" % (5 + c), 0, 16), wraps("S1", "CG", x, 256))
+
+    def price_lists(r, c):
+        at = where(r, "SNC", "AC", 8)
         for o in range(2):
             buf, y = at(own[c][o])
-            act(V(buf, y, y + 8), V("P%d" % (2 + c), o, 16, 2), F.Copy)
+            act(V(buf, y, y + 8), V("P%d" % (5 + c), o, 16, 2), F.Copy)
 
     def rnd(r):
         parents(r)
         children(r)
-        search()
         mb = r * 16 + me * 4
+        search()
+
+        def bound(c):
+            ts(V("MB", mb + 2 * c, mb + 2 * c + 1), TH(c, 5), Q(r, 0), O.add, OFFS + 0.5, O.add)
+
         kept(0)
-        decide(1, 4)
         for o in range(2):
             act(V("YW", o * 272, o * 272 + 256), V("P4", 0, 256), F.Identity, bias=LMN)
+        act(V("CH", 3072, 4096), V("D", 3072, 4096), F.Abs)
         ranks(0)
-        places(0)
+        decide(1, 4)
+        bound(0)
+        ts(V("MB", mb + 1, mb + 2), C(27), Q(r, 0), O.add)
+        ends(0)
         kept(1)
-        first(0)
-        ranks(1)
-        first_list(0)
-        red(C(16), V("YW", 0, 256), O.min)
-        second(0)
-        places(1)
-        ts(V("MD"), V("LM"), C(16), O.mult, 0.0, O.min)
-        mm(V("P6", 0, 16), [(V("BLK"), V("CE")), (V("BLK"), V("MD"))])
-        first(1)
-        second_list(0)
-        first_list(1)
-        third(0)
-        for c in range(2):
-            ts(V("MB", mb + 2 * c, mb + 2 * c + 1), TH(c, 5), Q(r, 0), O.add, OFFS + 0.5, O.add)
-        red(V("MB", mb + 1, mb + 2), V("P6", 0, 16), O.min)
+        bound(1)
         send(r, "b", lambda o: ("MB", mb), others)
         arrive(r, "b")
-        second(1)
-        states(r, 0)
-        second_list(1)
+        first(0)
+        places(0)
+        ranks(1)
+        first_list(0)
+        second(0)
+        first(1)
+        ends(1)
+        places(1)
         if not r:
             consts3()
         pre(r)
-        third(1)
+        first_list(1)
+        second_list(0)
+        columns(0)
+        third(0)
+        second(1)
         prices(r, 0)
-        states(r, 1)
+        states(r, 0)
+        second_list(1)
+        columns(1)
+        price_lists(r, 0)
+        early = [o for o in own[0] if o != me] if r == NR - 1 else []
+        if early:
+            send(r, "c", where(r, "SNC", "AC", 8), early)
+        third(1)
         prices(r, 1)
-        send(r, "c", where(r, "SNC", "AC", 8), others)
+        states(r, 1)
+        price_lists(r, 1)
+        send(r, "c", where(r, "SNC", "AC", 8), [o for o in others if o not in early])
         arrive(r, "a")
         arrive(r, "c")
-        if r == 1:
-            consts4()
+        if r == 0:
+            counts4()
         level(r)
+        if r == NR - 2:
+            consts4()
 
     for r in range(NR):
         rnd(r)
@@ -770,15 +828,12 @@ def rank_program(g, core, T, topo):
         act(V("YL", a, b), IND(V("A"), V("OP3", l * 32, l * 32 + 32)), F.Copy)
         dma("Y", EXT(T.yl[:, a:b]), V("YL", a, b), "o%d" % (1 + l))
 
-    states3(0)
-    prices3(0)
-    states3(1)
-    prices3(1)
-    states3(2)
-    prices3(2)
     for l in range(3):
-        a, b = l * 512, l * 512 + 512
-        ts(V("YF", a, b, P=8), V("P%d" % (4 + l), 0, 512, P=8), 1023.0, O.add)
+        states3(l)
+        prices3(l)
+    for l in range(2):
+        act(V("YF", l * 512, l * 512 + 512, P=8), V("P%d" % (4 + l), 0, 512, P=8), F.Identity, bias=1023.0)
+    ts(V("YF", 1024, 1536, P=8), V("P6", 0, 512, P=8), 1023.0, O.add)
     dma("S", EXT(T.yf[:, :]), V("YF", P=8), "o4")
     for k in range(4):
         g.sync.wait_ge(T.sem["o%d" % k], 16)

@@ -3,41 +3,53 @@ from concourse.mybir import AluOpType as O, AxisListType, ActivationFunctionType
 
 NR = 8
 SL = 512
-EMPTY = 9
+EMPTY = 8
 WT = [1, 3, 7, 13, 21, 35, 49, 67, 85, 107, 129, 155, 181, 211, 241, 253]
 KA = [17, 101, 263, 389, 547, 701, 859, 1021]
 MAGIC = float(3 << 22)
 OFFS = 6144.0
 STEPS = [256, 64, 16, 4, 1]
+CYCLE, WAKE, ISSUE, HOP, PASSES = 0.9, 200.0, 300.0, 2500.0, 3
+QUEUED = 800.0
+TENSOR = 0.5
 
 _f, _b, _h, _i, _u = "float32", "bfloat16", "float16", "int32", "uint16"
 PSUM = ["P%d" % k for k in range(8)]
 SCRATCH = {}
 for _n, _w, _d in (
-        ("A", 10 * SL, _b), ("AC", 320, _f), ("OPW", 4096, _b), ("SND", NR * SL, _b), ("SNC", NR * 32, _f), ("MB", NR * 16, _f),
-        ("S", 512, _b), ("FSA", 64, _f), ("FSP", 64, _f), ("FS", 64, _h), ("D", 4096, _b), ("CH", 4112, _b),
+        ("A", 10 * SL + 16, _b), ("AC", 320, _f), ("OPW", 4096, _b), ("SND", NR * SL, _b), ("SNC", NR * 32, _f), ("MB", NR * 16, _f),
+        ("S", 512, _b), ("FSP", 64, _f), ("FS", 64, _h), ("D", 4096, _b), ("CH", 4112, _b), ("CB", 32, _h), ("ID16", 128, _b),
         ("OFA", 32, _u), ("OFF", 4, _u), ("OFO", 256, _u), ("OFB", 32, _u), ("OFW", 32, _u), ("OFN", 32, _u), ("OFQ", 2, _u),
-        ("MR", 32, _f), ("SQ", 32, _f), ("TJ", 256, _f), ("VJ", 256, _i), ("VK", 256, _i),
+        ("MR", 32, _f), ("SQ", 32, _f), ("S1H", 144, _b), ("BLKH", 128, _b), ("NUTH", 128, _b), ("TJ", 256, _f), ("VJ", 256, _i), ("VK", 256, _i),
         ("YH", 256, _h), ("QQ", 256, _f), ("DD", 256, _b), ("PEN", 768, _b), ("XH", 512, _h), ("YW", 544, _f),
         ("DV", 1536, _h), ("RS", 1536, _h), ("DA", 1536, _b), ("CN", 8, _f), ("CAND", 64, _f), ("TT", 32, _f),
         ("KP", 1024, _b), ("R", 1024, _b), ("V1", 768, _b), ("EBW", 1088, _b), ("W", 1088, _b), ("IB", 512, _b), ("OH", 1536, _b), ("CG", 1536, _h),
-        ("TB", 64, _f), ("CB", 32, _h), ("AM", NR * 32, _f), ("OLD", 32, _h), ("OFM", 2, _u), ("WMU", 144, _b), ("XBN", 144, _h), ("SV", 32, _f), ("MD", 16, _h),
+        ("TB", 64, _f), ("AM", NR * 32, _f), ("OLD", 64, _h), ("OM", 32, _f), ("CU", 64, _b), ("OFM", 2, _u), ("WMU", 144, _b), ("XBN", 144, _h), ("SV", 32, _f), ("MD", 16, _h),
         ("ONE", 256, _b), ("ZH", 256, _h), ("BLK", 128, _b), ("NBH", 128, _b), ("NBF", 128, _f), ("NBD", 128, _b), ("NUT", 128, _b),
-        ("ID", 128, _b), ("IDN", 128, _b), ("ID16", 128, _b), ("ID2K", 128, _b), ("IDP", 128, _b), ("IDM", 128, _b), ("IDF", 128, _f),
+        ("ID", 128, _b), ("IDN", 128, _b), ("ID2K", 128, _b), ("IDP", 128, _b), ("IDM", 128, _b), ("IDF", 128, _f),
         ("S1", 144, _b), ("SD", 144, _b), ("SN", 144, _b), ("WM", 144, _b), ("XB", 144, _h),
         ("K", 256, _b), ("K1", 256, _b), ("K13", 512, _b), ("KD", 256, _b), ("DT", 256, _b), ("CL", 32, _f), ("CLF", 4, _f),
-        ("CZ", 64, _h), ("M2", 64, _b), ("CA", 4, _b), ("CO", 16, _b), ("CT", 80, _f), ("C8", 2, _f),
-        ("LM", 16, _f), ("RW", 80, _f), ("RX", 80, _f), ("LC", 24, _f), ("LI", 8, _i), ("G8", 8, _h), ("G8F", 8, _f),
-        ("DB", 24, _f), ("FIN", 16, _f), ("F3", 96, _f), ("KP3", 96, _b), ("R3", 96, _b), ("RM", 96, _b), ("W3", 96, _b), ("V3", 96, _f),
-        ("KD3", 768, _b), ("DT3", 768, _b), ("C3", 96, _b), ("OF3", 96, _u), ("OG3", 8, _u), ("OP3", 96, _u), ("YL", 1536, _b)):
+        ("CZ", 64, _h), ("M2", 64, _b), ("CA", 4, _b), ("CO", 16, _b), ("CT", 80, _f),
+        ("LM", 16, _f), ("RW", 80, _f), ("RX", 80, _f), ("LC", 32, _f), ("LI", 8, _i), ("G8", 8, _h), ("G8F", 8, _f),
+        ("F3", 96, _f), ("KP3", 96, _b), ("R3", 96, _b), ("RM", 32, _b), ("W3", 96, _b), ("V3", 96, _f),
+        ("EV", 128, _f), ("GM", 40, _h), ("OPF", 96, _f),
+        ("KD3", 256, _b), ("DT3", 256, _b), ("C3", 32, _b), ("OF3", 96, _u), ("OG3", 14, _u), ("OP3", 96, _u), ("YL", 1536, _b)):
     SCRATCH[_n] = ("sbuf", [128, _w], _d)
 for _n, _w, _d in (("B8", 144, _h), ("F8I", 512, _i), ("F8", 512, _h), ("YF", 1536, _f), ("YT8", 8, _f)):
     SCRATCH[_n] = ("sbuf", [8, _w], _d)
 for _n in PSUM:
     SCRATCH[_n] = ("psum", [128, 512], _f)
-SEMAPHORES = (["sV", "sS", "sT", "sG", "ls"] + ["%s%d" % (s, r) for s in "abc" for r in range(NR)]
-              + ["l%d" % k for k in range(7)] + ["o%d" % k for k in range(5)])
+PARTS = {"DB": (48, 24), "FIN": (72, 16), "C8": (88, 2)}
+ROWS = ("P5", "P6")
+for _n in ROWS:
+    SCRATCH[_n] = ("psum", [128, 32, 16], _f)
+SEMAPHORES = (["sV", "sS", "sT", "sG", "ls"] + ["%s%d%s" % (s, r, k) for s in "abc" for r in range(NR) for k in "nf"]
+              + ["l%d" % k for k in range(10)] + ["o%d" % k for k in range(5)])
 MSG = {"b": ("MB", 16, 4, 0), "a": ("A", SL, 128, 1), "c": ("AC", 32, 8, 1)}
+
+
+def slot(r):
+    return r + 1 if r + 1 < EMPTY else r + 2
 
 
 def ways(core, T, topo):
@@ -64,9 +76,8 @@ def bits(es):
 def hop_engines(core, hop, topo, s):
     far = [d for d in hop if hop[d] != d]
     res = {d: topo.engines(core, d) for d in hop if hop[d] == d}
-    used = [] if s == "a" else [e for d in res for e in res[d]]
     for k, d in enumerate(far):
-        rest = [e for e in topo.engines(core, hop[d]) if e not in used]
+        rest = topo.engines(core, hop[d])
         n = len(rest) // len(far)
         res[d] = rest[k * n:(k + 1) * n]
     return res
@@ -82,10 +93,10 @@ def relay(g, core, T, topo):
             rid, pid = topo.addr(d, core)
             m = topo.mask(core, d)
             for r in range(NR):
-                for s in "bac":
+                for s in ("bac" if r < NR - 1 else "bca"):
                     buf, wr, w, r0 = MSG[s]
-                    x = (r + r0) * wr + q * w
-                    sem = T.sem["%s%d" % (s, r)]
+                    x = (slot(r) if r0 else r) * wr + q * w
+                    sem = T.sem["%s%df" % (s, r)]
                     g.wait_ge(sem, len(hop_engines(rk, hop, topo, s)[d]))
                     g.remote_dma(T[buf][:, x:x + w], T[buf][:, x:x + w], sem, T.sem.ls, pid, rid, m)
                     local += len(topo.engines(core, d))
@@ -101,17 +112,24 @@ def rank_program(g, core, T, topo):
     hop = ways(core, T, topo)
     far = [T.cores.index(d) for d in hop if hop[d] != d]
     own = sorted([(2, 0), (1, 3)], key=lambda p: -len([o for o in p if o in far]))
+    home = me
     queue = {"V": g.vector, "S": g.scalar, "T": g.tensor, "G": g, "Y": g.sync}
     count = {"V": 0, "S": 0, "T": 0, "G": 0, "ls": 0}
     known = {q: {} for q in queue}
     logs = {}
 
     def V(name, a=None, b=None, s=1, P=128):
+        if name in PARTS:
+            x, w = PARTS[name]
+            return V("EV", x + (a or 0), x + (w if b is None else b), s, P)
         t = T[name]
         if a is None:
             a, b = 0, t.shape[-1]
-        ap = t[0:P, a:b:s] if s != 1 else t[0:P, a:b]
-        return {"ap": ap, "r": [(name, a, b, s)]}
+        if name in ROWS:
+            ap = t[0:P, a // 16, a % 16:b - a // 16 * 16:s] if b - a // 16 * 16 <= 16 else t[0:P, a // 16:b // 16, :]
+        else:
+            ap = t[0:P, a:b:s] if s != 1 else t[0:P, a:b]
+        return {"ap": ap, "r": [(name, a, b, s)], "n": len(range(a, b, s)), "w": 2 if SCRATCH[name][2] in (_b, _h, _u) else 4}
 
     def meet(a, b, s, x, y, z):
         return x < b and a < y and (s != z or (a - x) % s == 0)
@@ -120,7 +138,7 @@ def rank_program(g, core, T, topo):
         return a <= x and y <= b and (s == 1 or (s == z and (a - x) % s == 0))
 
     def IND(w, o):
-        return {"ap": w["ap"].indirect(o["ap"]), "r": w["r"] + o["r"]}
+        return {"ap": w["ap"].indirect(o["ap"]), "r": w["r"] + o["r"], "n": 16 * o["n"], "w": 4}
 
     def begin(e, outs, ins, adds=False):
         recs = {}
@@ -151,19 +169,97 @@ def rank_program(g, core, T, topo):
                     old = [z for z in logs.get(n, []) if not (covers(a, b, s, z[0], z[1], z[7]) and (wr or (not z[2] and z[3] == e)))]
                     logs[n] = old + [(a, b, wr, e, sem, val, clk, s)]
 
-    def op(e, outs, ins, call, adds=False):
-        begin(e, outs, ins, adds)
-        count[e] += 1
-        call(queue[e]).then_inc(T.sem["s" + e], 1)
-        done(e, known[e], "s" + e, count[e], outs, ins)
+    calls = []
+    wrote, read, turn = {}, {}, {}
+
+    def note(e, outs, ins, busy, issue, adds=False, late=0.0, after=()):
+        me_, pre_ = len(calls), {}
+        for k in after:
+            pre_[k] = 0.0
+        for views, wr in ((ins, False), (outs, True)):
+            for v in views:
+                for n, a, b, s in v["r"]:
+                    for x, y, z, k in wrote.get(n, []) + (read.get(n, []) if wr else []):
+                        if k != me_ and meet(a, b, s, x, y, z):
+                            same = adds and wr and calls[k][0] == e and (x, y) == (a, b)
+                            pre_[k] = max(pre_.get(k, 0.0), 0.0 if same else WAKE)
+                    if n in PSUM:
+                        who, now, before = turn.get(n, (e, [], []))
+                        if who != e:
+                            who, now, before = e, [], now
+                        for k in before:
+                            pre_[k] = WAKE
+                        if e == "T" and now and now[-1] != me_:
+                            pre_[now[-1]] = pre_.get(now[-1], 0.0)
+                        turn[n] = (who, now + [me_], before)
+                    if wr:
+                        wrote[n] = [q for q in wrote.get(n, []) if not covers(a, b, s, q[0], q[1], q[2])] + [(a, b, s, me_)]
+                        read[n] = [q for q in read.get(n, []) if not covers(a, b, s, q[0], q[1], q[2])]
+                    else:
+                        read.setdefault(n, []).append((a, b, s, me_))
+        calls.append((e, busy, busy + late, pre_, issue))
+        return me_
+
+    def issue_all():
+        n = len(calls)
+        ahead = [[(p, calls[p][2] + w) for p, w in c[3].items()] for c in calls]
+        behind = [[] for _ in calls]
+        for k, c in enumerate(calls):
+            for p, w in c[3].items():
+                behind[p].append((k, c[1] + w + calls[p][2] - calls[p][1]))
+
+        def place(seq, edges):
+            start, used = [0.0] * n, {}
+            for k in seq:
+                t, d = max([start[p] + w for p, w in edges[k]] + [0.0]), calls[k][1]
+                u = used.setdefault(calls[k][0], [])
+                i = len(u)
+                while i and u[i - 1][1] > t:
+                    i -= 1
+                while i < len(u) and u[i][0] < t + d:
+                    t = max(t, u[i][1])
+                    i += 1
+                u.insert(i, (t, t + d))
+                start[k] = t
+            return start
+
+        urgent, best = list(range(n)), None
+        for _ in range(PASSES):
+            start = place(sorted(range(n), key=lambda k: (urgent[k], k)), ahead)
+            end = max([start[k] + calls[k][2] for k in range(n)])
+            if best is None or end < best[0]:
+                best = (end, start)
+            back = place(sorted(range(n), key=lambda k: (-start[k] - calls[k][1], -k)), behind)
+            urgent = [-back[k] - calls[k][1] for k in range(n)]
+            for k in range(n):
+                urgent[k] = max([urgent[k] + end] + [urgent[p] + 1.0 for p, w in ahead[k]])
+        for k in sorted(range(n), key=lambda x: (best[1][x], x)):
+            calls[k][4]()
+
+    def op(e, outs, ins, call, adds=False, cycles=None):
+        def issue():
+            begin(e, outs, ins, adds)
+            count[e] += 1
+            call(queue[e]).then_inc(T.sem["s" + e], 1)
+            done(e, known[e], "s" + e, count[e], outs, ins)
+        if cycles is None:
+            n = max([v["n"] for v in outs + ins])
+            wide = [v for v in outs + ins if v["n"] == n]
+            if [v for v in ins if len(v["r"]) > 1]:
+                cycles = 60 + 1.56 * outs[0]["n"]
+            else:
+                cycles = max(64, n / 2 if e == "V" and all([v["w"] == 2 for v in wide]) else n)
+        note(e, outs, ins, cycles * CYCLE, issue, adds)
 
     def dma(e, out, in_, sem):
-        begin(e, [out], [in_])
-        queue[e].dma_start(out["ap"], in_["ap"]).then_inc(T.sem[sem], 16)
-        done("dma" + sem, {}, sem, 16, [out], [in_])
+        def issue():
+            begin(e, [out], [in_])
+            queue[e].dma_start(out["ap"], in_["ap"]).then_inc(T.sem[sem], 16)
+            done("dma" + sem, {}, sem, 16, [out], [in_])
+        note(e, [out], [in_], 50.0, issue, late=HOP)
 
     def EXT(ap):
-        return {"ap": ap, "r": []}
+        return {"ap": ap, "r": [], "n": 0, "w": 4}
 
     def val(s):
         return s["ap"] if isinstance(s, dict) else s
@@ -178,13 +274,14 @@ def rank_program(g, core, T, topo):
             op("V", [out], vs(a, s1, s2), lambda q: q.tensor_scalar(out["ap"], a["ap"], val(s1), val(s2), op0, op1))
 
     def tt(out, a, b, o):
-        op("V", [out], [a, b], lambda q: q.tensor_tensor(out["ap"], a["ap"], b["ap"], o))
+        n = out["n"] * (1 if a["r"][0][0] in PSUM else 2)
+        op("V", [out], [a, b], lambda q: q.tensor_tensor(out["ap"], a["ap"], b["ap"], o), cycles=None if len(a["r"]) > 1 else max(64, n))
 
     def cp(out, a):
         op("V", [out], [a], lambda q: q.tensor_copy(out["ap"], a["ap"]))
 
     def red(out, a, o):
-        op("V", [out], [a], lambda q: q.tensor_reduce(out["ap"], a["ap"], AxisListType.X, o))
+        op("V", [out], [a], lambda q: q.tensor_reduce(out["ap"], a["ap"], AxisListType.X, o), cycles=max(64, a["n"]))
 
     def fill(out, c):
         op("V", [out], [], lambda q: q.memset(out["ap"], c))
@@ -210,46 +307,58 @@ def rank_program(g, core, T, topo):
             for k, (o, l, r) in enumerate(triples):
                 x = q.matmul(o["ap"], l["ap"], r["ap"], start and k == 0, stop and k == n - 1)
             return x
-        op("T", [p[0] for p in triples], [v for p in triples for v in p[1:]], call, not start)
+        op("T", [p[0] for p in triples], [v for p in triples for v in p[1:]], call, not start,
+           sum([max(min(64, l["n"]), r["n"]) * (4 if r["w"] == 4 else 1) * TENSOR for o, l, r in triples]))
 
     def mm(out, pairs, start=True, stop=True):
         mms([(out, l, r) for l, r in pairs], start, stop)
 
     def iota(out, pattern, base, cm=0):
-        op("G", [out], [], lambda q: q.iota(out["ap"], pattern, base, cm, allow_small_or_imprecise_dtypes=True))
+        op("G", [out], [], lambda q: q.iota(out["ap"], pattern, base, cm, allow_small_or_imprecise_dtypes=True), cycles=150 + 2 * out["n"])
 
     def sel(out, a, pattern, cmp_, base, cm, other=0.0):
-        op("G", [out], [a], lambda q: q.affine_select(out["ap"], a["ap"], pattern, cmp_, other, base, cm))
+        op("G", [out], [a], lambda q: q.affine_select(out["ap"], a["ap"], pattern, cmp_, other, base, cm), cycles=190 + 2 * out["n"])
 
     def wraps(base, buf, x, w):
         return [(V(base, 15 - i, 143 - i), V(buf, x + i, x + w, 16)) for i in range(16)]
 
     def send(r, s, src, owners):
         buf, wr, w, r0 = MSG[s]
-        x = (r + r0) * wr + me * w
-        begin("G", [], [V(src(o)[0], src(o)[1], src(o)[1] + w) for o in owners])
+        ins = [V(src(o)[0], src(o)[1], src(o)[1] + w) for o in owners]
         eng = hop_engines(core, hop, topo, s)
         tr = []
         for o in owners:
             d = T.cores[o]
+            x = (slot(r) if r0 else r) * wr + me * w
             rid, pid = topo.addr(hop[d], core)
-            tr.append(RemoteDMATransfer(dst_ids=[DstId(rid=rid, pnc=pid)], dma_engine_mask=bits(eng[d]), remote_sem=T.sem["%s%d" % (s, r)],
+            tr.append(RemoteDMATransfer(dst_ids=[DstId(rid=rid, pnc=pid)], dma_engine_mask=bits(eng[d]),
+                                        remote_sem=T.sem["%s%d%s" % (s, r, "f" if o in far else "n")],
                                         src=T[src(o)[0]][:, src(o)[1]:src(o)[1] + w], dst=T[buf][:, x:x + w]))
             count["ls"] += len(eng[d])
-        g.remote_dma_fused(tr, local_sem=T.sem.ls)
+
+        def issue():
+            begin("G", [], ins)
+            g.remote_dma_fused(tr, local_sem=T.sem.ls)
+        k = note("G", [], ins, ISSUE, issue, after=sent.get("last", ()))
+        sent["last"] = [k]
+        for o in owners:
+            sent[s + ("f" if o in far else "n")] = k
 
     def arrive(r, s):
         buf, wr, w, r0 = MSG[s]
-        n = 0
-        for c in T.cores:
-            if c != core:
-                h = ways(c, T, topo)
-                n += len(hop_engines(c, h, topo, s)[core]) if h[core] == core else len(topo.engines(h[core], core))
-        sem = "%s%d" % (s, r)
-        for q in range(4):
-            if q != me:
-                x = (r + r0) * wr + q * w
-                logs[buf] = logs.get(buf, []) + [(x, x + w, True, "net", sem, n, {sem: n}, 1)]
+        for kind, qs in (("n", [q for q in others if q not in far]), ("f", far)):
+            n = 0
+            for q in qs:
+                h = ways(T.cores[q], T, topo)
+                n += len(hop_engines(T.cores[q], h, topo, s)[core]) if h[core] == core else len(topo.engines(h[core], core))
+            landing(buf, [(slot(r) if r0 else r) * wr + q * w for q in qs], w, "%s%d%s" % (s, r, kind), n, s + kind)
+
+    def landing(buf, xs, w, sem, n, kind):
+        def issue():
+            logs[buf] = logs.get(buf, []) + [(x, x + w, True, "net", sem, n, {sem: n}, 1) for x in xs]
+        note(sem, [V(buf, x, x + w) for x in xs], [], 1.0, issue, late=(HOP if kind[1] == "n" else 2 * HOP + ISSUE) + QUEUED * (kind[0] == "c"), after=[sent[kind]])
+
+    sent = {}
 
     others = [o for o in range(4) if o != me]
 
@@ -285,17 +394,19 @@ def rank_program(g, core, T, topo):
     iota(V("DT", 15, 256, 32), [[0, 8]], 272)
     sel(V("NUT"), V("NUT"), [[-1, 128]], O.not_equal, 0, 1, 128.0)
     iota(V("DT", 31, 256, 32), [[0, 8]], 0)
-    for out, a, x in (("IDP", "ID", 16777216.0), ("IDM", "ID", -16777216.0), ("ID2K", "ID", 2048.0), ("IDF", "ID", 16.0), ("ID16", "ID", 16.0),
-                      ("NBH", "BLK", -32768.0), ("NBF", "BLK", -16384.0), ("NBD", "BLK", -2048.0)):
+    for out, a, x in (("IDP", "ID", 16777216.0), ("IDM", "ID", -16777216.0), ("ID2K", "ID", 4096.0), ("IDF", "ID", 16.0), ("ID16", "ID", 16.0),
+                      ("NBH", "BLK", -32768.0), ("NBF", "BLK", -16384.0), ("NBD", "BLK", -2048.0), ("BLKH", "BLK", 0.5),
+                      ("S1H", "S1", 0.5)):
         act(V(out), V(a), F.Copy, scale=x)
     iota(V("K"), [[16, 8], [0, 2], [1, 16]], 0)
     iota(V("K1"), [[16, 8], [0, 2], [1, 16]], 129)
     iota(V("CO"), [[0, 8], [-4352, 2]], 0)
+    iota(V("EBW"), [[0, 1088]], 0)
     iota(V("CL"), [[16, 32]], 0)
     for k in range(4):
         iota(V("RW", 16 * k, 16 * k + 16), [[1, 16]], (1, 0, -1, 8)[k])
     for k, row in enumerate(({0: 15, 2: 0, 6: 3, 10: 7, 13: 11, 14: 18, 15: 15}, {0: 16},
-                             {0: 17, 1: 15, 3: 6, 7: 10, 11: 13, 14: 19, 15: 15}, {0: 3, 1: 4, 2: 5, 8: 19, 9: 20, 10: 21, 15: 8})):
+                             {0: 17, 1: 15, 3: 6, 7: 10, 11: 13, 14: 19, 15: 15}, {0: 3, 1: 4, 2: 5})):
         for i in row:
             iota(V("RW", 16 * k + i, 16 * k + i + 1), [[1, 1]], row[i])
 
@@ -333,6 +444,7 @@ def rank_program(g, core, T, topo):
 
     U, U0, U2, LO1, LIM, LMN, THR, MN = [C(k) for k in range(8)]
     CE8 = C(26)
+    fill(V("CU"), -128.0)
     fill(V("TB"), 0.0)
     fill(U, 1023.0)
     fill(V("TB", 3, 4), 100000.0)
@@ -343,18 +455,21 @@ def rank_program(g, core, T, topo):
         ts(V("LI", 5, 6), V("LI", 4, 5), 3, O.bitwise_and)
         ts(V("F8", P=8), V("F8I", P=8), -1023.0, O.add)
         ts(L(6), V("LI", 5, 6), -1.0, O.mult, 1026.0, O.add)
-        fill(V("EBW"), 0.0)
-        mm(V("P5", 0, 32), [(V("B8", 15 - i, 143 - i, P=8), V("F8", i, 512, 16, P=8)) for i in range(16)])
+        mm(V("P2", 0, 32), [(V("B8", 15 - i, 143 - i, P=8), V("F8", i, 512, 16, P=8)) for i in range(16)])
         ts(V("XB"), V("S1"), L(6), O.mult, 1.0 / 4096, O.mult)
         ts(V("CLF"), V("CLF"), L(7), O.add)
         ts(V("XBN"), V("S1"), L(6), O.mult, -1.0 / 4096, O.mult)
-        act(V("AC", 0, 32), V("P5", 0, 32), F.Copy)
+        act(V("AC", 0, 32), V("P2", 0, 32), F.Copy)
+        ts(L(21), lane, 0.5, O.mult, 56.5, O.add)
+
+    def consts2():
+        act(V("NUTH"), V("NUT"), F.Copy, scale=0.5)
         fill(V("CH", 4096, 4112), 0.0)
         for c in range(4):
             fill(V("W", c * 272 + 256, c * 272 + 272), 0.0)
         fill(V("YW", 256, 272), 0.0)
         fill(V("YW", 528, 544), 0.0)
-        fill(V("MB", me * 4 + 3, NR * 16, 16), 5000.0)
+        fill(V("MB", home * 4 + 3, NR * 16, 16), 5000.0)
 
     def consts3():
         for k in range(4):
@@ -369,9 +484,9 @@ def rank_program(g, core, T, topo):
 
     def counts4():
         iota(V("K13"), [[0, 4], [1, 128]], 129)
-        iota(V("KD3"), [[16, 8], [0, 96]], 0)
-        iota(V("DT3"), [[0, 8], [1, 96]], 1)
-        iota(V("RM"), [[0, 12], [1, 8]], 0)
+        iota(V("KD3"), [[16, 8], [0, 32]], 0)
+        iota(V("DT3"), [[0, 8], [1, 32]], 1)
+        iota(V("RM"), [[0, 4], [1, 8]], 0)
         sel(V("G8"), V("ONE", 0, 8), [[-16, 8]], O.is_ge, 0, 1)
         sel(V("G8"), V("G8"), [[16, 8]], O.is_ge, 15, -1)
 
@@ -382,8 +497,16 @@ def rank_program(g, core, T, topo):
         ts(V("KD3"), V("KD3"), lane, O.add, 0.5, O.add)
         ts(V("SN"), V("S1"), -8192.0, O.mult)
         ts(V("G8F"), V("G8"), 1.0 / 16, O.mult)
-        fill(V("DT3", 95, 768, 96), 0.0)
-        fill(V("KD3", 7, 768, 8), 200.0)
+        fill(V("A", 10 * SL, 10 * SL + 16), 0.0)
+        fill(V("DT3", 31, 256, 32), 0.0)
+        fill(V("KD3", 7, 256, 8), 200.0)
+        ts(L(24), lane, 3.0, O.is_equal)
+        ts(L(25), L(10), L(18), O.subtract)
+        ts(L(26), L(11), L(24), O.add, -1.0, O.mult)
+        ts(L(28), L(10), 9.0, O.mult, 4.0, O.add)
+        ts(L(29), L(11), 11.0, O.mult, L(28), O.add)
+        ts(L(30), L(24), 3.0, O.mult, L(29), O.add)
+        ts(L(27), L(30), L(18), O.subtract)
         fill(V("C3"), 8192.0)
         fill(V("DB"), 0.0)
 
@@ -391,23 +514,24 @@ def rank_program(g, core, T, topo):
         return V("TB", r % 2 * 32 + k, r % 2 * 32 + k + n)
 
     def derived(r):
-        ts(CE8, Q(r, 14), 2047.75, O.add)
-        ts(LMN, Q(r, 0), -1023.0, O.add)
-        ts(THR, Q(r, 3), -1023.0, O.add)
+        act(CE8, Q(r, 14), F.Identity, bias=2047.75)
+        act(LMN, Q(r, 0), F.Identity, bias=-1023.0)
+        act(THR, Q(r, 3), F.Identity, bias=-1023.0)
+        act(LIM, Q(r, 0), F.Identity, bias=1022.5 - OFFS, scale=-1.0)
         ts(V("CZ"), V("M2"), LMN, O.mult, L(15), O.add)
-        ts(LIM, Q(r, 0), -1.0, O.mult, 1022.5 - OFFS, O.add)
 
     def pre(r):
-        ts(LO1, Q(r, 0), 1.0, O.add)
-        ts(U0, Q(r, 11), 5000.0, O.mult, U, O.add)
-        ts(U2, Q(r, 12), -5000.0, O.mult, U, O.add)
+        act(LO1, Q(r, 0), F.Identity, bias=1.0)
+        act(U0, Q(r, 11), F.Identity, bias=U, scale=5000.0)
+        act(U2, Q(r, 12), F.Identity, bias=U, scale=-5000.0)
         ts(Q(r, 17), Q(r, 2), 1.0, O.add, Q(r, 3), O.max)
-        ts(Q(r, 18, 2), V("C8"), Q(r, 14), O.add)
-        fill(Q(r, 8), float((r + 1) * SL))
+        act(Q(r, 18, 2), V("C8"), F.Identity, bias=Q(r, 14))
+        act(Q(r, 8), Q(r, 15), F.Identity, bias=float(slot(r) * SL))
 
     def level(r):
         B, m = Q(r, 4), MN
         gone, over, last, rt, back, w = [C(k) for k in range(8, 14)]
+        up, down, same = C(25), C(28), C(29)
         red(B, V("MB", r * 16, r * 16 + 16, 2), O.min)
         red(m, V("MB", r * 16 + 1, r * 16 + 16, 2), O.min)
         ts(over, B, LO1, O.max, U0, O.is_ge)
@@ -416,97 +540,98 @@ def rank_program(g, core, T, topo):
         tt(Q(r, 16), B, LO1, O.max)
         ts(rt, gone, m, O.max, U2, O.is_ge)
         ts(back, over, last, O.max, DB_, O.mult)
-        ts(C(14), last, -5000.0, O.mult, m, O.add)
+        if r < NR - 1:
+            ts(up, gone, m, O.max, U2, O.is_lt)
+            tt(down, over, last, O.max)
+            ts(same, over, last, O.max, 0.5, O.is_lt)
         ts(w, back, DA_, O.add, rt, O.mult)
-        ts(U, C(14), 5000.0, O.add, U, O.min)
+        if r < NR - 1:
+            act(V("WMU"), V("WM"), F.Identity, scale=up)
+            act(V("CU", 0, 32), V("CU", 32, 64), F.Identity, scale=up)
+            ts(V("OLD", 0, 32), V("AM", r * 32, r * 32 + 32), rt, O.mult, same, O.mult)
+            ts(V("OLD", 32, 64), V("OM"), rt, O.mult, down, O.mult)
         ts(V("OFQ", 0, 1), w, L0, O.add)
+        ts(C(14), last, -5000.0, O.mult, m, O.add)
         cp(Q(r + 1, 0, 16), IND(Q(r, 0, 24), V("OFQ", 0, 1)))
+        ts(U, C(14), 5000.0, O.add, U, O.min)
 
     def parents(r):
         if r:
             ts(V("OFF"), V("CLF"), Q(r, 7), O.add, 1.0 / 16, O.mult)
             ts(V("OFA"), V("CL"), Q(r, 7), O.add)
-            ts(C(24), C(11), 4096.0, O.mult, -2048.0, O.add)
-            ts(C(25), C(11), -1.0, O.mult, 1.0, O.add)
-            ts(V("OFM"), V("OFF", 0, 2), r * 32 - 1.0, O.min)
-            ts(V("WMU"), V("WM"), C(25), O.mult)
         derived(r)
-        if r:
-            ts(V("OLD"), IND(V("AM", 0, r * 32), V("OFM")), C(24), O.min)
-        else:
-            fill(V("OLD"), -2048.0)
-        mm(V("P4", 0, 32), [(V("ID"), V("OLD"))], True, False)
-        mm(V("P4", 0, 32), wraps("WMU" if r else "WM", "A", r * SL, 512), False, True)
-        if r:
-            lay = V("A", 0, (r + 1) * SL)
-            cp(V("S", 0, 256), IND(lay, V("OFA", 0, 16)))
-            act(V("S", 256, 512), IND(lay, V("OFA", 16, 32)), F.Copy)
+
+    def former(r):
+        ts(C(24), Q(r, 10), float(r * SL), O.min)
+        ts(V("OFM"), V("CLF", 0, 2), C(24), O.add, 1.0 / 16, O.mult)
+        act(V("OM"), IND(V("AM", 0, r * 32 + 32), V("OFM")), F.Copy)
 
     def children(r):
-        par = V("S" if r else "A", 0, 512)
-        if not r:
-            consts1()
-            ts(V("OFF"), V("CLF"), 1.0 / 16, O.mult)
         apart = {1: "P0", 3: "P1", 5: "P7"}
-        for k in apart:
-            mm(V(apart[k]), [(V("IDN"), par)], True, False)
+        par = V("S" if r else "A", 0, 512)
         mz = V("AM", r * 32, r * 32 + 32)
-        ts(V("MR"), V("P4", 0, 32), MAGIC * 4096, O.add, MAGIC * 4096, O.subtract)
-        tt(mz, V("P4", 0, 32), V("MR"), O.subtract)
-        act(V("SQ"), mz, F.Square, bias=512.0, scale=0.25)
-        for j in range(4):
-            ts(V("TJ", j * 32, j * 32 + 32), mz, float(KA[j]), O.mult, CE8, O.add)
-        for j in range(4, 8):
-            act(V("TJ", j * 32, j * 32 + 32), mz, F.Identity, bias=CE8, scale=float(KA[j]))
 
-        def add(j0, j1):
-            for j in range(j0, j1):
-                tt(V("VJ", j * 32, j * 32 + 32), V("TJ", j * 32, j * 32 + 32), V("SQ"), O.add)
+        def J(name, j0, j1=None, w=32):
+            return V(name, j0 * w, (j0 + 1 if j1 is None else j1) * w)
 
-        def rest(j0, j1):
-            ts(V("VK", j0 * 32, j1 * 32), V("VJ", j0 * 32, j1 * 32), 4095, O.bitwise_and)
+        def numbers():
+            out = V("P4", 0, 32)
+            mm(out, [(V("BLK"), V("CU", 0, 32))] + [(V("ID"), V("OLD", x, x + 32)) for x in (0, 32) if r], True, False)
+            mm(out, wraps("WMU" if r else "WM", "A", r * SL, 512), False, True)
+            if r:
+                lay = V("A", 0, (r + 1) * SL)
+                cp(V("S", 0, 256), IND(lay, V("OFA", 0, 16)))
+                act(V("S", 256, 512), IND(lay, V("OFA", 16, 32)), F.Copy)
+                for j in apart:
+                    mm(V(apart[j]), [(V("IDN"), par)], True, False)
+            ts(V("MR"), out, MAGIC * 4096, O.add, MAGIC * 4096, O.subtract)
+            tt(mz, out, V("MR"), O.subtract)
+            act(V("SQ"), mz, F.Square, bias=512.0, scale=0.25)
+            for j in range(3):
+                ts(J("TJ", j), mz, float(KA[j]), O.mult, CE8, O.add)
+            for j in range(3, 8):
+                act(J("TJ", j), mz, F.Identity, bias=CE8, scale=float(KA[j]))
+            for j0, j1 in ((0, 4), (4, 8)):
+                for j in range(j0, j1):
+                    tt(J("VJ", j), J("TJ", j), V("SQ"), O.add)
+                ts(J("VK", j0, j1), J("VJ", j0, j1), 4095, O.bitwise_and)
+                cp(J("OFO", j0, j1), J("VK", j0, j1))
 
-        def lists(j0, j1):
-            cp(V("OFO", j0 * 32, j1 * 32), V("VK", j0 * 32, j1 * 32))
+        def gather(j):
+            tt(J("D", j, w=512), IND(V("OPW"), J("OFO", j)), par, O.subtract)
 
-        def gather(k):
-            x, y = k * 512, k * 512 + 512
-            tt(V("D", x, y), IND(V("OPW"), V("OFO", k * 32, k * 32 + 32)), par, O.subtract)
+        def other(j):
+            act(J("D", j, w=512), IND(V("OPW"), J("OFO", j)), F.Copy)
+            mm(V(apart[j]), [(V("ID"), J("D", j, w=512))], False, True)
 
-        def other(k):
-            x, y = k * 512, k * 512 + 512
-            act(V("D", x, y), IND(V("OPW"), V("OFO", k * 32, k * 32 + 32)), F.Copy)
-            mm(V(apart[k]), [(V("ID"), V("D", x, y))], False, True)
+        def size(j):
+            act(J("CH", j, w=512), V(apart[j]) if j in apart else J("D", j, w=512), F.Abs)
 
-        def size(k):
-            x, y = k * 512, k * 512 + 512
-            act(V("CH", x, y), V(apart[k]) if k in apart else V("D", x, y), F.Abs)
+        def Z(k):
+            return V(ROWS[k // 2], k % 2 * 64, k % 2 * 64 + 64)
 
         def opens(k):
-            z = V("P%d" % (2 + k // 2), k % 2 * 64, k % 2 * 64 + 64)
-            mm(z, [(V("ID"), V("FS")), (V("BLK"), V("CZ"))], True, False)
+            mm(Z(k), [(V("ID"), V("FS")), (V("BLK"), V("CZ"))], True, False)
             if k == 3:
-                mm(z, wraps("XBN", "D", k * 1024, 1024), False, False)
+                mm(Z(k), wraps("XBN", "D", 3072, 1024), False, False)
 
         def sums(k):
             if k < 3:
                 opens(k)
-            mm(V("P%d" % (2 + k // 2), k % 2 * 64, k % 2 * 64 + 64), wraps("XB", "CH", k * 1024, 1024), False, True)
+            mm(Z(k), wraps("XB", "CH", k * 1024, 1024), False, True)
 
-        def twice(k):
-            x, y = k * 512, k * 512 + 512
-            ts(V("CH", x, y), V("D", x, y), 0.0, O.max, 2.0, O.mult)
+        def twice(j):
+            ts(J("CH", j, w=512), J("D", j, w=512), 0.0, O.max, 2.0, O.mult)
 
         def costs():
-            act(V("FSA"), IND(V("AC", 0, (r + 1) * 32), V("OFF")), F.Copy)
-            ts(V("FSP"), IND(V("AC", 0, (r + 1) * 32), V("OFF")), THR, O.is_lt, -4096.0, O.mult)
+            ts(V("FSP"), IND(V("AC", 0, r * 32 + 32), V("OFF")), THR, O.is_lt, -4096.0, O.mult)
 
         def costs2():
-            tt(V("FS"), V("FSA"), V("FSP"), O.max)
+            tt(V("FS"), IND(V("AC", 0, r * 32 + 32), V("OFF")), V("FSP"), O.max)
 
         def keys(h):
             a, b = h * 128, h * 128 + 128
-            z = V("P%d" % (2 + h), 0, 128)
+            z = {"ap": T[ROWS[h]][:, 0:8, :], "r": [(ROWS[h], 0, 512, 1)], "n": 128, "w": 4}
             ts(V("QQ", a, b), z, MAGIC / 1024, O.add, MAGIC / 1024, O.subtract)
             ts(V("YH", a, b), z, MAGIC, O.add, MAGIC, O.subtract)
             tt(V("DD", a, b), z, V("QQ", a, b), O.subtract)
@@ -524,17 +649,18 @@ def rank_program(g, core, T, topo):
             mm(out, base, True, p == 4)
             if p < 2:
                 mm(out, [(V("IDM" if own[p][1] else "IDP"), V("DD", a, b))], False, True)
-            if p > 4:
-                mm(out, [(V("ID"), V("PEN", p * 256 - 1024 + a, p * 256 - 1024 + b))], False, True)
+            elif p < 4:
+                mm(out, [(V("ID"), V("PEN", p * 256 - 256 + a, p * 256 - 256 + b))], False, True)
 
         def halves(h, c):
-            cp(V("XH", c * 256 + h * 128, c * 256 + h * 128 + 128), V("P%d" % (5 + c), h * 128, h * 128 + 128))
+            cp(V("XH", c * 256 + h * 128, c * 256 + h * 128 + 128), V("P%d" % (2 + c), h * 128, h * 128 + 128))
 
-        add(0, 8)
-        rest(0, 4)
-        rest(4, 8)
-        lists(0, 4)
-        lists(4, 8)
+        numbers()
+        if not r:
+            consts1()
+            ts(V("OFF"), V("CLF"), 1.0 / 16, O.mult)
+            for j in apart:
+                mm(V(apart[j]), [(V("IDN"), par)], True, False)
         other(1)
         gather(0)
         other(3)
@@ -562,32 +688,31 @@ def rank_program(g, core, T, topo):
         keys(0)
         owners(0)
         sums(2)
-        for c in range(2):
-            mix(0, 5 + c)
-        mix(0, 4)
-        for c in range(2):
-            mix(0, c)
+        for p in (2, 3, 4, 0, 1):
+            mix(0, p)
         keys(1)
         halves(0, 0)
         owners(1)
         halves(0, 1)
-        for p in (4, 5, 0, 6, 1):
+        for p in (4, 2, 0, 3, 1):
             mix(1, p)
         red(C(16), V("P4", 0, 256), O.min)
         signs(0, 0)
         signs(1, 0)
         halves(1, 0)
         ts(V("MD"), V("LM"), C(16), O.mult, 2047.0, O.min)
-        mm(V("P7", 0, 16), [(V("BLK"), V("MD"))])
         below(0, 0)
         halves(1, 1)
+        mm(V("P3", 256, 272), [(V("BLK"), V("MD"))])
 
     def TH(c, i):
         return T0 if i == 0 else V("TT", c * 16 + i % 2 * 8 + 5, c * 16 + i % 2 * 8 + 6)
 
     def cand(c, i):
         x = c * 32 + i % 2 * 16
-        if i < 4:
+        if 0 < i < 4 and c:
+            act(V("CAND", x, x + 9), V("CT", 16 * i, 16 * i + 9), F.Identity, bias=TH(c, i))
+        elif i < 4:
             ts(V("CAND", x, x + 9), V("CT", 16 * i, 16 * i + 9), TH(c, i), O.add)
         else:
             ts(V("CAND", x, x + 9), V("CT", 16 * i, 16 * i + 9), TH(c, i), O.add, LIM, O.min)
@@ -618,8 +743,6 @@ def rank_program(g, core, T, topo):
         scan(V("TT", y, y + 6), V("P%d" % (5 + c), 0, 6), V("CAND", x, x + 6), V("CAND", x + 6, x + 7), O.min, O.max)
 
     def search():
-        for c in range(2):
-            mm(V("P%d" % (2 + c), 0, 256), [(V("ID2K"), V("KD"))], True, False)
         tally(0, (0, 1, 2))
         totals(0)
         below(1, 0)
@@ -630,7 +753,9 @@ def rank_program(g, core, T, topo):
             tally(1 - c, (1, 2))
             totals(1 - c)
             if n == 1:
-                red(C(27), V("P7", 0, 16), O.min)
+                red(C(27), V("P3", 256, 272), O.min)
+                for k in range(2):
+                    mm(V("P%d" % (2 + k), 0, 256), [(V("ID2K"), V("KD"))], True, False)
             if i < 4:
                 cand(c, i + 1)
                 signs(c, i + 1)
@@ -640,30 +765,30 @@ def rank_program(g, core, T, topo):
     def kept(c):
         x = c * 512
         ts(V("KP", x, x + 256), V("XH", c * 256, c * 256 + 256), TH(c, 5), O.subtract, OFFS, O.is_lt)
-        ts(V("KP", x + 256, x + 512), V("P%d" % c, 0, 256), TH(c, 5), O.is_lt)
+        act(V("KP", x + 256, x + 512), V("P%d" % c, 0, 256), F.Sign, bias=TH(c, 5), scale=-1.0)
 
     def ranks(c):
         x = c * 512
         for o in range(2):
             y = x + o * 256
-            scan(V("R", y, y + 256), V("KP", y, y + 256), V("ZH"), 0.0, O.add, O.add)
+            scan(V("R", y, y + 256), V("KP", y, y + 256), V("ONE") if o else V("KP", y, y + 256), 0.0, O.add, O.add)
         mms([(V("P%d" % (2 + c), k * 32, k * 32 + 32), V("NBD"), V("R", x + 15, x + 512, 16)) for k in range(8)], False, True)
 
     def ends(c):
         x = c * 512
-        mm(V("P%d" % (5 + c), 0, 32), wraps("S1", "R", x, 512))
+        mm(V("P%d" % (5 + c), 0, 32), wraps("S1H", "R", x, 512))
         for o in range(2):
             y = c * 544 + o * 272
             act(V("EBW", y, y + 256, 16), V("P%d" % (5 + c), o * 16, o * 16 + 16), F.Copy)
 
     def places(c):
-        p = ("P7", "P4")[c]
+        p = "P7"
         for o in range(2):
             y = c * 512 + o * 256
-            mm(V(p, o * 256, o * 256 + 256), [(V("BLK"), V("R", y, y + 256)), (V("NUT"), V("KP", y, y + 256))])
+            mm(V(p, o * 256, o * 256 + 256), [(V("BLKH"), V("R", y, y + 256)), (V("NUTH" if o else "NUT"), V("KP", y, y + 256))])
         for o in range(2):
             y = c * 544 + o * 272
-            act(V("W", y, y + 256), V(p, o * 256, o * 256 + 256), F.Copy)
+            act(V("W", y, y + 256), V(p, o * 256, o * 256 + 256), F.Identity, bias=L(21) if o else 0.0)
 
     def first(c):
         scan(V("V1", c * 256, c * 256 + 256), V("P%d" % (2 + c), 0, 256), V("DT"), 0.0, O.max, O.min)
@@ -690,84 +815,157 @@ def rank_program(g, core, T, topo):
         tt(V("OH", x, x + 256), IND(V("W", c * 544, c * 544 + 544), V("OFW", c * 16, c * 16 + 16)), V("K1"), O.is_equal)
         mm(V("P%d" % c, 0, 16), wraps("SD", "OH", x, 256), False, True)
 
-    def where(r, buf, home, w):
-        return lambda o: (home, ((r + 1) * 4 + o) * w) if o == me else (buf, (r * 4 + o) * w)
+    def where(r, buf, stays, w):
+        return lambda o: (stays, (slot(r) * 4 + home) * w) if o == me else (buf, (r * 4 + o) * w)
+
+    def third_list(c):
+        for o in (1, 0):
+            cp(V("OFN", c * 16 + o * 8, c * 16 + o * 8 + 8), V("P%d" % c, o, 16, 2))
 
     def states(r, c):
         at = where(r, "SND", "A", 128)
         for o in (1, 0):
-            cp(V("OFN", c * 16 + o * 8, c * 16 + o * 8 + 8), V("P%d" % c, o, 16, 2))
-        for o in (1, 0):
             buf, x = at(own[c][o])
             v = IND(V("CH"), V("OFN", c * 16 + o * 8, c * 16 + o * 8 + 8))
-            if o:
+            if o or c:
                 act(V(buf, x, x + 128), v, F.Copy)
             else:
                 cp(V(buf, x, x + 128), v)
         send(r, "a", at, [o for o in own[c] if o != me])
 
-    def prices(r, c):
+    def prices(c):
         x = c * 256
         tt(V("CG", x, x + 256), IND(V("YW"), V("OFW", c * 16, c * 16 + 16)), V("OH", x, x + 256), O.mult)
-        mm(V("P%d" % (5 + c), 0, 16), wraps("S1", "CG", x, 256))
 
-    def price_lists(r, c):
+    def price_lists(r, cs):
         at = where(r, "SNC", "AC", 8)
-        for o in range(2):
-            buf, y = at(own[c][o])
-            act(V(buf, y, y + 8), V("P%d" % (5 + c), o, 16, 2), F.Copy)
+        mm(V("P4", cs[0] * 16, cs[-1] * 16 + 16), wraps("S1", "CG", cs[0] * 256, len(cs) * 256))
+        for c in cs:
+            for o in range(2):
+                buf, y = at(own[c][o])
+                act(V(buf, y, y + 8), V("P4", c * 16 + o, c * 16 + 16, 2), F.Copy)
+
+    def E(k, n=1):
+        return V("EV", k, k + n)
+
+    def older():
+        r = NR - 1
+        is0, is1, is2 = Q(r, 11), Q(r, 13), Q(r, 12)
+        for x, y in ((3, 0), (3, 4), (7, 8), (7, 12)):
+            act(E(16 + y, 4), Q(r, x, 4), F.Copy)
+        ts(E(0), is2, 2.0, O.mult, is1, O.add)
+        ts(E(1), L(25), is0, O.mult, L(27), O.add)
+        ts(E(2), L(26), is2, O.mult, E(1), O.add)
+        ts(V("OG3", 12, 13), E(2), E(0), O.subtract)
+        cp(E(32, 16), IND(E(16, 16), V("OG3", 12, 13)))
+        ts(E(3), is0, 64.0, O.mult)
+        ts(E(6), is2, 32.0, O.mult)
+        ts(E(4), is1, 64.0, O.mult, E(6), O.add)
+        ts(E(5), E(6), 32.0, O.add)
+        for l in range(3):
+            ts(V("OG3", 6 + l * 2, 8 + l * 2), V("CL", 0, 2), E(3 + l), O.add)
+        for k, x in enumerate((is0, is1, is2)):
+            ts(V("GM", k * 8, k * 8 + 8), V("G8"), x, O.mult)
+        tt(V("GM", 24, 32), V("G8"), V("GM", 0, 8), O.subtract)
+        tt(V("GM", 32, 40), V("G8"), V("GM", 16, 24), O.subtract)
+        fill(E(11), float(slot(r) * SL))
+        for t in range(2):
+            gaps(t, V("AC", 0, slot(r) * 32), E(34 + t), E(32 + t))
+
+    def gaps(t, costs, bound, at):
+        a, b, x, y = t * 32, t * 32 + 32, (t + 1) % 3 * 512, 0 if t == 2 else 512
+        d, p = "P%d" % (2 + t % 2), V("P%d" % (t % 2), 0, 32)
+        mm(V(d, 0, 256), [(V("ID2K"), V("KD3"))], True, False)
+        ts(V("OG3", t * 2, t * 2 + 2), V("CLF", 0, 2), at, O.add, 1.0 / 16, O.mult)
+        ts(E(8 + t), bound, -1023.0, O.add)
+        ts(V("KP3", a, b), IND(costs, V("OG3", t * 2, t * 2 + 2)), E(8 + t), O.is_lt, 2.0, O.mult)
+        act(V("F3", a, b), IND(costs, V("OG3", t * 2, t * 2 + 2)), F.Copy)
+        scan(V("R3", a, b), V("RM"), V("KP3", a, b), 0.0, O.mult, O.add)
+        mms([(V(d, k * 32, k * 32 + 32), V("NBD"), V("R3", a, b)) for k in range(8)], False, True)
+        mm(V("P7", 0, 32), [(V("BLKH"), V("R3", a, b)), (V("NUTH"), V("KP3", a, b))])
+        act(V("W3", a, b), V("P7", 0, 32), F.Copy)
+        scan(V("V1", y, y + 256), V(d, 0, 256), V("DT3"), 0.0, O.max, O.min)
+        for k in range(8):
+            cp(V("OF3", a + k, b, 8), V("V1", y + k * 32 + 6, y + k * 32 + 32, 8))
+        tt(V("OH", x, x + 512), IND(V("W3", a, b), V("OF3", a, b)), V("K13"), O.is_equal)
+        cp(V("V3", a, b), V("OF3", a, b))
+        mm(p, [(V("IDF"), V("V3", a, b)), (V("ID"), V("C3"))], True, False)
+        mm(p, wraps("SD", "OH", x, 512) + wraps("SN", "OH", x, 512), False, True)
+        for z in (0, 256):
+            tt(V("CG", x + z, x + z + 256), IND(V("F3", a, b), V("OF3", a + z // 16, a + z // 16 + 16)), V("OH", x + z, x + z + 256), O.mult)
+        ts(V("OPF", a, b), p, at, O.add, 10.0 * SL, O.min)
+        for l, m in (((0, 3), (1, 0)), ((1, 2), (2, 4)), ((0, 0), (1, 1), (2, 2)))[t]:
+            mm(V("P%d" % (4 + l), 0, 512, P=8), [(V("GM", m * 8, m * 8 + 8), V("CG", x, x + 512))], (t, l) in ((0, 0), (0, 1), (1, 2)), t == 2)
 
     def rnd(r):
         parents(r)
         children(r)
-        mb = r * 16 + me * 4
+        mb = r * 16 + home * 4
         search()
 
         def bound(c):
             ts(V("MB", mb + 2 * c, mb + 2 * c + 1), TH(c, 5), Q(r, 0), O.add, OFFS + 0.5, O.add)
 
+        def sizes(j):
+            act(V("CH", j * 512, j * 512 + 512), V("D", j * 512, j * 512 + 512), F.Abs)
+
+        if not r:
+            consts2()
         kept(0)
-        for o in range(2):
-            act(V("YW", o * 272, o * 272 + 256), V("P4", 0, 256), F.Identity, bias=LMN)
-        act(V("CH", 3072, 4096), V("D", 3072, 4096), F.Abs)
-        ranks(0)
-        decide(1, 4)
         bound(0)
         ts(V("MB", mb + 1, mb + 2), C(27), Q(r, 0), O.add)
-        ends(0)
+        ranks(0)
+        decide(1, 4)
         kept(1)
+        ends(0)
         bound(1)
-        send(r, "b", lambda o: ("MB", mb), others)
+        send(r, "b", lambda o: ("MB", mb), far)
+        send(r, "b", lambda o: ("MB", mb), [o for o in others if o not in far])
         arrive(r, "b")
         first(0)
         places(0)
         ranks(1)
         first_list(0)
         second(0)
-        first(1)
         ends(1)
-        places(1)
-        if not r:
-            consts3()
-        pre(r)
+        first(1)
         first_list(1)
         second_list(0)
         columns(0)
         third(0)
         second(1)
-        prices(r, 0)
-        states(r, 0)
+        places(1)
+        for j in (6, 7):
+            sizes(j)
+        if r < NR - 1:
+            third_list(0)
+            states(r, 0)
         second_list(1)
         columns(1)
-        price_lists(r, 0)
-        early = [o for o in own[0] if o != me] if r == NR - 1 else []
-        if early:
-            send(r, "c", where(r, "SNC", "AC", 8), early)
         third(1)
-        prices(r, 1)
-        states(r, 1)
-        price_lists(r, 1)
-        send(r, "c", where(r, "SNC", "AC", 8), [o for o in others if o not in early])
+        for o in range(2):
+            act(V("YW", o * 272, o * 272 + 256), V("P4", 0, 256), F.Identity, bias=LMN)
+        if not r:
+            consts3()
+        pre(r)
+        if r < NR - 1:
+            third_list(1)
+            states(r, 1)
+            prices(0)
+            prices(1)
+            price_lists(r, (0, 1))
+            send(r, "c", where(r, "SNC", "AC", 8), far)
+            send(r, "c", where(r, "SNC", "AC", 8), [o for o in others if o not in far])
+            former(r)
+        else:
+            for c in range(2):
+                prices(c)
+                price_lists(r, (c,))
+                send(r, "c", where(r, "SNC", "AC", 8), [o for o in own[c] if o != me])
+            for c in range(2):
+                third_list(c)
+                states(r, c)
+            older()
         arrive(r, "a")
         arrive(r, "c")
         if r == 0:
@@ -779,62 +977,36 @@ def rank_program(g, core, T, topo):
     for r in range(NR):
         rnd(r)
 
-    for h in range(2):
-        mm(V("P%d" % (2 + h), 0, 384), [(V("ID2K"), V("KD3", h * 384, h * 384 + 384))], True, False)
+    gaps(2, V("AC"), Q(NR - 1, 4), E(11))
+    for l in range(2):
+        act(V("YF", l * 512, l * 512 + 512, P=8), V("P%d" % (4 + l), 0, 512, P=8), F.Identity, bias=1023.0)
+    for l in range(3):
+        cp(V("OP3", l * 32, l * 32 + 32), IND(V("OPF"), V("OG3", 6 + l * 2, 8 + l * 2)))
+    for l in range(3):
+        if l == 2:
+            ts(V("YF", 1024, 1536, P=8), V("P6", 0, 512, P=8), 1023.0, O.add)
+            dma("Y", EXT(T.yf[:, :]), V("YF", P=8), "o4")
+        for h in range(2):
+            a = l * 512 + h * 256
+            v = IND(V("A"), V("OP3", a // 16, a // 16 + 16))
+            if h:
+                act(V("YL", a, a + 256), v, F.Copy)
+            else:
+                cp(V("YL", a, a + 256), v)
+        dma("YS"[l // 2], EXT(T.yl[:, l * 512:l * 512 + 512]), V("YL", l * 512, l * 512 + 512), "o%d" % (1 + l))
+
     ts(C(17), Q(NR, 12), 2.0, O.mult, Q(NR, 13), O.add)
-    for x, y, n in ((0, 0, 3), (3, 6, 4), (7, 14, 4)):
+    for x, y, n in ((0, 0, 3), (3, 6, 4)):
         cp(V("DB", y, y + n), Q(NR, x, n))
         act(V("DB", y + n, y + 2 * n), Q(NR, x, n), F.Copy)
     ts(V("OFQ", 0, 1), FB, C(17), O.subtract)
     cp(V("FIN"), IND(V("DB"), V("OFQ", 0, 1)))
-    for l in range(3):
-        ts(V("OG3", l * 2, l * 2 + 2), V("CLF", 0, 2), V("FIN", 8 + l, 9 + l), O.add, 1.0 / 16, O.mult)
-    ts(C(18, 3), V("FIN", 3, 6), -1023.0, O.add)
-    for l in range(3):
-        ts(C(21 + l), V("FIN", 8 + l, 9 + l), -512.0 * l, O.add)
     cp(V("FIN", 6, 7), C(17))
     cp(V("FIN", 7, 8), U)
-    mm(V("P7", 0, 8, P=8), [(V("G8F"), V("FIN", 0, 8))])
-    act(V("YT8", P=8), V("P7", 0, 8, P=8), F.Copy)
+    mm(V("P3", 0, 8, P=8), [(V("G8F"), V("FIN", 0, 8))])
+    act(V("YT8", P=8), V("P3", 0, 8, P=8), F.Copy)
     dma("Y", EXT(T.yt[:, :]), V("YT8", P=8), "o0")
-    for l in range(3):
-        a, b = l * 32, l * 32 + 32
-        ts(V("KP3", a, b), IND(V("AC"), V("OG3", l * 2, l * 2 + 2)), C(18 + l), O.is_lt)
-        act(V("F3", a, b), IND(V("AC"), V("OG3", l * 2, l * 2 + 2)), F.Copy)
-    scan(V("R3"), V("RM"), V("KP3"), 0.0, O.mult, O.add)
-    for h in range(2):
-        mms([(V("P%d" % (2 + h), k * 96, k * 96 + 96), V("NBD"), V("R3")) for k in range(4)], False, True)
-    mm(V("P4", 0, 96), [(V("BLK"), V("R3")), (V("NUT"), V("KP3"))])
-    act(V("W3"), V("P4", 0, 96), F.Copy)
-    for h in range(2):
-        scan(V("V1", h * 384, h * 384 + 384), V("P%d" % (2 + h), 0, 384), V("DT3", h * 384, h * 384 + 384), 0.0, O.max, O.min)
-    for k in range(8):
-        cp(V("OF3", k, 96, 8), V("V1", k * 96 + 6, k * 96 + 96, 8))
-    cp(V("V3"), V("OF3"))
-    for l in range(3):
-        a, b, p = l * 512, l * 512 + 512, V("P%d" % l, 0, 32)
-        tt(V("OH", a, b), IND(V("W3"), V("OF3", l * 32, l * 32 + 32)), V("K13"), O.is_equal)
-        mm(p, [(V("IDF"), V("V3", l * 32, l * 32 + 32)), (V("ID"), V("C3", 0, 32))], True, False)
-        mm(p, wraps("SD", "OH", a, 512) + wraps("SN", "OH", a, 512), False, True)
-
-    def prices3(l):
-        a, b = l * 512, l * 512 + 512
-        tt(V("CG", a, b), IND(V("F3"), V("OF3", l * 32, l * 32 + 32)), V("OH", a, b), O.mult)
-        mm(V("P%d" % (4 + l), 0, 512, P=8), [(V("G8"), V("CG", a, b))])
-
-    def states3(l):
-        a, b = l * 512, l * 512 + 512
-        ts(V("OP3", l * 32, l * 32 + 32), V("P%d" % l, 0, 32), C(21 + l), O.add, 10.0 * SL - 1, O.min)
-        act(V("YL", a, b), IND(V("A"), V("OP3", l * 32, l * 32 + 32)), F.Copy)
-        dma("Y", EXT(T.yl[:, a:b]), V("YL", a, b), "o%d" % (1 + l))
-
-    for l in range(3):
-        states3(l)
-        prices3(l)
-    for l in range(2):
-        act(V("YF", l * 512, l * 512 + 512, P=8), V("P%d" % (4 + l), 0, 512, P=8), F.Identity, bias=1023.0)
-    ts(V("YF", 1024, 1536, P=8), V("P6", 0, 512, P=8), 1023.0, O.add)
-    dma("S", EXT(T.yf[:, :]), V("YF", P=8), "o4")
+    issue_all()
     for k in range(4):
         g.sync.wait_ge(T.sem["o%d" % k], 16)
     for k in range(6):

@@ -7,9 +7,27 @@ EMPTY = 8
 WT = [1, 3, 7, 13, 21, 35, 49, 67, 85, 107, 129, 155, 181, 211, 241, 253]
 KA = [17, 101, 263, 389, 547, 701, 859, 1021]
 MAGIC = float(3 << 22)
-OFFS = 6144.0
 STEPS = [256, 64, 16, 4, 1]
-CYCLE, WAKE, ISSUE, HOP, PASSES = 0.9, 200.0, 300.0, 2500.0, 3
+SHIFT = 918 * 4096
+KEY = 1537.0
+SHARE = ((3, 3, 3, 3, 3), (3, 3, 3, 3, 3))
+CANDS = "VS"
+PIECES = ((0, 128), (128, 192), (192, 256))
+FLOW = ("q1 q0 q2 q3 w1 w0 w2 w3 m1 m0 m2 m3 f1 f0 f2 f3 a0 a1 o3 a2 x3 g0 o5 x5 g1 c0 t0 c1 t1 p0 s0 o7 x7 g2 g4 g6 z3 z5 z7 z2 s1 z4 s2 z6 s3"
+        " | d0 d1 k0 k1 e0 e1 k2")
+DIRECT = False
+APART, TW = (3, 5, 7), 0
+EARLY = 192
+XKE = "SSV"
+PAIR = True
+ZB = (("P5", 0), ("P5", 64), ("P6", 0), ("P3", 0))
+STRICT = ""
+ROW = 3.0
+FETCH = "VS"
+ORDER = "bmac"
+SCHED, PATIENCE, MIX = 0, 0.0, 1.0
+TURNS = "001" + "010101" * 5
+CYCLE, WAKE, ISSUE, HOP, PASSES = 0.9, 200.0, 300.0, 2000.0, 3
 QUEUED = 800.0
 TENSOR = 0.5
 
@@ -18,18 +36,19 @@ PSUM = ["P%d" % k for k in range(8)]
 SCRATCH = {}
 for _n, _w, _d in (
         ("A", 10 * SL + 16, _b), ("AC", 320, _f), ("OPW", 4096, _b), ("SND", NR * SL, _b), ("SNC", NR * 32, _f), ("MB", NR * 16, _f),
-        ("S", 512, _b), ("FSP", 64, _f), ("FS", 64, _h), ("D", 4096, _b), ("CH", 4112, _b), ("CB", 32, _h), ("ID16", 128, _b),
+        ("S", 512, _b), ("FSP", 64, _f), ("FS", 64, _h), ("D", 4096, _b), ("CH", 4112, _b), ("CB", 128, _h), ("ID16", 128, _b),
         ("OFA", 32, _u), ("OFF", 4, _u), ("OFO", 256, _u), ("OFB", 32, _u), ("OFW", 32, _u), ("OFN", 32, _u), ("OFQ", 2, _u),
-        ("MR", 32, _f), ("SQ", 32, _f), ("S1H", 144, _b), ("BLKH", 128, _b), ("NUTH", 128, _b), ("TJ", 256, _f), ("VJ", 256, _i), ("VK", 256, _i),
-        ("YH", 256, _h), ("QQ", 256, _f), ("DD", 256, _b), ("PEN", 768, _b), ("XH", 512, _h), ("YW", 544, _f),
-        ("DV", 1536, _h), ("RS", 1536, _h), ("DA", 1536, _b), ("CN", 8, _f), ("CAND", 64, _f), ("TT", 32, _f),
-        ("KP", 1024, _b), ("R", 1024, _b), ("V1", 768, _b), ("EBW", 1088, _b), ("W", 1088, _b), ("IB", 512, _b), ("OH", 1536, _b), ("CG", 1536, _h),
-        ("TB", 64, _f), ("AM", NR * 32, _f), ("OLD", 64, _h), ("OM", 32, _f), ("CU", 64, _b), ("OFM", 2, _u), ("WMU", 144, _b), ("XBN", 144, _h), ("SV", 32, _f), ("MD", 16, _h),
+        ("MR", 64, _f), ("CJ", 224, _f), ("C4", 944, _b), ("BLKH", 128, _b), ("NUTH", 128, _b), ("TJ", 256, _f), ("VJ", 256, _i), ("VK", 256, _i),
+        ("YH", 256, _h), ("QQ", 256, _f), ("DD", 256, _b), ("PEN", 256, _b), ("XK", 256, _h), ("YW", 544, _f),
+        ("DV", 2048, _h), ("RS", 1024, _h), ("DA", 1536, _b), ("CN", 32, _f), ("CAND", 80, _f), ("TT", 40, _f),
+        ("SG", 1168, _b), ("MS", 128, _f), ("NBG", 128, _b), ("CM", 16, _h),
+        ("KP", 1024, _b), ("R", 1024, _b), ("V1", 768, _b), ("EBW", 288, _b), ("W", 1088, _b), ("IB", 512, _b), ("OH", 1536, _b), ("CG", 1536, _h),
+        ("TB", 64, _f), ("AM", NR * 128, _f), ("SNM", NR * 128, _f), ("YM", 544, _f), ("CU", 32, _b), ("OFM", 2, _u), ("WMN", 144, _b), ("CGM", 512, _h), ("XBN", 144, _h), ("SV", 32, _f), ("MD", 16, _h),
         ("ONE", 256, _b), ("ZH", 256, _h), ("BLK", 128, _b), ("NBH", 128, _b), ("NBF", 128, _f), ("NBD", 128, _b), ("NUT", 128, _b),
-        ("ID", 128, _b), ("IDN", 128, _b), ("ID2K", 128, _b), ("IDP", 128, _b), ("IDM", 128, _b), ("IDF", 128, _f),
+        ("ID", 128, _b), ("IDN", 128, _b), ("ID2K", 128, _b), ("IDP", 128, _b), ("IDF", 128, _f),
         ("S1", 144, _b), ("SD", 144, _b), ("SN", 144, _b), ("WM", 144, _b), ("XB", 144, _h),
         ("K", 256, _b), ("K1", 256, _b), ("K13", 512, _b), ("KD", 256, _b), ("DT", 256, _b), ("CL", 32, _f), ("CLF", 4, _f),
-        ("CZ", 64, _h), ("M2", 64, _b), ("CA", 4, _b), ("CO", 16, _b), ("CT", 80, _f),
+        ("CZ", 64, _h), ("M2", 64, _b), ("CA", 4, _b), ("CT", 80, _f),
         ("LM", 16, _f), ("RW", 80, _f), ("RX", 80, _f), ("LC", 32, _f), ("LI", 8, _i), ("G8", 8, _h), ("G8F", 8, _f),
         ("F3", 96, _f), ("KP3", 96, _b), ("R3", 96, _b), ("RM", 32, _b), ("W3", 96, _b), ("V3", 96, _f),
         ("EV", 128, _f), ("GM", 40, _h), ("OPF", 96, _f),
@@ -39,13 +58,16 @@ for _n, _w, _d in (("B8", 144, _h), ("F8I", 512, _i), ("F8", 512, _h), ("YF", 15
     SCRATCH[_n] = ("sbuf", [8, _w], _d)
 for _n in PSUM:
     SCRATCH[_n] = ("psum", [128, 512], _f)
-PARTS = {"DB": (48, 24), "FIN": (72, 16), "C8": (88, 2)}
-ROWS = ("P5", "P6")
+PARTS = {"DB": ("EV", 48, 24), "FIN": ("EV", 72, 16), "C8": ("EV", 88, 2),
+         "DBN": ("SG", 512, 256), "RSB": ("SG", 768, 128), "BASE": ("SG", 896, 12),
+         "S4": ("C4", 0, 144), "S4H": ("C4", 144, 144), "SD4": ("C4", 288, 144), "NEG4": ("C4", 432, 128), "CO4": ("C4", 560, 64), "M4": ("C4", 624, 128),
+         "M4N": ("C4", 752, 64), "MC": ("C4", 816, 128), "MQ": ("SG", 912, 256), "CLM": ("LC", 22, 2)}
+ROWS = ("P2", "P3")
 for _n in ROWS:
-    SCRATCH[_n] = ("psum", [128, 32, 16], _f)
-SEMAPHORES = (["sV", "sS", "sT", "sG", "ls"] + ["%s%d%s" % (s, r, k) for s in "abc" for r in range(NR) for k in "nf"]
+    SCRATCH[_n] = ("psum", [128, 2, 256], _f)
+SEMAPHORES = (["sV", "sS", "sT", "sG", "ls"] + ["%s%d%s" % (s, r, k) for s in "abcm" for r in range(NR) for k in "nf"]
               + ["l%d" % k for k in range(10)] + ["o%d" % k for k in range(5)])
-MSG = {"b": ("MB", 16, 4, 0), "a": ("A", SL, 128, 1), "c": ("AC", 32, 8, 1)}
+MSG = {"b": ("MB", 16, 4, 0), "a": ("A", SL, 128, 1), "c": ("AC", 32, 8, 1), "m": ("AM", 128, 32, 1)}
 
 
 def slot(r):
@@ -93,7 +115,7 @@ def relay(g, core, T, topo):
             rid, pid = topo.addr(d, core)
             m = topo.mask(core, d)
             for r in range(NR):
-                for s in ("bac" if r < NR - 1 else "bca"):
+                for s in (ORDER if r < NR - 1 else "bca"):
                     buf, wr, w, r0 = MSG[s]
                     x = (slot(r) if r0 else r) * wr + q * w
                     sem = T.sem["%s%df" % (s, r)]
@@ -111,7 +133,8 @@ def rank_program(g, core, T, topo):
         return
     hop = ways(core, T, topo)
     far = [T.cores.index(d) for d in hop if hop[d] != d]
-    own = sorted([(2, 0), (1, 3)], key=lambda p: -len([o for o in p if o in far]))
+    own = sorted([(0, 2), (1, 3)], key=lambda p: -len([o for o in p if o in far]))
+    off = [1024.0 * p[1] - 2048.0 for p in own]
     home = me
     queue = {"V": g.vector, "S": g.scalar, "T": g.tensor, "G": g, "Y": g.sync}
     count = {"V": 0, "S": 0, "T": 0, "G": 0, "ls": 0}
@@ -120,13 +143,13 @@ def rank_program(g, core, T, topo):
 
     def V(name, a=None, b=None, s=1, P=128):
         if name in PARTS:
-            x, w = PARTS[name]
-            return V("EV", x + (a or 0), x + (w if b is None else b), s, P)
+            buf, x, w = PARTS[name]
+            return V(buf, x + (a or 0), x + (w if b is None else b), s, P)
         t = T[name]
         if a is None:
-            a, b = 0, t.shape[-1]
+            a, b = 0, 512 if name in ROWS else t.shape[-1]
         if name in ROWS:
-            ap = t[0:P, a // 16, a % 16:b - a // 16 * 16:s] if b - a // 16 * 16 <= 16 else t[0:P, a // 16:b // 16, :]
+            ap = t[0:P, a // 256, a % 256:b - a // 256 * 256:s]
         else:
             ap = t[0:P, a:b:s] if s != 1 else t[0:P, a:b]
         return {"ap": ap, "r": [(name, a, b, s)], "n": len(range(a, b, s)), "w": 2 if SCRATCH[name][2] in (_b, _h, _u) else 4}
@@ -170,12 +193,14 @@ def rank_program(g, core, T, topo):
                     logs[n] = old + [(a, b, wr, e, sem, val, clk, s)]
 
     calls = []
-    wrote, read, turn = {}, {}, {}
+    wrote, read, turn, strict = {}, {}, {}, {}
 
     def note(e, outs, ins, busy, issue, adds=False, late=0.0, after=()):
         me_, pre_ = len(calls), {}
-        for k in after:
+        for k in list(after) + strict.get(e, []):
             pre_[k] = 0.0
+        if e in strict:
+            strict[e] = [me_]
         for views, wr in ((ins, False), (outs, True)):
             for v in views:
                 for n, a, b, s in v["r"]:
@@ -223,6 +248,50 @@ def rank_program(g, core, T, topo):
                 start[k] = t
             return start
 
+        def run(edges, back, level):
+            start, left, ready, free, pool = [0.0] * n, [len(x) for x in edges], [0.0] * n, {}, {}
+            for k in range(n):
+                free[calls[k][0]] = 0.0
+                pool.setdefault(calls[k][0], [])
+                if not left[k]:
+                    pool[calls[k][0]].append(k)
+            for _ in range(n):
+                t, e = min([(max(free[q], min([ready[k] for k in pool[q]])), q) for q in pool if pool[q]])
+                k = max([x for x in pool[e] if ready[x] <= t], key=lambda x: (level[x], -x))
+                for h in sorted(pool[e], key=lambda x: -level[x]):
+                    if level[h] > level[k] and ready[h] < t + calls[k][1] and \
+                            max(level[h] + ready[h], level[k] + ready[h] + calls[h][1]) < level[h] + t + calls[k][1] - PATIENCE:
+                        k = h
+                        break
+                pool[e].remove(k)
+                start[k] = max(t, ready[k])
+                free[e] = start[k] + calls[k][1]
+                for x, w in back[k]:
+                    ready[x] = max(ready[x], start[k] + w)
+                    left[x] -= 1
+                    if not left[x]:
+                        pool[calls[x][0]].append(x)
+            return start
+
+        if SCHED:
+            after = [[] for _ in calls]
+            for k in range(n):
+                for p, w in ahead[k]:
+                    after[p].append((k, w))
+            level = [0.0] * n
+            for k in reversed(range(n)):
+                level[k] = max([calls[k][2]] + [w + level[x] for x, w in after[k]])
+            best = None
+            for _ in range(SCHED):
+                start = run(ahead, after, level)
+                end = max([start[k] + calls[k][2] for k in range(n)])
+                if best is None or end < best[0]:
+                    best = (end, start)
+                back = place(sorted(range(n), key=lambda k: (-start[k] - calls[k][1], -k)), behind)
+                level = [(1 - MIX) * level[k] + MIX * (back[k] + calls[k][1]) for k in range(n)]
+            for k in sorted(range(n), key=lambda x: (best[1][x], x)):
+                calls[k][4]()
+            return
         urgent, best = list(range(n)), None
         for _ in range(PASSES):
             start = place(sorted(range(n), key=lambda k: (urgent[k], k)), ahead)
@@ -322,6 +391,12 @@ def rank_program(g, core, T, topo):
     def wraps(base, buf, x, w):
         return [(V(base, 15 - i, 143 - i), V(buf, x + i, x + w, 16)) for i in range(16)]
 
+    def fours(base, buf, x, w):
+        return [(V(base, 3 - i, 131 - i), V(buf, x + i, x + w, 4)) for i in range(4)]
+
+    def pick(out, a):
+        scan(out, V("M4", 0, a["n"]), a, 0.0, O.mult, O.max)
+
     def send(r, s, src, owners):
         buf, wr, w, r0 = MSG[s]
         ins = [V(src(o)[0], src(o)[1], src(o)[1] + w) for o in owners]
@@ -356,7 +431,8 @@ def rank_program(g, core, T, topo):
     def landing(buf, xs, w, sem, n, kind):
         def issue():
             logs[buf] = logs.get(buf, []) + [(x, x + w, True, "net", sem, n, {sem: n}, 1) for x in xs]
-        note(sem, [V(buf, x, x + w) for x in xs], [], 1.0, issue, late=(HOP if kind[1] == "n" else 2 * HOP + ISSUE) + QUEUED * (kind[0] == "c"), after=[sent[kind]])
+        note(sem, [V(buf, x, x + w) for x in xs], [], 1.0, issue, late=(HOP + ROW * w * V(buf)["w"]) * (1 if kind[1] == "n" else 2) + ISSUE * (kind[1] == "f") + QUEUED * (kind[0] == "c"),
+             after=[sent[kind]])
 
     sent = {}
 
@@ -370,7 +446,7 @@ def rank_program(g, core, T, topo):
     def L(k):
         return V("LC", k, k + 1)
 
-    lane, L0, DA_, DB_, FB, WL, INI, T0 = L(0), L(1), L(2), L(3), L(4), L(5), L(8), L(9)
+    lane, L0, DA_, DB_, FB, WL, INI, T0 = L(0), L(1), L(2), L(3), L(4), L(5), L(8), (L(9), L(12))
     fill(V("ONE"), 1.0)
     iota(V("LI", 0, 1), [[1, 1]], 0, 1)
     iota(V("LM"), [[1, 16]], 0)
@@ -381,27 +457,30 @@ def rank_program(g, core, T, topo):
     sel(V("S1", 15, 144, 16), V("RX", 0, 9), [[16, 9]], O.is_ge, 15, -1)
     sel(V("B8", P=8), V("ONE", 0, 144, P=8), [[1, 144]], O.is_equal, -15, -16)
     sel(V("BLK"), V("BLK"), [[16, 8], [0, 16]], O.is_ge, 15, -1)
+    for j in range(7):
+        iota(V("CJ", j * 32, j * 32 + 32), [[0, 32]], -4 * KA[j] * KA[j] % 4096)
     iota(V("CLF"), [[0, 2], [256, 2]], 0)
-    iota(V("KD"), [[16, 8], [0, 32]], 0)
+    iota(V("KD"), [[0, 2], [16, 8], [0, 16]], 0)
     for i, s in enumerate(STEPS):
         iota(V("CT", 16 * i, 16 * i + 6), [[-s, 3], [0, 2]], s // 2)
         iota(V("CT", 16 * i + 6, 16 * i + 7), [[1, 1]], s + s // 2)
         iota(V("CT", 16 * i + 7, 16 * i + 9), [[-2 * s, 2]], s)
-    iota(V("DT"), [[0, 8], [272, 2], [16, 16]], 16)
+    iota(V("DT"), [[272, 2], [0, 8], [16, 16]], 16)
     act(V("IDN"), V("ID"), F.Copy, scale=-1.0)
     act(V("NUT"), V("BLK"), F.Copy, scale=-1.0)
     sel(V("NUT"), V("NUT"), [[-1, 128]], O.is_gt, 0, 1)
-    iota(V("DT", 15, 256, 32), [[0, 8]], 272)
+    iota(V("DT", 15, 112, 16), [[0, 7]], 0)
     sel(V("NUT"), V("NUT"), [[-1, 128]], O.not_equal, 0, 1, 128.0)
-    iota(V("DT", 31, 256, 32), [[0, 8]], 0)
-    for out, a, x in (("IDP", "ID", 16777216.0), ("IDM", "ID", -16777216.0), ("ID2K", "ID", 4096.0), ("IDF", "ID", 16.0), ("ID16", "ID", 16.0),
-                      ("NBH", "BLK", -32768.0), ("NBF", "BLK", -16384.0), ("NBD", "BLK", -2048.0), ("BLKH", "BLK", 0.5),
-                      ("S1H", "S1", 0.5)):
+    iota(V("DT", 127, 256, 16), [[0, 9]], 272)
+    for out, a, x in (("IDP", "ID", 4194304.0), ("ID2K", "ID", 4096.0), ("IDF", "ID", 16.0), ("ID16", "ID", 16.0),
+                      ("NBH", "BLK", -32768.0), ("NBF", "BLK", -16384.0), ("NBG", "BLK", -16384.0), ("NBD", "BLK", -2048.0), ("BLKH", "BLK", 0.5)):
         act(V(out), V(a), F.Copy, scale=x)
-    iota(V("K"), [[16, 8], [0, 2], [1, 16]], 0)
-    iota(V("K1"), [[16, 8], [0, 2], [1, 16]], 129)
-    iota(V("CO"), [[0, 8], [-4352, 2]], 0)
-    iota(V("EBW"), [[0, 1088]], 0)
+    iota(V("K"), [[0, 2], [1, 128]], 0)
+    iota(V("K1"), [[0, 2], [1, 128]], 129)
+    iota(V("CO4"), [[-4352, 2], [0, 32]], 0)
+    iota(V("M4"), [[0, 32], [1, 4]], 0)
+    iota(V("S4"), [[0, 144]], 0)
+    iota(V("EBW"), [[0, 288]], 0)
     iota(V("CL"), [[16, 32]], 0)
     for k in range(4):
         iota(V("RW", 16 * k, 16 * k + 16), [[1, 16]], (1, 0, -1, 8)[k])
@@ -429,12 +508,15 @@ def rank_program(g, core, T, topo):
     ts(V("M2"), V("ONE", 0, 64), L(18), O.mult)
     red(WL, V("RX", 64, 80), O.add)
     ts(L(15), L(10), -1600.0 / 4096, O.mult, L(14), O.add)
-    ts(L(17), L(10), -16384.0 * 3840, O.mult, L(16), O.add)
-    fill(V("ZH"), 0.0)
-    fill(T0, 2.0 * STEPS[0] - 0.5 - OFFS)
+    ts(L(17), L(10), 16384.0 * 256, O.mult, L(16), O.add)
+    fill(V("ZH", 0, 16), 0.0)
+    for c in range(2):
+        fill(T0[c], 2.0 * STEPS[0] - 0.5 + off[c])
     ts(V("WM"), V("S1"), WL, O.mult)
     cp(V("LI", 4, 5), WL)
-    act(V("CA"), V("ONE", 0, 4), F.Identity, scale=L(17))
+    act(V("CA", 0, 3), V("ONE", 0, 3), F.Identity, scale=L(17))
+    act(V("CA", 3, 4), L(10), F.Copy, scale=16384.0 * 4096)
+    ts(V("CM"), V("ONE", 0, 16), L(10), O.mult, 1023.0, O.mult)
     act(V("SD"), V("S1"), F.Identity, scale=lane)
     act(V("KD"), V("KD"), F.Identity, bias=L(19))
     iota(V("KD", 15, 256, 16), [[0, 16]], 200)
@@ -442,8 +524,8 @@ def rank_program(g, core, T, topo):
     def C(k, n=1):
         return V("SV", k, k + n)
 
-    U, U0, U2, LO1, LIM, LMN, THR, MN = [C(k) for k in range(8)]
-    CE8 = C(26)
+    U, U0, U2, LO1, LMW, LMN, THR, MN = [C(k) for k in range(8)]
+    CE8, LIM = C(26), (C(30), C(31))
     fill(V("CU"), -128.0)
     fill(V("TB"), 0.0)
     fill(U, 1023.0)
@@ -455,15 +537,33 @@ def rank_program(g, core, T, topo):
         ts(V("LI", 5, 6), V("LI", 4, 5), 3, O.bitwise_and)
         ts(V("F8", P=8), V("F8I", P=8), -1023.0, O.add)
         ts(L(6), V("LI", 5, 6), -1.0, O.mult, 1026.0, O.add)
-        mm(V("P2", 0, 32), [(V("B8", 15 - i, 143 - i, P=8), V("F8", i, 512, 16, P=8)) for i in range(16)])
+        mm(V("P7", 0, 32), [(V("B8", 15 - i, 143 - i, P=8), V("F8", i, 512, 16, P=8)) for i in range(16)])
         ts(V("XB"), V("S1"), L(6), O.mult, 1.0 / 4096, O.mult)
         ts(V("CLF"), V("CLF"), L(7), O.add)
         ts(V("XBN"), V("S1"), L(6), O.mult, -1.0 / 4096, O.mult)
-        act(V("AC", 0, 32), V("P2", 0, 32), F.Copy)
-        ts(L(21), lane, 0.5, O.mult, 56.5, O.add)
+        act(V("AC", 0, 32), V("P7", 0, 32), F.Copy)
 
     def consts2():
         act(V("NUTH"), V("NUT"), F.Copy, scale=0.5)
+        ts(V("LI", 2, 3), V("LI", 1, 2), 2, O.arith_shift_right)
+        cp(L(21), V("LI", 2, 3))
+        act(V("S4", 3, 131, 4), V("BLK", 0, 128, 4), F.Copy)
+        act(V("S4H"), V("S4"), F.Copy, scale=0.5)
+        act(V("SD4"), V("S4"), F.Identity, scale=lane)
+        ts(V("NEG4"), V("M4"), L(21), O.not_equal, -16384.0, O.mult)
+        ts(V("M4N"), V("M4", 0, 64), 0.0, O.is_equal, -32768.0, O.mult)
+        ts(V("M4"), V("M4"), 0.0, O.is_gt)
+        act(V("WMN"), V("WM"), F.Copy, scale=-1.0)
+        ts(L(31), L(10), 4096.0 * 192, O.mult)
+        ts(L(31), L(11), -2048.0, O.mult, L(31), O.add)
+        act(V("MC"), V("BLK"), F.Identity, scale=L(31))
+        fill(V("YM", 256, 272), 0.0)
+        fill(V("YM", 528, 544), 0.0)
+        for h in range(3):
+            fill(V("AM", h, 128, 4), 0.0)
+        for k in range(2):
+            ts(V("CLM", k, k + 1), lane, 16.0, O.mult, 256.0 * k + 12.0, O.add)
+        tt(V("CO4"), V("CO4"), V("NEG4", 0, 64), O.add)
         fill(V("CH", 4096, 4112), 0.0)
         for c in range(4):
             fill(V("W", c * 272 + 256, c * 272 + 272), 0.0)
@@ -514,10 +614,13 @@ def rank_program(g, core, T, topo):
         return V("TB", r % 2 * 32 + k, r % 2 * 32 + k + n)
 
     def derived(r):
-        act(CE8, Q(r, 14), F.Identity, bias=2047.75)
+        act(CE8, Q(r, 14), F.Identity, bias=-0.25 - SHIFT)
+        act(V("TJ", 0, 224), V("CJ"), F.Identity, bias=CE8)
         act(LMN, Q(r, 0), F.Identity, bias=-1023.0)
+        act(LMW, Q(r, 0), F.Identity, bias=-2048.0)
         act(THR, Q(r, 3), F.Identity, bias=-1023.0)
-        act(LIM, Q(r, 0), F.Identity, bias=1022.5 - OFFS, scale=-1.0)
+        for c in range(2):
+            act(LIM[c], Q(r, 0), F.Identity, bias=1022.5 + off[c], scale=-1.0)
         ts(V("CZ"), V("M2"), LMN, O.mult, L(15), O.add)
 
     def pre(r):
@@ -531,7 +634,6 @@ def rank_program(g, core, T, topo):
     def level(r):
         B, m = Q(r, 4), MN
         gone, over, last, rt, back, w = [C(k) for k in range(8, 14)]
-        up, down, same = C(25), C(28), C(29)
         red(B, V("MB", r * 16, r * 16 + 16, 2), O.min)
         red(m, V("MB", r * 16 + 1, r * 16 + 16, 2), O.min)
         ts(over, B, LO1, O.max, U0, O.is_ge)
@@ -540,16 +642,7 @@ def rank_program(g, core, T, topo):
         tt(Q(r, 16), B, LO1, O.max)
         ts(rt, gone, m, O.max, U2, O.is_ge)
         ts(back, over, last, O.max, DB_, O.mult)
-        if r < NR - 1:
-            ts(up, gone, m, O.max, U2, O.is_lt)
-            tt(down, over, last, O.max)
-            ts(same, over, last, O.max, 0.5, O.is_lt)
         ts(w, back, DA_, O.add, rt, O.mult)
-        if r < NR - 1:
-            act(V("WMU"), V("WM"), F.Identity, scale=up)
-            act(V("CU", 0, 32), V("CU", 32, 64), F.Identity, scale=up)
-            ts(V("OLD", 0, 32), V("AM", r * 32, r * 32 + 32), rt, O.mult, same, O.mult)
-            ts(V("OLD", 32, 64), V("OM"), rt, O.mult, down, O.mult)
         ts(V("OFQ", 0, 1), w, L0, O.add)
         ts(C(14), last, -5000.0, O.mult, m, O.add)
         cp(Q(r + 1, 0, 16), IND(Q(r, 0, 24), V("OFQ", 0, 1)))
@@ -557,66 +650,88 @@ def rank_program(g, core, T, topo):
 
     def parents(r):
         if r:
-            ts(V("OFF"), V("CLF"), Q(r, 7), O.add, 1.0 / 16, O.mult)
+            ts(V("OFM"), V("CLM"), Q(r, 7), O.add, 0.25, O.mult)
             ts(V("OFA"), V("CL"), Q(r, 7), O.add)
+            ts(V("OFF"), V("CLF"), Q(r, 7), O.add, 1.0 / 16, O.mult)
         derived(r)
 
-    def former(r):
-        ts(C(24), Q(r, 10), float(r * SL), O.min)
-        ts(V("OFM"), V("CLF", 0, 2), C(24), O.add, 1.0 / 16, O.mult)
-        act(V("OM"), IND(V("AM", 0, r * 32 + 32), V("OFM")), F.Copy)
+    def marks():
+        parts = [(V("P1", k * 64, k * 64 + 64), l, x) for k in range(4) for l, x in wraps("WM", "CH", k * 1024, 1024)]
+        parts += [(V("P1", TW * 64, TW * 64 + 64), l, x) for l, x in wraps("WMN", "D", TW * 1024, 1024)]
+        mm(V("P1", 0, 256), [(V("MC"), V("ONE"))], True, False)
+        for k in range(0, len(parts), 4):
+            mms(parts[k:k + 4], False, k + 4 == len(parts))
+        act(V("MQ"), V("P1", 0, 256), F.Copy)
+        tt(V("YM", 0, 256), V("P1", 0, 256), V("MQ"), O.subtract)
+        act(V("YM", 272, 528), V("YM", 0, 256), F.Copy)
 
     def children(r):
-        apart = {1: "P0", 3: "P1", 5: "P7"}
+        apart = dict(zip(APART, ("P0", "P1", "P7")))
         par = V("S" if r else "A", 0, 512)
-        mz = V("AM", r * 32, r * 32 + 32)
+        mz = V("MR", 32, 64) if r else V("AM", 3, 128, 4)
 
         def J(name, j0, j1=None, w=32):
             return V(name, j0 * w, (j0 + 1 if j1 is None else j1) * w)
 
         def numbers():
-            out = V("P4", 0, 32)
-            mm(out, [(V("BLK"), V("CU", 0, 32))] + [(V("ID"), V("OLD", x, x + 32)) for x in (0, 32) if r], True, False)
-            mm(out, wraps("WMU" if r else "WM", "A", r * SL, 512), False, True)
             if r:
-                lay = V("A", 0, (r + 1) * SL)
-                cp(V("S", 0, 256), IND(lay, V("OFA", 0, 16)))
-                act(V("S", 256, 512), IND(lay, V("OFA", 16, 32)), F.Copy)
+                cp(mz, IND(V("AM", 0, (r + 1) * 128), V("OFM")))
+            else:
+                out = V("P4", 0, 32)
+                mm(out, [(V("BLK"), V("CU"))] + wraps("WM", "A", 0, 512))
+                ts(V("MR", 0, 32), out, MAGIC * 4096, O.add, MAGIC * 4096, O.subtract)
+                tt(mz, out, V("MR", 0, 32), O.subtract)
+
+        def squares(k):
+            for j in (2 * k, 2 * k + 1):
+                act(V(("P2", "P3", "P5", "P6")[k], j % 2 * 32, j % 2 * 32 + 32), mz, F.Square, bias=512.0 + 2 * KA[min(j, 6)], scale=0.25)
+            if k == 3:
+                act(J("TJ", 7), mz, F.Identity, bias=V("TJ", 192, 193), scale=float(KA[7] - KA[6]))
+
+        def fetch(h):
+            lay = V("A", 0, (r + 1) * SL)
+            if r and h < 2:
+                v = IND(lay, V("OFA", h * 16, h * 16 + 16))
+                if FETCH[h] == "V":
+                    cp(V("S", h * 256, h * 256 + 256), v)
+                else:
+                    act(V("S", h * 256, h * 256 + 256), v, F.Copy)
+            elif h == 2:
                 for j in apart:
                     mm(V(apart[j]), [(V("IDN"), par)], True, False)
-            ts(V("MR"), out, MAGIC * 4096, O.add, MAGIC * 4096, O.subtract)
-            tt(mz, out, V("MR"), O.subtract)
-            act(V("SQ"), mz, F.Square, bias=512.0, scale=0.25)
-            for j in range(3):
-                ts(J("TJ", j), mz, float(KA[j]), O.mult, CE8, O.add)
-            for j in range(3, 8):
-                act(J("TJ", j), mz, F.Identity, bias=CE8, scale=float(KA[j]))
-            for j0, j1 in ((0, 4), (4, 8)):
-                for j in range(j0, j1):
-                    tt(J("VJ", j), J("TJ", j), V("SQ"), O.add)
-                ts(J("VK", j0, j1), J("VJ", j0, j1), 4095, O.bitwise_and)
-                cp(J("OFO", j0, j1), J("VK", j0, j1))
+
+        def whole(k):
+            tt(J("VJ", k, w=64), V(("P2", "P3", "P5", "P6")[k], 0, 64), J("TJ", k, w=64), O.add)
+
+        def mod(k):
+            ts(J("OFO" if DIRECT else "VK", k, w=64), J("VJ", k, w=64), 4095, O.bitwise_and)
+
+        def offsets(k):
+            if not DIRECT:
+                cp(J("OFO", k, w=64), J("VK", k, w=64))
 
         def gather(j):
             tt(J("D", j, w=512), IND(V("OPW"), J("OFO", j)), par, O.subtract)
 
         def other(j):
             act(J("D", j, w=512), IND(V("OPW"), J("OFO", j)), F.Copy)
+
+        def less(j):
             mm(V(apart[j]), [(V("ID"), J("D", j, w=512))], False, True)
 
         def size(j):
             act(J("CH", j, w=512), V(apart[j]) if j in apart else J("D", j, w=512), F.Abs)
 
         def Z(k):
-            return V(ROWS[k // 2], k % 2 * 64, k % 2 * 64 + 64)
+            return V(ZB[k][0], ZB[k][1], ZB[k][1] + 64)
 
         def opens(k):
             mm(Z(k), [(V("ID"), V("FS")), (V("BLK"), V("CZ"))], True, False)
-            if k == 3:
-                mm(Z(k), wraps("XBN", "D", 3072, 1024), False, False)
+            if k == TW:
+                mm(Z(k), wraps("XBN", "D", k * 1024, 1024), False, False)
 
         def sums(k):
-            if k < 3:
+            if k != TW:
                 opens(k)
             mm(Z(k), wraps("XB", "CH", k * 1024, 1024), False, True)
 
@@ -629,202 +744,255 @@ def rank_program(g, core, T, topo):
         def costs2():
             tt(V("FS"), IND(V("AC", 0, r * 32 + 32), V("OFF")), V("FSP"), O.max)
 
-        def keys(h):
-            a, b = h * 128, h * 128 + 128
-            z = {"ap": T[ROWS[h]][:, 0:8, :], "r": [(ROWS[h], 0, 512, 1)], "n": 128, "w": 4}
+        def keys(a, b):
+            z = V(ZB[a // 64][0], ZB[a // 64][1], ZB[a // 64][1] + b - a)
             ts(V("QQ", a, b), z, MAGIC / 1024, O.add, MAGIC / 1024, O.subtract)
-            ts(V("YH", a, b), z, MAGIC, O.add, MAGIC, O.subtract)
+            ts(V("YH", a, b), z, 1025.0, O.add, 2048.0, O.min)
             tt(V("DD", a, b), z, V("QQ", a, b), O.subtract)
-            ts(V("PEN", a, b), V("YH", a, b), 0.0, O.is_lt, 8192.0, O.mult)
-
-        def owners(h):
-            a, b = h * 128, h * 128 + 128
-            for c in range(2):
-                x = 256 + c * 256
-                ts(V("PEN", x + a, x + b), V("DD", a, b), (own[c][0] - 1.5) / 4096, O.not_equal, 8192.0, O.mult)
-
-        def mix(h, p):
-            a, b = h * 128, h * 128 + 128
-            out, base = V("P%d" % p, a, b), [(V("ID"), V("YH", a, b)), (V("ID"), V("PEN", a, b))]
-            mm(out, base, True, p == 4)
-            if p < 2:
-                mm(out, [(V("IDM" if own[p][1] else "IDP"), V("DD", a, b))], False, True)
-            elif p < 4:
-                mm(out, [(V("ID"), V("PEN", p * 256 - 256 + a, p * 256 - 256 + b))], False, True)
-
-        def halves(h, c):
-            cp(V("XH", c * 256 + h * 128, c * 256 + h * 128 + 128), V("P%d" % (2 + c), h * 128, h * 128 + 128))
+            ts(V("PEN", a, b), V("YH", a, b), 1024.5, O.is_lt, 8192.0, O.mult)
+            base = [(V("ID"), V("YH", a, b)), (V("ID"), V("PEN", a, b))]
+            key = V(("P0", "P1", "P2")[PIECES.index((a, b))], a, b)
+            mm(key, base[:1], True, False)
+            mm(key, [(V("IDP"), V("DD", a, b))], False, False)
+            mm(key, base[1:], False, True)
+            if XKE[PIECES.index((a, b))] == "V":
+                ts(V("XK", a, b), key, -KEY, O.add)
+            else:
+                act(V("XK", a, b), key, F.Identity, bias=-KEY)
+            mm(V("P4", a, b), base)
 
         numbers()
         if not r:
             consts1()
             ts(V("OFF"), V("CLF"), 1.0 / 16, O.mult)
-            for j in apart:
-                mm(V(apart[j]), [(V("IDN"), par)], True, False)
-        other(1)
-        gather(0)
-        other(3)
-        gather(2)
-        costs()
-        gather(6)
-        costs2()
-        gather(7)
-        twice(6)
-        twice(7)
-        gather(4)
-        size(0)
-        size(1)
-        sums(0)
-        other(5)
-        opens(3)
-        size(2)
-        size(3)
-        sums(1)
-        sums(3)
-        size(5)
-        size(4)
-        for c in range(2):
-            cand(c, 0)
-        keys(0)
-        owners(0)
-        sums(2)
-        for p in (2, 3, 4, 0, 1):
-            mix(0, p)
-        keys(1)
-        halves(0, 0)
-        owners(1)
-        halves(0, 1)
-        for p in (4, 2, 0, 3, 1):
-            mix(1, p)
-        red(C(16), V("P4", 0, 256), O.min)
-        signs(0, 0)
-        signs(1, 0)
-        halves(1, 0)
-        ts(V("MD"), V("LM"), C(16), O.mult, 2047.0, O.min)
-        below(0, 0)
-        halves(1, 1)
-        mm(V("P3", 256, 272), [(V("BLK"), V("MD"))])
+        do = {"q": squares, "a": fetch, "x": less, "w": whole, "m": mod, "f": offsets, "o": other, "g": gather, "t": twice, "z": size, "s": sums, "p": opens,
+              "c": lambda k: (costs, costs2)[k](), "k": lambda k: keys(*PIECES[k]), "d": lambda c: cand(c, 0), "e": early}
+        strict.update({e: [] for e in STRICT})
+        for x in FLOW.split():
+            if x == "|":
+                strict.clear()
+            else:
+                do[x[0]](int(x[1]))
+        strict.clear()
 
     def TH(c, i):
-        return T0 if i == 0 else V("TT", c * 16 + i % 2 * 8 + 5, c * 16 + i % 2 * 8 + 6)
+        return T0[c] if i == 0 else V("TT", c * 16 + i % 2 * 8 + 5, c * 16 + i % 2 * 8 + 6)
 
     def cand(c, i):
         x = c * 32 + i % 2 * 16
-        if 0 < i < 4 and c:
+        if i == 4:
+            ts(V("CAND", x, x + 9), V("CT", 16 * i, 16 * i + 9), TH(c, i), O.add, LIM[c], O.min)
+            if own[c][0]:
+                act(V("CAND", 64, 71), V("CAND", x, x + 7), F.Identity, bias=rel(c, 0))
+        elif i and CANDS[c] == "S":
             act(V("CAND", x, x + 9), V("CT", 16 * i, 16 * i + 9), F.Identity, bias=TH(c, i))
-        elif i < 4:
-            ts(V("CAND", x, x + 9), V("CT", 16 * i, 16 * i + 9), TH(c, i), O.add)
         else:
-            ts(V("CAND", x, x + 9), V("CT", 16 * i, 16 * i + 9), TH(c, i), O.add, LIM, O.min)
+            ts(V("CAND", x, x + 9), V("CT", 16 * i, 16 * i + 9), TH(c, i), O.add)
 
-    def signs(c, i):
+    def rel(c, o):
+        return 1024.0 * (own[c][o] - own[c][1])
+
+    def lowers(c, a, b, at):
+        act(V("SG", c * 256 + a, c * 256 + b), V("XK", a, b), F.Sign, bias=0.5 - off[c], acc=V("CN", at + c * 4 + 3, at + c * 4 + 4))
+        if own[c][0]:
+            ts(V("DBN", a, b), V("XK", a, b), off[c] - 0.5 + rel(c, 0), O.is_lt, -2.0, O.mult)
+
+    def early(c):
+        lowers(c, 0, EARLY, 16)
+        signs(c, 0, 0, EARLY, 16)
+        below(c, 0, 0, EARLY)
+
+    def bases(c):
+        lowers(c, EARLY, 256, 0)
+        act(V("BASE", c * 4, c * 4 + 3), V("ONE", 0, 3), F.Identity, scale=V("CN", c * 4 + 3, c * 4 + 4), bias=V("CN", c * 4 + 19, c * 4 + 20))
+        if own[c][0]:
+            scan(V("RSB"), V("DBN", 0, 128), V("DBN", 128, 256), 0.0, O.add, O.add)
+            act(V("BASE", 8, 11), V("ZH", 0, 3), F.Identity, bias=V("RSB", 127, 128))
+
+    def signs(c, i, a, b, at):
         x = c * 32 + i % 2 * 16
-        for k, bias in ((1, TH(c, i)), (0, V("CAND", x + 7, x + 8)), (2, V("CAND", x + 8, x + 9))):
+        for k, bias in ((1, TH(c, i)), (0, V("CAND", x + 7, x + 8)), (2, V("CAND", x + 8, x + 9)))[:SHARE[c][i]]:
             y = c * 768 + k * 256
-            act(V("DA", y, y + 256), V("P%d" % c, 0, 256), F.Sign, bias=bias, scale=-1.0, acc=V("CN", c * 4 + k, c * 4 + k + 1))
+            act(V("DA", y + a, y + b), V("XK", a, b), F.Sign, bias=bias, scale=-1.0, acc=V("CN", at + c * 4 + k, at + c * 4 + k + 1))
 
-    def below(c, i):
-        for k in range(3):
-            y = c * 768 + k * 256
-            ts(V("DV", y, y + 256), V("XH", c * 256, c * 256 + 256), TH(c, i), O.subtract, OFFS + (1 - k) * STEPS[i], O.is_lt)
+    def units(c, i):
+        return [(0, 0), (0, 1), (0, 2), (1, 2)][:6 - SHARE[c][i]]
 
-    def tally(c, ks):
-        for k in ks:
-            y = c * 768 + k * 256
-            scan(V("RS", y, y + 256), V("DV", y, y + 256), V("ZH"), INI, O.add, O.add)
+    def below(c, i, a, b):
+        for n, (o, k) in enumerate(units(c, i)):
+            y = c * 1024 + n * 256
+            ts(V("DV", y + a, y + b), V("XK", a, b), TH(c, i), O.subtract, rel(c, o) + (1 - k) * STEPS[i], O.is_lt)
 
-    def totals(c):
-        p = "P%d" % (5 + c)
-        mm(V(p, 1, 6, 2), [(V("BLK"), V("CA", 0, 3)), (V("NBF"), V("CN", c * 4, c * 4 + 3))])
-        mm(V(p, 0, 6, 2), [(V("NBH"), V("RS", c * 768 + 255, c * 768 + 768, 256))])
+    def tally(c, i, ns):
+        for n in ns:
+            if n < len(units(c, i)):
+                y, x = c * 1024 + n * 256, c * 512 + n * 128
+                scan(V("RS", x, x + 128), V("DV", y, y + 128), V("DV", y + 128, y + 256), INI, O.add, O.add)
+
+    def opening(c, i):
+        p, n = "P%d" % (5 + c), SHARE[c][i]
+        mm(V(p, 1, 2 * n, 2), [(V("BLK"), V("CA", 0, n))] + [(V("NBF"), V("CN", 16 + c * 4, 16 + c * 4 + n))] * (i == 0), True, False)
+        mm(V(p, 1, 2 * n, 2), [(V("NBG"), V("BASE", c * 4, c * 4 + n))], False, False)
+        if n < 3:
+            mm(V(p, 5, 6, 2), [(V("BLK"), V("CA", 3, 4)), (V("NBG"), V("BASE", c * 4, c * 4 + 1))], False, False)
+        if own[c][0] and i:
+            mm(V(p, 0, 6, 2), [(V("NBG"), V("BASE", 8, 11))], False, False)
+
+    def totals(c, i):
+        p, n, x = "P%d" % (5 + c), SHARE[c][i], c * 512 + 127
+        mine = (V(p, 1, 2 * n, 2), [(V("NBF"), V("CN", c * 4, c * 4 + n))])
+        if n < 3:
+            mm(*mine, False, False)
+        mms([(V(p, 0, 6, 2), V("NBH"), V("RS", x, x + 257, 128))]
+            + [(V(p, k, k + 1, 2), V("NBG"), V("RSB", 127, 128)) for k in (0, 2, 4) if own[c][0] and not i], False, False)
+        if n < 3:
+            mm(V(p, 5, 6, 2), [(V("NBH"), V("RS", x + 384, x + 385))], False, True)
+        else:
+            mm(*mine, False, True)
 
     def decide(c, i):
         x, y = c * 32 + i % 2 * 16, c * 16 + (i + 1) % 2 * 8
+        if i == 4 and own[c][0]:
+            scan(V("TT", 32, 38), V("P%d" % (5 + c), 0, 6), V("CAND", 64, 70), V("CAND", 70, 71), O.min, O.max)
         scan(V("TT", y, y + 6), V("P%d" % (5 + c), 0, 6), V("CAND", x, x + 6), V("CAND", x + 6, x + 7), O.min, O.max)
 
-    def search():
-        tally(0, (0, 1, 2))
-        totals(0)
-        below(1, 0)
-        tally(1, (0,))
-        for n in range(9):
-            c, i = n % 2, n // 2
+    def step(c, i):
+        def count():
+            if i:
+                cand(c, i)
+            else:
+                bases(c)
+            signs(c, i, 0 if i else EARLY, 256, 0)
+            opening(c, i)
+            below(c, i, 0 if i else EARLY, 256)
+            tally(c, i, (0,))
+
+        def total():
+            tally(c, i, (1, 2, 3))
+            totals(c, i)
+
+        def choose():
             decide(c, i)
-            tally(1 - c, (1, 2))
-            totals(1 - c)
-            if n == 1:
-                red(C(27), V("P3", 256, 272), O.min)
-                for k in range(2):
-                    mm(V("P%d" % (2 + k), 0, 256), [(V("ID2K"), V("KD"))], True, False)
-            if i < 4:
-                cand(c, i + 1)
-                signs(c, i + 1)
-                below(c, i + 1)
-                tally(c, (0,))
+            if not i:
+                mm(both(c, 0, 128), [(V("ID2K"), V("KD"))], True, False)
+                places0(c)
+        return [count, total, choose]
+
+    def least(r):
+        for o in range(2):
+            act(V("YW", o * 272, o * 272 + 256), V("P4", 0, 256), F.Identity, bias=LMW)
+        scan(V("QQ", 0, 128), V("YW", 0, 128), V("YW", 128, 256), 5000.0, O.min, O.min)
+        ts(V("MD"), V("LM"), V("QQ", 127, 128), O.mult, 2047.0, O.min)
+        mm(V("P4", 256, 272), [(V("BLK"), V("CM")), (V("BLK"), V("MD"))])
+        red(V("MB", r * 16 + home * 4 + 1, r * 16 + home * 4 + 2), V("P4", 256, 272), O.min)
+
+    def lists(r, c):
+        def mark_list(c):
+            if r == NR - 1:
+                return
+            x, p, at = c * 256, "P%d" % (2 + c), where(r, "SNM", "AM", 32)
+            mm(V(p, 0, 64), [(V("ID"), V("NEG4", 0, 64))], True, False)
+            tt(V("CGM", x, x + 256), IND(V("YM"), V("OFW", c * 16, c * 16 + 16)), V("OH", x, x + 256), O.mult)
+            mm(V(p, 0, 64), fours("S4", "CGM", x, 256), False, True)
+            for o, n in ((0, 32), (1, 32)) if c else ((0, 64),):
+                buf, y = at(own[c][o])
+                scan(V(buf, y, y + n), V("M4N", 0, n), V(p, o * 32, o * 32 + n), 0.0, O.add, O.max)
+            send(r, "m", at, [o for o in own[c] if o != me])
+        return [lambda f=f: [x(c) for x in f] for f in ((kept, places1, ranks), (first, ends, first_list, places), (second,),
+                                                        (second_list, columns), (third,), (mark_list, third_list))]
 
     def kept(c):
         x = c * 512
-        ts(V("KP", x, x + 256), V("XH", c * 256, c * 256 + 256), TH(c, 5), O.subtract, OFFS, O.is_lt)
-        act(V("KP", x + 256, x + 512), V("P%d" % c, 0, 256), F.Sign, bias=TH(c, 5), scale=-1.0)
+        if own[c][0]:
+            ts(V("KP", x, x + 256), V("XK"), V("TT", 37, 38), O.is_lt, 2.0, O.mult)
+        else:
+            ts(V("KP", x, x + 256), V("XK"), TH(c, 5), O.subtract, rel(c, 0), O.is_lt)
+        act(V("KP", x + 256, x + 512), V("XK"), F.Sign, bias=TH(c, 5), scale=-1.0)
+
+    def lower(c, o):
+        return V("SG", c * 256, c * 256 + 256) if o else V("DBN") if own[c][0] else V("KP", c * 512, c * 512 + 256)
+
+    def both(c, a, b):
+        p = "P%d" % (2 + c)
+        return {"ap": T[p][:, :, a:b], "r": [(p, 0, 512, 1)], "n": 2 * (b - a), "w": 4}
 
     def ranks(c):
         x = c * 512
         for o in range(2):
             y = x + o * 256
-            scan(V("R", y, y + 256), V("KP", y, y + 256), V("ONE") if o else V("KP", y, y + 256), 0.0, O.add, O.add)
-        mms([(V("P%d" % (2 + c), k * 32, k * 32 + 32), V("NBD"), V("R", x + 15, x + 512, 16)) for k in range(8)], False, True)
+            scan(V("R", y, y + 256), V("KP", y, y + 256), lower(c, o), 0.0, O.add, O.add)
+        mms([(both(c, k * 16, k * 16 + 16), V("NBD"), V("R", x + 15, x + 512, 16)) for k in range(8)], False, True)
 
     def ends(c):
-        x = c * 512
-        mm(V("P%d" % (5 + c), 0, 32), wraps("S1H", "R", x, 512))
+        x, p = c * 512, "P%d" % (5 + c)
+        mm(V(p, 0, 128), [(V("ID"), V("NEG4"))], True, False)
+        mm(V(p, 0, 128), fours("S4H", "R", x, 512), False, True)
         for o in range(2):
-            y = c * 544 + o * 272
-            act(V("EBW", y, y + 256, 16), V("P%d" % (5 + c), o * 16, o * 16 + 16), F.Copy)
+            y = c * 144 + o * 68
+            pick(V("EBW", y, y + 64), V(p, o * 64, o * 64 + 64))
 
-    def places(c):
-        p = "P7"
+    def PL(c, o):
+        return V(("P7", "P0")[c], o * 256, o * 256 + 256)
+
+    def places0(c):
+        os_ = [o for o in (1, 0) if o or own[c][0]]
+        for o in os_:
+            mm(PL(c, o), [(V("NUTH"), lower(c, o))], o == 1, False)
+
+    def places1(c):
         for o in range(2):
             y = c * 512 + o * 256
-            mm(V(p, o * 256, o * 256 + 256), [(V("BLKH"), V("R", y, y + 256)), (V("NUTH" if o else "NUT"), V("KP", y, y + 256))])
+            mm(PL(c, o), [(V("NUTH" if o or own[c][0] else "NUT"), V("KP", y, y + 256))], False, False)
+
+    def places(c):
+        for o in range(2):
+            y = c * 512 + o * 256
+            mm(PL(c, o), [(V("BLKH"), V("R", y, y + 256))], False, o == 1)
         for o in range(2):
             y = c * 544 + o * 272
-            act(V("W", y, y + 256), V(p, o * 256, o * 256 + 256), F.Identity, bias=L(21) if o else 0.0)
+            act(V("W", y, y + 256), PL(c, o), F.Copy)
 
     def first(c):
-        scan(V("V1", c * 256, c * 256 + 256), V("P%d" % (2 + c), 0, 256), V("DT"), 0.0, O.max, O.min)
+        for o in range(2):
+            x = c * 256 + o * 128
+            scan(V("V1", x, x + 128), V("P%d" % (2 + c), o * 256, o * 256 + 128), V("DT", o * 128, o * 128 + 128), 272.0 * o, O.max, O.min)
 
     def first_list(c):
         v1 = V("V1", c * 256 + 14, c * 256 + 256, 16)
-        cp(V("OFB", c * 16, c * 16 + 16), v1)
-        mm(V("P%d" % (2 + c), 0, 16), [(V("ID"), v1)], True, False)
+        p = "P%d" % (2 + c)
+        ts(V("OFB", c * 16, c * 16 + 16), v1, 0.25, O.mult, 3.0, O.add)
+        mms([(V(p, 0, 64), V("ID"), V("NEG4", 0, 64))] + [(V(p, h, 64, 4), V("ID"), v1) for h in range(4)], True, False)
 
     def second(c):
         x = c * 256
-        tt(V("IB", x, x + 256), IND(V("EBW", c * 544, c * 544 + 544), V("OFB", c * 16, c * 16 + 16)), V("K"), O.is_le)
-        mm(V("P%d" % (2 + c), 0, 16), wraps("S1", "IB", x, 256), False, True)
+        tt(V("IB", x, x + 256), IND(V("EBW", c * 144, c * 144 + 144), V("OFB", c * 16, c * 16 + 16)), V("K"), O.is_le)
+        mm(V("P%d" % (2 + c), 0, 64), fours("S4", "IB", x, 256), False, True)
 
     def second_list(c):
-        cp(V("OFW", c * 16, c * 16 + 16), V("P%d" % (2 + c), 0, 16))
+        pick(V("CB", c * 64, c * 64 + 64), V("P%d" % (2 + c), 0, 64))
+        cp(V("OFW", c * 16, c * 16 + 16), V("CB", c * 64 + 3, c * 64 + 64, 4))
 
     def columns(c):
-        cp(V("CB", c * 16, c * 16 + 16), V("P%d" % (2 + c), 0, 16))
-        mm(V("P%d" % c, 0, 16), [(V("ID"), V("CO")), (V("ID16"), V("CB", c * 16, c * 16 + 16))], True, False)
+        mm(V("P%d" % (5 + c), 0, 64), [(V("ID"), V("CO4")), (V("ID16"), V("CB", c * 64, c * 64 + 64))], True, False)
 
     def third(c):
         x = c * 256
         tt(V("OH", x, x + 256), IND(V("W", c * 544, c * 544 + 544), V("OFW", c * 16, c * 16 + 16)), V("K1"), O.is_equal)
-        mm(V("P%d" % c, 0, 16), wraps("SD", "OH", x, 256), False, True)
+        mm(V("P%d" % (5 + c), 0, 64), fours("SD4", "OH", x, 256), False, True)
 
     def where(r, buf, stays, w):
-        return lambda o: (stays, (slot(r) * 4 + home) * w) if o == me else (buf, (r * 4 + o) * w)
+        return lambda o: (stays, (slot(r) * 4 + home) * w) if o == me else (buf, (r * 4 + (own[0] + own[1]).index(o)) * w)
 
     def third_list(c):
-        for o in (1, 0):
-            cp(V("OFN", c * 16 + o * 8, c * 16 + o * 8 + 8), V("P%d" % c, o, 16, 2))
+        pick(V("MS", c * 64, c * 64 + 64), V("P%d" % (5 + c), 0, 64))
+        cp(V("OFN", c * 16, c * 16 + 16), V("MS", c * 64 + 3, c * 64 + 64, 4))
 
     def states(r, c):
         at = where(r, "SND", "A", 128)
-        for o in (1, 0):
+        if PAIR and not c:
+            buf, x = at(own[c][0])
+            act(V(buf, x, x + 256), IND(V("CH"), V("OFN", 0, 16)), F.Copy)
+        for o in sorted(range(2), key=lambda o: (own[c][o] == me, -o)) * (c or not PAIR):
             buf, x = at(own[c][o])
             v = IND(V("CH"), V("OFN", c * 16 + o * 8, c * 16 + o * 8 + 8))
             if o or c:
@@ -841,9 +1009,9 @@ def rank_program(g, core, T, topo):
         at = where(r, "SNC", "AC", 8)
         mm(V("P4", cs[0] * 16, cs[-1] * 16 + 16), wraps("S1", "CG", cs[0] * 256, len(cs) * 256))
         for c in cs:
-            for o in range(2):
+            for o, n in ((0, 8), (1, 8)) if c else ((0, 16),):
                 buf, y = at(own[c][o])
-                act(V(buf, y, y + 8), V("P4", c * 16 + o, c * 16 + 16, 2), F.Copy)
+                act(V(buf, y, y + n), V("P4", c * 16 + o * 8, c * 16 + o * 8 + n), F.Copy)
 
     def E(k, n=1):
         return V("EV", k, k + n)
@@ -901,69 +1069,50 @@ def rank_program(g, core, T, topo):
         parents(r)
         children(r)
         mb = r * 16 + home * 4
-        search()
+        if not r:
+            consts2()
 
         def bound(c):
-            ts(V("MB", mb + 2 * c, mb + 2 * c + 1), TH(c, 5), Q(r, 0), O.add, OFFS + 0.5, O.add)
+            ts(V("MB", mb + 2 * c, mb + 2 * c + 1), TH(c, 5), Q(r, 0), O.add, 0.5 - off[c], O.add)
 
         def sizes(j):
             act(V("CH", j * 512, j * 512 + 512), V("D", j * 512, j * 512 + 512), F.Abs)
 
-        if not r:
-            consts2()
-        kept(0)
-        bound(0)
-        ts(V("MB", mb + 1, mb + 2), C(27), Q(r, 0), O.add)
-        ranks(0)
-        decide(1, 4)
-        kept(1)
-        ends(0)
-        bound(1)
-        send(r, "b", lambda o: ("MB", mb), far)
-        send(r, "b", lambda o: ("MB", mb), [o for o in others if o not in far])
-        arrive(r, "b")
-        first(0)
-        places(0)
-        ranks(1)
-        first_list(0)
-        second(0)
-        ends(1)
-        first(1)
-        first_list(1)
-        second_list(0)
-        columns(0)
-        third(0)
-        second(1)
-        places(1)
-        for j in (6, 7):
-            sizes(j)
+        def bounds():
+            for c in range(2):
+                bound(c)
+            send(r, "b", lambda o: ("MB", mb), far)
+            send(r, "b", lambda o: ("MB", mb), [o for o in others if o not in far])
+            arrive(r, "b")
+
+        work = [[f for i in range(5) for f in step(c, i)] + lists(r, c) for c in range(2)]
+        work[1].insert(15, bounds)
+        work[1].insert(9, lambda: least(r))
         if r < NR - 1:
-            third_list(0)
-            states(r, 0)
-        second_list(1)
-        columns(1)
-        third(1)
-        for o in range(2):
-            act(V("YW", o * 272, o * 272 + 256), V("P4", 0, 256), F.Identity, bias=LMN)
+            work[0].insert(18, marks)
+        work[0].append(lambda: [sizes(j) for j in (2 * TW, 2 * TW + 1)])
+        if r < NR - 1:
+            work[0].append(lambda: states(r, 0))
+        for c in TURNS + "01" * 24:
+            if work[int(c)]:
+                work[int(c)].pop(0)()
         if not r:
             consts3()
         pre(r)
         if r < NR - 1:
-            third_list(1)
             states(r, 1)
             prices(0)
             prices(1)
             price_lists(r, (0, 1))
             send(r, "c", where(r, "SNC", "AC", 8), far)
             send(r, "c", where(r, "SNC", "AC", 8), [o for o in others if o not in far])
-            former(r)
+            arrive(r, "m")
         else:
             for c in range(2):
                 prices(c)
                 price_lists(r, (c,))
                 send(r, "c", where(r, "SNC", "AC", 8), [o for o in own[c] if o != me])
             for c in range(2):
-                third_list(c)
                 states(r, c)
             older()
         arrive(r, "a")

@@ -9,8 +9,9 @@ KA = [17, 101, 263, 389, 547, 701, 859, 1021]
 MAGIC = float(3 << 22)
 STEPS = [256, 64, 16, 4, 1]
 SHIFT = 918 * 4096
-KEY = 1537.0
-SHARE = ((3, 3, 3, 3, 3), (3, 3, 3, 3, 3))
+UNDER = -1.0 - 1.0 / 8192
+KEY = 1536.0
+SHARE = ((2, 2, 2, 2, 2), (3, 3, 3, 3, 3))
 CANDS = "VS"
 PIECES = ((0, 128), (128, 192), (192, 256))
 FLOW = ("q1 q0 q2 q3 w1 w0 w2 w3 m1 m0 m2 m3 f1 f0 f2 f3 a0 a1 o3 a2 x3 g0 o5 x5 g1 c0 t0 c1 t1 p0 s0 o7 x7 g2 g4 g6 z3 z5 z7 z2 s1 z4 s2 z6 s3"
@@ -27,7 +28,7 @@ FETCH = "VS"
 ORDER = "bmac"
 SCHED, PATIENCE, MIX = 0, 0.0, 1.0
 TURNS = "001" + "010101" * 5
-CYCLE, WAKE, ISSUE, HOP, PASSES = 0.9, 200.0, 300.0, 2000.0, 3
+CYCLE, WAKE, ISSUE, HOP, PASSES = 0.9, 160.0, 300.0, 2000.0, 3
 QUEUED = 800.0
 TENSOR = 0.5
 
@@ -40,7 +41,7 @@ for _n, _w, _d in (
         ("OFA", 32, _u), ("OFF", 4, _u), ("OFO", 256, _u), ("OFB", 32, _u), ("OFW", 32, _u), ("OFN", 32, _u), ("OFQ", 2, _u),
         ("MR", 64, _f), ("CJ", 224, _f), ("C4", 944, _b), ("BLKH", 128, _b), ("NUTH", 128, _b), ("TJ", 256, _f), ("VJ", 256, _i), ("VK", 256, _i),
         ("YH", 256, _h), ("QQ", 256, _f), ("DD", 256, _b), ("PEN", 256, _b), ("XK", 256, _h), ("YW", 544, _f),
-        ("DV", 2048, _h), ("RS", 1024, _h), ("DA", 1536, _b), ("CN", 32, _f), ("CAND", 80, _f), ("TT", 40, _f),
+        ("DV", 2048, _h), ("RS", 1024, _h), ("DA", 1536, _b), ("CN", 32, _f), ("CAND", 80, _f), ("TT", 48, _h),
         ("SG", 1168, _b), ("MS", 128, _f), ("NBG", 128, _b), ("CM", 16, _h),
         ("KP", 1024, _b), ("R", 1024, _b), ("V1", 768, _b), ("EBW", 288, _b), ("W", 1088, _b), ("IB", 512, _b), ("OH", 1536, _b), ("CG", 1536, _h),
         ("TB", 64, _f), ("AM", NR * 128, _f), ("SNM", NR * 128, _f), ("YM", 544, _f), ("CU", 32, _b), ("OFM", 2, _u), ("WMN", 144, _b), ("CGM", 512, _h), ("XBN", 144, _h), ("SV", 32, _f), ("MD", 16, _h),
@@ -134,7 +135,7 @@ def rank_program(g, core, T, topo):
     hop = ways(core, T, topo)
     far = [T.cores.index(d) for d in hop if hop[d] != d]
     own = sorted([(0, 2), (1, 3)], key=lambda p: -len([o for o in p if o in far]))
-    off = [1024.0 * p[1] - 2048.0 for p in own]
+    off = [1024.0 * p[1] - 2047.0 for p in own]
     home = me
     queue = {"V": g.vector, "S": g.scalar, "T": g.tensor, "G": g, "Y": g.sync}
     count = {"V": 0, "S": 0, "T": 0, "G": 0, "ls": 0}
@@ -446,7 +447,7 @@ def rank_program(g, core, T, topo):
     def L(k):
         return V("LC", k, k + 1)
 
-    lane, L0, DA_, DB_, FB, WL, INI, T0 = L(0), L(1), L(2), L(3), L(4), L(5), L(8), (L(9), L(12))
+    lane, L0, DA_, DB_, FB, WL, T0 = L(0), L(1), L(2), L(3), L(4), L(5), (V("TT", 38, 39), V("TT", 39, 40))
     fill(V("ONE"), 1.0)
     iota(V("LI", 0, 1), [[1, 1]], 0, 1)
     iota(V("LM"), [[1, 16]], 0)
@@ -504,18 +505,17 @@ def rank_program(g, core, T, topo):
     tt(V("RX", 64, 80), V("RW", 64, 80), V("LM"), O.mult)
     ts(L(14), L(11), -1.5 / 4096, O.mult)
     ts(L(16), L(11), 16384.0, O.mult)
-    ts(INI, L(10), -128.5, O.mult)
     ts(V("M2"), V("ONE", 0, 64), L(18), O.mult)
     red(WL, V("RX", 64, 80), O.add)
     ts(L(15), L(10), -1600.0 / 4096, O.mult, L(14), O.add)
     ts(L(17), L(10), 16384.0 * 256, O.mult, L(16), O.add)
     fill(V("ZH", 0, 16), 0.0)
     for c in range(2):
-        fill(T0[c], 2.0 * STEPS[0] - 0.5 + off[c])
+        fill(T0[c], 2.0 * STEPS[0] + off[c])
     ts(V("WM"), V("S1"), WL, O.mult)
     cp(V("LI", 4, 5), WL)
     act(V("CA", 0, 3), V("ONE", 0, 3), F.Identity, scale=L(17))
-    act(V("CA", 3, 4), L(10), F.Copy, scale=16384.0 * 4096)
+    ts(V("CA", 3, 4), L(18), -16384.0 * 4096, O.mult, L(17), O.add)
     ts(V("CM"), V("ONE", 0, 16), L(10), O.mult, 1023.0, O.mult)
     act(V("SD"), V("S1"), F.Identity, scale=lane)
     act(V("KD"), V("KD"), F.Identity, bias=L(19))
@@ -525,7 +525,7 @@ def rank_program(g, core, T, topo):
         return V("SV", k, k + n)
 
     U, U0, U2, LO1, LMW, LMN, THR, MN = [C(k) for k in range(8)]
-    CE8, LIM = C(26), (C(30), C(31))
+    CE8, LIM = C(26), (V("TT", 40, 41), V("TT", 41, 42))
     fill(V("CU"), -128.0)
     fill(V("TB"), 0.0)
     fill(U, 1023.0)
@@ -620,7 +620,7 @@ def rank_program(g, core, T, topo):
         act(LMW, Q(r, 0), F.Identity, bias=-2048.0)
         act(THR, Q(r, 3), F.Identity, bias=-1023.0)
         for c in range(2):
-            act(LIM[c], Q(r, 0), F.Identity, bias=1022.5 + off[c], scale=-1.0)
+            act(LIM[c], Q(r, 0), F.Identity, bias=1023.0 + off[c], scale=-1.0)
         ts(V("CZ"), V("M2"), LMN, O.mult, L(15), O.add)
 
     def pre(r):
@@ -813,7 +813,7 @@ def rank_program(g, core, T, topo):
         x = c * 32 + i % 2 * 16
         for k, bias in ((1, TH(c, i)), (0, V("CAND", x + 7, x + 8)), (2, V("CAND", x + 8, x + 9)))[:SHARE[c][i]]:
             y = c * 768 + k * 256
-            act(V("DA", y + a, y + b), V("XK", a, b), F.Sign, bias=bias, scale=-1.0, acc=V("CN", at + c * 4 + k, at + c * 4 + k + 1))
+            act(V("DA", y + a, y + b), V("XK", a, b), F.Sign, bias=bias, scale=UNDER, acc=V("CN", at + c * 4 + k, at + c * 4 + k + 1))
 
     def units(c, i):
         return [(0, 0), (0, 1), (0, 2), (1, 2)][:6 - SHARE[c][i]]
@@ -827,7 +827,7 @@ def rank_program(g, core, T, topo):
         for n in ns:
             if n < len(units(c, i)):
                 y, x = c * 1024 + n * 256, c * 512 + n * 128
-                scan(V("RS", x, x + 128), V("DV", y, y + 128), V("DV", y + 128, y + 256), INI, O.add, O.add)
+                scan(V("RS", x, x + 128), V("DV", y, y + 128), V("DV", y + 128, y + 256), 0.0, O.add, O.add)
 
     def opening(c, i):
         p, n = "P%d" % (5 + c), SHARE[c][i]
@@ -835,8 +835,7 @@ def rank_program(g, core, T, topo):
         mm(V(p, 1, 2 * n, 2), [(V("NBG"), V("BASE", c * 4, c * 4 + n))], False, False)
         if n < 3:
             mm(V(p, 5, 6, 2), [(V("BLK"), V("CA", 3, 4)), (V("NBG"), V("BASE", c * 4, c * 4 + 1))], False, False)
-        if own[c][0] and i:
-            mm(V(p, 0, 6, 2), [(V("NBG"), V("BASE", 8, 11))], False, False)
+        mm(V(p, 0, 6, 2), [(V("BLK"), V("CA", 0, 3))] + [(V("NBG"), V("BASE", 8, 11))] * bool(own[c][0] and i), False, False)
 
     def totals(c, i):
         p, n, x = "P%d" % (5 + c), SHARE[c][i], c * 512 + 127
@@ -907,7 +906,7 @@ def rank_program(g, core, T, topo):
             ts(V("KP", x, x + 256), V("XK"), V("TT", 37, 38), O.is_lt, 2.0, O.mult)
         else:
             ts(V("KP", x, x + 256), V("XK"), TH(c, 5), O.subtract, rel(c, 0), O.is_lt)
-        act(V("KP", x + 256, x + 512), V("XK"), F.Sign, bias=TH(c, 5), scale=-1.0)
+        act(V("KP", x + 256, x + 512), V("XK"), F.Sign, bias=TH(c, 5), scale=UNDER)
 
     def lower(c, o):
         return V("SG", c * 256, c * 256 + 256) if o else V("DBN") if own[c][0] else V("KP", c * 512, c * 512 + 256)
@@ -1073,7 +1072,7 @@ def rank_program(g, core, T, topo):
             consts2()
 
         def bound(c):
-            ts(V("MB", mb + 2 * c, mb + 2 * c + 1), TH(c, 5), Q(r, 0), O.add, 0.5 - off[c], O.add)
+            ts(V("MB", mb + 2 * c, mb + 2 * c + 1), TH(c, 5), Q(r, 0), O.add, -off[c], O.add)
 
         def sizes(j):
             act(V("CH", j * 512, j * 512 + 512), V("D", j * 512, j * 512 + 512), F.Abs)

@@ -11,40 +11,42 @@ STEPS = [256, 64, 16, 4, 1]
 SHIFT = 918 * 4096
 UNDER = -1.0 - 1.0 / 8192
 KEY = 1536.0
-SHARE = ((2, 2, 2, 2, 2), (3, 3, 3, 3, 3))
-CANDS = "VS"
+SHARE = ((2, 2, 2, 2, 2), (2, 3, 3, 3, 3))
+CANDS = "SS"
 PIECES = ((0, 128), (128, 192), (192, 256))
-FLOW = ("q1 q0 q2 q3 w1 w0 w2 w3 m1 m0 m2 m3 f1 f0 f2 f3 a0 a1 o3 a2 x3 g0 o5 x5 g1 c0 t0 c1 t1 p0 s0 o7 x7 g2 g4 g6 z3 z5 z7 z2 s1 z4 s2 z6 s3"
-        " | d0 d1 k0 k1 e0 e1 k2")
+FLOW = ("q0 q1 q2 q3 w0 w1 w2 w3 m0 m1 m2 m3 f0 f1 f2 f3 a0 a1 o1 a2 x1 g0 o6 x6 g2 g3 p0 p1 n1 t2 t3 z0 z1 c0 c1 s0 s1 b0 b1 o7 x7 g4 g5 p2 b2 z4 z5 s2 p3 b3 z6 z7 s3"
+        " d0 d1 k0 k1 e0 e1 k2")
 DIRECT = False
-APART, TW = (3, 5, 7), 0
-EARLY = 192
+APART, TW = (1, 6, 7), (1,)
+LIFT = 300.0
+CHUNK = 4
+LOAD = 5000.0
+EARLY = 128
 XKE = "SSV"
 PAIR = True
 ZB = (("P5", 0), ("P5", 64), ("P6", 0), ("P3", 0))
-STRICT = ""
-ROW = 3.0
 FETCH = "VS"
 ORDER = "bmac"
-SCHED, PATIENCE, MIX = 0, 0.0, 1.0
 TURNS = "001" + "010101" * 5
-CYCLE, WAKE, ISSUE, HOP, PASSES = 0.9, 160.0, 300.0, 2000.0, 3
-QUEUED = 800.0
-TENSOR = 0.5
+PACES = ((0.87, 1.5, 230.0, 250.0, 900.0, 30.0, 0.07, 300.0, 0.5), (1.1, 1.85, 160.0, 300.0, 700.0, 20.0, 0.06, 250.0, 0.22),
+         (0.85, 1.25, 300.0, 450.0, 2200.0, 70.0, 0.1, 600.0, 0.25))
+HOP, TRIES, SLACK, FIRST = 2000.0, (7000, 1200, 1200), 200.0, 2000.0
+TENSOR = 0.52
+FOUND = {}
 
 _f, _b, _h, _i, _u = "float32", "bfloat16", "float16", "int32", "uint16"
 PSUM = ["P%d" % k for k in range(8)]
 SCRATCH = {}
 for _n, _w, _d in (
         ("A", 10 * SL + 16, _b), ("AC", 320, _f), ("OPW", 4096, _b), ("SND", NR * SL, _b), ("SNC", NR * 32, _f), ("MB", NR * 16, _f),
-        ("S", 512, _b), ("FSP", 64, _f), ("FS", 64, _h), ("D", 4096, _b), ("CH", 4112, _b), ("CB", 128, _h), ("ID16", 128, _b),
+        ("S", 512, _b), ("FS", 128, _h), ("D", 4096, _b), ("CH", 4112, _b), ("CB", 128, _h), ("ID16", 128, _b), ("GV", 1024, _h),
         ("OFA", 32, _u), ("OFF", 4, _u), ("OFO", 256, _u), ("OFB", 32, _u), ("OFW", 32, _u), ("OFN", 32, _u), ("OFQ", 2, _u),
-        ("MR", 64, _f), ("CJ", 224, _f), ("C4", 944, _b), ("BLKH", 128, _b), ("NUTH", 128, _b), ("TJ", 256, _f), ("VJ", 256, _i), ("VK", 256, _i),
-        ("YH", 256, _h), ("QQ", 256, _f), ("DD", 256, _b), ("PEN", 256, _b), ("XK", 256, _h), ("YW", 544, _f),
+        ("MR", 64, _f), ("CJ", 226, _f), ("C4", 1088, _b), ("BLKH", 128, _b), ("NUTH", 128, _b), ("TJ", 258, _f), ("VJ", 256, _i), ("VK", 256, _i),
+        ("YH", 256, _h), ("QQ", 256, _f), ("DD", 256, _b), ("PEN", 256, _b), ("XK", 256, _h), ("YW", 272, _f), ("CO4", 64, _b),
         ("DV", 2048, _h), ("RS", 1024, _h), ("DA", 1536, _b), ("CN", 32, _f), ("CAND", 80, _f), ("TT", 48, _h),
         ("SG", 1168, _b), ("MS", 128, _f), ("NBG", 128, _b), ("CM", 16, _h),
         ("KP", 1024, _b), ("R", 1024, _b), ("V1", 768, _b), ("EBW", 288, _b), ("W", 1088, _b), ("IB", 512, _b), ("OH", 1536, _b), ("CG", 1536, _h),
-        ("TB", 64, _f), ("AM", NR * 128, _f), ("SNM", NR * 128, _f), ("YM", 544, _f), ("CU", 32, _b), ("OFM", 2, _u), ("WMN", 144, _b), ("CGM", 512, _h), ("XBN", 144, _h), ("SV", 32, _f), ("MD", 16, _h),
+        ("TB", 64, _f), ("AM", NR * 128, _f), ("SNM", NR * 128, _f), ("YM", 272, _f), ("CU", 32, _b), ("OFM", 2, _u), ("WMN", 144, _b), ("CGM", 512, _h), ("XBN", 144, _h), ("SV", 32, _f), ("MD", 16, _h),
         ("ONE", 256, _b), ("ZH", 256, _h), ("BLK", 128, _b), ("NBH", 128, _b), ("NBF", 128, _f), ("NBD", 128, _b), ("NUT", 128, _b),
         ("ID", 128, _b), ("IDN", 128, _b), ("ID2K", 128, _b), ("IDP", 128, _b), ("IDF", 128, _f),
         ("S1", 144, _b), ("SD", 144, _b), ("SN", 144, _b), ("WM", 144, _b), ("XB", 144, _h),
@@ -61,7 +63,7 @@ for _n in PSUM:
     SCRATCH[_n] = ("psum", [128, 512], _f)
 PARTS = {"DB": ("EV", 48, 24), "FIN": ("EV", 72, 16), "C8": ("EV", 88, 2),
          "DBN": ("SG", 512, 256), "RSB": ("SG", 768, 128), "BASE": ("SG", 896, 12),
-         "S4": ("C4", 0, 144), "S4H": ("C4", 144, 144), "SD4": ("C4", 288, 144), "NEG4": ("C4", 432, 128), "CO4": ("C4", 560, 64), "M4": ("C4", 624, 128),
+         "S4": ("C4", 0, 144), "S4H": ("C4", 144, 144), "SD4": ("C4", 288, 144), "NEG4": ("C4", 432, 128), "S4N": ("C4", 944, 144), "M4": ("C4", 624, 128),
          "M4N": ("C4", 752, 64), "MC": ("C4", 816, 128), "MQ": ("SG", 912, 256), "CLM": ("LC", 22, 2)}
 ROWS = ("P2", "P3")
 for _n in ROWS:
@@ -134,8 +136,12 @@ def rank_program(g, core, T, topo):
         return
     hop = ways(core, T, topo)
     far = [T.cores.index(d) for d in hop if hop[d] != d]
-    own = sorted([(0, 2), (1, 3)], key=lambda p: -len([o for o in p if o in far]))
-    off = [1024.0 * p[1] - 2047.0 for p in own]
+    turn_ = min(far) % 2
+    pos = [(0, 2), (1, 3)]
+    own = [tuple((x - turn_) % 4 for x in p) for p in pos]
+    off = [1024.0 * p[1] - 2047.0 for p in pos]
+    odd = [float(p[0] % 2) for p in own]
+    mine = own[1].index(me)
     home = me
     queue = {"V": g.vector, "S": g.scalar, "T": g.tensor, "G": g, "Y": g.sync}
     count = {"V": 0, "S": 0, "T": 0, "G": 0, "ls": 0}
@@ -194,139 +200,227 @@ def rank_program(g, core, T, topo):
                     logs[n] = old + [(a, b, wr, e, sem, val, clk, s)]
 
     calls = []
-    wrote, read, turn, strict = {}, {}, {}, {}
+    wrote, read, turn = {}, {}, {}
+    tag = [-1, "", 0]
 
-    def note(e, outs, ins, busy, issue, adds=False, late=0.0, after=()):
-        me_, pre_ = len(calls), {}
-        for k in list(after) + strict.get(e, []):
-            pre_[k] = 0.0
-        if e in strict:
-            strict[e] = [me_]
+    def part(r, name):
+        tag[:] = [r, name, 0]
+
+    def note(e, outs, ins, busy, issue, adds=False, late=0.0, after=(), rows=None):
+        me_, pre_ = len(calls), dict(after)
         for views, wr in ((ins, False), (outs, True)):
             for v in views:
                 for n, a, b, s in v["r"]:
                     for x, y, z, k in wrote.get(n, []) + (read.get(n, []) if wr else []):
                         if k != me_ and meet(a, b, s, x, y, z):
                             same = adds and wr and calls[k][0] == e and (x, y) == (a, b)
-                            pre_[k] = max(pre_.get(k, 0.0), 0.0 if same else WAKE)
+                            pre_[k] = max(pre_.get(k, 0), 0 if same else 1 if calls[k][0] in queue else 2)
                     if n in PSUM:
                         who, now, before = turn.get(n, (e, [], []))
                         if who != e:
                             who, now, before = e, [], now
                         for k in before:
-                            pre_[k] = WAKE
+                            pre_[k] = 1
                         if e == "T" and now and now[-1] != me_:
-                            pre_[now[-1]] = pre_.get(now[-1], 0.0)
+                            pre_[now[-1]] = pre_.get(now[-1], 0)
                         turn[n] = (who, now + [me_], before)
                     if wr:
                         wrote[n] = [q for q in wrote.get(n, []) if not covers(a, b, s, q[0], q[1], q[2])] + [(a, b, s, me_)]
                         read[n] = [q for q in read.get(n, []) if not covers(a, b, s, q[0], q[1], q[2])]
                     else:
                         read.setdefault(n, []).append((a, b, s, me_))
-        calls.append((e, busy, busy + late, pre_, issue))
+        calls.append((e, busy, late, pre_, issue, rows, tuple(tag)))
+        tag[2] += 1
         return me_
 
     def issue_all():
         n = len(calls)
-        ahead = [[(p, calls[p][2] + w) for p, w in c[3].items()] for c in calls]
-        behind = [[] for _ in calls]
-        for k, c in enumerate(calls):
-            for p, w in c[3].items():
-                behind[p].append((k, c[1] + w + calls[p][2] - calls[p][1]))
 
-        def place(seq, edges):
-            start, used = [0.0] * n, {}
+        def frame(ks):
+            at = {k: i for i, k in enumerate(ks)}
+            es = sorted(set([calls[k][0] for k in ks]))
+            before = [[at[p] for p in calls[k][3] if p in at] for k in ks]
+            paced = []
+            for s, x in enumerate(PACES):
+                paced.append([(es.index(calls[k][0]), [at[p] for p, w in calls[k][3].items() if w and p in at], calls[k][1][s],
+                               calls[k][5][s] if calls[k][5] else 0.0, calls[k][2] + (x[2] if calls[k][0] in queue and not calls[k][5] else 0.0)) for k in ks])
+            d = paced[0]
+            span = [x[2] + x[4] + (PACES[0][4] + x[3] + PACES[0][7] if x[3] else 0.0) for x in d]
+            ahead = [[(p, span[p] if p in d[k][1] else d[p][2]) for p in before[k]] for k in range(len(ks))]
+            behind = [[] for _ in ks]
+            for k in range(len(ks)):
+                for p, w in ahead[k]:
+                    behind[p].append((k, d[k][2] + w - d[p][2]))
+            return before, paced, len(es), ahead, behind, span
+
+        def place(fr, seq, edges, least):
+            data = fr[1][0]
+            heads, tails, start = [[] for _ in range(fr[2])], [[] for _ in range(fr[2])], [0.0] * len(seq)
             for k in seq:
-                t, d = max([start[p] + w for p, w in edges[k]] + [0.0]), calls[k][1]
-                u = used.setdefault(calls[k][0], [])
-                i = len(u)
-                while i and u[i - 1][1] > t:
-                    i -= 1
-                while i < len(u) and u[i][0] < t + d:
-                    t = max(t, u[i][1])
-                    i += 1
-                u.insert(i, (t, t + d))
+                e, d, t = data[k][0], data[k][2], least[k]
+                for p, w in edges[k]:
+                    if start[p] + w > t:
+                        t = start[p] + w
+                a, b = heads[e], tails[e]
+                i = m = len(a)
+                if m and b[m - 1] > t:
+                    while i and b[i - 1] > t:
+                        i -= 1
+                    while i < m and a[i] < t + d:
+                        if b[i] > t:
+                            t = b[i]
+                        i += 1
+                a.insert(i, t)
+                b.insert(i, t + d)
                 start[k] = t
             return start
 
-        def run(edges, back, level):
-            start, left, ready, free, pool = [0.0] * n, [len(x) for x in edges], [0.0] * n, {}, {}
-            for k in range(n):
-                free[calls[k][0]] = 0.0
-                pool.setdefault(calls[k][0], [])
-                if not left[k]:
-                    pool[calls[k][0]].append(k)
-            for _ in range(n):
-                t, e = min([(max(free[q], min([ready[k] for k in pool[q]])), q) for q in pool if pool[q]])
-                k = max([x for x in pool[e] if ready[x] <= t], key=lambda x: (level[x], -x))
-                for h in sorted(pool[e], key=lambda x: -level[x]):
-                    if level[h] > level[k] and ready[h] < t + calls[k][1] and \
-                            max(level[h] + ready[h], level[k] + ready[h] + calls[h][1]) < level[h] + t + calls[k][1] - PATIENCE:
-                        k = h
-                        break
-                pool[e].remove(k)
-                start[k] = max(t, ready[k])
-                free[e] = start[k] + calls[k][1]
-                for x, w in back[k]:
-                    ready[x] = max(ready[x], start[k] + w)
-                    left[x] -= 1
-                    if not left[x]:
-                        pool[calls[x][0]].append(x)
-            return start
+        def forward(fr, rank):
+            eff = list(rank)
+            for k, ps in enumerate(fr[0]):
+                x = eff[k]
+                for p in ps:
+                    if eff[p] > x:
+                        x = eff[p]
+                eff[k] = x
+            return place(fr, sorted(range(len(eff)), key=lambda k: eff[k]), fr[3], [0.0] * len(eff))
 
-        if SCHED:
-            after = [[] for _ in calls]
-            for k in range(n):
-                for p, w in ahead[k]:
-                    after[p].append((k, w))
-            level = [0.0] * n
-            for k in reversed(range(n)):
-                level[k] = max([calls[k][2]] + [w + level[x] for x, w in after[k]])
-            best = None
-            for _ in range(SCHED):
-                start = run(ahead, after, level)
-                end = max([start[k] + calls[k][2] for k in range(n)])
-                if best is None or end < best[0]:
-                    best = (end, start)
-                back = place(sorted(range(n), key=lambda k: (-start[k] - calls[k][1], -k)), behind)
-                level = [(1 - MIX) * level[k] + MIX * (back[k] + calls[k][1]) for k in range(n)]
-            for k in sorted(range(n), key=lambda x: (best[1][x], x)):
-                calls[k][4]()
-            return
-        urgent, best = list(range(n)), None
-        for _ in range(PASSES):
-            start = place(sorted(range(n), key=lambda k: (urgent[k], k)), ahead)
-            end = max([start[k] + calls[k][2] for k in range(n)])
-            if best is None or end < best[0]:
-                best = (end, start)
-            back = place(sorted(range(n), key=lambda k: (-start[k] - calls[k][1], -k)), behind)
-            urgent = [-back[k] - calls[k][1] for k in range(n)]
-            for k in range(n):
-                urgent[k] = max([urgent[k] + end] + [urgent[p] + 1.0 for p, w in ahead[k]])
-        for k in sorted(range(n), key=lambda x: (best[1][x], x)):
+        def replay(fr, seq, s):
+            first, woken, data, m = PACES[s][4], PACES[s][7], fr[1][s], len(seq)
+            free, moved, last, fin, start, why = [0.0] * fr[2], [0.0] * fr[2], [-1] * fr[2], [0.0] * m, [0.0] * m, [-1] * m
+            for k in seq:
+                e, pre_, busy, rows, late = data[k]
+                t, y = free[e], last[e]
+                for p in pre_:
+                    if fin[p] > t:
+                        t, y = fin[p], p
+                start[k], why[k], last[e] = t, y, k
+                free[e] = t = t + busy
+                if rows:
+                    t = moved[e] = max(t + first, moved[e]) + rows
+                    t += woken
+                fin[k] = t + late
+            end = max(fin)
+            return end, start, why, fin.index(end)
+
+        seed = [12345]
+
+        def draw():
+            seed[0] = seed[0] * 16807 % 2147483647
+            return seed[0] / 2147483647.0
+
+        def improve(ks, tries, mid=None):
+            fr, m = frame(ks), len(ks)
+            busy, chain, before = [x[2] for x in fr[1][0]], [calls[k][6][1][:1] for k in ks], fr[0]
+            rest = [fr[5][k] - busy[k] for k in range(m)]
+            at = {calls[k][6]: i for i, k in enumerate(ks)}
+            like = [at[(mid,) + calls[k][6][1:]] if mid else i for i, k in enumerate(ks)]
+            apart = [calls[k][6][0] - mid if mid else 0 for k in ks]
+            free = [k for k in range(m) if like[k] == k]
+
+            def tied(rank, paced):
+                pace = paced[at[mid + 1, "g0", 0]] - paced[at[mid, "g0", 0]] if mid else 0.0
+                return [rank[like[k]] + apart[k] * pace for k in range(m)]
+
+            def latest(rank):
+                start = forward(fr, rank)
+                back = place(fr, sorted(range(m), key=lambda k: (-start[k], -k)), fr[4], rest)
+                return [-back[k] - busy[k] for k in range(m)]
+
+            def value(rank):
+                start = forward(fr, rank)
+                seq = sorted(range(m), key=lambda k: start[k])
+                runs = [replay(fr, seq, s) for s in range(len(PACES))]
+                return sum([x[0] * PACES[s][8] for s, x in enumerate(runs)]), rank, runs
+            rank = latest(latest(latest(list(range(m)))))
+            now = best = value(tied(rank, rank))
+            for it in range(tries):
+                old = tied(now[2][0][1], now[2][0][1]) if draw() < 0.2 else now[1]
+                rank, u = list(old), draw()
+                if u < 0.4:
+                    _, _, why, z = now[2][int(draw() * len(PACES))]
+                    pairs = []
+                    while why[z] >= 0:
+                        if why[z] not in before[z]:
+                            pairs.append((why[z], z))
+                        z = why[z]
+                    if not pairs:
+                        continue
+                    a, b = pairs[int(draw() * len(pairs))]
+                    by = 400.0 * draw() * draw()
+                    if u < 0.2:
+                        rank[like[a]] += max(0.0, old[b] - old[a]) + by
+                    else:
+                        todo, seen, limit = [b], set(), min(old[a], old[b]) - by
+                        while todo:
+                            k = todo.pop()
+                            if k not in seen and old[k] > limit:
+                                seen.add(k)
+                                rank[like[k]] = old[like[k]] + limit - old[k]
+                                todo += before[k]
+                else:
+                    low, high = min([old[k] for k in free]), max([old[k] for k in free])
+                    x, c = low + (high - low) * draw(), "01"[int(2 * draw())]
+                    if u < 0.7:
+                        wide, by = (500.0, 1000.0, 2000.0, 4000.0)[int(4 * draw())], (200.0, 500.0, 1000.0, 2000.0)[int(4 * draw())]
+                    else:
+                        wide, by = (1000.0, 3000.0, 8000.0)[int(3 * draw())], 1200.0 * (draw() + draw() + draw() - 1.5)
+                    for k in free:
+                        if abs(old[k] - x) < wide:
+                            rank[k] += by * (draw() - 0.5) if u < 0.7 else by * (chain[k] == c)
+                rank = tied(rank, old)
+                if u >= 0.4 and draw() < 0.6:
+                    rank = latest(rank)
+                    rank = tied(rank, rank)
+                new = value(rank)
+                if new[0] < now[0] + SLACK * draw() * (1.0 - it / tries):
+                    now = new
+                    if new[0] < best[0]:
+                        best = new
+            return dict(zip(ks, best[2][0][1]))
+
+        def stage(k):
+            r, x, _ = calls[k][6]
+            return r - 0.5 * (x in FLOW.split() + ["parents", "first"])
+
+        if n not in FOUND:
+            start = improve([k for k in range(n) if 3 <= stage(k) < 5], TRIES[0], 4)
+            key = {calls[k][6]: k for k in range(n)}
+            pace = start[key[5, "g0", 0]] - start[key[4, "g0", 0]]
+            rank = [start[key[(4,) + c[6][1:]]] + (c[6][0] - 4) * pace if 0 < stage(k) < NR - 1 else 0.0 for k, c in enumerate(calls)]
+            for low, high, fix, tries in ((-1, 1, (1, "g0", 0), TRIES[1]), (NR - 1.5, NR + 1, (NR - 1, FLOW.split()[-1], 0), TRIES[2])):
+                start = improve([k for k in range(n) if low <= stage(k) < high], tries)
+                for k in start:
+                    if not 0 < stage(k) < NR - 1:
+                        rank[k] = start[k] - start[key[fix]] + rank[key[fix]]
+            FOUND[n] = rank
+        eff = list(FOUND[n])
+        for k in range(n):
+            eff[k] = max([eff[k]] + [eff[p] for p in calls[k][3]])
+        for k in sorted(range(n), key=lambda k: eff[k]):
             calls[k][4]()
 
-    def op(e, outs, ins, call, adds=False, cycles=None):
+    def op(e, outs, ins, call, adds=False, cycles=None, more=0.0):
         def issue():
             begin(e, outs, ins, adds)
             count[e] += 1
             call(queue[e]).then_inc(T.sem["s" + e], 1)
             done(e, known[e], "s" + e, count[e], outs, ins)
+        picked = 0
         if cycles is None:
             n = max([v["n"] for v in outs + ins])
-            wide = [v for v in outs + ins if v["n"] == n]
             if [v for v in ins if len(v["r"]) > 1]:
-                cycles = 60 + 1.56 * outs[0]["n"]
+                cycles, picked = 60 if e == "V" else 78, outs[0]["n"]
             else:
-                cycles = max(64, n / 2 if e == "V" and all([v["w"] == 2 for v in wide]) else n)
-        note(e, outs, ins, cycles * CYCLE, issue, adds)
+                cycles = max(64, n / 2 if e == "V" and all([v["w"] == 2 for v in outs + ins]) else n)
+        note(e, outs, ins, [(cycles + picked * x[1]) * x[0] + more + 8.0 for x in PACES], issue, adds)
 
     def dma(e, out, in_, sem):
         def issue():
             begin(e, [out], [in_])
             queue[e].dma_start(out["ap"], in_["ap"]).then_inc(T.sem[sem], 16)
             done("dma" + sem, {}, sem, 16, [out], [in_])
-        note(e, [out], [in_], 50.0, issue, late=HOP)
+        note(e, [out], [in_], [50.0] * len(PACES), issue, late=LOAD if out["n"] == 1024 else HOP)
 
     def EXT(ap):
         return {"ap": ap, "r": [], "n": 0, "w": 4}
@@ -367,7 +461,7 @@ def rank_program(g, core, T, topo):
             kw["scale"] = val(scale)
         if acc is not None:
             kw["accum_out"] = acc["ap"]
-        op("S", vs(out, acc), vs(a, bias, scale), lambda q: q.activation(out["ap"], a["ap"], f, **kw))
+        op("S", vs(out, acc), vs(a, bias, scale), lambda q: q.activation(out["ap"], a["ap"], f, **kw), more=20.0 * (acc is not None))
 
     def mms(triples, start=True, stop=True):
         n = len(triples)
@@ -398,6 +492,9 @@ def rank_program(g, core, T, topo):
     def pick(out, a):
         scan(out, V("M4", 0, a["n"]), a, 0.0, O.mult, O.max)
 
+    def times(out, mask, a):
+        scan(out, mask, a, 0.0, O.max, O.mult)
+
     def send(r, s, src, owners):
         buf, wr, w, r0 = MSG[s]
         ins = [V(src(o)[0], src(o)[1], src(o)[1] + w) for o in owners]
@@ -415,10 +512,13 @@ def rank_program(g, core, T, topo):
         def issue():
             begin("G", [], ins)
             g.remote_dma_fused(tr, local_sem=T.sem.ls)
-        k = note("G", [], ins, ISSUE, issue, after=sent.get("last", ()))
-        sent["last"] = [k]
-        for o in owners:
-            sent[s + ("f" if o in far else "n")] = k
+        kind = "f" if owners[0] in far else "n"
+        k = note("G", [], ins, [x[3] for x in PACES], issue, after=sent.get(kind, ()), rows=moving(buf, w))
+        sent[kind] = [(k, 0)]
+        sent[s + kind] = k
+
+    def moving(buf, w):
+        return [16 * (x[5] + x[6] * w * V(buf)["w"]) + FIRST * (tag[0] == 0 and buf == "MB") for x in PACES]
 
     def arrive(r, s):
         buf, wr, w, r0 = MSG[s]
@@ -432,8 +532,11 @@ def rank_program(g, core, T, topo):
     def landing(buf, xs, w, sem, n, kind):
         def issue():
             logs[buf] = logs.get(buf, []) + [(x, x + w, True, "net", sem, n, {sem: n}, 1) for x in xs]
-        note(sem, [V(buf, x, x + w) for x in xs], [], 1.0, issue, late=(HOP + ROW * w * V(buf)["w"]) * (1 if kind[1] == "n" else 2) + ISSUE * (kind[1] == "f") + QUEUED * (kind[0] == "c"),
-             after=[sent[kind]])
+        outs = [V(buf, x, x + w) for x in xs]
+        if kind[1] == "n":
+            note(sem, outs, [], [0.0] * len(PACES), issue, after=[(sent[kind], 2)])
+        else:
+            sent["R"] = [(note("R", outs, [], [x[3] for x in PACES], issue, after=sent.get("R", []) + [(sent[kind], 2)], rows=moving(buf, w)), 0)]
 
     sent = {}
 
@@ -459,7 +562,8 @@ def rank_program(g, core, T, topo):
     sel(V("B8", P=8), V("ONE", 0, 144, P=8), [[1, 144]], O.is_equal, -15, -16)
     sel(V("BLK"), V("BLK"), [[16, 8], [0, 16]], O.is_ge, 15, -1)
     for j in range(7):
-        iota(V("CJ", j * 32, j * 32 + 32), [[0, 32]], -4 * KA[j] * KA[j] % 4096)
+        iota(V("CJ", j * 32 + 2, j * 32 + 34), [[0, 32]], -4 * KA[j] * KA[j] % 4096)
+    iota(V("CJ", 0, 2), [[0, 2]], -4 * KA[6] * KA[6] % 4096 + (KA[7] - KA[6]) * (me % 2 - 2048))
     iota(V("CLF"), [[0, 2], [256, 2]], 0)
     iota(V("KD"), [[0, 2], [16, 8], [0, 16]], 0)
     for i, s in enumerate(STEPS):
@@ -478,7 +582,7 @@ def rank_program(g, core, T, topo):
         act(V(out), V(a), F.Copy, scale=x)
     iota(V("K"), [[0, 2], [1, 128]], 0)
     iota(V("K1"), [[0, 2], [1, 128]], 129)
-    iota(V("CO4"), [[-4352, 2], [0, 32]], 0)
+    iota(V("CO4"), [[-272, 2], [0, 32]], 0)
     iota(V("M4"), [[0, 32], [1, 4]], 0)
     iota(V("S4"), [[0, 144]], 0)
     iota(V("EBW"), [[0, 288]], 0)
@@ -503,7 +607,7 @@ def rank_program(g, core, T, topo):
     ts(L(19), lane, 0.5, O.add)
     ts(L(7), lane, 16.0, O.mult)
     tt(V("RX", 64, 80), V("RW", 64, 80), V("LM"), O.mult)
-    ts(L(14), L(11), -1.5 / 4096, O.mult)
+    ts(L(14), L(11), (turn_ - 1.5) / 4096, O.mult)
     ts(L(16), L(11), 16384.0, O.mult)
     ts(V("M2"), V("ONE", 0, 64), L(18), O.mult)
     red(WL, V("RX", 64, 80), O.add)
@@ -549,6 +653,7 @@ def rank_program(g, core, T, topo):
         cp(L(21), V("LI", 2, 3))
         act(V("S4", 3, 131, 4), V("BLK", 0, 128, 4), F.Copy)
         act(V("S4H"), V("S4"), F.Copy, scale=0.5)
+        act(V("S4N"), V("S4"), F.Copy, scale=-1.0)
         act(V("SD4"), V("S4"), F.Identity, scale=lane)
         ts(V("NEG4"), V("M4"), L(21), O.not_equal, -16384.0, O.mult)
         ts(V("M4N"), V("M4", 0, 64), 0.0, O.is_equal, -32768.0, O.mult)
@@ -558,7 +663,6 @@ def rank_program(g, core, T, topo):
         ts(L(31), L(11), -2048.0, O.mult, L(31), O.add)
         act(V("MC"), V("BLK"), F.Identity, scale=L(31))
         fill(V("YM", 256, 272), 0.0)
-        fill(V("YM", 528, 544), 0.0)
         for h in range(3):
             fill(V("AM", h, 128, 4), 0.0)
         for k in range(2):
@@ -568,7 +672,6 @@ def rank_program(g, core, T, topo):
         for c in range(4):
             fill(V("W", c * 272 + 256, c * 272 + 272), 0.0)
         fill(V("YW", 256, 272), 0.0)
-        fill(V("YW", 528, 544), 0.0)
         fill(V("MB", home * 4 + 3, NR * 16, 16), 5000.0)
 
     def consts3():
@@ -615,8 +718,8 @@ def rank_program(g, core, T, topo):
 
     def derived(r):
         act(CE8, Q(r, 14), F.Identity, bias=-0.25 - SHIFT)
-        act(V("TJ", 0, 224), V("CJ"), F.Identity, bias=CE8)
-        act(LMN, Q(r, 0), F.Identity, bias=-1023.0)
+        act(V("TJ", 0, 226), V("CJ"), F.Identity, bias=CE8)
+        act(LMN, Q(r, 0), F.Identity, bias=LIFT - 1023.0)
         act(LMW, Q(r, 0), F.Identity, bias=-2048.0)
         act(THR, Q(r, 3), F.Identity, bias=-1023.0)
         for c in range(2):
@@ -656,14 +759,13 @@ def rank_program(g, core, T, topo):
         derived(r)
 
     def marks():
-        parts = [(V("P1", k * 64, k * 64 + 64), l, x) for k in range(4) for l, x in wraps("WM", "CH", k * 1024, 1024)]
-        parts += [(V("P1", TW * 64, TW * 64 + 64), l, x) for l, x in wraps("WMN", "D", TW * 1024, 1024)]
+        parts = [(V("P1", k * 64, k * 64 + 64), l, x) for k in range(4) for l, x in wraps("WM", "D" if k in TW else "CH", k * 1024, 1024)]
+        parts += [(V("P1", k * 64, k * 64 + 64), l, x) for k in TW for l, x in wraps("WMN", "CH", k * 1024, 1024)]
         mm(V("P1", 0, 256), [(V("MC"), V("ONE"))], True, False)
-        for k in range(0, len(parts), 4):
-            mms(parts[k:k + 4], False, k + 4 == len(parts))
+        for k in range(0, len(parts), CHUNK):
+            mms(parts[k:k + CHUNK], False, k + CHUNK >= len(parts))
         act(V("MQ"), V("P1", 0, 256), F.Copy)
         tt(V("YM", 0, 256), V("P1", 0, 256), V("MQ"), O.subtract)
-        act(V("YM", 272, 528), V("YM", 0, 256), F.Copy)
 
     def children(r):
         apart = dict(zip(APART, ("P0", "P1", "P7")))
@@ -680,13 +782,14 @@ def rank_program(g, core, T, topo):
                 out = V("P4", 0, 32)
                 mm(out, [(V("BLK"), V("CU"))] + wraps("WM", "A", 0, 512))
                 ts(V("MR", 0, 32), out, MAGIC * 4096, O.add, MAGIC * 4096, O.subtract)
-                tt(mz, out, V("MR", 0, 32), O.subtract)
+                tt(V("MR", 32, 64), out, V("MR", 0, 32), O.subtract)
+                ts(mz, V("MR", 32, 64), 2048.0 - odd[1], O.add)
 
         def squares(k):
             for j in (2 * k, 2 * k + 1):
-                act(V(("P2", "P3", "P5", "P6")[k], j % 2 * 32, j % 2 * 32 + 32), mz, F.Square, bias=512.0 + 2 * KA[min(j, 6)], scale=0.25)
+                act(V(("P2", "P3", "P5", "P6")[k], j % 2 * 32, j % 2 * 32 + 32), mz, F.Square, bias=odd[1] / 4 + 2 * KA[min(j, 6)], scale=0.25)
             if k == 3:
-                act(J("TJ", 7), mz, F.Identity, bias=V("TJ", 192, 193), scale=float(KA[7] - KA[6]))
+                act(V("TJ", 226, 258), mz, F.Identity, bias=V("TJ", 0, 1), scale=float(KA[7] - KA[6]))
 
         def fetch(h):
             lay = V("A", 0, (r + 1) * SL)
@@ -701,7 +804,7 @@ def rank_program(g, core, T, topo):
                     mm(V(apart[j]), [(V("IDN"), par)], True, False)
 
         def whole(k):
-            tt(J("VJ", k, w=64), V(("P2", "P3", "P5", "P6")[k], 0, 64), J("TJ", k, w=64), O.add)
+            tt(J("VJ", k, w=64), V(("P2", "P3", "P5", "P6")[k], 0, 64), V("TJ", k * 64 + 2, k * 64 + 66), O.add)
 
         def mod(k):
             ts(J("OFO" if DIRECT else "VK", k, w=64), J("VJ", k, w=64), 4095, O.bitwise_and)
@@ -711,7 +814,7 @@ def rank_program(g, core, T, topo):
                 cp(J("OFO", k, w=64), J("VK", k, w=64))
 
         def gather(j):
-            tt(J("D", j, w=512), IND(V("OPW"), J("OFO", j)), par, O.subtract)
+            tt(J("CH" if j // 2 in TW else "D", j, w=512), IND(V("OPW"), J("OFO", j)), par, O.subtract)
 
         def other(j):
             act(J("D", j, w=512), IND(V("OPW"), J("OFO", j)), F.Copy)
@@ -725,29 +828,35 @@ def rank_program(g, core, T, topo):
         def Z(k):
             return V(ZB[k][0], ZB[k][1], ZB[k][1] + 64)
 
+        def adds_(x, k, pairs):
+            mates = [y for y in FLOW.split() if y[0] in "pnbs" and ZB[int(y[1])][0] == ZB[k][0]]
+            mm(Z(k), pairs, x + str(k) == mates[0], x + str(k) == mates[-1])
+
         def opens(k):
-            mm(Z(k), [(V("ID"), V("FS")), (V("BLK"), V("CZ"))], True, False)
-            if k == TW:
-                mm(Z(k), wraps("XBN", "D", k * 1024, 1024), False, False)
+            adds_("p", k, [(V("BLK"), V("CZ"))])
+
+        def above(k):
+            adds_("b", k, [(V("ID"), V("FS", 0, 64)), (V("ID"), V("FS", 64, 128))])
+
+        def signed(k):
+            adds_("n", k, wraps("XBN", "CH", k * 1024, 1024))
 
         def sums(k):
-            if k != TW:
-                opens(k)
-            mm(Z(k), wraps("XB", "CH", k * 1024, 1024), False, True)
+            adds_("s", k, wraps("XB", "D" if k in TW else "CH", k * 1024, 1024))
 
         def twice(j):
-            ts(J("CH", j, w=512), J("D", j, w=512), 0.0, O.max, 2.0, O.mult)
+            ts(J("D", j, w=512), J("CH", j, w=512), 0.0, O.max, 2.0, O.mult)
 
         def costs():
-            ts(V("FSP"), IND(V("AC", 0, r * 32 + 32), V("OFF")), THR, O.is_lt, -4096.0, O.mult)
+            act(V("FS", 0, 64), IND(V("AC", 0, r * 32 + 32), V("OFF")), F.Copy)
 
         def costs2():
-            tt(V("FS"), IND(V("AC", 0, r * 32 + 32), V("OFF")), V("FSP"), O.max)
+            ts(V("FS", 64, 128), V("FS", 0, 64), THR, O.is_ge, 1023.0, O.mult)
 
         def keys(a, b):
             z = V(ZB[a // 64][0], ZB[a // 64][1], ZB[a // 64][1] + b - a)
             ts(V("QQ", a, b), z, MAGIC / 1024, O.add, MAGIC / 1024, O.subtract)
-            ts(V("YH", a, b), z, 1025.0, O.add, 2048.0, O.min)
+            ts(V("YH", a, b), z, 1025.0 + LIFT, O.add, 2048.0, O.min)
             tt(V("DD", a, b), z, V("QQ", a, b), O.subtract)
             ts(V("PEN", a, b), V("YH", a, b), 1024.5, O.is_lt, 8192.0, O.mult)
             base = [(V("ID"), V("YH", a, b)), (V("ID"), V("PEN", a, b))]
@@ -765,15 +874,11 @@ def rank_program(g, core, T, topo):
         if not r:
             consts1()
             ts(V("OFF"), V("CLF"), 1.0 / 16, O.mult)
-        do = {"q": squares, "a": fetch, "x": less, "w": whole, "m": mod, "f": offsets, "o": other, "g": gather, "t": twice, "z": size, "s": sums, "p": opens,
+        do = {"q": squares, "a": fetch, "x": less, "w": whole, "m": mod, "f": offsets, "o": other, "g": gather, "t": twice, "z": size, "s": sums, "p": opens, "n": signed, "b": above,
               "c": lambda k: (costs, costs2)[k](), "k": lambda k: keys(*PIECES[k]), "d": lambda c: cand(c, 0), "e": early}
-        strict.update({e: [] for e in STRICT})
         for x in FLOW.split():
-            if x == "|":
-                strict.clear()
-            else:
-                do[x[0]](int(x[1]))
-        strict.clear()
+            part(r, x)
+            do[x[0]](int(x[1]))
 
     def TH(c, i):
         return T0[c] if i == 0 else V("TT", c * 16 + i % 2 * 8 + 5, c * 16 + i % 2 * 8 + 6)
@@ -782,7 +887,7 @@ def rank_program(g, core, T, topo):
         x = c * 32 + i % 2 * 16
         if i == 4:
             ts(V("CAND", x, x + 9), V("CT", 16 * i, 16 * i + 9), TH(c, i), O.add, LIM[c], O.min)
-            if own[c][0]:
+            if pos[c][0]:
                 act(V("CAND", 64, 71), V("CAND", x, x + 7), F.Identity, bias=rel(c, 0))
         elif i and CANDS[c] == "S":
             act(V("CAND", x, x + 9), V("CT", 16 * i, 16 * i + 9), F.Identity, bias=TH(c, i))
@@ -790,11 +895,11 @@ def rank_program(g, core, T, topo):
             ts(V("CAND", x, x + 9), V("CT", 16 * i, 16 * i + 9), TH(c, i), O.add)
 
     def rel(c, o):
-        return 1024.0 * (own[c][o] - own[c][1])
+        return 1024.0 * (pos[c][o] - pos[c][1])
 
     def lowers(c, a, b, at):
         act(V("SG", c * 256 + a, c * 256 + b), V("XK", a, b), F.Sign, bias=0.5 - off[c], acc=V("CN", at + c * 4 + 3, at + c * 4 + 4))
-        if own[c][0]:
+        if pos[c][0]:
             ts(V("DBN", a, b), V("XK", a, b), off[c] - 0.5 + rel(c, 0), O.is_lt, -2.0, O.mult)
 
     def early(c):
@@ -805,7 +910,7 @@ def rank_program(g, core, T, topo):
     def bases(c):
         lowers(c, EARLY, 256, 0)
         act(V("BASE", c * 4, c * 4 + 3), V("ONE", 0, 3), F.Identity, scale=V("CN", c * 4 + 3, c * 4 + 4), bias=V("CN", c * 4 + 19, c * 4 + 20))
-        if own[c][0]:
+        if pos[c][0]:
             scan(V("RSB"), V("DBN", 0, 128), V("DBN", 128, 256), 0.0, O.add, O.add)
             act(V("BASE", 8, 11), V("ZH", 0, 3), F.Identity, bias=V("RSB", 127, 128))
 
@@ -835,7 +940,7 @@ def rank_program(g, core, T, topo):
         mm(V(p, 1, 2 * n, 2), [(V("NBG"), V("BASE", c * 4, c * 4 + n))], False, False)
         if n < 3:
             mm(V(p, 5, 6, 2), [(V("BLK"), V("CA", 3, 4)), (V("NBG"), V("BASE", c * 4, c * 4 + 1))], False, False)
-        mm(V(p, 0, 6, 2), [(V("BLK"), V("CA", 0, 3))] + [(V("NBG"), V("BASE", 8, 11))] * bool(own[c][0] and i), False, False)
+        mm(V(p, 0, 6, 2), [(V("BLK"), V("CA", 0, 3))] + [(V("NBG"), V("BASE", 8, 11))] * bool(pos[c][0] and i), False, False)
 
     def totals(c, i):
         p, n, x = "P%d" % (5 + c), SHARE[c][i], c * 512 + 127
@@ -843,7 +948,7 @@ def rank_program(g, core, T, topo):
         if n < 3:
             mm(*mine, False, False)
         mms([(V(p, 0, 6, 2), V("NBH"), V("RS", x, x + 257, 128))]
-            + [(V(p, k, k + 1, 2), V("NBG"), V("RSB", 127, 128)) for k in (0, 2, 4) if own[c][0] and not i], False, False)
+            + [(V(p, k, k + 1, 2), V("NBG"), V("RSB", 127, 128)) for k in (0, 2, 4) if pos[c][0] and not i], False, False)
         if n < 3:
             mm(V(p, 5, 6, 2), [(V("NBH"), V("RS", x + 384, x + 385))], False, True)
         else:
@@ -851,7 +956,7 @@ def rank_program(g, core, T, topo):
 
     def decide(c, i):
         x, y = c * 32 + i % 2 * 16, c * 16 + (i + 1) % 2 * 8
-        if i == 4 and own[c][0]:
+        if i == 4 and pos[c][0]:
             scan(V("TT", 32, 38), V("P%d" % (5 + c), 0, 6), V("CAND", 64, 70), V("CAND", 70, 71), O.min, O.max)
         scan(V("TT", y, y + 6), V("P%d" % (5 + c), 0, 6), V("CAND", x, x + 6), V("CAND", x + 6, x + 7), O.min, O.max)
 
@@ -878,8 +983,7 @@ def rank_program(g, core, T, topo):
         return [count, total, choose]
 
     def least(r):
-        for o in range(2):
-            act(V("YW", o * 272, o * 272 + 256), V("P4", 0, 256), F.Identity, bias=LMW)
+        act(V("YW", 0, 256), V("P4", 0, 256), F.Identity, bias=LMW)
         scan(V("QQ", 0, 128), V("YW", 0, 128), V("YW", 128, 256), 5000.0, O.min, O.min)
         ts(V("MD"), V("LM"), V("QQ", 127, 128), O.mult, 2047.0, O.min)
         mm(V("P4", 256, 272), [(V("BLK"), V("CM")), (V("BLK"), V("MD"))])
@@ -891,9 +995,10 @@ def rank_program(g, core, T, topo):
                 return
             x, p, at = c * 256, "P%d" % (2 + c), where(r, "SNM", "AM", 32)
             mm(V(p, 0, 64), [(V("ID"), V("NEG4", 0, 64))], True, False)
-            tt(V("CGM", x, x + 256), IND(V("YM"), V("OFW", c * 16, c * 16 + 16)), V("OH", x, x + 256), O.mult)
-            mm(V(p, 0, 64), fours("S4", "CGM", x, 256), False, True)
-            for o, n in ((0, 32), (1, 32)) if c else ((0, 64),):
+            act(V("GV", x, x + 256), IND(V("YM"), V("OFW", c * 16, c * 16 + 16)), F.Identity, bias=odd[c] - 2048.0, scale=-1.0)
+            times(V("CGM", x, x + 256), V("OH", x, x + 256), V("GV", x, x + 256))
+            mm(V(p, 0, 64), fours("S4N", "CGM", x, 256), False, True)
+            for o, n in ((1 - mine, 32), (mine, 32)) if c else ((0, 64),):
                 buf, y = at(own[c][o])
                 scan(V(buf, y, y + n), V("M4N", 0, n), V(p, o * 32, o * 32 + n), 0.0, O.add, O.max)
             send(r, "m", at, [o for o in own[c] if o != me])
@@ -902,14 +1007,14 @@ def rank_program(g, core, T, topo):
 
     def kept(c):
         x = c * 512
-        if own[c][0]:
+        if pos[c][0]:
             ts(V("KP", x, x + 256), V("XK"), V("TT", 37, 38), O.is_lt, 2.0, O.mult)
         else:
             ts(V("KP", x, x + 256), V("XK"), TH(c, 5), O.subtract, rel(c, 0), O.is_lt)
         act(V("KP", x + 256, x + 512), V("XK"), F.Sign, bias=TH(c, 5), scale=UNDER)
 
     def lower(c, o):
-        return V("SG", c * 256, c * 256 + 256) if o else V("DBN") if own[c][0] else V("KP", c * 512, c * 512 + 256)
+        return V("SG", c * 256, c * 256 + 256) if o else V("DBN") if pos[c][0] else V("KP", c * 512, c * 512 + 256)
 
     def both(c, a, b):
         p = "P%d" % (2 + c)
@@ -934,14 +1039,14 @@ def rank_program(g, core, T, topo):
         return V(("P7", "P0")[c], o * 256, o * 256 + 256)
 
     def places0(c):
-        os_ = [o for o in (1, 0) if o or own[c][0]]
+        os_ = [o for o in (1, 0) if o or pos[c][0]]
         for o in os_:
             mm(PL(c, o), [(V("NUTH"), lower(c, o))], o == 1, False)
 
     def places1(c):
         for o in range(2):
             y = c * 512 + o * 256
-            mm(PL(c, o), [(V("NUTH" if o or own[c][0] else "NUT"), V("KP", y, y + 256))], False, False)
+            mm(PL(c, o), [(V("NUTH" if o or pos[c][0] else "NUT"), V("KP", y, y + 256))], False, False)
 
     def places(c):
         for o in range(2):
@@ -960,7 +1065,7 @@ def rank_program(g, core, T, topo):
         v1 = V("V1", c * 256 + 14, c * 256 + 256, 16)
         p = "P%d" % (2 + c)
         ts(V("OFB", c * 16, c * 16 + 16), v1, 0.25, O.mult, 3.0, O.add)
-        mms([(V(p, 0, 64), V("ID"), V("NEG4", 0, 64))] + [(V(p, h, 64, 4), V("ID"), v1) for h in range(4)], True, False)
+        mms([(V(p, 0, 64), V("ID"), V("CO4"))] + [(V(p, h, 64, 4), V("ID"), v1) for h in range(4)], True, False)
 
     def second(c):
         x = c * 256
@@ -972,11 +1077,13 @@ def rank_program(g, core, T, topo):
         cp(V("OFW", c * 16, c * 16 + 16), V("CB", c * 64 + 3, c * 64 + 64, 4))
 
     def columns(c):
-        mm(V("P%d" % (5 + c), 0, 64), [(V("ID"), V("CO4")), (V("ID16"), V("CB", c * 64, c * 64 + 64))], True, False)
+        mm(V("P%d" % (5 + c), 0, 64), [(V("ID"), V("NEG4", 0, 64)), (V("ID16"), V("CB", c * 64, c * 64 + 64))], True, False)
 
     def third(c):
         x = c * 256
-        tt(V("OH", x, x + 256), IND(V("W", c * 544, c * 544 + 544), V("OFW", c * 16, c * 16 + 16)), V("K1"), O.is_equal)
+        for o in range(2):
+            y, w, k = x + o * 128, c * 544 + o * 272, c * 16 + o * 8
+            tt(V("OH", y, y + 128), IND(V("W", w, w + 272), V("OFW", k, k + 8)), V("K1", 0, 128), O.is_equal)
         mm(V("P%d" % (5 + c), 0, 64), fours("SD4", "OH", x, 256), False, True)
 
     def where(r, buf, stays, w):
@@ -990,25 +1097,22 @@ def rank_program(g, core, T, topo):
         at = where(r, "SND", "A", 128)
         if PAIR and not c:
             buf, x = at(own[c][0])
-            act(V(buf, x, x + 256), IND(V("CH"), V("OFN", 0, 16)), F.Copy)
+            act(V(buf, x, x + 256), IND(V("CH"), V("OFN", 0, 16)), F.Abs)
         for o in sorted(range(2), key=lambda o: (own[c][o] == me, -o)) * (c or not PAIR):
             buf, x = at(own[c][o])
-            v = IND(V("CH"), V("OFN", c * 16 + o * 8, c * 16 + o * 8 + 8))
-            if o or c:
-                act(V(buf, x, x + 128), v, F.Copy)
-            else:
-                cp(V(buf, x, x + 128), v)
+            act(V(buf, x, x + 128), IND(V("CH"), V("OFN", c * 16 + o * 8, c * 16 + o * 8 + 8)), F.Abs)
         send(r, "a", at, [o for o in own[c] if o != me])
 
     def prices(c):
         x = c * 256
-        tt(V("CG", x, x + 256), IND(V("YW"), V("OFW", c * 16, c * 16 + 16)), V("OH", x, x + 256), O.mult)
+        act(V("GV", 512 + x, 768 + x), IND(V("YW"), V("OFW", c * 16, c * 16 + 16)), F.Copy)
+        times(V("CG", x, x + 256), V("OH", x, x + 256), V("GV", 512 + x, 768 + x))
 
     def price_lists(r, cs):
         at = where(r, "SNC", "AC", 8)
         mm(V("P4", cs[0] * 16, cs[-1] * 16 + 16), wraps("S1", "CG", cs[0] * 256, len(cs) * 256))
         for c in cs:
-            for o, n in ((0, 8), (1, 8)) if c else ((0, 16),):
+            for o, n in ((1 - mine, 8), (mine, 8)) if c else ((0, 16),):
                 buf, y = at(own[c][o])
                 act(V(buf, y, y + n), V("P4", c * 16 + o * 8, c * 16 + o * 8 + n), F.Copy)
 
@@ -1065,17 +1169,16 @@ def rank_program(g, core, T, topo):
             mm(V("P%d" % (4 + l), 0, 512, P=8), [(V("GM", m * 8, m * 8 + 8), V("CG", x, x + 512))], (t, l) in ((0, 0), (0, 1), (1, 2)), t == 2)
 
     def rnd(r):
+        part(r, "parents" if r else "first")
         parents(r)
         children(r)
         mb = r * 16 + home * 4
         if not r:
+            part(r, "consts2")
             consts2()
 
         def bound(c):
             ts(V("MB", mb + 2 * c, mb + 2 * c + 1), TH(c, 5), Q(r, 0), O.add, -off[c], O.add)
-
-        def sizes(j):
-            act(V("CH", j * 512, j * 512 + 512), V("D", j * 512, j * 512 + 512), F.Abs)
 
         def bounds():
             for c in range(2):
@@ -1087,18 +1190,22 @@ def rank_program(g, core, T, topo):
         work = [[f for i in range(5) for f in step(c, i)] + lists(r, c) for c in range(2)]
         work[1].insert(15, bounds)
         work[1].insert(9, lambda: least(r))
-        if r < NR - 1:
-            work[0].insert(18, marks)
-        work[0].append(lambda: [sizes(j) for j in (2 * TW, 2 * TW + 1)])
+        work[0].insert(18, marks if r < NR - 1 else list)
         if r < NR - 1:
             work[0].append(lambda: states(r, 0))
+        work = [[("%d.%d" % (c, k), f) for k, f in enumerate(w)] for c, w in enumerate(work)]
         for c in TURNS + "01" * 24:
             if work[int(c)]:
-                work[int(c)].pop(0)()
+                x, f = work[int(c)].pop(0)
+                part(r, x)
+                f()
         if not r:
+            part(r, "consts3")
             consts3()
+        part(r, "pre")
         pre(r)
         if r < NR - 1:
+            part(r, "rest")
             states(r, 1)
             prices(0)
             prices(1)
@@ -1106,7 +1213,10 @@ def rank_program(g, core, T, topo):
             send(r, "c", where(r, "SNC", "AC", 8), far)
             send(r, "c", where(r, "SNC", "AC", 8), [o for o in others if o not in far])
             arrive(r, "m")
+            arrive(r, "a")
+            arrive(r, "c")
         else:
+            part(r, "last")
             for c in range(2):
                 prices(c)
                 price_lists(r, (c,))
@@ -1114,16 +1224,18 @@ def rank_program(g, core, T, topo):
             for c in range(2):
                 states(r, c)
             older()
-        arrive(r, "a")
-        arrive(r, "c")
-        if r == 0:
-            counts4()
+            arrive(r, "c")
+            arrive(r, "a")
+        part(r, "level")
         level(r)
-        if r == NR - 2:
+        if r == 0:
+            part(r, "consts4")
+            counts4()
             consts4()
 
     for r in range(NR):
         rnd(r)
+    part(NR, "end")
 
     gaps(2, V("AC"), Q(NR - 1, 4), E(11))
     for l in range(2):

from concourse.bass import DstId, RemoteDMATransfer
from concourse.mybir import AluOpType as O, AxisListType, ActivationFunctionType as F

NR = 8
SL = 512
EMPTY = 8
WT = [1, 3, 7, 13, 21, 35, 49, 67, 85, 107, 129, 155, 181, 211, 241, 253]
KA = [17, 101, 263, 389, 547, 701, 859, 1021]
MAGIC = float(3 << 22)
STEPS = [256, 64, 16, 4, 1]
SHIFT = 918 * 4096
UNDER = -1.0 - 1.0 / 8192
KEY = 1536.0
SHARE = ((2, 2, 2, 2, 2), (2, 3, 3, 3, 3))
CANDS = "SS"
PIECES = ((0, 128), (128, 192), (192, 256))
FLOW = ("q0 q1 q2 q3 w0 w1 w2 w3 m0 m1 m2 m3 f0 f1 f2 f3 a0 a1 o1 a2 x1 g0 o6 x6 g2 g3 p0 p1 n1 t2 t3 z0 z1 c0 c1 s0 s1 b0 b1 o7 x7 g4 g5 p2 b2 z4 z5 s2 p3 b3 z6 z7 s3"
        " d0 d1 k0 k1 e0 e1 k2")
DIRECT = False
APART, TW = (1, 6, 7), (1,)
LIFT = 300.0
CHUNK = 4
LOAD = 5000.0
EARLY = 128
XKE = "SSV"
PAIR = True
ZB = (("P5", 0), ("P5", 64), ("P6", 0), ("P3", 0))
FETCH = "VS"
ORDER = "bmac"
TURNS = "001" + "010101" * 5
PACES = ((0.87, 1.5, 230.0, 250.0, 900.0, 30.0, 0.07, 300.0, 0.5), (1.1, 1.85, 160.0, 300.0, 700.0, 20.0, 0.06, 250.0, 0.22),
         (0.85, 1.25, 300.0, 450.0, 2200.0, 70.0, 0.1, 600.0, 0.25))
HOP, TRIES, SLACK, FIRST = 2000.0, (7000, 1200, 1200), 200.0, 2000.0
TENSOR = 0.52
FOUND = {}

_f, _b, _h, _i, _u = "float32", "bfloat16", "float16", "int32", "uint16"
PSUM = ["P%d" % k for k in range(8)]
SCRATCH = {}
for _n, _w, _d in (
        ("A", 10 * SL + 16, _b), ("AC", 320, _f), ("OPW", 4096, _b), ("SND", NR * SL, _b), ("SNC", NR * 32, _f), ("MB", NR * 16, _f),
        ("S", 512, _b), ("FS", 128, _h), ("D", 4096, _b), ("CH", 4112, _b), ("CB", 128, _h), ("ID16", 128, _b), ("GV", 1024, _h),
        ("OFA", 32, _u), ("OFF", 4, _u), ("OFO", 256, _u), ("OFB", 32, _u), ("OFW", 32, _u), ("OFN", 32, _u), ("OFQ", 2, _u),
        ("MR", 64, _f), ("CJ", 226, _f), ("C4", 1088, _b), ("BLKH", 128, _b), ("NUTH", 128, _b), ("TJ", 258, _f), ("VJ", 256, _i), ("VK", 256, _i),
        ("YH", 256, _h), ("QQ", 256, _f), ("DD", 256, _b), ("PEN", 256, _b), ("XK", 256, _h), ("YW", 272, _f), ("CO4", 64, _b),
        ("DV", 2048, _h), ("RS", 1024, _h), ("DA", 1536, _b), ("CN", 32, _f), ("CAND", 80, _f), ("TT", 48, _h),
        ("SG", 1168, _b), ("MS", 128, _f), ("NBG", 128, _b), ("CM", 16, _h),
        ("KP", 1024, _b), ("R", 1024, _b), ("V1", 768, _b), ("EBW", 288, _b), ("W", 1088, _b), ("IB", 512, _b), ("OH", 1536, _b), ("CG", 1536, _h),
        ("TB", 64, _f), ("AM", NR * 128, _f), ("SNM", NR * 128, _f), ("YM", 272, _f), ("CU", 32, _b), ("OFM", 2, _u), ("WMN", 144, _b), ("CGM", 512, _h), ("XBN", 144, _h), ("SV", 32, _f), ("MD", 16, _h),
        ("ONE", 256, _b), ("ZH", 256, _h), ("BLK", 128, _b), ("NBH", 128, _b), ("NBF", 128, _f), ("NBD", 128, _b), ("NUT", 128, _b),
        ("ID", 128, _b), ("IDN", 128, _b), ("ID2K", 128, _b), ("IDP", 128, _b), ("IDF", 128, _f),
        ("S1", 144, _b), ("SD", 144, _b), ("SN", 144, _b), ("WM", 144, _b), ("XB", 144, _h),
        ("K", 256, _b), ("K1", 256, _b), ("K13", 512, _b), ("KD", 256, _b), ("DT", 256, _b), ("CL", 32, _f), ("CLF", 4, _f),
        ("CZ", 64, _h), ("M2", 64, _b), ("CA", 4, _b), ("CT", 80, _f),
        ("LM", 16, _f), ("RW", 80, _f), ("RX", 80, _f), ("LC", 32, _f), ("LI", 8, _i), ("G8", 8, _h), ("G8F", 8, _f),
        ("F3", 96, _f), ("KP3", 96, _b), ("R3", 96, _b), ("RM", 32, _b), ("W3", 96, _b), ("V3", 96, _f),
        ("EV", 128, _f), ("GM", 40, _h), ("OPF", 96, _f),
        ("KD3", 256, _b), ("DT3", 256, _b), ("C3", 32, _b), ("OF3", 96, _u), ("OG3", 14, _u), ("OP3", 96, _u), ("YL", 1536, _b)):
    SCRATCH[_n] = ("sbuf", [128, _w], _d)
for _n, _w, _d in (("B8", 144, _h), ("F8I", 512, _i), ("F8", 512, _h), ("YF", 1536, _f), ("YT8", 8, _f)):
    SCRATCH[_n] = ("sbuf", [8, _w], _d)
for _n in PSUM:
    SCRATCH[_n] = ("psum", [128, 512], _f)
PARTS = {"DB": ("EV", 48, 24), "FIN": ("EV", 72, 16), "C8": ("EV", 88, 2),
         "DBN": ("SG", 512, 256), "RSB": ("SG", 768, 128), "BASE": ("SG", 896, 12),
         "S4": ("C4", 0, 144), "S4H": ("C4", 144, 144), "SD4": ("C4", 288, 144), "NEG4": ("C4", 432, 128), "S4N": ("C4", 944, 144), "M4": ("C4", 624, 128),
         "M4N": ("C4", 752, 64), "MC": ("C4", 816, 128), "MQ": ("SG", 912, 256), "CLM": ("LC", 22, 2)}
ROWS = ("P2", "P3")
for _n in ROWS:
    SCRATCH[_n] = ("psum", [128, 2, 256], _f)
SEMAPHORES = (["sV", "sS", "sT", "sG", "ls"] + ["%s%d%s" % (s, r, k) for s in "abcm" for r in range(NR) for k in "nf"]
              + ["l%d" % k for k in range(10)] + ["o%d" % k for k in range(5)])
MSG = {"b": ("MB", 16, 4, 0), "a": ("A", SL, 128, 1), "c": ("AC", 32, 8, 1), "m": ("AM", 128, 32, 1)}


def slot(r):
    return r + 1 if r + 1 < EMPTY else r + 2


def ways(core, T, topo):
    hop, used = {}, []
    for d in T.cores:
        if d == core:
            continue
        if topo.may_write(core, d):
            hop[d] = d
        else:
            c = [x for x in topo.cores_of(core) if x != core and x not in used and topo.die(x) == topo.die(core) and topo.may_write(x, d)]
            hop[d] = c[0]
            used.append(c[0])
    return hop


def bits(es):
    m = 0
    for e in es:
        m |= 1 << e
    return m


def hop_engines(core, hop, topo, s):
    far = [d for d in hop if hop[d] != d]
    res = {d: topo.engines(core, d) for d in hop if hop[d] == d}
    for k, d in enumerate(far):
        rest = topo.engines(core, hop[d])
        n = len(rest) // len(far)
        res[d] = rest[k * n:(k + 1) * n]
    return res


def relay(g, core, T, topo):
    local = 0
    for q, rk in enumerate(T.cores):
        hop = ways(rk, T, topo)
        for d in hop:
            if hop[d] != core or d == core:
                continue
            rid, pid = topo.addr(d, core)
            m = topo.mask(core, d)
            for r in range(NR):
                for s in (ORDER if r < NR - 1 else "bca"):
                    buf, wr, w, r0 = MSG[s]
                    x = (slot(r) if r0 else r) * wr + q * w
                    sem = T.sem["%s%df" % (s, r)]
                    g.wait_ge(sem, len(hop_engines(rk, hop, topo, s)[d]))
                    g.remote_dma(T[buf][:, x:x + w], T[buf][:, x:x + w], sem, T.sem.ls, pid, rid, m)
                    local += len(topo.engines(core, d))
    if local:
        g.wait_ge(T.sem.ls, local)


def rank_program(g, core, T, topo):
    me = T.rank_of(core)
    if me is None:
        relay(g, core, T, topo)
        return
    hop = ways(core, T, topo)
    far = [T.cores.index(d) for d in hop if hop[d] != d]
    turn_ = min(far) % 2
    pos = [(0, 2), (1, 3)]
    own = [tuple((x - turn_) % 4 for x in p) for p in pos]
    off = [1024.0 * p[1] - 2047.0 for p in pos]
    odd = [float(p[0] % 2) for p in own]
    mine = own[1].index(me)
    home = me
    queue = {"V": g.vector, "S": g.scalar, "T": g.tensor, "G": g, "Y": g.sync}
    count = {"V": 0, "S": 0, "T": 0, "G": 0, "ls": 0}
    known = {q: {} for q in queue}
    logs = {}

    def V(name, a=None, b=None, s=1, P=128):
        if name in PARTS:
            buf, x, w = PARTS[name]
            return V(buf, x + (a or 0), x + (w if b is None else b), s, P)
        t = T[name]
        if a is None:
            a, b = 0, 512 if name in ROWS else t.shape[-1]
        if name in ROWS:
            ap = t[0:P, a // 256, a % 256:b - a // 256 * 256:s]
        else:
            ap = t[0:P, a:b:s] if s != 1 else t[0:P, a:b]
        return {"ap": ap, "r": [(name, a, b, s)], "n": len(range(a, b, s)), "w": 2 if SCRATCH[name][2] in (_b, _h, _u) else 4}

    def meet(a, b, s, x, y, z):
        return x < b and a < y and (s != z or (a - x) % s == 0)

    def covers(a, b, s, x, y, z):
        return a <= x and y <= b and (s == 1 or (s == z and (a - x) % s == 0))

    def IND(w, o):
        return {"ap": w["ap"].indirect(o["ap"]), "r": w["r"] + o["r"], "n": 16 * o["n"], "w": 4}

    def begin(e, outs, ins, adds=False):
        recs = {}
        for views, wr in ((ins, False), (outs, True)):
            for v in views:
                for n, a, b, s in v["r"]:
                    for (x, y, w, e2, sem, val, clk, z) in logs.get(n, []):
                        if adds and wr and e2 == e and (x, y) == (a, b):
                            continue
                        if (meet(a, b, s, x, y, z) and (wr or w)) or (n in PSUM and e2 != e):
                            if sem not in recs or recs[sem][1] < val:
                                recs[sem] = (sem, val, clk)
        k = known[e]
        for sem, val, clk in sorted(recs.values(), key=lambda z: -len(z[2])):
            if k.get(sem, 0) < val:
                queue[e].wait_ge(T.sem[sem], val)
                k[sem] = val
                for x in clk:
                    if k.get(x, 0) < clk[x]:
                        k[x] = clk[x]

    def done(e, clk, sem, val, outs, ins):
        clk = dict(clk)
        clk[sem] = val
        for views, wr in ((ins, False), (outs, True)):
            for v in views:
                for n, a, b, s in v["r"]:
                    old = [z for z in logs.get(n, []) if not (covers(a, b, s, z[0], z[1], z[7]) and (wr or (not z[2] and z[3] == e)))]
                    logs[n] = old + [(a, b, wr, e, sem, val, clk, s)]

    calls = []
    wrote, read, turn = {}, {}, {}
    tag = [-1, "", 0]

    def part(r, name):
        tag[:] = [r, name, 0]

    def note(e, outs, ins, busy, issue, adds=False, late=0.0, after=(), rows=None):
        me_, pre_ = len(calls), dict(after)
        for views, wr in ((ins, False), (outs, True)):
            for v in views:
                for n, a, b, s in v["r"]:
                    for x, y, z, k in wrote.get(n, []) + (read.get(n, []) if wr else []):
                        if k != me_ and meet(a, b, s, x, y, z):
                            same = adds and wr and calls[k][0] == e and (x, y) == (a, b)
                            pre_[k] = max(pre_.get(k, 0), 0 if same else 1 if calls[k][0] in queue else 2)
                    if n in PSUM:
                        who, now, before = turn.get(n, (e, [], []))
                        if who != e:
                            who, now, before = e, [], now
                        for k in before:
                            pre_[k] = 1
                        if e == "T" and now and now[-1] != me_:
                            pre_[now[-1]] = pre_.get(now[-1], 0)
                        turn[n] = (who, now + [me_], before)
                    if wr:
                        wrote[n] = [q for q in wrote.get(n, []) if not covers(a, b, s, q[0], q[1], q[2])] + [(a, b, s, me_)]
                        read[n] = [q for q in read.get(n, []) if not covers(a, b, s, q[0], q[1], q[2])]
                    else:
                        read.setdefault(n, []).append((a, b, s, me_))
        calls.append((e, busy, late, pre_, issue, rows, tuple(tag)))
        tag[2] += 1
        return me_

    def issue_all():
        n = len(calls)

        def frame(ks):
            at = {k: i for i, k in enumerate(ks)}
            es = sorted(set([calls[k][0] for k in ks]))
            before = [[at[p] for p in calls[k][3] if p in at] for k in ks]
            paced = []
            for s, x in enumerate(PACES):
                paced.append([(es.index(calls[k][0]), [at[p] for p, w in calls[k][3].items() if w and p in at], calls[k][1][s],
                               calls[k][5][s] if calls[k][5] else 0.0, calls[k][2] + (x[2] if calls[k][0] in queue and not calls[k][5] else 0.0)) for k in ks])
            d = paced[0]
            span = [x[2] + x[4] + (PACES[0][4] + x[3] + PACES[0][7] if x[3] else 0.0) for x in d]
            ahead = [[(p, span[p] if p in d[k][1] else d[p][2]) for p in before[k]] for k in range(len(ks))]
            behind = [[] for _ in ks]
            for k in range(len(ks)):
                for p, w in ahead[k]:
                    behind[p].append((k, d[k][2] + w - d[p][2]))
            return before, paced, len(es), ahead, behind, span

        def place(fr, seq, edges, least):
            data = fr[1][0]
            heads, tails, start = [[] for _ in range(fr[2])], [[] for _ in range(fr[2])], [0.0] * len(seq)
            for k in seq:
                e, d, t = data[k][0], data[k][2], least[k]
                for p, w in edges[k]:
                    if start[p] + w > t:
                        t = start[p] + w
                a, b = heads[e], tails[e]
                i = m = len(a)
                if m and b[m - 1] > t:
                    while i and b[i - 1] > t:
                        i -= 1
                    while i < m and a[i] < t + d:
                        if b[i] > t:
                            t = b[i]
                        i += 1
                a.insert(i, t)
                b.insert(i, t + d)
                start[k] = t
            return start

        def forward(fr, rank):
            eff = list(rank)
            for k, ps in enumerate(fr[0]):
                x = eff[k]
                for p in ps:
                    if eff[p] > x:
                        x = eff[p]
                eff[k] = x
            return place(fr, sorted(range(len(eff)), key=lambda k: eff[k]), fr[3], [0.0] * len(eff))

        def replay(fr, seq, s):
            first, woken, data, m = PACES[s][4], PACES[s][7], fr[1][s], len(seq)
            free, moved, last, fin, start, why = [0.0] * fr[2], [0.0] * fr[2], [-1] * fr[2], [0.0] * m, [0.0] * m, [-1] * m
            for k in seq:
                e, pre_, busy, rows, late = data[k]
                t, y = free[e], last[e]
                for p in pre_:
                    if fin[p] > t:
                        t, y = fin[p], p
                start[k], why[k], last[e] = t, y, k
                free[e] = t = t + busy
                if rows:
                    t = moved[e] = max(t + first, moved[e]) + rows
                    t += woken
                fin[k] = t + late
            end = max(fin)
            return end, start, why, fin.index(end)

        seed = [12345]

        def draw():
            seed[0] = seed[0] * 16807 % 2147483647
            return seed[0] / 2147483647.0

        def improve(ks, tries, mid=None):
            fr, m = frame(ks), len(ks)
            busy, chain, before = [x[2] for x in fr[1][0]], [calls[k][6][1][:1] for k in ks], fr[0]
            rest = [fr[5][k] - busy[k] for k in range(m)]
            at = {calls[k][6]: i for i, k in enumerate(ks)}
            like = [at[(mid,) + calls[k][6][1:]] if mid else i for i, k in enumerate(ks)]
            apart = [calls[k][6][0] - mid if mid else 0 for k in ks]
            free = [k for k in range(m) if like[k] == k]

            def tied(rank, paced):
                pace = paced[at[mid + 1, "g0", 0]] - paced[at[mid, "g0", 0]] if mid else 0.0
                return [rank[like[k]] + apart[k] * pace for k in range(m)]

            def latest(rank):
                start = forward(fr, rank)
                back = place(fr, sorted(range(m), key=lambda k: (-start[k], -k)), fr[4], rest)
                return [-back[k] - busy[k] for k in range(m)]

            def value(rank):
                start = forward(fr, rank)
                seq = sorted(range(m), key=lambda k: start[k])
                runs = [replay(fr, seq, s) for s in range(len(PACES))]
                return sum([x[0] * PACES[s][8] for s, x in enumerate(runs)]), rank, runs
            rank = latest(latest(latest(list(range(m)))))
            now = best = value(tied(rank, rank))
            for it in range(tries):
                old = tied(now[2][0][1], now[2][0][1]) if draw() < 0.2 else now[1]
                rank, u = list(old), draw()
                if u < 0.4:
                    _, _, why, z = now[2][int(draw() * len(PACES))]
                    pairs = []
                    while why[z] >= 0:
                        if why[z] not in before[z]:
                            pairs.append((why[z], z))
                        z = why[z]
                    if not pairs:
                        continue
                    a, b = pairs[int(draw() * len(pairs))]
                    by = 400.0 * draw() * draw()
                    if u < 0.2:
                        rank[like[a]] += max(0.0, old[b] - old[a]) + by
                    else:
                        todo, seen, limit = [b], set(), min(old[a], old[b]) - by
                        while todo:
                            k = todo.pop()
                            if k not in seen and old[k] > limit:
                                seen.add(k)
                                rank[like[k]] = old[like[k]] + limit - old[k]
                                todo += before[k]
                else:
                    low, high = min([old[k] for k in free]), max([old[k] for k in free])
                    x, c = low + (high - low) * draw(), "01"[int(2 * draw())]
                    if u < 0.7:
                        wide, by = (500.0, 1000.0, 2000.0, 4000.0)[int(4 * draw())], (200.0, 500.0, 1000.0, 2000.0)[int(4 * draw())]
                    else:
                        wide, by = (1000.0, 3000.0, 8000.0)[int(3 * draw())], 1200.0 * (draw() + draw() + draw() - 1.5)
                    for k in free:
                        if abs(old[k] - x) < wide:
                            rank[k] += by * (draw() - 0.5) if u < 0.7 else by * (chain[k] == c)
                rank = tied(rank, old)
                if u >= 0.4 and draw() < 0.6:
                    rank = latest(rank)
                    rank = tied(rank, rank)
                new = value(rank)
                if new[0] < now[0] + SLACK * draw() * (1.0 - it / tries):
                    now = new
                    if new[0] < best[0]:
                        best = new
            return dict(zip(ks, best[2][0][1]))

        def stage(k):
            r, x, _ = calls[k][6]
            return r - 0.5 * (x in FLOW.split() + ["parents", "first"])

        if n not in FOUND:
            start = improve([k for k in range(n) if 3 <= stage(k) < 5], TRIES[0], 4)
            key = {calls[k][6]: k for k in range(n)}
            pace = start[key[5, "g0", 0]] - start[key[4, "g0", 0]]
            rank = [start[key[(4,) + c[6][1:]]] + (c[6][0] - 4) * pace if 0 < stage(k) < NR - 1 else 0.0 for k, c in enumerate(calls)]
            for low, high, fix, tries in ((-1, 1, (1, "g0", 0), TRIES[1]), (NR - 1.5, NR + 1, (NR - 1, FLOW.split()[-1], 0), TRIES[2])):
                start = improve([k for k in range(n) if low <= stage(k) < high], tries)
                for k in start:
                    if not 0 < stage(k) < NR - 1:
                        rank[k] = start[k] - start[key[fix]] + rank[key[fix]]
            FOUND[n] = rank
        eff = list(FOUND[n])
        for k in range(n):
            eff[k] = max([eff[k]] + [eff[p] for p in calls[k][3]])
        for k in sorted(range(n), key=lambda k: eff[k]):
            calls[k][4]()

    def op(e, outs, ins, call, adds=False, cycles=None, more=0.0):
        def issue():
            begin(e, outs, ins, adds)
            count[e] += 1
            call(queue[e]).then_inc(T.sem["s" + e], 1)
            done(e, known[e], "s" + e, count[e], outs, ins)
        picked = 0
        if cycles is None:
            n = max([v["n"] for v in outs + ins])
            if [v for v in ins if len(v["r"]) > 1]:
                cycles, picked = 60 if e == "V" else 78, outs[0]["n"]
            else:
                cycles = max(64, n / 2 if e == "V" and all([v["w"] == 2 for v in outs + ins]) else n)
        note(e, outs, ins, [(cycles + picked * x[1]) * x[0] + more + 8.0 for x in PACES], issue, adds)

    def dma(e, out, in_, sem):
        def issue():
            begin(e, [out], [in_])
            queue[e].dma_start(out["ap"], in_["ap"]).then_inc(T.sem[sem], 16)
            done("dma" + sem, {}, sem, 16, [out], [in_])
        note(e, [out], [in_], [50.0] * len(PACES), issue, late=LOAD if out["n"] == 1024 else HOP)

    def EXT(ap):
        return {"ap": ap, "r": [], "n": 0, "w": 4}

    def val(s):
        return s["ap"] if isinstance(s, dict) else s

    def vs(*a):
        return [x for x in a if isinstance(x, dict)]

    def ts(out, a, s1, op0, s2=None, op1=None):
        if op1 is None:
            op("V", [out], vs(a, s1), lambda q: q.tensor_scalar(out["ap"], a["ap"], val(s1), None, op0))
        else:
            op("V", [out], vs(a, s1, s2), lambda q: q.tensor_scalar(out["ap"], a["ap"], val(s1), val(s2), op0, op1))

    def tt(out, a, b, o):
        n = out["n"] * (1 if a["r"][0][0] in PSUM else 2)
        op("V", [out], [a, b], lambda q: q.tensor_tensor(out["ap"], a["ap"], b["ap"], o), cycles=None if len(a["r"]) > 1 else max(64, n))

    def cp(out, a):
        op("V", [out], [a], lambda q: q.tensor_copy(out["ap"], a["ap"]))

    def red(out, a, o):
        op("V", [out], [a], lambda q: q.tensor_reduce(out["ap"], a["ap"], AxisListType.X, o), cycles=max(64, a["n"]))

    def fill(out, c):
        op("V", [out], [], lambda q: q.memset(out["ap"], c))

    def scan(out, a, z, first, op0, op1):
        op("V", [out], vs(a, z, first), lambda q: q.tensor_tensor_scan(out["ap"], a["ap"], z["ap"], val(first), op0, op1))

    def act(out, a, f, bias=None, scale=None, acc=None):
        kw = {}
        if bias is not None:
            kw["bias"] = val(bias)
        if scale is not None:
            kw["scale"] = val(scale)
        if acc is not None:
            kw["accum_out"] = acc["ap"]
        op("S", vs(out, acc), vs(a, bias, scale), lambda q: q.activation(out["ap"], a["ap"], f, **kw), more=20.0 * (acc is not None))

    def mms(triples, start=True, stop=True):
        n = len(triples)

        def call(q):
            x = None
            for k, (o, l, r) in enumerate(triples):
                x = q.matmul(o["ap"], l["ap"], r["ap"], start and k == 0, stop and k == n - 1)
            return x
        op("T", [p[0] for p in triples], [v for p in triples for v in p[1:]], call, not start,
           sum([max(min(64, l["n"]), r["n"]) * (4 if r["w"] == 4 else 1) * TENSOR for o, l, r in triples]))

    def mm(out, pairs, start=True, stop=True):
        mms([(out, l, r) for l, r in pairs], start, stop)

    def iota(out, pattern, base, cm=0):
        op("G", [out], [], lambda q: q.iota(out["ap"], pattern, base, cm, allow_small_or_imprecise_dtypes=True), cycles=150 + 2 * out["n"])

    def sel(out, a, pattern, cmp_, base, cm, other=0.0):
        op("G", [out], [a], lambda q: q.affine_select(out["ap"], a["ap"], pattern, cmp_, other, base, cm), cycles=190 + 2 * out["n"])

    def wraps(base, buf, x, w):
        return [(V(base, 15 - i, 143 - i), V(buf, x + i, x + w, 16)) for i in range(16)]

    def fours(base, buf, x, w):
        return [(V(base, 3 - i, 131 - i), V(buf, x + i, x + w, 4)) for i in range(4)]

    def pick(out, a):
        scan(out, V("M4", 0, a["n"]), a, 0.0, O.mult, O.max)

    def times(out, mask, a):
        scan(out, mask, a, 0.0, O.max, O.mult)

    def send(r, s, src, owners):
        buf, wr, w, r0 = MSG[s]
        ins = [V(src(o)[0], src(o)[1], src(o)[1] + w) for o in owners]
        eng = hop_engines(core, hop, topo, s)
        tr = []
        for o in owners:
            d = T.cores[o]
            x = (slot(r) if r0 else r) * wr + me * w
            rid, pid = topo.addr(hop[d], core)
            tr.append(RemoteDMATransfer(dst_ids=[DstId(rid=rid, pnc=pid)], dma_engine_mask=bits(eng[d]),
                                        remote_sem=T.sem["%s%d%s" % (s, r, "f" if o in far else "n")],
                                        src=T[src(o)[0]][:, src(o)[1]:src(o)[1] + w], dst=T[buf][:, x:x + w]))
            count["ls"] += len(eng[d])

        def issue():
            begin("G", [], ins)
            g.remote_dma_fused(tr, local_sem=T.sem.ls)
        kind = "f" if owners[0] in far else "n"
        k = note("G", [], ins, [x[3] for x in PACES], issue, after=sent.get(kind, ()), rows=moving(buf, w))
        sent[kind] = [(k, 0)]
        sent[s + kind] = k

    def moving(buf, w):
        return [16 * (x[5] + x[6] * w * V(buf)["w"]) + FIRST * (tag[0] == 0 and buf == "MB") for x in PACES]

    def arrive(r, s):
        buf, wr, w, r0 = MSG[s]
        for kind, qs in (("n", [q for q in others if q not in far]), ("f", far)):
            n = 0
            for q in qs:
                h = ways(T.cores[q], T, topo)
                n += len(hop_engines(T.cores[q], h, topo, s)[core]) if h[core] == core else len(topo.engines(h[core], core))
            landing(buf, [(slot(r) if r0 else r) * wr + q * w for q in qs], w, "%s%d%s" % (s, r, kind), n, s + kind)

    def landing(buf, xs, w, sem, n, kind):
        def issue():
            logs[buf] = logs.get(buf, []) + [(x, x + w, True, "net", sem, n, {sem: n}, 1) for x in xs]
        outs = [V(buf, x, x + w) for x in xs]
        if kind[1] == "n":
            note(sem, outs, [], [0.0] * len(PACES), issue, after=[(sent[kind], 2)])
        else:
            sent["R"] = [(note("R", outs, [], [x[3] for x in PACES], issue, after=sent.get("R", []) + [(sent[kind], 2)], rows=moving(buf, w)), 0)]

    sent = {}

    others = [o for o in range(4) if o != me]

    dma("Y", V("A", 0, SL), EXT(T.s0[:, :]), "l1")
    dma("S", V("F8I", P=8), EXT(T.f0[:, :]), "l0")
    for q in range(4):
        dma("S" if q % 2 else "Y", V("OPW", q * 1024, q * 1024 + 1024), EXT(T.opr[:, q * 1024:q * 1024 + 1024]), "l%d" % (2 + q))

    def L(k):
        return V("LC", k, k + 1)

    lane, L0, DA_, DB_, FB, WL, T0 = L(0), L(1), L(2), L(3), L(4), L(5), (V("TT", 38, 39), V("TT", 39, 40))
    fill(V("ONE"), 1.0)
    iota(V("LI", 0, 1), [[1, 1]], 0, 1)
    iota(V("LM"), [[1, 16]], 0)
    sel(V("S1"), V("ONE", 0, 144), [[1, 144]], O.is_equal, 1000, 0)
    sel(V("ID"), V("ONE", 0, 128), [[-1, 128]], O.is_equal, 0, 1)
    sel(V("RX", 0, 9), V("ONE", 0, 9), [[-16, 9]], O.is_ge, 0, 1)
    sel(V("BLK"), V("ONE", 0, 128), [[-16, 8], [0, 16]], O.is_ge, 0, 1)
    sel(V("S1", 15, 144, 16), V("RX", 0, 9), [[16, 9]], O.is_ge, 15, -1)
    sel(V("B8", P=8), V("ONE", 0, 144, P=8), [[1, 144]], O.is_equal, -15, -16)
    sel(V("BLK"), V("BLK"), [[16, 8], [0, 16]], O.is_ge, 15, -1)
    for j in range(7):
        iota(V("CJ", j * 32 + 2, j * 32 + 34), [[0, 32]], -4 * KA[j] * KA[j] % 4096)
    iota(V("CJ", 0, 2), [[0, 2]], -4 * KA[6] * KA[6] % 4096 + (KA[7] - KA[6]) * (me % 2 - 2048))
    iota(V("CLF"), [[0, 2], [256, 2]], 0)
    iota(V("KD"), [[0, 2], [16, 8], [0, 16]], 0)
    for i, s in enumerate(STEPS):
        iota(V("CT", 16 * i, 16 * i + 6), [[-s, 3], [0, 2]], s // 2)
        iota(V("CT", 16 * i + 6, 16 * i + 7), [[1, 1]], s + s // 2)
        iota(V("CT", 16 * i + 7, 16 * i + 9), [[-2 * s, 2]], s)
    iota(V("DT"), [[272, 2], [0, 8], [16, 16]], 16)
    act(V("IDN"), V("ID"), F.Copy, scale=-1.0)
    act(V("NUT"), V("BLK"), F.Copy, scale=-1.0)
    sel(V("NUT"), V("NUT"), [[-1, 128]], O.is_gt, 0, 1)
    iota(V("DT", 15, 112, 16), [[0, 7]], 0)
    sel(V("NUT"), V("NUT"), [[-1, 128]], O.not_equal, 0, 1, 128.0)
    iota(V("DT", 127, 256, 16), [[0, 9]], 272)
    for out, a, x in (("IDP", "ID", 4194304.0), ("ID2K", "ID", 4096.0), ("IDF", "ID", 16.0), ("ID16", "ID", 16.0),
                      ("NBH", "BLK", -32768.0), ("NBF", "BLK", -16384.0), ("NBG", "BLK", -16384.0), ("NBD", "BLK", -2048.0), ("BLKH", "BLK", 0.5)):
        act(V(out), V(a), F.Copy, scale=x)
    iota(V("K"), [[0, 2], [1, 128]], 0)
    iota(V("K1"), [[0, 2], [1, 128]], 129)
    iota(V("CO4"), [[-272, 2], [0, 32]], 0)
    iota(V("M4"), [[0, 32], [1, 4]], 0)
    iota(V("S4"), [[0, 144]], 0)
    iota(V("EBW"), [[0, 288]], 0)
    iota(V("CL"), [[16, 32]], 0)
    for k in range(4):
        iota(V("RW", 16 * k, 16 * k + 16), [[1, 16]], (1, 0, -1, 8)[k])
    for k, row in enumerate(({0: 15, 2: 0, 6: 3, 10: 7, 13: 11, 14: 18, 15: 15}, {0: 16},
                             {0: 17, 1: 15, 3: 6, 7: 10, 11: 13, 14: 19, 15: 15}, {0: 3, 1: 4, 2: 5})):
        for i in row:
            iota(V("RW", 16 * k + i, 16 * k + i + 1), [[1, 1]], row[i])

    for i in range(16):
        if i == 6:
            ts(V("LI", 1, 2), V("LI", 0, 1), 15, O.bitwise_and)
        if i == 11:
            cp(lane, V("LI", 1, 2))
        fill(V("RW", 64 + i, 65 + i), float(WT[i]))
    ts(V("LM"), V("LM"), lane, O.is_equal)
    ts(L(10), lane, 0.0, O.is_equal)
    ts(L(11), lane, 1.0, O.is_equal)
    ts(L(18), lane, 2.0, O.is_equal, -1.0, O.mult)
    ts(L(19), lane, 0.5, O.add)
    ts(L(7), lane, 16.0, O.mult)
    tt(V("RX", 64, 80), V("RW", 64, 80), V("LM"), O.mult)
    ts(L(14), L(11), (turn_ - 1.5) / 4096, O.mult)
    ts(L(16), L(11), 16384.0, O.mult)
    ts(V("M2"), V("ONE", 0, 64), L(18), O.mult)
    red(WL, V("RX", 64, 80), O.add)
    ts(L(15), L(10), -1600.0 / 4096, O.mult, L(14), O.add)
    ts(L(17), L(10), 16384.0 * 256, O.mult, L(16), O.add)
    fill(V("ZH", 0, 16), 0.0)
    for c in range(2):
        fill(T0[c], 2.0 * STEPS[0] + off[c])
    ts(V("WM"), V("S1"), WL, O.mult)
    cp(V("LI", 4, 5), WL)
    act(V("CA", 0, 3), V("ONE", 0, 3), F.Identity, scale=L(17))
    ts(V("CA", 3, 4), L(18), -16384.0 * 4096, O.mult, L(17), O.add)
    ts(V("CM"), V("ONE", 0, 16), L(10), O.mult, 1023.0, O.mult)
    act(V("SD"), V("S1"), F.Identity, scale=lane)
    act(V("KD"), V("KD"), F.Identity, bias=L(19))
    iota(V("KD", 15, 256, 16), [[0, 16]], 200)

    def C(k, n=1):
        return V("SV", k, k + n)

    U, U0, U2, LO1, LMW, LMN, THR, MN = [C(k) for k in range(8)]
    CE8, LIM = C(26), (V("TT", 40, 41), V("TT", 41, 42))
    fill(V("CU"), -128.0)
    fill(V("TB"), 0.0)
    fill(U, 1023.0)
    fill(V("TB", 3, 4), 100000.0)
    fill(V("TB", 8, 11), float(EMPTY * SL))
    fill(V("TB", 11, 12), 1.0)

    def consts1():
        ts(V("LI", 5, 6), V("LI", 4, 5), 3, O.bitwise_and)
        ts(V("F8", P=8), V("F8I", P=8), -1023.0, O.add)
        ts(L(6), V("LI", 5, 6), -1.0, O.mult, 1026.0, O.add)
        mm(V("P7", 0, 32), [(V("B8", 15 - i, 143 - i, P=8), V("F8", i, 512, 16, P=8)) for i in range(16)])
        ts(V("XB"), V("S1"), L(6), O.mult, 1.0 / 4096, O.mult)
        ts(V("CLF"), V("CLF"), L(7), O.add)
        ts(V("XBN"), V("S1"), L(6), O.mult, -1.0 / 4096, O.mult)
        act(V("AC", 0, 32), V("P7", 0, 32), F.Copy)

    def consts2():
        act(V("NUTH"), V("NUT"), F.Copy, scale=0.5)
        ts(V("LI", 2, 3), V("LI", 1, 2), 2, O.arith_shift_right)
        cp(L(21), V("LI", 2, 3))
        act(V("S4", 3, 131, 4), V("BLK", 0, 128, 4), F.Copy)
        act(V("S4H"), V("S4"), F.Copy, scale=0.5)
        act(V("S4N"), V("S4"), F.Copy, scale=-1.0)
        act(V("SD4"), V("S4"), F.Identity, scale=lane)
        ts(V("NEG4"), V("M4"), L(21), O.not_equal, -16384.0, O.mult)
        ts(V("M4N"), V("M4", 0, 64), 0.0, O.is_equal, -32768.0, O.mult)
        ts(V("M4"), V("M4"), 0.0, O.is_gt)
        act(V("WMN"), V("WM"), F.Copy, scale=-1.0)
        ts(L(31), L(10), 4096.0 * 192, O.mult)
        ts(L(31), L(11), -2048.0, O.mult, L(31), O.add)
        act(V("MC"), V("BLK"), F.Identity, scale=L(31))
        fill(V("YM", 256, 272), 0.0)
        for h in range(3):
            fill(V("AM", h, 128, 4), 0.0)
        for k in range(2):
            ts(V("CLM", k, k + 1), lane, 16.0, O.mult, 256.0 * k + 12.0, O.add)
        tt(V("CO4"), V("CO4"), V("NEG4", 0, 64), O.add)
        fill(V("CH", 4096, 4112), 0.0)
        for c in range(4):
            fill(V("W", c * 272 + 256, c * 272 + 272), 0.0)
        fill(V("YW", 256, 272), 0.0)
        fill(V("MB", home * 4 + 3, NR * 16, 16), 5000.0)

    def consts3():
        for k in range(4):
            tt(V("RX", 16 * k, 16 * k + 16), V("RW", 16 * k, 16 * k + 16), V("LM"), O.mult)
        for k in range(4):
            red(L(1 + k), V("RX", 16 * k, 16 * k + 16), O.add)
        ts(V("CL"), V("CL"), lane, O.add)
        fill(V("C8", 0, 1), 811.0)
        fill(V("C8", 1, 2), -811.0)
        tt(DB_, DB_, DA_, O.subtract)
        tt(DA_, DA_, L0, O.subtract)

    def counts4():
        iota(V("K13"), [[0, 4], [1, 128]], 129)
        iota(V("KD3"), [[16, 8], [0, 32]], 0)
        iota(V("DT3"), [[0, 8], [1, 32]], 1)
        iota(V("RM"), [[0, 4], [1, 8]], 0)
        sel(V("G8"), V("ONE", 0, 8), [[-16, 8]], O.is_ge, 0, 1)
        sel(V("G8"), V("G8"), [[16, 8]], O.is_ge, 15, -1)

    def consts4():
        fill(V("A", EMPTY * SL, EMPTY * SL + SL), 0.0)
        fill(V("AC", EMPTY * 32, EMPTY * 32 + 32), 0.0)
        ts(V("RM"), V("RM"), 0.0, O.is_gt)
        ts(V("KD3"), V("KD3"), lane, O.add, 0.5, O.add)
        ts(V("SN"), V("S1"), -8192.0, O.mult)
        ts(V("G8F"), V("G8"), 1.0 / 16, O.mult)
        fill(V("A", 10 * SL, 10 * SL + 16), 0.0)
        fill(V("DT3", 31, 256, 32), 0.0)
        fill(V("KD3", 7, 256, 8), 200.0)
        ts(L(24), lane, 3.0, O.is_equal)
        ts(L(25), L(10), L(18), O.subtract)
        ts(L(26), L(11), L(24), O.add, -1.0, O.mult)
        ts(L(28), L(10), 9.0, O.mult, 4.0, O.add)
        ts(L(29), L(11), 11.0, O.mult, L(28), O.add)
        ts(L(30), L(24), 3.0, O.mult, L(29), O.add)
        ts(L(27), L(30), L(18), O.subtract)
        fill(V("C3"), 8192.0)
        fill(V("DB"), 0.0)

    def Q(r, k, n=1):
        return V("TB", r % 2 * 32 + k, r % 2 * 32 + k + n)

    def derived(r):
        act(CE8, Q(r, 14), F.Identity, bias=-0.25 - SHIFT)
        act(V("TJ", 0, 226), V("CJ"), F.Identity, bias=CE8)
        act(LMN, Q(r, 0), F.Identity, bias=LIFT - 1023.0)
        act(LMW, Q(r, 0), F.Identity, bias=-2048.0)
        act(THR, Q(r, 3), F.Identity, bias=-1023.0)
        for c in range(2):
            act(LIM[c], Q(r, 0), F.Identity, bias=1023.0 + off[c], scale=-1.0)
        ts(V("CZ"), V("M2"), LMN, O.mult, L(15), O.add)

    def pre(r):
        act(LO1, Q(r, 0), F.Identity, bias=1.0)
        act(U0, Q(r, 11), F.Identity, bias=U, scale=5000.0)
        act(U2, Q(r, 12), F.Identity, bias=U, scale=-5000.0)
        ts(Q(r, 17), Q(r, 2), 1.0, O.add, Q(r, 3), O.max)
        act(Q(r, 18, 2), V("C8"), F.Identity, bias=Q(r, 14))
        act(Q(r, 8), Q(r, 15), F.Identity, bias=float(slot(r) * SL))

    def level(r):
        B, m = Q(r, 4), MN
        gone, over, last, rt, back, w = [C(k) for k in range(8, 14)]
        red(B, V("MB", r * 16, r * 16 + 16, 2), O.min)
        red(m, V("MB", r * 16 + 1, r * 16 + 16, 2), O.min)
        ts(over, B, LO1, O.max, U0, O.is_ge)
        ts(gone, m, B, O.is_ge, 4000.0, O.mult)
        ts(last, m, B, O.is_lt, Q(r, 12), O.mult)
        tt(Q(r, 16), B, LO1, O.max)
        ts(rt, gone, m, O.max, U2, O.is_ge)
        ts(back, over, last, O.max, DB_, O.mult)
        ts(w, back, DA_, O.add, rt, O.mult)
        ts(V("OFQ", 0, 1), w, L0, O.add)
        ts(C(14), last, -5000.0, O.mult, m, O.add)
        cp(Q(r + 1, 0, 16), IND(Q(r, 0, 24), V("OFQ", 0, 1)))
        ts(U, C(14), 5000.0, O.add, U, O.min)

    def parents(r):
        if r:
            ts(V("OFM"), V("CLM"), Q(r, 7), O.add, 0.25, O.mult)
            ts(V("OFA"), V("CL"), Q(r, 7), O.add)
            ts(V("OFF"), V("CLF"), Q(r, 7), O.add, 1.0 / 16, O.mult)
        derived(r)

    def marks():
        parts = [(V("P1", k * 64, k * 64 + 64), l, x) for k in range(4) for l, x in wraps("WM", "D" if k in TW else "CH", k * 1024, 1024)]
        parts += [(V("P1", k * 64, k * 64 + 64), l, x) for k in TW for l, x in wraps("WMN", "CH", k * 1024, 1024)]
        mm(V("P1", 0, 256), [(V("MC"), V("ONE"))], True, False)
        for k in range(0, len(parts), CHUNK):
            mms(parts[k:k + CHUNK], False, k + CHUNK >= len(parts))
        act(V("MQ"), V("P1", 0, 256), F.Copy)
        tt(V("YM", 0, 256), V("P1", 0, 256), V("MQ"), O.subtract)

    def children(r):
        apart = dict(zip(APART, ("P0", "P1", "P7")))
        par = V("S" if r else "A", 0, 512)
        mz = V("MR", 32, 64) if r else V("AM", 3, 128, 4)

        def J(name, j0, j1=None, w=32):
            return V(name, j0 * w, (j0 + 1 if j1 is None else j1) * w)

        def numbers():
            if r:
                cp(mz, IND(V("AM", 0, (r + 1) * 128), V("OFM")))
            else:
                out = V("P4", 0, 32)
                mm(out, [(V("BLK"), V("CU"))] + wraps("WM", "A", 0, 512))
                ts(V("MR", 0, 32), out, MAGIC * 4096, O.add, MAGIC * 4096, O.subtract)
                tt(V("MR", 32, 64), out, V("MR", 0, 32), O.subtract)
                ts(mz, V("MR", 32, 64), 2048.0 - odd[1], O.add)

        def squares(k):
            for j in (2 * k, 2 * k + 1):
                act(V(("P2", "P3", "P5", "P6")[k], j % 2 * 32, j % 2 * 32 + 32), mz, F.Square, bias=odd[1] / 4 + 2 * KA[min(j, 6)], scale=0.25)
            if k == 3:
                act(V("TJ", 226, 258), mz, F.Identity, bias=V("TJ", 0, 1), scale=float(KA[7] - KA[6]))

        def fetch(h):
            lay = V("A", 0, (r + 1) * SL)
            if r and h < 2:
                v = IND(lay, V("OFA", h * 16, h * 16 + 16))
                if FETCH[h] == "V":
                    cp(V("S", h * 256, h * 256 + 256), v)
                else:
                    act(V("S", h * 256, h * 256 + 256), v, F.Copy)
            elif h == 2:
                for j in apart:
                    mm(V(apart[j]), [(V("IDN"), par)], True, False)

        def whole(k):
            tt(J("VJ", k, w=64), V(("P2", "P3", "P5", "P6")[k], 0, 64), V("TJ", k * 64 + 2, k * 64 + 66), O.add)

        def mod(k):
            ts(J("OFO" if DIRECT else "VK", k, w=64), J("VJ", k, w=64), 4095, O.bitwise_and)

        def offsets(k):
            if not DIRECT:
                cp(J("OFO", k, w=64), J("VK", k, w=64))

        def gather(j):
            tt(J("CH" if j // 2 in TW else "D", j, w=512), IND(V("OPW"), J("OFO", j)), par, O.subtract)

        def other(j):
            act(J("D", j, w=512), IND(V("OPW"), J("OFO", j)), F.Copy)

        def less(j):
            mm(V(apart[j]), [(V("ID"), J("D", j, w=512))], False, True)

        def size(j):
            act(J("CH", j, w=512), V(apart[j]) if j in apart else J("D", j, w=512), F.Abs)

        def Z(k):
            return V(ZB[k][0], ZB[k][1], ZB[k][1] + 64)

        def adds_(x, k, pairs):
            mates = [y for y in FLOW.split() if y[0] in "pnbs" and ZB[int(y[1])][0] == ZB[k][0]]
            mm(Z(k), pairs, x + str(k) == mates[0], x + str(k) == mates[-1])

        def opens(k):
            adds_("p", k, [(V("BLK"), V("CZ"))])

        def above(k):
            adds_("b", k, [(V("ID"), V("FS", 0, 64)), (V("ID"), V("FS", 64, 128))])

        def signed(k):
            adds_("n", k, wraps("XBN", "CH", k * 1024, 1024))

        def sums(k):
            adds_("s", k, wraps("XB", "D" if k in TW else "CH", k * 1024, 1024))

        def twice(j):
            ts(J("D", j, w=512), J("CH", j, w=512), 0.0, O.max, 2.0, O.mult)

        def costs():
            act(V("FS", 0, 64), IND(V("AC", 0, r * 32 + 32), V("OFF")), F.Copy)

        def costs2():
            ts(V("FS", 64, 128), V("FS", 0, 64), THR, O.is_ge, 1023.0, O.mult)

        def keys(a, b):
            z = V(ZB[a // 64][0], ZB[a // 64][1], ZB[a // 64][1] + b - a)
            ts(V("QQ", a, b), z, MAGIC / 1024, O.add, MAGIC / 1024, O.subtract)
            ts(V("YH", a, b), z, 1025.0 + LIFT, O.add, 2048.0, O.min)
            tt(V("DD", a, b), z, V("QQ", a, b), O.subtract)
            ts(V("PEN", a, b), V("YH", a, b), 1024.5, O.is_lt, 8192.0, O.mult)
            base = [(V("ID"), V("YH", a, b)), (V("ID"), V("PEN", a, b))]
            key = V(("P0", "P1", "P2")[PIECES.index((a, b))], a, b)
            mm(key, base[:1], True, False)
            mm(key, [(V("IDP"), V("DD", a, b))], False, False)
            mm(key, base[1:], False, True)
            if XKE[PIECES.index((a, b))] == "V":
                ts(V("XK", a, b), key, -KEY, O.add)
            else:
                act(V("XK", a, b), key, F.Identity, bias=-KEY)
            mm(V("P4", a, b), base)

        numbers()
        if not r:
            consts1()
            ts(V("OFF"), V("CLF"), 1.0 / 16, O.mult)
        do = {"q": squares, "a": fetch, "x": less, "w": whole, "m": mod, "f": offsets, "o": other, "g": gather, "t": twice, "z": size, "s": sums, "p": opens, "n": signed, "b": above,
              "c": lambda k: (costs, costs2)[k](), "k": lambda k: keys(*PIECES[k]), "d": lambda c: cand(c, 0), "e": early}
        for x in FLOW.split():
            part(r, x)
            do[x[0]](int(x[1]))

    def TH(c, i):
        return T0[c] if i == 0 else V("TT", c * 16 + i % 2 * 8 + 5, c * 16 + i % 2 * 8 + 6)

    def cand(c, i):
        x = c * 32 + i % 2 * 16
        if i == 4:
            ts(V("CAND", x, x + 9), V("CT", 16 * i, 16 * i + 9), TH(c, i), O.add, LIM[c], O.min)
            if pos[c][0]:
                act(V("CAND", 64, 71), V("CAND", x, x + 7), F.Identity, bias=rel(c, 0))
        elif i and CANDS[c] == "S":
            act(V("CAND", x, x + 9), V("CT", 16 * i, 16 * i + 9), F.Identity, bias=TH(c, i))
        else:
            ts(V("CAND", x, x + 9), V("CT", 16 * i, 16 * i + 9), TH(c, i), O.add)

    def rel(c, o):
        return 1024.0 * (pos[c][o] - pos[c][1])

    def lowers(c, a, b, at):
        act(V("SG", c * 256 + a, c * 256 + b), V("XK", a, b), F.Sign, bias=0.5 - off[c], acc=V("CN", at + c * 4 + 3, at + c * 4 + 4))
        if pos[c][0]:
            ts(V("DBN", a, b), V("XK", a, b), off[c] - 0.5 + rel(c, 0), O.is_lt, -2.0, O.mult)

    def early(c):
        lowers(c, 0, EARLY, 16)
        signs(c, 0, 0, EARLY, 16)
        below(c, 0, 0, EARLY)

    def bases(c):
        lowers(c, EARLY, 256, 0)
        act(V("BASE", c * 4, c * 4 + 3), V("ONE", 0, 3), F.Identity, scale=V("CN", c * 4 + 3, c * 4 + 4), bias=V("CN", c * 4 + 19, c * 4 + 20))
        if pos[c][0]:
            scan(V("RSB"), V("DBN", 0, 128), V("DBN", 128, 256), 0.0, O.add, O.add)
            act(V("BASE", 8, 11), V("ZH", 0, 3), F.Identity, bias=V("RSB", 127, 128))

    def signs(c, i, a, b, at):
        x = c * 32 + i % 2 * 16
        for k, bias in ((1, TH(c, i)), (0, V("CAND", x + 7, x + 8)), (2, V("CAND", x + 8, x + 9)))[:SHARE[c][i]]:
            y = c * 768 + k * 256
            act(V("DA", y + a, y + b), V("XK", a, b), F.Sign, bias=bias, scale=UNDER, acc=V("CN", at + c * 4 + k, at + c * 4 + k + 1))

    def units(c, i):
        return [(0, 0), (0, 1), (0, 2), (1, 2)][:6 - SHARE[c][i]]

    def below(c, i, a, b):
        for n, (o, k) in enumerate(units(c, i)):
            y = c * 1024 + n * 256
            ts(V("DV", y + a, y + b), V("XK", a, b), TH(c, i), O.subtract, rel(c, o) + (1 - k) * STEPS[i], O.is_lt)

    def tally(c, i, ns):
        for n in ns:
            if n < len(units(c, i)):
                y, x = c * 1024 + n * 256, c * 512 + n * 128
                scan(V("RS", x, x + 128), V("DV", y, y + 128), V("DV", y + 128, y + 256), 0.0, O.add, O.add)

    def opening(c, i):
        p, n = "P%d" % (5 + c), SHARE[c][i]
        mm(V(p, 1, 2 * n, 2), [(V("BLK"), V("CA", 0, n))] + [(V("NBF"), V("CN", 16 + c * 4, 16 + c * 4 + n))] * (i == 0), True, False)
        mm(V(p, 1, 2 * n, 2), [(V("NBG"), V("BASE", c * 4, c * 4 + n))], False, False)
        if n < 3:
            mm(V(p, 5, 6, 2), [(V("BLK"), V("CA", 3, 4)), (V("NBG"), V("BASE", c * 4, c * 4 + 1))], False, False)
        mm(V(p, 0, 6, 2), [(V("BLK"), V("CA", 0, 3))] + [(V("NBG"), V("BASE", 8, 11))] * bool(pos[c][0] and i), False, False)

    def totals(c, i):
        p, n, x = "P%d" % (5 + c), SHARE[c][i], c * 512 + 127
        mine = (V(p, 1, 2 * n, 2), [(V("NBF"), V("CN", c * 4, c * 4 + n))])
        if n < 3:
            mm(*mine, False, False)
        mms([(V(p, 0, 6, 2), V("NBH"), V("RS", x, x + 257, 128))]
            + [(V(p, k, k + 1, 2), V("NBG"), V("RSB", 127, 128)) for k in (0, 2, 4) if pos[c][0] and not i], False, False)
        if n < 3:
            mm(V(p, 5, 6, 2), [(V("NBH"), V("RS", x + 384, x + 385))], False, True)
        else:
            mm(*mine, False, True)

    def decide(c, i):
        x, y = c * 32 + i % 2 * 16, c * 16 + (i + 1) % 2 * 8
        if i == 4 and pos[c][0]:
            scan(V("TT", 32, 38), V("P%d" % (5 + c), 0, 6), V("CAND", 64, 70), V("CAND", 70, 71), O.min, O.max)
        scan(V("TT", y, y + 6), V("P%d" % (5 + c), 0, 6), V("CAND", x, x + 6), V("CAND", x + 6, x + 7), O.min, O.max)

    def step(c, i):
        def count():
            if i:
                cand(c, i)
            else:
                bases(c)
            signs(c, i, 0 if i else EARLY, 256, 0)
            opening(c, i)
            below(c, i, 0 if i else EARLY, 256)
            tally(c, i, (0,))

        def total():
            tally(c, i, (1, 2, 3))
            totals(c, i)

        def choose():
            decide(c, i)
            if not i:
                mm(both(c, 0, 128), [(V("ID2K"), V("KD"))], True, False)
                places0(c)
        return [count, total, choose]

    def least(r):
        act(V("YW", 0, 256), V("P4", 0, 256), F.Identity, bias=LMW)
        scan(V("QQ", 0, 128), V("YW", 0, 128), V("YW", 128, 256), 5000.0, O.min, O.min)
        ts(V("MD"), V("LM"), V("QQ", 127, 128), O.mult, 2047.0, O.min)
        mm(V("P4", 256, 272), [(V("BLK"), V("CM")), (V("BLK"), V("MD"))])
        red(V("MB", r * 16 + home * 4 + 1, r * 16 + home * 4 + 2), V("P4", 256, 272), O.min)

    def lists(r, c):
        def mark_list(c):
            if r == NR - 1:
                return
            x, p, at = c * 256, "P%d" % (2 + c), where(r, "SNM", "AM", 32)
            mm(V(p, 0, 64), [(V("ID"), V("NEG4", 0, 64))], True, False)
            act(V("GV", x, x + 256), IND(V("YM"), V("OFW", c * 16, c * 16 + 16)), F.Identity, bias=odd[c] - 2048.0, scale=-1.0)
            times(V("CGM", x, x + 256), V("OH", x, x + 256), V("GV", x, x + 256))
            mm(V(p, 0, 64), fours("S4N", "CGM", x, 256), False, True)
            for o, n in ((1 - mine, 32), (mine, 32)) if c else ((0, 64),):
                buf, y = at(own[c][o])
                scan(V(buf, y, y + n), V("M4N", 0, n), V(p, o * 32, o * 32 + n), 0.0, O.add, O.max)
            send(r, "m", at, [o for o in own[c] if o != me])
        return [lambda f=f: [x(c) for x in f] for f in ((kept, places1, ranks), (first, ends, first_list, places), (second,),
                                                        (second_list, columns), (third,), (mark_list, third_list))]

    def kept(c):
        x = c * 512
        if pos[c][0]:
            ts(V("KP", x, x + 256), V("XK"), V("TT", 37, 38), O.is_lt, 2.0, O.mult)
        else:
            ts(V("KP", x, x + 256), V("XK"), TH(c, 5), O.subtract, rel(c, 0), O.is_lt)
        act(V("KP", x + 256, x + 512), V("XK"), F.Sign, bias=TH(c, 5), scale=UNDER)

    def lower(c, o):
        return V("SG", c * 256, c * 256 + 256) if o else V("DBN") if pos[c][0] else V("KP", c * 512, c * 512 + 256)

    def both(c, a, b):
        p = "P%d" % (2 + c)
        return {"ap": T[p][:, :, a:b], "r": [(p, 0, 512, 1)], "n": 2 * (b - a), "w": 4}

    def ranks(c):
        x = c * 512
        for o in range(2):
            y = x + o * 256
            scan(V("R", y, y + 256), V("KP", y, y + 256), lower(c, o), 0.0, O.add, O.add)
        mms([(both(c, k * 16, k * 16 + 16), V("NBD"), V("R", x + 15, x + 512, 16)) for k in range(8)], False, True)

    def ends(c):
        x, p = c * 512, "P%d" % (5 + c)
        mm(V(p, 0, 128), [(V("ID"), V("NEG4"))], True, False)
        mm(V(p, 0, 128), fours("S4H", "R", x, 512), False, True)
        for o in range(2):
            y = c * 144 + o * 68
            pick(V("EBW", y, y + 64), V(p, o * 64, o * 64 + 64))

    def PL(c, o):
        return V(("P7", "P0")[c], o * 256, o * 256 + 256)

    def places0(c):
        os_ = [o for o in (1, 0) if o or pos[c][0]]
        for o in os_:
            mm(PL(c, o), [(V("NUTH"), lower(c, o))], o == 1, False)

    def places1(c):
        for o in range(2):
            y = c * 512 + o * 256
            mm(PL(c, o), [(V("NUTH" if o or pos[c][0] else "NUT"), V("KP", y, y + 256))], False, False)

    def places(c):
        for o in range(2):
            y = c * 512 + o * 256
            mm(PL(c, o), [(V("BLKH"), V("R", y, y + 256))], False, o == 1)
        for o in range(2):
            y = c * 544 + o * 272
            act(V("W", y, y + 256), PL(c, o), F.Copy)

    def first(c):
        for o in range(2):
            x = c * 256 + o * 128
            scan(V("V1", x, x + 128), V("P%d" % (2 + c), o * 256, o * 256 + 128), V("DT", o * 128, o * 128 + 128), 272.0 * o, O.max, O.min)

    def first_list(c):
        v1 = V("V1", c * 256 + 14, c * 256 + 256, 16)
        p = "P%d" % (2 + c)
        ts(V("OFB", c * 16, c * 16 + 16), v1, 0.25, O.mult, 3.0, O.add)
        mms([(V(p, 0, 64), V("ID"), V("CO4"))] + [(V(p, h, 64, 4), V("ID"), v1) for h in range(4)], True, False)

    def second(c):
        x = c * 256
        tt(V("IB", x, x + 256), IND(V("EBW", c * 144, c * 144 + 144), V("OFB", c * 16, c * 16 + 16)), V("K"), O.is_le)
        mm(V("P%d" % (2 + c), 0, 64), fours("S4", "IB", x, 256), False, True)

    def second_list(c):
        pick(V("CB", c * 64, c * 64 + 64), V("P%d" % (2 + c), 0, 64))
        cp(V("OFW", c * 16, c * 16 + 16), V("CB", c * 64 + 3, c * 64 + 64, 4))

    def columns(c):
        mm(V("P%d" % (5 + c), 0, 64), [(V("ID"), V("NEG4", 0, 64)), (V("ID16"), V("CB", c * 64, c * 64 + 64))], True, False)

    def third(c):
        x = c * 256
        for o in range(2):
            y, w, k = x + o * 128, c * 544 + o * 272, c * 16 + o * 8
            tt(V("OH", y, y + 128), IND(V("W", w, w + 272), V("OFW", k, k + 8)), V("K1", 0, 128), O.is_equal)
        mm(V("P%d" % (5 + c), 0, 64), fours("SD4", "OH", x, 256), False, True)

    def where(r, buf, stays, w):
        return lambda o: (stays, (slot(r) * 4 + home) * w) if o == me else (buf, (r * 4 + (own[0] + own[1]).index(o)) * w)

    def third_list(c):
        pick(V("MS", c * 64, c * 64 + 64), V("P%d" % (5 + c), 0, 64))
        cp(V("OFN", c * 16, c * 16 + 16), V("MS", c * 64 + 3, c * 64 + 64, 4))

    def states(r, c):
        at = where(r, "SND", "A", 128)
        if PAIR and not c:
            buf, x = at(own[c][0])
            act(V(buf, x, x + 256), IND(V("CH"), V("OFN", 0, 16)), F.Abs)
        for o in sorted(range(2), key=lambda o: (own[c][o] == me, -o)) * (c or not PAIR):
            buf, x = at(own[c][o])
            act(V(buf, x, x + 128), IND(V("CH"), V("OFN", c * 16 + o * 8, c * 16 + o * 8 + 8)), F.Abs)
        send(r, "a", at, [o for o in own[c] if o != me])

    def prices(c):
        x = c * 256
        act(V("GV", 512 + x, 768 + x), IND(V("YW"), V("OFW", c * 16, c * 16 + 16)), F.Copy)
        times(V("CG", x, x + 256), V("OH", x, x + 256), V("GV", 512 + x, 768 + x))

    def price_lists(r, cs):
        at = where(r, "SNC", "AC", 8)
        mm(V("P4", cs[0] * 16, cs[-1] * 16 + 16), wraps("S1", "CG", cs[0] * 256, len(cs) * 256))
        for c in cs:
            for o, n in ((1 - mine, 8), (mine, 8)) if c else ((0, 16),):
                buf, y = at(own[c][o])
                act(V(buf, y, y + n), V("P4", c * 16 + o * 8, c * 16 + o * 8 + n), F.Copy)

    def E(k, n=1):
        return V("EV", k, k + n)

    def older():
        r = NR - 1
        is0, is1, is2 = Q(r, 11), Q(r, 13), Q(r, 12)
        for x, y in ((3, 0), (3, 4), (7, 8), (7, 12)):
            act(E(16 + y, 4), Q(r, x, 4), F.Copy)
        ts(E(0), is2, 2.0, O.mult, is1, O.add)
        ts(E(1), L(25), is0, O.mult, L(27), O.add)
        ts(E(2), L(26), is2, O.mult, E(1), O.add)
        ts(V("OG3", 12, 13), E(2), E(0), O.subtract)
        cp(E(32, 16), IND(E(16, 16), V("OG3", 12, 13)))
        ts(E(3), is0, 64.0, O.mult)
        ts(E(6), is2, 32.0, O.mult)
        ts(E(4), is1, 64.0, O.mult, E(6), O.add)
        ts(E(5), E(6), 32.0, O.add)
        for l in range(3):
            ts(V("OG3", 6 + l * 2, 8 + l * 2), V("CL", 0, 2), E(3 + l), O.add)
        for k, x in enumerate((is0, is1, is2)):
            ts(V("GM", k * 8, k * 8 + 8), V("G8"), x, O.mult)
        tt(V("GM", 24, 32), V("G8"), V("GM", 0, 8), O.subtract)
        tt(V("GM", 32, 40), V("G8"), V("GM", 16, 24), O.subtract)
        fill(E(11), float(slot(r) * SL))
        for t in range(2):
            gaps(t, V("AC", 0, slot(r) * 32), E(34 + t), E(32 + t))

    def gaps(t, costs, bound, at):
        a, b, x, y = t * 32, t * 32 + 32, (t + 1) % 3 * 512, 0 if t == 2 else 512
        d, p = "P%d" % (2 + t % 2), V("P%d" % (t % 2), 0, 32)
        mm(V(d, 0, 256), [(V("ID2K"), V("KD3"))], True, False)
        ts(V("OG3", t * 2, t * 2 + 2), V("CLF", 0, 2), at, O.add, 1.0 / 16, O.mult)
        ts(E(8 + t), bound, -1023.0, O.add)
        ts(V("KP3", a, b), IND(costs, V("OG3", t * 2, t * 2 + 2)), E(8 + t), O.is_lt, 2.0, O.mult)
        act(V("F3", a, b), IND(costs, V("OG3", t * 2, t * 2 + 2)), F.Copy)
        scan(V("R3", a, b), V("RM"), V("KP3", a, b), 0.0, O.mult, O.add)
        mms([(V(d, k * 32, k * 32 + 32), V("NBD"), V("R3", a, b)) for k in range(8)], False, True)
        mm(V("P7", 0, 32), [(V("BLKH"), V("R3", a, b)), (V("NUTH"), V("KP3", a, b))])
        act(V("W3", a, b), V("P7", 0, 32), F.Copy)
        scan(V("V1", y, y + 256), V(d, 0, 256), V("DT3"), 0.0, O.max, O.min)
        for k in range(8):
            cp(V("OF3", a + k, b, 8), V("V1", y + k * 32 + 6, y + k * 32 + 32, 8))
        tt(V("OH", x, x + 512), IND(V("W3", a, b), V("OF3", a, b)), V("K13"), O.is_equal)
        cp(V("V3", a, b), V("OF3", a, b))
        mm(p, [(V("IDF"), V("V3", a, b)), (V("ID"), V("C3"))], True, False)
        mm(p, wraps("SD", "OH", x, 512) + wraps("SN", "OH", x, 512), False, True)
        for z in (0, 256):
            tt(V("CG", x + z, x + z + 256), IND(V("F3", a, b), V("OF3", a + z // 16, a + z // 16 + 16)), V("OH", x + z, x + z + 256), O.mult)
        ts(V("OPF", a, b), p, at, O.add, 10.0 * SL, O.min)
        for l, m in (((0, 3), (1, 0)), ((1, 2), (2, 4)), ((0, 0), (1, 1), (2, 2)))[t]:
            mm(V("P%d" % (4 + l), 0, 512, P=8), [(V("GM", m * 8, m * 8 + 8), V("CG", x, x + 512))], (t, l) in ((0, 0), (0, 1), (1, 2)), t == 2)

    def rnd(r):
        part(r, "parents" if r else "first")
        parents(r)
        children(r)
        mb = r * 16 + home * 4
        if not r:
            part(r, "consts2")
            consts2()

        def bound(c):
            ts(V("MB", mb + 2 * c, mb + 2 * c + 1), TH(c, 5), Q(r, 0), O.add, -off[c], O.add)

        def bounds():
            for c in range(2):
                bound(c)
            send(r, "b", lambda o: ("MB", mb), far)
            send(r, "b", lambda o: ("MB", mb), [o for o in others if o not in far])
            arrive(r, "b")

        work = [[f for i in range(5) for f in step(c, i)] + lists(r, c) for c in range(2)]
        work[1].insert(15, bounds)
        work[1].insert(9, lambda: least(r))
        work[0].insert(18, marks if r < NR - 1 else list)
        if r < NR - 1:
            work[0].append(lambda: states(r, 0))
        work = [[("%d.%d" % (c, k), f) for k, f in enumerate(w)] for c, w in enumerate(work)]
        for c in TURNS + "01" * 24:
            if work[int(c)]:
                x, f = work[int(c)].pop(0)
                part(r, x)
                f()
        if not r:
            part(r, "consts3")
            consts3()
        part(r, "pre")
        pre(r)
        if r < NR - 1:
            part(r, "rest")
            states(r, 1)
            prices(0)
            prices(1)
            price_lists(r, (0, 1))
            send(r, "c", where(r, "SNC", "AC", 8), far)
            send(r, "c", where(r, "SNC", "AC", 8), [o for o in others if o not in far])
            arrive(r, "m")
            arrive(r, "a")
            arrive(r, "c")
        else:
            part(r, "last")
            for c in range(2):
                prices(c)
                price_lists(r, (c,))
                send(r, "c", where(r, "SNC", "AC", 8), [o for o in own[c] if o != me])
            for c in range(2):
                states(r, c)
            older()
            arrive(r, "c")
            arrive(r, "a")
        part(r, "level")
        level(r)
        if r == 0:
            part(r, "consts4")
            counts4()
            consts4()

    for r in range(NR):
        rnd(r)
    part(NR, "end")

    gaps(2, V("AC"), Q(NR - 1, 4), E(11))
    for l in range(2):
        act(V("YF", l * 512, l * 512 + 512, P=8), V("P%d" % (4 + l), 0, 512, P=8), F.Identity, bias=1023.0)
    for l in range(3):
        cp(V("OP3", l * 32, l * 32 + 32), IND(V("OPF"), V("OG3", 6 + l * 2, 8 + l * 2)))
    for l in range(3):
        if l == 2:
            ts(V("YF", 1024, 1536, P=8), V("P6", 0, 512, P=8), 1023.0, O.add)
            dma("Y", EXT(T.yf[:, :]), V("YF", P=8), "o4")
        for h in range(2):
            a = l * 512 + h * 256
            v = IND(V("A"), V("OP3", a // 16, a // 16 + 16))
            if h:
                act(V("YL", a, a + 256), v, F.Copy)
            else:
                cp(V("YL", a, a + 256), v)
        dma("YS"[l // 2], EXT(T.yl[:, l * 512:l * 512 + 512]), V("YL", l * 512, l * 512 + 512), "o%d" % (1 + l))

    ts(C(17), Q(NR, 12), 2.0, O.mult, Q(NR, 13), O.add)
    for x, y, n in ((0, 0, 3), (3, 6, 4)):
        cp(V("DB", y, y + n), Q(NR, x, n))
        act(V("DB", y + n, y + 2 * n), Q(NR, x, n), F.Copy)
    ts(V("OFQ", 0, 1), FB, C(17), O.subtract)
    cp(V("FIN"), IND(V("DB"), V("OFQ", 0, 1)))
    cp(V("FIN", 6, 7), C(17))
    cp(V("FIN", 7, 8), U)
    mm(V("P3", 0, 8, P=8), [(V("G8F"), V("FIN", 0, 8))])
    act(V("YT8", P=8), V("P3", 0, 8, P=8), F.Copy)
    dma("Y", EXT(T.yt[:, :]), V("YT8", P=8), "o0")
    issue_all()
    for k in range(4):
        g.sync.wait_ge(T.sem["o%d" % k], 16)
    for k in range(6):
        g.sync.wait_ge(T.sem["l%d" % k], 16)
    g.scalar.wait_ge(T.sem.o4, 16)
    for e in ("V", "S", "T", "G"):
        g.wait_ge(T.sem["s" + e], count[e])
    g.wait_ge(T.sem.ls, count["ls"])
